import numpy as np
import ml_dtypes


def mxq(x, axis, fmt="e4m3"):
    dtype, down = {"e4m3": (ml_dtypes.float8_e4m3fn, 7), "e5m2": (ml_dtypes.float8_e5m2, 14)}[fmt]
    v = np.moveaxis(np.asarray(x, np.float32).astype(ml_dtypes.bfloat16).astype(np.float64), axis, -1)
    blocks = v.reshape(v.shape[:-1] + (-1, 32))
    amax = np.abs(blocks).max(-1, keepdims=True)
    byte = np.maximum(np.where(amax > 0, np.frexp(amax)[1] - 1 + 127, 0) - down, 1)
    scale = np.exp2(byte - 127.0)
    codes = (blocks / scale).astype(np.float32).astype(dtype).astype(np.float64)
    return np.moveaxis((codes * scale).reshape(v.shape), -1, axis)


WIDE = False


def mx_kscale(k):
    if not WIDE:
        return np.ones(k)
    levels = np.array([10, -10, 5, -5, 0])
    if k % 512:
        return np.exp2(np.random.permutation(np.resize(levels, k // 32))).repeat(32)
    a = np.empty((k // 512, 16))
    for p in range(k // 512):
        a[p, :8] = np.random.permutation(np.resize(levels, 8))
        for g in range(8):
            far = levels[np.abs(levels - a[p, g]) >= 10]
            a[p, g + 8] = far[np.random.randint(len(far))]
    return np.exp2(a.ravel()).repeat(32)


BF16 = ml_dtypes.bfloat16


def bf(x):
    return np.asarray(x, np.float32).astype(BF16)


def f64(x):
    return np.asarray(x).astype(np.float64)

E4M3FN = np.array([(-1.0 if i & 128 else 1.0) * ((1.0 + (i & 7) / 8.0) * 2.0 ** (((i >> 3) & 15) - 7) if i & 120 else (i & 7) * 2.0 ** -9) for i in range(256)])


def e4m3fn_bytes(y):
    return np.clip(np.asarray(y, np.float64), -448.0, 448.0).astype(np.float32).astype(ml_dtypes.float8_e4m3fn).view(np.uint8)


def e4m3fn_values(b):
    return E4M3FN[b]


T, M, N, B = 1024, 1024, 2048, 128


def setup_inputs():
    s, t = mx_kscale(N), mx_kscale(M)
    d = np.exp(0.4 * np.random.standard_normal(N))
    length = np.random.uniform(0.6, 1.6, (M, 1))
    S = length * np.random.standard_normal((M, N)) / np.sqrt(N)
    Y = S * d + 0.3 * length * np.random.standard_normal((M, N)) / np.sqrt(N)
    c = np.sum(S * Y, axis=1)
    store = {}
    for name, X in (("S", S / s), ("Y", Y / t[:, None])):
        scale = (np.abs(X).reshape(M // B, B, N // B, B).max(axis=(1, 3)) / 448.0).astype(np.float32)
        store[name] = e4m3fn_bytes(X / np.repeat(np.repeat(f64(scale), B, axis=0), B, axis=1)), scale
    return {"G": bf(np.random.standard_normal((T, N)) * s),
            "S_bytes": store["S"][0], "S_scale": store["S"][1],
            "Y_bytes": store["Y"][0], "Y_scale": store["Y"][1],
            "c": bf(c / t),
            "h": bf(1.0 / d)}


def reference(G, S_bytes, S_scale, Y_bytes, Y_scale, c, h):
    S = e4m3fn_values(S_bytes) * np.repeat(np.repeat(f64(S_scale), B, axis=0), B, axis=1)
    Y = e4m3fn_values(Y_bytes) * np.repeat(np.repeat(f64(Y_scale), B, axis=0), B, axis=1)
    U = mxq(f64(G), 1, "e4m3") @ mxq(S, 1, "e4m3").T
    A = U / f64(c)
    P = mxq(A, 1, "e4m3") @ mxq(Y, 0, "e4m3")
    return P * f64(h)

@@ -1,0 +1,281 @@
+from contextlib import ExitStack
+
+import concourse.mybir as mybir
+from concourse.masks import make_identity
+
+T, M, N = 1024, 1024, 2048
+FLOPS = 2 * 2 * T * M * N
+
+F32 = mybir.dt.float32
+BF16 = mybir.dt.bfloat16
+U32 = mybir.dt.uint32
+U8 = mybir.dt.uint8
+FP8 = mybir.dt.float8_e4m3fn
+FP8X4 = mybir.dt.float8_e4m3fn_x4
+MULT = mybir.AluOpType.mult
+COPY = mybir.ActivationFunctionType.Copy
+
+P = 128
+TC = 256
+NCH = T // TC
+
+PSUM_TAG = {"turn": "turn", "first": "acc", "second": "acc"}
+PSUM_BUFS = {"turn": 4, "acc": 4}
+S_ON_SCALAR = ()
+Y_ON_VECTOR = ()
+A_BUFS = 4
+Y_BUFS = 3
+RES_BUFS = 6
+ORDER = [
+    ("load_small",), ("pick_scales",), ("load_s", 1), ("load_g", 0), ("load_s", 0), ("load_g", 1), ("WS", 1), ("TS", 1),
+    ("WS", 0), ("ES", 1), ("TG", 0, 1), ("load_s", 4), ("TS", 0), ("load_s", 3), ("EG", 0, 1), ("ES", 0),
+    ("load_y", 1, 0), ("load_g", 2), ("TG", 0, 0), ("WS", 3), ("TS", 3), ("EG", 0, 0), ("load_y", 0, 0), ("load_c",),
+    ("IY", 0, 1), ("ES", 3), ("load_g", 3), ("TG", 1, 0), ("WS", 4), ("invert_c",), ("QG", 0, 1), ("TG", 1, 1),
+    ("load_s", 2), ("WY", 0, 1), ("QS", 1), ("load_g", 4), ("WS", 2), ("QS", 0), ("load_s", 5), ("EG", 1, 0),
+    ("QG", 0, 0), ("load_g", 5), ("IY", 1, 0), ("EG", 1, 1), ("load_s", 6), ("TS", 2), ("QG", 1, 1), ("load_y", 0, 1),
+    ("TS", 4), ("ES", 2), ("QS", 3), ("load_g", 7), ("QY", 0, 1), ("QS", 2), ("load_h",), ("IY", 0, 0),
+    ("load_s", 7), ("ES", 4), ("TG", 2, 1), ("WS", 5), ("load_g", 6), ("WS", 6), ("QG", 1, 0), ("EG", 2, 1),
+    ("M1", 0, 0), ("M1", 0, 1), ("TG", 2, 0), ("QS", 4), ("WY", 1, 0), ("load_y", 1, 1), ("EU", 0, 0), ("TS", 6),
+    ("WY", 0, 0), ("QG", 2, 1), ("M1", 1, 1), ("IY", 1, 1), ("EG", 2, 0), ("ES", 6), ("TG", 3, 0), ("TS", 5),
+    ("EU", 0, 1), ("QG", 2, 0), ("WS", 7), ("M1", 1, 0), ("IA", 0, 0), ("ES", 5), ("M1", 2, 1), ("QS", 5),
+    ("EG", 3, 0), ("EU", 1, 0), ("TS", 7), ("TG", 3, 1), ("IY", 2, 0), ("QY", 0, 0), ("M1", 2, 0), ("IY", 2, 1),
+    ("QA", 0, 0), ("QY", 1, 0), ("EU", 1, 1), ("QS", 6), ("M1", 0, 2), ("EU", 2, 1), ("ES", 7), ("EG", 3, 1),
+    ("QS", 7), ("M1", 1, 2), ("M1", 1, 3), ("IA", 1, 0), ("EU", 2, 0), ("M1", 0, 3), ("EU", 1, 2), ("QG", 3, 0),
+    ("IA", 2, 0), ("EU", 0, 2), ("QA", 1, 0), ("EU", 1, 3), ("M1", 2, 3), ("QA", 2, 0), ("IA", 1, 1), ("EU", 0, 3),
+    ("WY", 1, 1), ("EU", 2, 3), ("QA", 1, 1), ("M2", 2, 0), ("IA", 0, 1), ("M1", 2, 2), ("QA", 0, 1), ("EU", 2, 2),
+    ("QG", 3, 1), ("M1", 3, 1), ("M2", 1, 0), ("FO", 2, 0), ("EU", 3, 1), ("IY", 3, 0), ("M2", 3, 0), ("WY", 2, 0),
+    ("QY", 1, 1), ("IA", 2, 1), ("M1", 3, 0), ("FO", 1, 0), ("EU", 3, 0), ("QA", 2, 1), ("M2", 1, 1), ("M1", 3, 3),
+    ("FO", 3, 0), ("FO", 1, 1), ("M2", 5, 0), ("IY", 3, 1), ("M2", 5, 1), ("M2", 0, 0), ("EU", 3, 3), ("IA", 3, 0),
+    ("M2", 0, 1), ("FO", 5, 0), ("WY", 2, 1), ("M1", 3, 2), ("QY", 2, 0), ("FO", 0, 0), ("EU", 3, 2), ("FO", 5, 1),
+    ("FO", 0, 1), ("QY", 2, 1), ("M2", 3, 1), ("M2", 2, 1), ("WY", 3, 1), ("WY", 3, 0), ("FO", 3, 1), ("M2", 4, 0),
+    ("IA", 3, 1), ("QA", 3, 0), ("QA", 3, 1), ("M2", 5, 2), ("FO", 2, 1), ("FO", 4, 0), ("M2", 4, 1), ("FO", 5, 2),
+    ("M2", 6, 0), ("M2", 0, 2), ("FO", 6, 0), ("FO", 4, 1), ("M2", 7, 0), ("FO", 0, 2), ("QY", 3, 1), ("M2", 6, 1),
+    ("M2", 1, 2), ("FO", 7, 0), ("M2", 2, 2), ("FO", 6, 1), ("M2", 7, 1), ("FO", 1, 2), ("M2", 4, 2), ("M2", 6, 2),
+    ("FO", 2, 2), ("FO", 7, 1), ("QY", 3, 0), ("M2", 1, 3), ("M2", 3, 2), ("FO", 4, 2), ("M2", 5, 3), ("FO", 6, 2),
+    ("FO", 1, 3), ("FO", 3, 2), ("FO", 5, 3), ("M2", 6, 3), ("FO", 6, 3), ("M2", 7, 2), ("M2", 2, 3), ("FO", 7, 2),
+    ("M2", 3, 3), ("FO", 2, 3), ("M2", 0, 3), ("FO", 3, 3), ("M2", 7, 3), ("M2", 4, 3), ("FO", 0, 3), ("FO", 7, 3),
+    ("FO", 4, 3),
+]
+
+
+def tile_curvature_scaled_pair_correction_d7_kernel(tc, G, S_bytes, S_scale, Y_bytes, Y_scale, c, h, out):
+    nc = tc.nc
+    with ExitStack() as ctx:
+        keep = ctx.enter_context(tc.tile_pool(name="keep", bufs=1))
+        work = ctx.enter_context(tc.tile_pool(name="work", bufs=3))
+        psum = ctx.enter_context(tc.psum_pool(name="psum", bufs=1))
+        ctx.enter_context(tc.manual_schedule())
+
+        ident = keep.tile([P, P], F32, name="ident")
+        make_identity(nc, ident[:])
+
+        tables = keep.tile([P, 2, 8 * 16], F32, name="tables")
+        scale = keep.tile([P, 2, 2, 16], F32, name="scale")
+        c_bf = keep.tile([P, 2, 4], BF16, name="c_bf")
+        c_inv = keep.tile([P, 8], F32, name="c_inv")
+        h_all = keep.tile([P, N], BF16, name="h_all")
+
+        s_codes = keep.tile([P, 8, 4, P], U32, name="s_codes", align_bytes=64)
+        s_scales = keep.tile([P, 8, 4, P], U8, name="s_scales", align_bytes=64)
+        g_codes = keep.tile([P, NCH, 4, TC], U32, name="g_codes", align_bytes=64)
+        g_scales = keep.tile([P, NCH, 4, TC], U8, name="g_scales", align_bytes=64)
+        a_codes = keep.tile([P, NCH, 2, TC], U32, name="a_codes", align_bytes=64)
+        a_scales = keep.tile([P, NCH, 2, TC], U8, name="a_scales", align_bytes=64)
+        y_codes = keep.tile([P, 4, 2, 512], U32, name="y_codes", align_bytes=64)
+        y_scales = keep.tile([P, 4, 2, 512], U8, name="y_scales", align_bytes=64)
+
+        s_rows = S_bytes.rearrange("(half r j) n -> half j r n", half=2, j=4)
+        y_rows = Y_bytes.rearrange("(half p j) n -> half p j n", half=2, j=4)
+        tiles = {}
+
+        def bank(kind, shape):
+            t = psum.tile(shape, F32, name="bank", tag=PSUM_TAG[kind], bufs=PSUM_BUFS[PSUM_TAG[kind]])
+            return t
+
+        def load_small():
+            nc.sync.dma_start(out=tables[:, 0, :], in_=S_scale.rearrange("a b -> (a b)").partition_broadcast(P))
+            nc.sync.dma_start(out=tables[:, 1, :], in_=Y_scale.rearrange("a b -> (a b)").partition_broadcast(P))
+
+        def load_c():
+            nc.sync.dma_start(out=c_bf[:], in_=c.rearrange("(half p j) -> p half j", half=2, j=4))
+
+        def pick_scales():
+            for q in range(4):
+                rows = slice(32 * q, 32 * q + 32)
+                src = tables[rows].rearrange("p w (half q k) -> p w half q k", half=2, q=4)
+                nc.scalar.activation(out=scale[rows], in_=src[:, :, :, q, :], func=COPY)
+
+        def invert_c():
+            nc.vector.reciprocal(out=c_inv[:], in_=c_bf[:].rearrange("p a b -> p (a b)"))
+
+        def load_h():
+            nc.sync.dma_start(out=h_all[:], in_=h.partition_broadcast(P))
+
+        def load_s(u):
+            t = keep.tile([P, N], U8, name="s_raw%d" % u)
+            nc.sync.dma_start(out=t[:], in_=s_rows[u // 4, u % 4])
+            tiles["s_raw", u] = t
+
+        def load_g(tt):
+            t = keep.tile([P, N], BF16, name="g_raw%d" % tt)
+            nc.sync.dma_start(out=t[:], in_=G[tt * P : (tt + 1) * P, :])
+            tiles["g_raw", tt] = t
+
+        def load_y(half, side):
+            t = keep.tile([P, 4, 1024], U8, name="y_raw%d%d" % (half, side))
+            nc.sync.dma_start(out=t[:], in_=y_rows[half][:, :, side * 1024 : (side + 1) * 1024])
+            tiles["y_raw", half, side] = t
+
+        def widen_s(u):
+            raw = tiles["s_raw", u]
+            wide = work.tile([P, N], BF16, name="s_wide", bufs=3)
+            tiles["s_wide", u] = wide
+            split = wide[:].rearrange("r (g u p e) -> r g p u e", g=4, u=2, e=2)
+            for kb in [4 * g + q for q in range(4) for g in range(4)]:
+                src = raw[:, kb * P : (kb + 1) * P].bitcast(FP8)
+                col = scale[:, 0, u // 4, kb : kb + 1]
+                if u in S_ON_SCALAR:
+                    nc.scalar.activation(out=wide[:, kb * P : (kb + 1) * P], in_=src, func=COPY, scale=col)
+                else:
+                    g, q = divmod(kb, 4)
+                    nc.vector.tensor_scalar(
+                        out=split[:, g, 32 * q : 32 * q + 32],
+                        in0=src.rearrange("r (p u e) -> r p u e", u=2, e=2),
+                        scalar1=col, scalar2=None, op0=MULT,
+                    )
+
+        def turn_s(u):
+            words = tiles["s_wide", u][:].bitcast(F32)
+            for b in range(2):
+                t = bank("turn", [P, 2, 2, P])
+                tiles["s_bank", u, b] = t
+                for gi in range(2):
+                    g = 2 * b + gi
+                    for w in range(2):
+                        if u in S_ON_SCALAR:
+                            src = words[:, 256 * g + w : 256 * (g + 1) : 2]
+                        else:
+                            src = words[:, 256 * g + P * w : 256 * g + P * (w + 1)]
+                        nc.tensor.transpose(t[:, w, gi, :], src, ident[:])
+
+        def empty_s(u):
+            st = work.tile([P, 2, 256, 2], F32, name="s_turned", bufs=3, align_bytes=64)
+            tiles["s_turned", u] = st
+            for b in range(2):
+                nc.scalar.copy(out=st[:, b], in_=tiles["s_bank", u, b][:].rearrange("p w g r -> p (g r) w"))
+
+        def quant_s(u):
+            nc.vector.quantize_mx(
+                out=s_codes[:, u].rearrange("p g r -> p (g r)").bitcast(FP8X4),
+                scales=s_scales[:, u].rearrange("p g r -> p (g r)"),
+                in_=tiles["s_turned", u][:].rearrange("p b x w -> p (b x w)").bitcast(BF16),
+            )
+
+        def turn_g(ch, b):
+            for g in (2 * b, 2 * b + 1):
+                t = bank("turn", [P, 2, 2, P])
+                tiles["g_bank", ch, g] = t
+                for i in range(2):
+                    words = tiles["g_raw", 2 * ch + i][:].bitcast(F32)
+                    for w in range(2):
+                        nc.tensor.transpose(t[:, w, i, :], words[:, 256 * g + w : 256 * (g + 1) : 2], ident[:])
+
+        def empty_g(ch, b):
+            st = work.tile([P, 2, TC, 2], F32, name="g_turned", bufs=3, align_bytes=64)
+            tiles["g_turned", ch, b] = st
+            for gi in range(2):
+                nc.scalar.copy(out=st[:, gi], in_=tiles["g_bank", ch, 2 * b + gi][:].rearrange("p w i r -> p (i r) w"))
+
+        def quant_g(ch, b):
+            nc.vector.quantize_mx(
+                out=g_codes[:, ch, 2 * b : 2 * b + 2].rearrange("p g t -> p (g t)").bitcast(FP8X4),
+                scales=g_scales[:, ch, 2 * b : 2 * b + 2].rearrange("p g t -> p (g t)"),
+                in_=tiles["g_turned", ch, b][:].rearrange("p g t w -> p (g t w)").bitcast(BF16),
+            )
+
+        def first_product(ch, pair):
+            t = bank("first", [P, 2, TC])
+            tiles["u_bank", ch, pair] = t
+            for i in range(2):
+                u = 2 * pair + i
+                for g in range(4):
+                    nc.tensor.matmul_mx(
+                        out=t[:, i, :],
+                        lhsT=s_codes[:, u, g, :].bitcast(FP8X4), lhsT_scale=s_scales[:, u, g, :],
+                        rhs=g_codes[:, ch, g, :].bitcast(FP8X4), rhs_scale=g_scales[:, ch, g, :],
+                        start=(g == 0), stop=(g == 3),
+                    )
+
+        def empty_u(ch, pair):
+            half = pair // 2
+            if ("a_planes", ch, half) not in tiles:
+                tiles["a_planes", ch, half] = work.tile([P, 4, TC], BF16, name="a_planes", bufs=A_BUFS)
+            planes = tiles["a_planes", ch, half]
+            for i in range(2):
+                u = 2 * pair + i
+                nc.scalar.activation(out=planes[:, u % 4, :], in_=tiles["u_bank", ch, pair][:, i, :], func=COPY, scale=c_inv[:, u : u + 1])
+
+        def weave_a(ch, half):
+            woven = work.tile([P, TC * 4], BF16, name="a_woven", bufs=2, align_bytes=64)
+            tiles["a_woven", ch, half] = woven
+            nc.vector.tensor_copy(
+                out=woven[:].rearrange("p (x i j) -> p x j i", i=4, j=4),
+                in_=tiles["a_planes", ch, half][:].rearrange("p j (x i) -> p x j i", i=4),
+            )
+
+        def quant_a(ch, half):
+            nc.vector.quantize_mx(out=a_codes[:, ch, half, :].bitcast(FP8X4), scales=a_scales[:, ch, half, :], in_=tiles["a_woven", ch, half][:])
+
+        def weave_y(nb, half):
+            woven = work.tile([P, 2048], U8, name="y_woven", bufs=Y_BUFS)
+            tiles["y_woven", nb, half] = woven
+            raw = tiles["y_raw", half, nb // 2][:, :, (nb % 2) * 512 : (nb % 2 + 1) * 512]
+            nc.vector.tensor_copy(
+                out=woven[:].rearrange("p (x i j) -> p x j i", i=4, j=4),
+                in_=raw.rearrange("p j (x i) -> p x j i", i=4),
+            )
+
+        def widen_y(nb, half):
+            wide = work.tile([P, 2048], BF16, name="y_wide", bufs=3, align_bytes=64)
+            tiles["y_wide", nb, half] = wide
+            for b in range(4):
+                cols = slice(512 * b, 512 * (b + 1))
+                src = tiles["y_woven", nb, half][:, cols].bitcast(FP8)
+                col = scale[:, 1, half, 4 * nb + b : 4 * nb + b + 1]
+                if (nb, half) in Y_ON_VECTOR:
+                    nc.vector.tensor_scalar(out=wide[:, cols], in0=src, scalar1=col, scalar2=None, op0=MULT)
+                else:
+                    nc.scalar.activation(out=wide[:, cols], in_=src, func=COPY, scale=col)
+
+        def quant_y(nb, half):
+            nc.vector.quantize_mx(out=y_codes[:, nb, half, :].bitcast(FP8X4), scales=y_scales[:, nb, half, :], in_=tiles["y_wide", nb, half][:])
+
+        def second_product(tt, nb):
+            t = bank("second", [P, 512])
+            tiles["p_bank", tt, nb] = t
+            ch, i = divmod(tt, TC // P)
+            for half in range(2):
+                nc.tensor.matmul_mx(
+                    out=t[:],
+                    lhsT=a_codes[:, ch, half, i * P : (i + 1) * P].bitcast(FP8X4), lhsT_scale=a_scales[:, ch, half, i * P : (i + 1) * P],
+                    rhs=y_codes[:, nb, half, :].bitcast(FP8X4), rhs_scale=y_scales[:, nb, half, :],
+                    start=(half == 0), stop=(half == 1),
+                )
+
+        def finish(tt, nb):
+            res = work.tile([P, 512], F32, name="res", bufs=RES_BUFS)
+            cols = slice(512 * nb, 512 * (nb + 1))
+            nc.vector.tensor_tensor(out=res[:], in0=tiles["p_bank", tt, nb][:], in1=h_all[:, cols], op=MULT)
+            nc.sync.dma_start(out=out[tt * P : (tt + 1) * P, cols], in_=res[:])
+
+        jobs = {
+            "load_small": load_small, "load_c": load_c, "pick_scales": pick_scales, "invert_c": invert_c, "load_h": load_h,
+            "load_s": load_s, "load_g": load_g, "load_y": load_y,
+            "WS": widen_s, "TS": turn_s, "ES": empty_s, "QS": quant_s,
+            "TG": turn_g, "EG": empty_g, "QG": quant_g,
+            "M1": first_product, "EU": empty_u, "IA": weave_a, "QA": quant_a,
+            "IY": weave_y, "WY": widen_y, "QY": quant_y, "M2": second_product, "FO": finish,
+        }
+        for entry in ORDER:
+            job, args = jobs[entry[0]], entry[1:]
+            job(*args)

@@ -21,40 +21,41 @@ NCH = T // TC
 
 PSUM_TAG = {"turn": "turn", "first": "acc", "second": "acc"}
 PSUM_BUFS = {"turn": 4, "acc": 4}
-S_ON_SCALAR = ()
+S_ON_SCALAR = (0, 0, 0, 0, 0, 0, 0, 0)
 Y_ON_VECTOR = ()
-A_BUFS = 4
-Y_BUFS = 3
-RES_BUFS = 6
+WARM = (4, 4)
+A_BUFS = 6
+Y_BUFS = 6
+RES_BUFS = 8
 ORDER = [
-    ("load_small",), ("pick_scales",), ("load_s", 1), ("load_g", 0), ("load_s", 0), ("load_g", 1), ("WS", 1), ("TS", 1),
-    ("WS", 0), ("ES", 1), ("TG", 0, 1), ("load_s", 4), ("TS", 0), ("load_s", 3), ("EG", 0, 1), ("ES", 0),
-    ("load_y", 1, 0), ("load_g", 2), ("TG", 0, 0), ("WS", 3), ("TS", 3), ("EG", 0, 0), ("load_y", 0, 0), ("load_c",),
-    ("IY", 0, 1), ("ES", 3), ("load_g", 3), ("TG", 1, 0), ("WS", 4), ("invert_c",), ("QG", 0, 1), ("TG", 1, 1),
-    ("load_s", 2), ("WY", 0, 1), ("QS", 1), ("load_g", 4), ("WS", 2), ("QS", 0), ("load_s", 5), ("EG", 1, 0),
-    ("QG", 0, 0), ("load_g", 5), ("IY", 1, 0), ("EG", 1, 1), ("load_s", 6), ("TS", 2), ("QG", 1, 1), ("load_y", 0, 1),
-    ("TS", 4), ("ES", 2), ("QS", 3), ("load_g", 7), ("QY", 0, 1), ("QS", 2), ("load_h",), ("IY", 0, 0),
-    ("load_s", 7), ("ES", 4), ("TG", 2, 1), ("WS", 5), ("load_g", 6), ("WS", 6), ("QG", 1, 0), ("EG", 2, 1),
-    ("M1", 0, 0), ("M1", 0, 1), ("TG", 2, 0), ("QS", 4), ("WY", 1, 0), ("load_y", 1, 1), ("EU", 0, 0), ("TS", 6),
-    ("WY", 0, 0), ("QG", 2, 1), ("M1", 1, 1), ("IY", 1, 1), ("EG", 2, 0), ("ES", 6), ("TG", 3, 0), ("TS", 5),
-    ("EU", 0, 1), ("QG", 2, 0), ("WS", 7), ("M1", 1, 0), ("IA", 0, 0), ("ES", 5), ("M1", 2, 1), ("QS", 5),
-    ("EG", 3, 0), ("EU", 1, 0), ("TS", 7), ("TG", 3, 1), ("IY", 2, 0), ("QY", 0, 0), ("M1", 2, 0), ("IY", 2, 1),
-    ("QA", 0, 0), ("QY", 1, 0), ("EU", 1, 1), ("QS", 6), ("M1", 0, 2), ("EU", 2, 1), ("ES", 7), ("EG", 3, 1),
-    ("QS", 7), ("M1", 1, 2), ("M1", 1, 3), ("IA", 1, 0), ("EU", 2, 0), ("M1", 0, 3), ("EU", 1, 2), ("QG", 3, 0),
-    ("IA", 2, 0), ("EU", 0, 2), ("QA", 1, 0), ("EU", 1, 3), ("M1", 2, 3), ("QA", 2, 0), ("IA", 1, 1), ("EU", 0, 3),
-    ("WY", 1, 1), ("EU", 2, 3), ("QA", 1, 1), ("M2", 2, 0), ("IA", 0, 1), ("M1", 2, 2), ("QA", 0, 1), ("EU", 2, 2),
-    ("QG", 3, 1), ("M1", 3, 1), ("M2", 1, 0), ("FO", 2, 0), ("EU", 3, 1), ("IY", 3, 0), ("M2", 3, 0), ("WY", 2, 0),
-    ("QY", 1, 1), ("IA", 2, 1), ("M1", 3, 0), ("FO", 1, 0), ("EU", 3, 0), ("QA", 2, 1), ("M2", 1, 1), ("M1", 3, 3),
-    ("FO", 3, 0), ("FO", 1, 1), ("M2", 5, 0), ("IY", 3, 1), ("M2", 5, 1), ("M2", 0, 0), ("EU", 3, 3), ("IA", 3, 0),
-    ("M2", 0, 1), ("FO", 5, 0), ("WY", 2, 1), ("M1", 3, 2), ("QY", 2, 0), ("FO", 0, 0), ("EU", 3, 2), ("FO", 5, 1),
-    ("FO", 0, 1), ("QY", 2, 1), ("M2", 3, 1), ("M2", 2, 1), ("WY", 3, 1), ("WY", 3, 0), ("FO", 3, 1), ("M2", 4, 0),
-    ("IA", 3, 1), ("QA", 3, 0), ("QA", 3, 1), ("M2", 5, 2), ("FO", 2, 1), ("FO", 4, 0), ("M2", 4, 1), ("FO", 5, 2),
-    ("M2", 6, 0), ("M2", 0, 2), ("FO", 6, 0), ("FO", 4, 1), ("M2", 7, 0), ("FO", 0, 2), ("QY", 3, 1), ("M2", 6, 1),
-    ("M2", 1, 2), ("FO", 7, 0), ("M2", 2, 2), ("FO", 6, 1), ("M2", 7, 1), ("FO", 1, 2), ("M2", 4, 2), ("M2", 6, 2),
-    ("FO", 2, 2), ("FO", 7, 1), ("QY", 3, 0), ("M2", 1, 3), ("M2", 3, 2), ("FO", 4, 2), ("M2", 5, 3), ("FO", 6, 2),
-    ("FO", 1, 3), ("FO", 3, 2), ("FO", 5, 3), ("M2", 6, 3), ("FO", 6, 3), ("M2", 7, 2), ("M2", 2, 3), ("FO", 7, 2),
-    ("M2", 3, 3), ("FO", 2, 3), ("M2", 0, 3), ("FO", 3, 3), ("M2", 7, 3), ("M2", 4, 3), ("FO", 0, 3), ("FO", 7, 3),
-    ("FO", 4, 3),
+    ("load_small",), ("SS",), ("pick_scales",), ("load_s", 0), ("WS", 0), ("load_h",), ("load_s", 2), ("load_s", 1),
+    ("load_g", 0), ("load_g", 1), ("load_s", 3), ("load_s", 4), ("load_g", 4), ("load_y", 0, 0), ("load_g", 5), ("load_g", 2),
+    ("load_c",), ("load_g", 3), ("load_s", 6), ("load_s", 5), ("load_g", 6), ("load_g", 7), ("load_y", 1, 0), ("load_s", 7),
+    ("load_y", 1, 1), ("load_y", 0, 1), ("W", 0), ("TS", 0), ("TG", 0, 0), ("WS", 1), ("WS", 2), ("ES", 0),
+    ("TS", 1), ("W", 1), ("SH", 0), ("ES", 1), ("EG", 0, 0), ("TG", 0, 1), ("TS", 2), ("WS", 4),
+    ("EH", 0), ("EG", 0, 1), ("ES", 2), ("WS", 3), ("QG", 0, 0), ("QS", 0), ("QG", 0, 1), ("TG", 2, 0),
+    ("EG", 2, 0), ("QS", 1), ("QS", 2), ("QG", 2, 0), ("SH", 1), ("TG", 2, 1), ("EG", 2, 1), ("QG", 2, 1),
+    ("WS", 5), ("TG", 1, 0), ("EG", 1, 0), ("TS", 4), ("QG", 1, 0), ("invert_c",), ("IY", 0, 0), ("TG", 1, 1),
+    ("ES", 4), ("EH", 1), ("EG", 1, 1), ("TG", 3, 1), ("TS", 5), ("EG", 3, 1), ("WY", 0, 0), ("ES", 5),
+    ("M1", 2, 0), ("M1", 0, 0), ("TS", 3), ("ES", 3), ("QG", 1, 1), ("IY", 0, 1), ("QS", 4), ("WS", 6),
+    ("WS", 7), ("QS", 5), ("TS", 6), ("TG", 3, 0), ("M1", 2, 2), ("ES", 6), ("EG", 3, 0), ("QS", 3),
+    ("M1", 0, 1), ("TS", 7), ("EU", 0, 0), ("EU", 2, 0), ("EU", 2, 2), ("ES", 7), ("M1", 2, 1), ("EU", 2, 1),
+    ("EU", 0, 1), ("M1", 1, 1), ("EU", 1, 1), ("WY", 0, 1), ("IY", 3, 0), ("QS", 6), ("IY", 1, 0), ("QG", 3, 0),
+    ("QG", 3, 1), ("QS", 7), ("IY", 3, 1), ("IY", 1, 1), ("IA", 0, 0), ("IA", 2, 0), ("M1", 1, 0), ("M1", 0, 2),
+    ("M1", 1, 3), ("M1", 0, 3), ("EU", 1, 0), ("M1", 2, 3), ("EU", 0, 2), ("EU", 0, 3), ("M1", 1, 2), ("EU", 2, 3),
+    ("EU", 1, 3), ("WY", 1, 0), ("QA", 0, 0), ("QA", 2, 0), ("M1", 3, 0), ("QY", 0, 0), ("IA", 1, 0), ("IA", 0, 1),
+    ("QA", 1, 0), ("QA", 0, 1), ("M1", 3, 2), ("EU", 1, 2), ("EU", 3, 2), ("M1", 3, 3), ("EU", 3, 0), ("IA", 2, 1),
+    ("IY", 2, 0), ("IY", 2, 1), ("IA", 1, 1), ("QY", 0, 1), ("QA", 2, 1), ("M1", 3, 1), ("EU", 3, 3), ("QA", 1, 1),
+    ("EU", 3, 1), ("WY", 1, 1), ("IA", 3, 1), ("M2", 0, 0), ("QY", 1, 0), ("M2", 5, 0), ("M2", 2, 0), ("QA", 3, 1),
+    ("FO", 0, 0), ("FO", 5, 0), ("FO", 2, 0), ("QY", 1, 1), ("IA", 3, 0), ("M2", 1, 0), ("M2", 4, 0), ("FO", 1, 0),
+    ("FO", 4, 0), ("M2", 3, 0), ("QA", 3, 0), ("FO", 3, 0), ("WY", 2, 1), ("WY", 2, 0), ("M2", 0, 1), ("M2", 2, 1),
+    ("FO", 0, 1), ("M2", 7, 0), ("FO", 2, 1), ("FO", 7, 0), ("QY", 2, 0), ("M2", 1, 1), ("M2", 5, 1), ("M2", 6, 0),
+    ("M2", 3, 1), ("FO", 6, 0), ("FO", 1, 1), ("FO", 3, 1), ("FO", 5, 1), ("QY", 2, 1), ("M2", 4, 1), ("M2", 6, 1),
+    ("FO", 4, 1), ("FO", 6, 1), ("WY", 3, 0), ("WY", 3, 1), ("M2", 2, 2), ("M2", 7, 1), ("FO", 2, 2), ("FO", 7, 1),
+    ("M2", 5, 2), ("M2", 4, 2), ("M2", 6, 2), ("FO", 5, 2), ("FO", 4, 2), ("QY", 3, 0), ("FO", 6, 2), ("M2", 7, 2),
+    ("M2", 3, 2), ("FO", 3, 2), ("FO", 7, 2), ("M2", 1, 2), ("M2", 0, 2), ("FO", 0, 2), ("QY", 3, 1), ("FO", 1, 2),
+    ("M2", 6, 3), ("FO", 6, 3), ("M2", 3, 3), ("FO", 3, 3), ("M2", 0, 3), ("FO", 0, 3), ("M2", 5, 3), ("FO", 5, 3),
+    ("M2", 2, 3), ("M2", 4, 3), ("FO", 4, 3), ("M2", 7, 3), ("FO", 7, 3), ("M2", 1, 3), ("FO", 1, 3), ("FO", 2, 3),
 ]
 
 
@@ -69,7 +70,16 @@ def tile_curvature_scaled_pair_correction_d7_kernel(tc, G, S_bytes, S_scale, Y_b
         ident = keep.tile([P, P], F32, name="ident")
         make_identity(nc, ident[:])
 
-        tables = keep.tile([P, 2, 8 * 16], F32, name="tables")
+        s_col = keep.tile([P, 1], F32, name="s_col")
+        y_col = keep.tile([P, 1], F32, name="y_col")
+        h_rows = keep.tile([P, 512], BF16, name="h_rows")
+        pick = keep.tile([P, 4], BF16, name="pick")
+        idle = keep.tile([P, 512], BF16, name="idle")
+        idle_out = keep.tile([P, 1], F32, name="idle_out")
+        nc.vector.memset(h_rows[:], 0.0)
+        nc.vector.memset(idle[:], 0.0)
+        nc.scalar.activation(out=idle_out[:], in_=idle[:, 0:1], func=COPY)
+        nc.gpsimd.tensor_copy(out=pick[:], in_=ident[:, 0:4])
         scale = keep.tile([P, 2, 2, 16], F32, name="scale")
         c_bf = keep.tile([P, 2, 4], BF16, name="c_bf")
         c_inv = keep.tile([P, 8], F32, name="c_inv")
@@ -88,13 +98,34 @@ def tile_curvature_scaled_pair_correction_d7_kernel(tc, G, S_bytes, S_scale, Y_b
         y_rows = Y_bytes.rearrange("(half p j) n -> half p j n", half=2, j=4)
         tiles = {}
 
-        def bank(kind, shape):
-            t = psum.tile(shape, F32, name="bank", tag=PSUM_TAG[kind], bufs=PSUM_BUFS[PSUM_TAG[kind]])
+        def bank(kind, shape, dtype=F32):
+            t = psum.tile(shape, dtype, name="bank", tag=PSUM_TAG[kind], bufs=PSUM_BUFS[PSUM_TAG[kind]])
             return t
 
         def load_small():
-            nc.sync.dma_start(out=tables[:, 0, :], in_=S_scale.rearrange("a b -> (a b)").partition_broadcast(P))
-            nc.sync.dma_start(out=tables[:, 1, :], in_=Y_scale.rearrange("a b -> (a b)").partition_broadcast(P))
+            nc.sync.dma_start(out=s_col[:], in_=S_scale.rearrange("a (b o) -> (a b) o", o=1))
+            nc.sync.dma_start(out=y_col[:], in_=Y_scale.rearrange("a (b o) -> (a b) o", o=1))
+
+        def spread_scales():
+            t = bank("first", [P, 2, P])
+            tiles["tables"] = t
+            nc.tensor.transpose(t[:, 0, :], s_col[:].to_broadcast([P, P]), ident[:])
+            nc.tensor.transpose(t[:, 1, :], y_col[:].to_broadcast([P, P]), ident[:])
+
+        def warm(k):
+            t = bank("first", [P, 512])
+            for i in range(WARM[k]):
+                nc.tensor.matmul(t[:], lhsT=idle[:, 0:P], rhs=idle[:], start=True, stop=True)
+
+        def spread_h(b):
+            t = bank("first", [P, 2, 512], BF16)
+            tiles["h_bank", b] = t
+            for i in range(2):
+                row = 2 * b + i
+                nc.tensor.matmul(t[:, i, :], lhsT=pick[:, row : row + 1].to_broadcast([P, P]), rhs=h_rows[:], start=True, stop=True)
+
+        def empty_h(b):
+            nc.scalar.copy(out=h_all[:, 1024 * b : 1024 * (b + 1)], in_=tiles["h_bank", b][:].rearrange("p i n -> p (i n)"))
 
         def load_c():
             nc.sync.dma_start(out=c_bf[:], in_=c.rearrange("(half p j) -> p half j", half=2, j=4))
@@ -102,14 +133,14 @@ def tile_curvature_scaled_pair_correction_d7_kernel(tc, G, S_bytes, S_scale, Y_b
         def pick_scales():
             for q in range(4):
                 rows = slice(32 * q, 32 * q + 32)
-                src = tables[rows].rearrange("p w (half q k) -> p w half q k", half=2, q=4)
-                nc.scalar.activation(out=scale[rows], in_=src[:, :, :, q, :], func=COPY)
+                src = tiles["tables"][rows].rearrange("p w (half q k) -> p w half q k", half=2, q=4)
+                nc.vector.tensor_copy(out=scale[rows], in_=src[:, :, :, q, :])
 
         def invert_c():
             nc.vector.reciprocal(out=c_inv[:], in_=c_bf[:].rearrange("p a b -> p (a b)"))
 
         def load_h():
-            nc.sync.dma_start(out=h_all[:], in_=h.partition_broadcast(P))
+            nc.sync.dma_start(out=h_rows[0:4, :], in_=h.rearrange("(c n) -> c n", c=4))
 
         def load_s(u):
             t = keep.tile([P, N], U8, name="s_raw%d" % u)
@@ -126,23 +157,29 @@ def tile_curvature_scaled_pair_correction_d7_kernel(tc, G, S_bytes, S_scale, Y_b
             nc.sync.dma_start(out=t[:], in_=y_rows[half][:, :, side * 1024 : (side + 1) * 1024])
             tiles["y_raw", half, side] = t
 
+        def wide_tile(u):
+            if ("s_wide", u) not in tiles:
+                tiles["s_wide", u] = work.tile([P, N], BF16, name="s_wide", bufs=3)
+            return tiles["s_wide", u]
+
         def widen_s(u):
             raw = tiles["s_raw", u]
-            wide = work.tile([P, N], BF16, name="s_wide", bufs=3)
-            tiles["s_wide", u] = wide
-            split = wide[:].rearrange("r (g u p e) -> r g p u e", g=4, u=2, e=2)
-            for kb in [4 * g + q for q in range(4) for g in range(4)]:
-                src = raw[:, kb * P : (kb + 1) * P].bitcast(FP8)
-                col = scale[:, 0, u // 4, kb : kb + 1]
-                if u in S_ON_SCALAR:
-                    nc.scalar.activation(out=wide[:, kb * P : (kb + 1) * P], in_=src, func=COPY, scale=col)
-                else:
-                    g, q = divmod(kb, 4)
+            split = wide_tile(u)[:].rearrange("r (g u p e) -> r g p u e", g=4, u=2, e=2)
+            for q in range(4):
+                for g in range(4 - S_ON_SCALAR[u]):
+                    kb = 4 * g + q
                     nc.vector.tensor_scalar(
                         out=split[:, g, 32 * q : 32 * q + 32],
-                        in0=src.rearrange("r (p u e) -> r p u e", u=2, e=2),
-                        scalar1=col, scalar2=None, op0=MULT,
+                        in0=raw[:, kb * P : (kb + 1) * P].bitcast(FP8).rearrange("r (p u e) -> r p u e", u=2, e=2),
+                        scalar1=scale[:, 0, u // 4, kb : kb + 1], scalar2=None, op0=MULT,
                     )
+
+        def widen_s_scalar(u):
+            raw = tiles["s_raw", u]
+            wide = wide_tile(u)
+            for kb in range(16 - 4 * S_ON_SCALAR[u], 16):
+                cols = slice(kb * P, (kb + 1) * P)
+                nc.scalar.activation(out=wide[:, cols], in_=raw[:, cols].bitcast(FP8), func=COPY, scale=scale[:, 0, u // 4, kb : kb + 1])
 
         def turn_s(u):
             words = tiles["s_wide", u][:].bitcast(F32)
@@ -152,7 +189,7 @@ def tile_curvature_scaled_pair_correction_d7_kernel(tc, G, S_bytes, S_scale, Y_b
                 for gi in range(2):
                     g = 2 * b + gi
                     for w in range(2):
-                        if u in S_ON_SCALAR:
+                        if g >= 4 - S_ON_SCALAR[u]:
                             src = words[:, 256 * g + w : 256 * (g + 1) : 2]
                         else:
                             src = words[:, 256 * g + P * w : 256 * g + P * (w + 1)]
@@ -268,7 +305,19 @@ def tile_curvature_scaled_pair_correction_d7_kernel(tc, G, S_bytes, S_scale, Y_b
             nc.vector.tensor_tensor(out=res[:], in0=tiles["p_bank", tt, nb][:], in1=h_all[:, cols], op=MULT)
             nc.sync.dma_start(out=out[tt * P : (tt + 1) * P, cols], in_=res[:])
 
+        def empty_p(tt, nb):
+            t = work.tile([P, 512], F32, name="p_copy", bufs=2)
+            tiles["p_copy", tt, nb] = t
+            nc.scalar.copy(out=t[:], in_=tiles["p_bank", tt, nb][:])
+
+        def finish_pool(tt, nb):
+            res = work.tile([P, 512], F32, name="res_pool", bufs=2)
+            cols = slice(512 * nb, 512 * (nb + 1))
+            nc.gpsimd.tensor_tensor(out=res[:], in0=tiles["p_copy", tt, nb][:], in1=h_all[:, cols], op=MULT)
+            nc.sync.dma_start(out=out[tt * P : (tt + 1) * P, cols], in_=res[:])
+
         jobs = {
+            "EP": empty_p, "FP": finish_pool, "SS": spread_scales, "W": warm, "SH": spread_h, "EH": empty_h, "WA": widen_s_scalar,
             "load_small": load_small, "load_c": load_c, "pick_scales": pick_scales, "invert_c": invert_c, "load_h": load_h,
             "load_s": load_s, "load_g": load_g, "load_y": load_y,
             "WS": widen_s, "TS": turn_s, "ES": empty_s, "QS": quant_s,

@@ -16,47 +16,65 @@ MULT = mybir.AluOpType.mult
 COPY = mybir.ActivationFunctionType.Copy
 
 P = 128
-TC = 256
-NCH = T // TC
+QUAD = 32
+PACK = 4
+K_PASS = P * PACK
+PASSES = N // K_PASS
+HALVES = M // K_PASS
+SLICES = HALVES * PACK
+COL_BLOCKS = N // P
+CHUNK = 256
+CHUNKS = T // CHUNK
+STRIP = 512
+STRIPS = N // STRIP
 
-PSUM_TAG = {"turn": "turn", "first": "acc", "second": "acc"}
-PSUM_BUFS = {"turn": 4, "acc": 4}
-S_ON_SCALAR = (0, 0, 0, 0, 0, 0, 0, 0)
-Y_ON_VECTOR = ()
-WARM = (4, 4)
-A_BUFS = 6
-Y_BUFS = 6
-RES_BUFS = 8
-ORDER = [
-    ("load_small",), ("SS",), ("pick_scales",), ("load_s", 0), ("WS", 0), ("load_h",), ("load_s", 2), ("load_s", 1),
-    ("load_g", 0), ("load_g", 1), ("load_s", 3), ("load_s", 4), ("load_g", 4), ("load_y", 0, 0), ("load_g", 5), ("load_g", 2),
-    ("load_c",), ("load_g", 3), ("load_s", 6), ("load_s", 5), ("load_g", 6), ("load_g", 7), ("load_y", 1, 0), ("load_s", 7),
-    ("load_y", 1, 1), ("load_y", 0, 1), ("W", 0), ("TS", 0), ("TG", 0, 0), ("WS", 1), ("WS", 2), ("ES", 0),
-    ("TS", 1), ("W", 1), ("SH", 0), ("ES", 1), ("EG", 0, 0), ("TG", 0, 1), ("TS", 2), ("WS", 4),
-    ("EH", 0), ("EG", 0, 1), ("ES", 2), ("WS", 3), ("QG", 0, 0), ("QS", 0), ("QG", 0, 1), ("TG", 2, 0),
-    ("EG", 2, 0), ("QS", 1), ("QS", 2), ("QG", 2, 0), ("SH", 1), ("TG", 2, 1), ("EG", 2, 1), ("QG", 2, 1),
-    ("WS", 5), ("TG", 1, 0), ("EG", 1, 0), ("TS", 4), ("QG", 1, 0), ("invert_c",), ("IY", 0, 0), ("TG", 1, 1),
-    ("ES", 4), ("EH", 1), ("EG", 1, 1), ("TG", 3, 1), ("TS", 5), ("EG", 3, 1), ("WY", 0, 0), ("ES", 5),
-    ("M1", 2, 0), ("M1", 0, 0), ("TS", 3), ("ES", 3), ("QG", 1, 1), ("IY", 0, 1), ("QS", 4), ("WS", 6),
-    ("WS", 7), ("QS", 5), ("TS", 6), ("TG", 3, 0), ("M1", 2, 2), ("ES", 6), ("EG", 3, 0), ("QS", 3),
-    ("M1", 0, 1), ("TS", 7), ("EU", 0, 0), ("EU", 2, 0), ("EU", 2, 2), ("ES", 7), ("M1", 2, 1), ("EU", 2, 1),
-    ("EU", 0, 1), ("M1", 1, 1), ("EU", 1, 1), ("WY", 0, 1), ("IY", 3, 0), ("QS", 6), ("IY", 1, 0), ("QG", 3, 0),
-    ("QG", 3, 1), ("QS", 7), ("IY", 3, 1), ("IY", 1, 1), ("IA", 0, 0), ("IA", 2, 0), ("M1", 1, 0), ("M1", 0, 2),
-    ("M1", 1, 3), ("M1", 0, 3), ("EU", 1, 0), ("M1", 2, 3), ("EU", 0, 2), ("EU", 0, 3), ("M1", 1, 2), ("EU", 2, 3),
-    ("EU", 1, 3), ("WY", 1, 0), ("QA", 0, 0), ("QA", 2, 0), ("M1", 3, 0), ("QY", 0, 0), ("IA", 1, 0), ("IA", 0, 1),
-    ("QA", 1, 0), ("QA", 0, 1), ("M1", 3, 2), ("EU", 1, 2), ("EU", 3, 2), ("M1", 3, 3), ("EU", 3, 0), ("IA", 2, 1),
-    ("IY", 2, 0), ("IY", 2, 1), ("IA", 1, 1), ("QY", 0, 1), ("QA", 2, 1), ("M1", 3, 1), ("EU", 3, 3), ("QA", 1, 1),
-    ("EU", 3, 1), ("WY", 1, 1), ("IA", 3, 1), ("M2", 0, 0), ("QY", 1, 0), ("M2", 5, 0), ("M2", 2, 0), ("QA", 3, 1),
-    ("FO", 0, 0), ("FO", 5, 0), ("FO", 2, 0), ("QY", 1, 1), ("IA", 3, 0), ("M2", 1, 0), ("M2", 4, 0), ("FO", 1, 0),
-    ("FO", 4, 0), ("M2", 3, 0), ("QA", 3, 0), ("FO", 3, 0), ("WY", 2, 1), ("WY", 2, 0), ("M2", 0, 1), ("M2", 2, 1),
-    ("FO", 0, 1), ("M2", 7, 0), ("FO", 2, 1), ("FO", 7, 0), ("QY", 2, 0), ("M2", 1, 1), ("M2", 5, 1), ("M2", 6, 0),
-    ("M2", 3, 1), ("FO", 6, 0), ("FO", 1, 1), ("FO", 3, 1), ("FO", 5, 1), ("QY", 2, 1), ("M2", 4, 1), ("M2", 6, 1),
-    ("FO", 4, 1), ("FO", 6, 1), ("WY", 3, 0), ("WY", 3, 1), ("M2", 2, 2), ("M2", 7, 1), ("FO", 2, 2), ("FO", 7, 1),
-    ("M2", 5, 2), ("M2", 4, 2), ("M2", 6, 2), ("FO", 5, 2), ("FO", 4, 2), ("QY", 3, 0), ("FO", 6, 2), ("M2", 7, 2),
-    ("M2", 3, 2), ("FO", 3, 2), ("FO", 7, 2), ("M2", 1, 2), ("M2", 0, 2), ("FO", 0, 2), ("QY", 3, 1), ("FO", 1, 2),
-    ("M2", 6, 3), ("FO", 6, 3), ("M2", 3, 3), ("FO", 3, 3), ("M2", 0, 3), ("FO", 0, 3), ("M2", 5, 3), ("FO", 5, 3),
-    ("M2", 2, 3), ("M2", 4, 3), ("FO", 4, 3), ("M2", 7, 3), ("FO", 7, 3), ("M2", 1, 3), ("FO", 1, 3), ("FO", 2, 3),
-]
+SCALAR_PASSES = (2, 1, 1, 0, 0, 0, 0, 0)
+RING_BANKS = 4
+FIRST_STRIP_ON_BOTH_RINGS = 2
+WARM_MATMULS = 4
+
+WIDE_S_BUFS = 4
+TURNED_BUFS = 3
+A_PLANE_BUFS = 6
+WOVEN_A_BUFS = 2
+WOVEN_Y_BUFS = 6
+WIDE_Y_BUFS = 3
+RESULT_BUFS = 7
+
+ORDER = """
+load_scales, spread_scales, pick_scales, load_s 0, widen_s 0, widen_s_scalar 0, load_h, load_s 2,
+widen_s_scalar 2, load_s 1, load_g 0, widen_s_scalar 1, load_g 1, load_s 3, load_g 4, load_y 1 0,
+load_g 5, load_s 4, load_g 3, load_s 5, load_s 7, load_g 6, load_c, load_y 1 1, load_g 2, load_s 6,
+load_y 0 1, load_y 0 0, load_g 7, warm_tensor, spread_h 0, turn_s 0, empty_s 0, turn_g 0 1, empty_g 0 1,
+widen_s 2, widen_s 1, widen_s 3, quant_s 0, turn_s 2, turn_g 0 0, empty_s 2, empty_g 0 0, spread_h 1,
+turn_s 1, empty_s 1, turn_s 3, empty_s 3, turn_g 2 1, quant_g 0 1, weave_y 0 1, widen_s 4, quant_s 2,
+quant_g 0 0, quant_s 1, widen_s 5, quant_s 3, invert_c, empty_g 2 1, turn_g 2 0, empty_g 2 0, empty_h 0,
+turn_s 4, empty_s 4, first_product 0 0, turn_s 5, widen_y 0 1, turn_g 1 1, quant_g 2 0, quant_g 2 1,
+empty_h 1, empty_g 1 1, empty_s 5, empty_u 0 0, first_product 0 1, first_product 2 0, first_product 2 1,
+widen_s 6, widen_s 7, turn_s 6, weave_y 0 0, quant_s 4, weave_y 3 1, quant_s 5, turn_s 7, empty_s 6,
+turn_g 1 0, empty_u 0 1, empty_s 7, first_product 2 2, empty_g 1 0, empty_u 2 1, empty_u 2 0,
+empty_u 2 2, turn_g 3 0, turn_g 3 1, empty_g 3 1, widen_y 0 0, first_product 0 2, empty_u 0 2,
+weave_y 3 0, weave_y 1 0, quant_g 1 0, quant_s 7, quant_s 6, quant_g 1 1, first_product 2 3,
+first_product 0 3, first_product 1 3, first_product 1 1, quant_y 0 1, quant_g 3 1, weave_y 2 0,
+weave_a 0 0, weave_a 2 0, quant_y 0 0, empty_u 2 3, empty_u 0 3, empty_g 3 0, empty_u 1 3, quant_a 0 0,
+weave_y 1 1, weave_y 2 1, quant_g 3 0, quant_a 2 0, weave_a 2 1, weave_a 0 1, quant_a 2 1, widen_y 1 0,
+empty_u 1 1, first_product 1 0, first_product 1 2, first_product 3 2, empty_u 1 0, empty_u 1 2,
+empty_u 3 2, first_product 3 3, second_product 5 0, second_product 4 0, first_product 3 0, empty_u 3 3,
+quant_a 0 1, weave_a 1 0, weave_a 1 1, widen_y 1 1, quant_y 1 0, quant_a 1 0, quant_a 1 1, finish 5 0,
+finish 4 0, weave_a 3 1, second_product 3 0, empty_u 3 0, widen_y 2 0, second_product 1 0,
+second_product 2 0, quant_y 1 1, finish 3 0, second_product 3 1, finish 2 0, finish 1 0, quant_a 3 1,
+finish 3 1, quant_y 2 0, first_product 3 1, second_product 0 0, empty_u 3 1, second_product 2 1,
+second_product 0 1, finish 0 0, weave_a 3 0, widen_y 2 1, widen_y 3 0, widen_y 3 1, finish 2 1,
+quant_a 3 0, finish 0 1, second_product 5 1, second_product 1 1, quant_y 2 1, second_product 7 0,
+finish 5 1, finish 7 0, second_product 6 0, finish 6 0, finish 1 1, second_product 2 2,
+second_product 7 1, second_product 0 2, finish 2 2, finish 7 1, second_product 4 1, finish 0 2,
+finish 4 1, second_product 6 1, second_product 5 2, quant_y 3 1, finish 5 2, second_product 6 2,
+second_product 1 2, second_product 3 2, finish 6 1, finish 1 2, finish 3 2, quant_y 3 0,
+second_product 4 2, finish 4 2, second_product 7 2, finish 6 2, second_product 2 3, second_product 3 3,
+finish 2 3, finish 7 2, finish 3 3, second_product 1 3, second_product 0 3, second_product 4 3,
+finish 1 3, finish 4 3, second_product 6 3, finish 0 3, finish 6 3, second_product 5 3, finish 5 3,
+second_product 7 3, finish 7 3
+"""
 
 
 def tile_curvature_scaled_pair_correction_d7_kernel(tc, G, S_bytes, S_scale, Y_bytes, Y_scale, c, h, out):
@@ -72,134 +90,145 @@ def tile_curvature_scaled_pair_correction_d7_kernel(tc, G, S_bytes, S_scale, Y_b
 
         s_col = keep.tile([P, 1], F32, name="s_col")
         y_col = keep.tile([P, 1], F32, name="y_col")
-        h_rows = keep.tile([P, 512], BF16, name="h_rows")
-        pick = keep.tile([P, 4], BF16, name="pick")
-        idle = keep.tile([P, 512], BF16, name="idle")
+        h_rows = keep.tile([P, STRIP], BF16, name="h_rows")
+        pick = keep.tile([P, STRIPS], BF16, name="pick")
+        idle = keep.tile([P, STRIP], BF16, name="idle")
         idle_out = keep.tile([P, 1], F32, name="idle_out")
         nc.vector.memset(h_rows[:], 0.0)
         nc.vector.memset(idle[:], 0.0)
         nc.scalar.activation(out=idle_out[:], in_=idle[:, 0:1], func=COPY)
-        nc.gpsimd.tensor_copy(out=pick[:], in_=ident[:, 0:4])
-        scale = keep.tile([P, 2, 2, 16], F32, name="scale")
-        c_bf = keep.tile([P, 2, 4], BF16, name="c_bf")
-        c_inv = keep.tile([P, 8], F32, name="c_inv")
+        nc.gpsimd.tensor_copy(out=pick[:], in_=ident[:, 0:STRIPS])
+
+        scale = keep.tile([P, 2, HALVES, COL_BLOCKS], F32, name="scale")
+        c_bf = keep.tile([P, HALVES, PACK], BF16, name="c_bf")
+        c_inv = keep.tile([P, SLICES], F32, name="c_inv")
         h_all = keep.tile([P, N], BF16, name="h_all")
 
-        s_codes = keep.tile([P, 8, 4, P], U32, name="s_codes", align_bytes=64)
-        s_scales = keep.tile([P, 8, 4, P], U8, name="s_scales", align_bytes=64)
-        g_codes = keep.tile([P, NCH, 4, TC], U32, name="g_codes", align_bytes=64)
-        g_scales = keep.tile([P, NCH, 4, TC], U8, name="g_scales", align_bytes=64)
-        a_codes = keep.tile([P, NCH, 2, TC], U32, name="a_codes", align_bytes=64)
-        a_scales = keep.tile([P, NCH, 2, TC], U8, name="a_scales", align_bytes=64)
-        y_codes = keep.tile([P, 4, 2, 512], U32, name="y_codes", align_bytes=64)
-        y_scales = keep.tile([P, 4, 2, 512], U8, name="y_scales", align_bytes=64)
+        s_codes = keep.tile([P, SLICES, PASSES, P], U32, name="s_codes", align_bytes=64)
+        s_scales = keep.tile([P, SLICES, PASSES, P], U8, name="s_scales", align_bytes=64)
+        g_codes = keep.tile([P, CHUNKS, PASSES, CHUNK], U32, name="g_codes", align_bytes=64)
+        g_scales = keep.tile([P, CHUNKS, PASSES, CHUNK], U8, name="g_scales", align_bytes=64)
+        a_codes = keep.tile([P, CHUNKS, HALVES, CHUNK], U32, name="a_codes", align_bytes=64)
+        a_scales = keep.tile([P, CHUNKS, HALVES, CHUNK], U8, name="a_scales", align_bytes=64)
+        y_codes = keep.tile([P, STRIPS, HALVES, STRIP], U32, name="y_codes", align_bytes=64)
+        y_scales = keep.tile([P, STRIPS, HALVES, STRIP], U8, name="y_scales", align_bytes=64)
 
-        s_rows = S_bytes.rearrange("(half r j) n -> half j r n", half=2, j=4)
-        y_rows = Y_bytes.rearrange("(half p j) n -> half p j n", half=2, j=4)
+        s_rows = S_bytes.rearrange("(half r j) n -> half j r n", half=HALVES, j=PACK)
+        y_rows = Y_bytes.rearrange("(half p j) n -> half p j n", half=HALVES, j=PACK)
         tiles = {}
 
-        def bank(kind, shape, dtype=F32):
-            t = psum.tile(shape, dtype, name="bank", tag=PSUM_TAG[kind], bufs=PSUM_BUFS[PSUM_TAG[kind]])
-            return t
+        def bank(ring, shape, dtype=F32):
+            return psum.tile(shape, dtype, name="bank", tag=ring, bufs=RING_BANKS)
 
-        def load_small():
+        def load_scales():
             nc.sync.dma_start(out=s_col[:], in_=S_scale.rearrange("a (b o) -> (a b) o", o=1))
             nc.sync.dma_start(out=y_col[:], in_=Y_scale.rearrange("a (b o) -> (a b) o", o=1))
 
         def spread_scales():
-            t = bank("first", [P, 2, P])
-            tiles["tables"] = t
-            nc.tensor.transpose(t[:, 0, :], s_col[:].to_broadcast([P, P]), ident[:])
-            nc.tensor.transpose(t[:, 1, :], y_col[:].to_broadcast([P, P]), ident[:])
-
-        def warm(k):
-            t = bank("first", [P, 512])
-            for i in range(WARM[k]):
-                nc.tensor.matmul(t[:], lhsT=idle[:, 0:P], rhs=idle[:], start=True, stop=True)
-
-        def spread_h(b):
-            t = bank("first", [P, 2, 512], BF16)
-            tiles["h_bank", b] = t
-            for i in range(2):
-                row = 2 * b + i
-                nc.tensor.matmul(t[:, i, :], lhsT=pick[:, row : row + 1].to_broadcast([P, P]), rhs=h_rows[:], start=True, stop=True)
-
-        def empty_h(b):
-            nc.scalar.copy(out=h_all[:, 1024 * b : 1024 * (b + 1)], in_=tiles["h_bank", b][:].rearrange("p i n -> p (i n)"))
-
-        def load_c():
-            nc.sync.dma_start(out=c_bf[:], in_=c.rearrange("(half p j) -> p half j", half=2, j=4))
+            tables = bank("acc", [P, 2, P])
+            tiles["tables"] = tables
+            nc.tensor.transpose(tables[:, 0, :], s_col[:].to_broadcast([P, P]), ident[:])
+            nc.tensor.transpose(tables[:, 1, :], y_col[:].to_broadcast([P, P]), ident[:])
 
         def pick_scales():
-            for q in range(4):
-                rows = slice(32 * q, 32 * q + 32)
-                src = tiles["tables"][rows].rearrange("p w (half q k) -> p w half q k", half=2, q=4)
-                nc.vector.tensor_copy(out=scale[rows], in_=src[:, :, :, q, :])
+            for q in range(P // QUAD):
+                rows = slice(QUAD * q, QUAD * (q + 1))
+                table = tiles["tables"][rows].rearrange("p s (half q k) -> p s half q k", half=HALVES, q=P // QUAD)
+                nc.vector.tensor_copy(out=scale[rows], in_=table[:, :, :, q, :])
+
+        def load_c():
+            nc.sync.dma_start(out=c_bf[:], in_=c.rearrange("(half p j) -> p half j", half=HALVES, j=PACK))
 
         def invert_c():
-            nc.vector.reciprocal(out=c_inv[:], in_=c_bf[:].rearrange("p a b -> p (a b)"))
+            nc.vector.reciprocal(out=c_inv[:], in_=c_bf[:].rearrange("p half j -> p (half j)"))
 
         def load_h():
-            nc.sync.dma_start(out=h_rows[0:4, :], in_=h.rearrange("(c n) -> c n", c=4))
+            nc.sync.dma_start(out=h_rows[0:STRIPS, :], in_=h.rearrange("(i n) -> i n", i=STRIPS))
+
+        def spread_h(b):
+            spread = bank("acc", [P, 2, STRIP], BF16)
+            tiles["h_bank", b] = spread
+            for i in range(2):
+                row = 2 * b + i
+                ones = pick[:, row : row + 1].to_broadcast([P, P])
+                nc.tensor.matmul(spread[:, i, :], lhsT=ones, rhs=h_rows[:], start=True, stop=True)
+
+        def empty_h(b):
+            cols = slice(2 * STRIP * b, 2 * STRIP * (b + 1))
+            nc.scalar.copy(out=h_all[:, cols], in_=tiles["h_bank", b][:].rearrange("p i n -> p (i n)"))
+
+        def warm_tensor():
+            unread = bank("acc", [P, STRIP])
+            for i in range(WARM_MATMULS):
+                nc.tensor.matmul(unread[:], lhsT=idle[:, 0:P], rhs=idle[:], start=True, stop=True)
 
         def load_s(u):
-            t = keep.tile([P, N], U8, name="s_raw%d" % u)
-            nc.sync.dma_start(out=t[:], in_=s_rows[u // 4, u % 4])
-            tiles["s_raw", u] = t
+            raw = keep.tile([P, N], U8, name="s_raw%d" % u)
+            nc.sync.dma_start(out=raw[:], in_=s_rows[u // PACK, u % PACK])
+            tiles["s_raw", u] = raw
 
-        def load_g(tt):
-            t = keep.tile([P, N], BF16, name="g_raw%d" % tt)
-            nc.sync.dma_start(out=t[:], in_=G[tt * P : (tt + 1) * P, :])
-            tiles["g_raw", tt] = t
+        def load_g(row_tile):
+            raw = keep.tile([P, N], BF16, name="g_raw%d" % row_tile)
+            nc.sync.dma_start(out=raw[:], in_=G[row_tile * P : (row_tile + 1) * P, :])
+            tiles["g_raw", row_tile] = raw
 
         def load_y(half, side):
-            t = keep.tile([P, 4, 1024], U8, name="y_raw%d%d" % (half, side))
-            nc.sync.dma_start(out=t[:], in_=y_rows[half][:, :, side * 1024 : (side + 1) * 1024])
-            tiles["y_raw", half, side] = t
+            raw = keep.tile([P, PACK, 2 * STRIP], U8, name="y_raw%d%d" % (half, side))
+            nc.sync.dma_start(out=raw[:], in_=y_rows[half][:, :, side * 2 * STRIP : (side + 1) * 2 * STRIP])
+            tiles["y_raw", half, side] = raw
 
-        def wide_tile(u):
+        def wide_s_tile(u):
             if ("s_wide", u) not in tiles:
-                tiles["s_wide", u] = work.tile([P, N], BF16, name="s_wide", bufs=3)
+                tiles["s_wide", u] = work.tile([P, N], BF16, name="s_wide", bufs=WIDE_S_BUFS)
             return tiles["s_wide", u]
 
         def widen_s(u):
             raw = tiles["s_raw", u]
-            split = wide_tile(u)[:].rearrange("r (g u p e) -> r g p u e", g=4, u=2, e=2)
-            for q in range(4):
-                for g in range(4 - S_ON_SCALAR[u]):
-                    kb = 4 * g + q
+            sorted_by_w = wide_s_tile(u)[:].rearrange("r (g w p e) -> r g p w e", g=PASSES, w=2, e=2)
+            for q in range(P // QUAD):
+                for g in range(PASSES - SCALAR_PASSES[u]):
+                    block = PACK * g + q
                     nc.vector.tensor_scalar(
-                        out=split[:, g, 32 * q : 32 * q + 32],
-                        in0=raw[:, kb * P : (kb + 1) * P].bitcast(FP8).rearrange("r (p u e) -> r p u e", u=2, e=2),
-                        scalar1=scale[:, 0, u // 4, kb : kb + 1], scalar2=None, op0=MULT,
+                        out=sorted_by_w[:, g, QUAD * q : QUAD * (q + 1)],
+                        in0=raw[:, block * P : (block + 1) * P].bitcast(FP8).rearrange("r (p w e) -> r p w e", w=2, e=2),
+                        scalar1=scale[:, 0, u // PACK, block : block + 1],
+                        scalar2=None,
+                        op0=MULT,
                     )
 
         def widen_s_scalar(u):
             raw = tiles["s_raw", u]
-            wide = wide_tile(u)
-            for kb in range(16 - 4 * S_ON_SCALAR[u], 16):
-                cols = slice(kb * P, (kb + 1) * P)
-                nc.scalar.activation(out=wide[:, cols], in_=raw[:, cols].bitcast(FP8), func=COPY, scale=scale[:, 0, u // 4, kb : kb + 1])
+            wide = wide_s_tile(u)
+            for block in range(COL_BLOCKS - PACK * SCALAR_PASSES[u], COL_BLOCKS):
+                cols = slice(block * P, (block + 1) * P)
+                factor = scale[:, 0, u // PACK, block : block + 1]
+                nc.scalar.activation(out=wide[:, cols], in_=raw[:, cols].bitcast(FP8), func=COPY, scale=factor)
 
         def turn_s(u):
             words = tiles["s_wide", u][:].bitcast(F32)
             for b in range(2):
-                t = bank("turn", [P, 2, 2, P])
-                tiles["s_bank", u, b] = t
-                for gi in range(2):
-                    g = 2 * b + gi
+                turned = bank("turn", [P, 2, 2, P])
+                tiles["s_bank", u, b] = turned
+                for i in range(2):
+                    g = 2 * b + i
                     for w in range(2):
-                        if g >= 4 - S_ON_SCALAR[u]:
-                            src = words[:, 256 * g + w : 256 * (g + 1) : 2]
+                        if g >= PASSES - SCALAR_PASSES[u]:
+                            src = words[:, 2 * P * g + w : 2 * P * (g + 1) : 2]
                         else:
-                            src = words[:, 256 * g + P * w : 256 * g + P * (w + 1)]
-                        nc.tensor.transpose(t[:, w, gi, :], src, ident[:])
+                            src = words[:, 2 * P * g + P * w : 2 * P * g + P * (w + 1)]
+                        nc.tensor.transpose(turned[:, w, i, :], src, ident[:])
+
+        def join_words(dst, turned):
+            nc.scalar.copy(
+                out=dst.rearrange("p (x i) w -> p x w i", i=2),
+                in_=turned[:].rearrange("p w a r -> p w (a r)").rearrange("p w (x i) -> p x w i", i=2),
+            )
 
         def empty_s(u):
-            st = work.tile([P, 2, 256, 2], F32, name="s_turned", bufs=3, align_bytes=64)
-            tiles["s_turned", u] = st
+            joined = work.tile([P, 2, 2 * P, 2], F32, name="s_turned", bufs=TURNED_BUFS, align_bytes=64)
+            tiles["s_turned", u] = joined
             for b in range(2):
-                nc.scalar.copy(out=st[:, b], in_=tiles["s_bank", u, b][:].rearrange("p w g r -> p (g r) w"))
+                join_words(joined[:, b], tiles["s_bank", u, b])
 
         def quant_s(u):
             nc.vector.quantize_mx(
@@ -208,123 +237,148 @@ def tile_curvature_scaled_pair_correction_d7_kernel(tc, G, S_bytes, S_scale, Y_b
                 in_=tiles["s_turned", u][:].rearrange("p b x w -> p (b x w)").bitcast(BF16),
             )
 
-        def turn_g(ch, b):
+        def turn_g(chunk, b):
             for g in (2 * b, 2 * b + 1):
-                t = bank("turn", [P, 2, 2, P])
-                tiles["g_bank", ch, g] = t
+                turned = bank("turn", [P, 2, 2, P])
+                tiles["g_bank", chunk, g] = turned
                 for i in range(2):
-                    words = tiles["g_raw", 2 * ch + i][:].bitcast(F32)
+                    words = tiles["g_raw", 2 * chunk + i][:].bitcast(F32)
                     for w in range(2):
-                        nc.tensor.transpose(t[:, w, i, :], words[:, 256 * g + w : 256 * (g + 1) : 2], ident[:])
+                        nc.tensor.transpose(turned[:, w, i, :], words[:, 2 * P * g + w : 2 * P * (g + 1) : 2], ident[:])
 
-        def empty_g(ch, b):
-            st = work.tile([P, 2, TC, 2], F32, name="g_turned", bufs=3, align_bytes=64)
-            tiles["g_turned", ch, b] = st
-            for gi in range(2):
-                nc.scalar.copy(out=st[:, gi], in_=tiles["g_bank", ch, 2 * b + gi][:].rearrange("p w i r -> p (i r) w"))
+        def empty_g(chunk, b):
+            joined = work.tile([P, 2, CHUNK, 2], F32, name="g_turned", bufs=TURNED_BUFS, align_bytes=64)
+            tiles["g_turned", chunk, b] = joined
+            for i in range(2):
+                join_words(joined[:, i], tiles["g_bank", chunk, 2 * b + i])
 
-        def quant_g(ch, b):
+        def quant_g(chunk, b):
             nc.vector.quantize_mx(
-                out=g_codes[:, ch, 2 * b : 2 * b + 2].rearrange("p g t -> p (g t)").bitcast(FP8X4),
-                scales=g_scales[:, ch, 2 * b : 2 * b + 2].rearrange("p g t -> p (g t)"),
-                in_=tiles["g_turned", ch, b][:].rearrange("p g t w -> p (g t w)").bitcast(BF16),
+                out=g_codes[:, chunk, 2 * b : 2 * b + 2].rearrange("p g t -> p (g t)").bitcast(FP8X4),
+                scales=g_scales[:, chunk, 2 * b : 2 * b + 2].rearrange("p g t -> p (g t)"),
+                in_=tiles["g_turned", chunk, b][:].rearrange("p g t w -> p (g t w)").bitcast(BF16),
             )
 
-        def first_product(ch, pair):
-            t = bank("first", [P, 2, TC])
-            tiles["u_bank", ch, pair] = t
+        def first_product(chunk, b):
+            sums = bank("acc", [P, 2, CHUNK])
+            tiles["u_bank", chunk, b] = sums
             for i in range(2):
-                u = 2 * pair + i
-                for g in range(4):
+                u = 2 * b + i
+                for g in range(PASSES):
                     nc.tensor.matmul_mx(
-                        out=t[:, i, :],
-                        lhsT=s_codes[:, u, g, :].bitcast(FP8X4), lhsT_scale=s_scales[:, u, g, :],
-                        rhs=g_codes[:, ch, g, :].bitcast(FP8X4), rhs_scale=g_scales[:, ch, g, :],
-                        start=(g == 0), stop=(g == 3),
+                        out=sums[:, i, :],
+                        lhsT=s_codes[:, u, g, :].bitcast(FP8X4),
+                        lhsT_scale=s_scales[:, u, g, :],
+                        rhs=g_codes[:, chunk, g, :].bitcast(FP8X4),
+                        rhs_scale=g_scales[:, chunk, g, :],
+                        start=(g == 0),
+                        stop=(g == PASSES - 1),
                     )
 
-        def empty_u(ch, pair):
-            half = pair // 2
-            if ("a_planes", ch, half) not in tiles:
-                tiles["a_planes", ch, half] = work.tile([P, 4, TC], BF16, name="a_planes", bufs=A_BUFS)
-            planes = tiles["a_planes", ch, half]
+        def empty_u(chunk, b):
+            half = b // 2
+            if ("a_planes", chunk, half) not in tiles:
+                tiles["a_planes", chunk, half] = work.tile([P, PACK, CHUNK], BF16, name="a_planes", bufs=A_PLANE_BUFS)
+            planes = tiles["a_planes", chunk, half]
             for i in range(2):
-                u = 2 * pair + i
-                nc.scalar.activation(out=planes[:, u % 4, :], in_=tiles["u_bank", ch, pair][:, i, :], func=COPY, scale=c_inv[:, u : u + 1])
+                u = 2 * b + i
+                sums = tiles["u_bank", chunk, b][:, i, :]
+                nc.scalar.activation(out=planes[:, u % PACK, :], in_=sums, func=COPY, scale=c_inv[:, u : u + 1])
 
-        def weave_a(ch, half):
-            woven = work.tile([P, TC * 4], BF16, name="a_woven", bufs=2, align_bytes=64)
-            tiles["a_woven", ch, half] = woven
+        def weave(dst, planes):
             nc.vector.tensor_copy(
-                out=woven[:].rearrange("p (x i j) -> p x j i", i=4, j=4),
-                in_=tiles["a_planes", ch, half][:].rearrange("p j (x i) -> p x j i", i=4),
+                out=dst.rearrange("p (x i j) -> p x j i", i=4, j=PACK),
+                in_=planes.rearrange("p j (x i) -> p x j i", i=4),
             )
 
-        def quant_a(ch, half):
-            nc.vector.quantize_mx(out=a_codes[:, ch, half, :].bitcast(FP8X4), scales=a_scales[:, ch, half, :], in_=tiles["a_woven", ch, half][:])
+        def weave_a(chunk, half):
+            woven = work.tile([P, CHUNK * PACK], BF16, name="a_woven", bufs=WOVEN_A_BUFS, align_bytes=64)
+            tiles["a_woven", chunk, half] = woven
+            weave(woven[:], tiles["a_planes", chunk, half][:])
 
-        def weave_y(nb, half):
-            woven = work.tile([P, 2048], U8, name="y_woven", bufs=Y_BUFS)
-            tiles["y_woven", nb, half] = woven
-            raw = tiles["y_raw", half, nb // 2][:, :, (nb % 2) * 512 : (nb % 2 + 1) * 512]
-            nc.vector.tensor_copy(
-                out=woven[:].rearrange("p (x i j) -> p x j i", i=4, j=4),
-                in_=raw.rearrange("p j (x i) -> p x j i", i=4),
+        def quant_a(chunk, half):
+            nc.vector.quantize_mx(
+                out=a_codes[:, chunk, half, :].bitcast(FP8X4),
+                scales=a_scales[:, chunk, half, :],
+                in_=tiles["a_woven", chunk, half][:],
             )
 
-        def widen_y(nb, half):
-            wide = work.tile([P, 2048], BF16, name="y_wide", bufs=3, align_bytes=64)
-            tiles["y_wide", nb, half] = wide
-            for b in range(4):
-                cols = slice(512 * b, 512 * (b + 1))
-                src = tiles["y_woven", nb, half][:, cols].bitcast(FP8)
-                col = scale[:, 1, half, 4 * nb + b : 4 * nb + b + 1]
-                if (nb, half) in Y_ON_VECTOR:
-                    nc.vector.tensor_scalar(out=wide[:, cols], in0=src, scalar1=col, scalar2=None, op0=MULT)
-                else:
-                    nc.scalar.activation(out=wide[:, cols], in_=src, func=COPY, scale=col)
+        def weave_y(strip, half):
+            woven = work.tile([P, STRIP * PACK], U8, name="y_woven", bufs=WOVEN_Y_BUFS)
+            tiles["y_woven", strip, half] = woven
+            first = (strip % 2) * STRIP
+            weave(woven[:], tiles["y_raw", half, strip // 2][:, :, first : first + STRIP])
 
-        def quant_y(nb, half):
-            nc.vector.quantize_mx(out=y_codes[:, nb, half, :].bitcast(FP8X4), scales=y_scales[:, nb, half, :], in_=tiles["y_wide", nb, half][:])
+        def widen_y(strip, half):
+            wide = work.tile([P, STRIP * PACK], BF16, name="y_wide", bufs=WIDE_Y_BUFS, align_bytes=64)
+            tiles["y_wide", strip, half] = wide
+            for i in range(STRIP // P):
+                span = slice(P * PACK * i, P * PACK * (i + 1))
+                block = strip * (STRIP // P) + i
+                src = tiles["y_woven", strip, half][:, span].bitcast(FP8)
+                nc.scalar.activation(out=wide[:, span], in_=src, func=COPY, scale=scale[:, 1, half, block : block + 1])
 
-        def second_product(tt, nb):
-            t = bank("second", [P, 512])
-            tiles["p_bank", tt, nb] = t
-            ch, i = divmod(tt, TC // P)
-            for half in range(2):
+        def quant_y(strip, half):
+            nc.vector.quantize_mx(
+                out=y_codes[:, strip, half, :].bitcast(FP8X4),
+                scales=y_scales[:, strip, half, :],
+                in_=tiles["y_wide", strip, half][:],
+            )
+
+        def second_product(row_tile, strip):
+            on_turn_ring = strip >= FIRST_STRIP_ON_BOTH_RINGS and row_tile % 2 == 0
+            sums = bank("turn" if on_turn_ring else "acc", [P, STRIP])
+            tiles["p_bank", row_tile, strip] = sums
+            chunk, i = divmod(row_tile, CHUNK // P)
+            for half in range(HALVES):
                 nc.tensor.matmul_mx(
-                    out=t[:],
-                    lhsT=a_codes[:, ch, half, i * P : (i + 1) * P].bitcast(FP8X4), lhsT_scale=a_scales[:, ch, half, i * P : (i + 1) * P],
-                    rhs=y_codes[:, nb, half, :].bitcast(FP8X4), rhs_scale=y_scales[:, nb, half, :],
-                    start=(half == 0), stop=(half == 1),
+                    out=sums[:],
+                    lhsT=a_codes[:, chunk, half, i * P : (i + 1) * P].bitcast(FP8X4),
+                    lhsT_scale=a_scales[:, chunk, half, i * P : (i + 1) * P],
+                    rhs=y_codes[:, strip, half, :].bitcast(FP8X4),
+                    rhs_scale=y_scales[:, strip, half, :],
+                    start=(half == 0),
+                    stop=(half == HALVES - 1),
                 )
 
-        def finish(tt, nb):
-            res = work.tile([P, 512], F32, name="res", bufs=RES_BUFS)
-            cols = slice(512 * nb, 512 * (nb + 1))
-            nc.vector.tensor_tensor(out=res[:], in0=tiles["p_bank", tt, nb][:], in1=h_all[:, cols], op=MULT)
-            nc.sync.dma_start(out=out[tt * P : (tt + 1) * P, cols], in_=res[:])
+        def finish(row_tile, strip):
+            res = work.tile([P, STRIP], F32, name="res", bufs=RESULT_BUFS)
+            cols = slice(STRIP * strip, STRIP * (strip + 1))
+            nc.vector.tensor_tensor(out=res[:], in0=tiles["p_bank", row_tile, strip][:], in1=h_all[:, cols], op=MULT)
+            nc.sync.dma_start(out=out[row_tile * P : (row_tile + 1) * P, cols], in_=res[:])
 
-        def empty_p(tt, nb):
-            t = work.tile([P, 512], F32, name="p_copy", bufs=2)
-            tiles["p_copy", tt, nb] = t
-            nc.scalar.copy(out=t[:], in_=tiles["p_bank", tt, nb][:])
-
-        def finish_pool(tt, nb):
-            res = work.tile([P, 512], F32, name="res_pool", bufs=2)
-            cols = slice(512 * nb, 512 * (nb + 1))
-            nc.gpsimd.tensor_tensor(out=res[:], in0=tiles["p_copy", tt, nb][:], in1=h_all[:, cols], op=MULT)
-            nc.sync.dma_start(out=out[tt * P : (tt + 1) * P, cols], in_=res[:])
-
-        jobs = {
-            "EP": empty_p, "FP": finish_pool, "SS": spread_scales, "W": warm, "SH": spread_h, "EH": empty_h, "WA": widen_s_scalar,
-            "load_small": load_small, "load_c": load_c, "pick_scales": pick_scales, "invert_c": invert_c, "load_h": load_h,
-            "load_s": load_s, "load_g": load_g, "load_y": load_y,
-            "WS": widen_s, "TS": turn_s, "ES": empty_s, "QS": quant_s,
-            "TG": turn_g, "EG": empty_g, "QG": quant_g,
-            "M1": first_product, "EU": empty_u, "IA": weave_a, "QA": quant_a,
-            "IY": weave_y, "WY": widen_y, "QY": quant_y, "M2": second_product, "FO": finish,
+        steps = {
+            "load_scales": load_scales,
+            "load_c": load_c,
+            "load_h": load_h,
+            "load_s": load_s,
+            "load_g": load_g,
+            "load_y": load_y,
+            "spread_scales": spread_scales,
+            "pick_scales": pick_scales,
+            "invert_c": invert_c,
+            "warm_tensor": warm_tensor,
+            "spread_h": spread_h,
+            "empty_h": empty_h,
+            "widen_s": widen_s,
+            "widen_s_scalar": widen_s_scalar,
+            "turn_s": turn_s,
+            "empty_s": empty_s,
+            "quant_s": quant_s,
+            "turn_g": turn_g,
+            "empty_g": empty_g,
+            "quant_g": quant_g,
+            "first_product": first_product,
+            "empty_u": empty_u,
+            "weave_a": weave_a,
+            "quant_a": quant_a,
+            "weave_y": weave_y,
+            "widen_y": widen_y,
+            "quant_y": quant_y,
+            "second_product": second_product,
+            "finish": finish,
         }
-        for entry in ORDER:
-            job, args = jobs[entry[0]], entry[1:]
+        for entry in ORDER.split(","):
+            parts = entry.split()
+            job, args = steps[parts[0]], [int(index) for index in parts[1:]]
             job(*args)

@@ -30,51 +30,15 @@ STRIPS = N // STRIP
 
 SCALAR_PASSES = (2, 1, 1, 0, 0, 0, 0, 0)
 RING_BANKS = 4
-FIRST_STRIP_ON_BOTH_RINGS = 2
-WARM_MATMULS = 4
+FIRST_CHUNK_WOVEN_BY_SCALAR = 2
 
 WIDE_S_BUFS = 4
-TURNED_BUFS = 3
-A_PLANE_BUFS = 6
+TURNED_BUFS = 4
+A_PLANE_BUFS = 4
 WOVEN_A_BUFS = 2
-WOVEN_Y_BUFS = 6
-WIDE_Y_BUFS = 3
-RESULT_BUFS = 7
-
-ORDER = """
-load_scales, spread_scales, pick_scales, load_s 0, widen_s 0, widen_s_scalar 0, load_h, load_s 2,
-widen_s_scalar 2, load_s 1, load_g 0, widen_s_scalar 1, load_g 1, load_s 3, load_g 4, load_y 1 0,
-load_g 5, load_s 4, load_g 3, load_s 5, load_s 7, load_g 6, load_c, load_y 1 1, load_g 2, load_s 6,
-load_y 0 1, load_y 0 0, load_g 7, warm_tensor, spread_h 0, turn_s 0, empty_s 0, turn_g 0 1, empty_g 0 1,
-widen_s 2, widen_s 1, widen_s 3, quant_s 0, turn_s 2, turn_g 0 0, empty_s 2, empty_g 0 0, spread_h 1,
-turn_s 1, empty_s 1, turn_s 3, empty_s 3, turn_g 2 1, quant_g 0 1, weave_y 0 1, widen_s 4, quant_s 2,
-quant_g 0 0, quant_s 1, widen_s 5, quant_s 3, invert_c, empty_g 2 1, turn_g 2 0, empty_g 2 0, empty_h 0,
-turn_s 4, empty_s 4, first_product 0 0, turn_s 5, widen_y 0 1, turn_g 1 1, quant_g 2 0, quant_g 2 1,
-empty_h 1, empty_g 1 1, empty_s 5, empty_u 0 0, first_product 0 1, first_product 2 0, first_product 2 1,
-widen_s 6, widen_s 7, turn_s 6, weave_y 0 0, quant_s 4, weave_y 3 1, quant_s 5, turn_s 7, empty_s 6,
-turn_g 1 0, empty_u 0 1, empty_s 7, first_product 2 2, empty_g 1 0, empty_u 2 1, empty_u 2 0,
-empty_u 2 2, turn_g 3 0, turn_g 3 1, empty_g 3 1, widen_y 0 0, first_product 0 2, empty_u 0 2,
-weave_y 3 0, weave_y 1 0, quant_g 1 0, quant_s 7, quant_s 6, quant_g 1 1, first_product 2 3,
-first_product 0 3, first_product 1 3, first_product 1 1, quant_y 0 1, quant_g 3 1, weave_y 2 0,
-weave_a 0 0, weave_a 2 0, quant_y 0 0, empty_u 2 3, empty_u 0 3, empty_g 3 0, empty_u 1 3, quant_a 0 0,
-weave_y 1 1, weave_y 2 1, quant_g 3 0, quant_a 2 0, weave_a 2 1, weave_a 0 1, quant_a 2 1, widen_y 1 0,
-empty_u 1 1, first_product 1 0, first_product 1 2, first_product 3 2, empty_u 1 0, empty_u 1 2,
-empty_u 3 2, first_product 3 3, second_product 5 0, second_product 4 0, first_product 3 0, empty_u 3 3,
-quant_a 0 1, weave_a 1 0, weave_a 1 1, widen_y 1 1, quant_y 1 0, quant_a 1 0, quant_a 1 1, finish 5 0,
-finish 4 0, weave_a 3 1, second_product 3 0, empty_u 3 0, widen_y 2 0, second_product 1 0,
-second_product 2 0, quant_y 1 1, finish 3 0, second_product 3 1, finish 2 0, finish 1 0, quant_a 3 1,
-finish 3 1, quant_y 2 0, first_product 3 1, second_product 0 0, empty_u 3 1, second_product 2 1,
-second_product 0 1, finish 0 0, weave_a 3 0, widen_y 2 1, widen_y 3 0, widen_y 3 1, finish 2 1,
-quant_a 3 0, finish 0 1, second_product 5 1, second_product 1 1, quant_y 2 1, second_product 7 0,
-finish 5 1, finish 7 0, second_product 6 0, finish 6 0, finish 1 1, second_product 2 2,
-second_product 7 1, second_product 0 2, finish 2 2, finish 7 1, second_product 4 1, finish 0 2,
-finish 4 1, second_product 6 1, second_product 5 2, quant_y 3 1, finish 5 2, second_product 6 2,
-second_product 1 2, second_product 3 2, finish 6 1, finish 1 2, finish 3 2, quant_y 3 0,
-second_product 4 2, finish 4 2, second_product 7 2, finish 6 2, second_product 2 3, second_product 3 3,
-finish 2 3, finish 7 2, finish 3 3, second_product 1 3, second_product 0 3, second_product 4 3,
-finish 1 3, finish 4 3, second_product 6 3, finish 0 3, finish 6 3, second_product 5 3, finish 5 3,
-second_product 7 3, finish 7 3
-"""
+WIDE_Y_BUFS = 6
+WOVEN_Y_BUFS = 2
+RESULT_BUFS = 8
 
 
 def tile_curvature_scaled_pair_correction_d7_kernel(tc, G, S_bytes, S_scale, Y_bytes, Y_scale, c, h, out):
@@ -88,18 +52,13 @@ def tile_curvature_scaled_pair_correction_d7_kernel(tc, G, S_bytes, S_scale, Y_b
         ident = keep.tile([P, P], F32, name="ident")
         make_identity(nc, ident[:])
 
-        s_col = keep.tile([P, 1], F32, name="s_col")
-        y_col = keep.tile([P, 1], F32, name="y_col")
         h_rows = keep.tile([P, STRIP], BF16, name="h_rows")
         pick = keep.tile([P, STRIPS], BF16, name="pick")
-        idle = keep.tile([P, STRIP], BF16, name="idle")
-        idle_out = keep.tile([P, 1], F32, name="idle_out")
         nc.vector.memset(h_rows[:], 0.0)
-        nc.vector.memset(idle[:], 0.0)
-        nc.scalar.activation(out=idle_out[:], in_=idle[:, 0:1], func=COPY)
         nc.gpsimd.tensor_copy(out=pick[:], in_=ident[:, 0:STRIPS])
 
-        scale = keep.tile([P, 2, HALVES, COL_BLOCKS], F32, name="scale")
+        s_factor = [keep.tile([P, COL_BLOCKS], F32, name="s_factor%d" % half) for half in range(HALVES)]
+        y_factor = [keep.tile([P, COL_BLOCKS], F32, name="y_factor%d" % half) for half in range(HALVES)]
         c_bf = keep.tile([P, HALVES, PACK], BF16, name="c_bf")
         c_inv = keep.tile([P, SLICES], F32, name="c_inv")
         h_all = keep.tile([P, N], BF16, name="h_all")
@@ -120,21 +79,9 @@ def tile_curvature_scaled_pair_correction_d7_kernel(tc, G, S_bytes, S_scale, Y_b
         def bank(ring, shape, dtype=F32):
             return psum.tile(shape, dtype, name="bank", tag=ring, bufs=RING_BANKS)
 
-        def load_scales():
-            nc.sync.dma_start(out=s_col[:], in_=S_scale.rearrange("a (b o) -> (a b) o", o=1))
-            nc.sync.dma_start(out=y_col[:], in_=Y_scale.rearrange("a (b o) -> (a b) o", o=1))
-
-        def spread_scales():
-            tables = bank("acc", [P, 2, P])
-            tiles["tables"] = tables
-            nc.tensor.transpose(tables[:, 0, :], s_col[:].to_broadcast([P, P]), ident[:])
-            nc.tensor.transpose(tables[:, 1, :], y_col[:].to_broadcast([P, P]), ident[:])
-
-        def pick_scales():
-            for q in range(P // QUAD):
-                rows = slice(QUAD * q, QUAD * (q + 1))
-                table = tiles["tables"][rows].rearrange("p s (half q k) -> p s half q k", half=HALVES, q=P // QUAD)
-                nc.vector.tensor_copy(out=scale[rows], in_=table[:, :, :, q, :])
+        def load_factor(factor, table, half):
+            rows = table[PACK * half : PACK * (half + 1), :].partition_broadcast(QUAD)
+            nc.sync.dma_start(out=factor[half][:], in_=rows.rearrange("r q k -> q r k"))
 
         def load_c():
             nc.sync.dma_start(out=c_bf[:], in_=c.rearrange("(half p j) -> p half j", half=HALVES, j=PACK))
@@ -157,25 +104,21 @@ def tile_curvature_scaled_pair_correction_d7_kernel(tc, G, S_bytes, S_scale, Y_b
             cols = slice(2 * STRIP * b, 2 * STRIP * (b + 1))
             nc.scalar.copy(out=h_all[:, cols], in_=tiles["h_bank", b][:].rearrange("p i n -> p (i n)"))
 
-        def warm_tensor():
-            unread = bank("acc", [P, STRIP])
-            for i in range(WARM_MATMULS):
-                nc.tensor.matmul(unread[:], lhsT=idle[:, 0:P], rhs=idle[:], start=True, stop=True)
-
         def load_s(u):
             raw = keep.tile([P, N], U8, name="s_raw%d" % u)
             nc.sync.dma_start(out=raw[:], in_=s_rows[u // PACK, u % PACK])
             tiles["s_raw", u] = raw
 
-        def load_g(row_tile):
-            raw = keep.tile([P, N], BF16, name="g_raw%d" % row_tile)
-            nc.sync.dma_start(out=raw[:], in_=G[row_tile * P : (row_tile + 1) * P, :])
-            tiles["g_raw", row_tile] = raw
+        def load_g(chunk, b):
+            raw = keep.tile([P, CHUNK // P, 2 * K_PASS], BF16, name="g_raw%d%d" % (chunk, b))
+            rows = G[chunk * CHUNK : (chunk + 1) * CHUNK, 2 * K_PASS * b : 2 * K_PASS * (b + 1)]
+            nc.sync.dma_start(out=raw[:], in_=rows.rearrange("(i r) n -> r i n", r=P))
+            tiles["g_raw", chunk, b] = raw
 
-        def load_y(half, side):
-            raw = keep.tile([P, PACK, 2 * STRIP], U8, name="y_raw%d%d" % (half, side))
-            nc.sync.dma_start(out=raw[:], in_=y_rows[half][:, :, side * 2 * STRIP : (side + 1) * 2 * STRIP])
-            tiles["y_raw", half, side] = raw
+        def load_y(strip, half):
+            raw = keep.tile([P, PACK, STRIP], U8, name="y_raw%d%d" % (strip, half))
+            nc.sync.dma_start(out=raw[:], in_=y_rows[half][:, :, strip * STRIP : (strip + 1) * STRIP])
+            tiles["y_raw", strip, half] = raw
 
         def wide_s_tile(u):
             if ("s_wide", u) not in tiles:
@@ -191,7 +134,7 @@ def tile_curvature_scaled_pair_correction_d7_kernel(tc, G, S_bytes, S_scale, Y_b
                     nc.vector.tensor_scalar(
                         out=sorted_by_w[:, g, QUAD * q : QUAD * (q + 1)],
                         in0=raw[:, block * P : (block + 1) * P].bitcast(FP8).rearrange("r (p w e) -> r p w e", w=2, e=2),
-                        scalar1=scale[:, 0, u // PACK, block : block + 1],
+                        scalar1=s_factor[u // PACK][:, block : block + 1],
                         scalar2=None,
                         op0=MULT,
                     )
@@ -201,7 +144,7 @@ def tile_curvature_scaled_pair_correction_d7_kernel(tc, G, S_bytes, S_scale, Y_b
             wide = wide_s_tile(u)
             for block in range(COL_BLOCKS - PACK * SCALAR_PASSES[u], COL_BLOCKS):
                 cols = slice(block * P, (block + 1) * P)
-                factor = scale[:, 0, u // PACK, block : block + 1]
+                factor = s_factor[u // PACK][:, block : block + 1]
                 nc.scalar.activation(out=wide[:, cols], in_=raw[:, cols].bitcast(FP8), func=COPY, scale=factor)
 
         def turn_s(u):
@@ -225,7 +168,7 @@ def tile_curvature_scaled_pair_correction_d7_kernel(tc, G, S_bytes, S_scale, Y_b
             )
 
         def empty_s(u):
-            joined = work.tile([P, 2, 2 * P, 2], F32, name="s_turned", bufs=TURNED_BUFS, align_bytes=64)
+            joined = work.tile([P, 2, 2 * P, 2], F32, name="s_turned", tag="turned", bufs=TURNED_BUFS, align_bytes=64)
             tiles["s_turned", u] = joined
             for b in range(2):
                 join_words(joined[:, b], tiles["s_bank", u, b])
@@ -238,16 +181,16 @@ def tile_curvature_scaled_pair_correction_d7_kernel(tc, G, S_bytes, S_scale, Y_b
             )
 
         def turn_g(chunk, b):
-            for g in (2 * b, 2 * b + 1):
+            for g in range(2):
                 turned = bank("turn", [P, 2, 2, P])
-                tiles["g_bank", chunk, g] = turned
+                tiles["g_bank", chunk, 2 * b + g] = turned
                 for i in range(2):
-                    words = tiles["g_raw", 2 * chunk + i][:].bitcast(F32)
+                    words = tiles["g_raw", chunk, b][:, i, :].bitcast(F32)
                     for w in range(2):
                         nc.tensor.transpose(turned[:, w, i, :], words[:, 2 * P * g + w : 2 * P * (g + 1) : 2], ident[:])
 
         def empty_g(chunk, b):
-            joined = work.tile([P, 2, CHUNK, 2], F32, name="g_turned", bufs=TURNED_BUFS, align_bytes=64)
+            joined = work.tile([P, 2, CHUNK, 2], F32, name="g_turned", tag="turned", bufs=TURNED_BUFS, align_bytes=64)
             tiles["g_turned", chunk, b] = joined
             for i in range(2):
                 join_words(joined[:, i], tiles["g_bank", chunk, 2 * b + i])
@@ -285,16 +228,15 @@ def tile_curvature_scaled_pair_correction_d7_kernel(tc, G, S_bytes, S_scale, Y_b
                 sums = tiles["u_bank", chunk, b][:, i, :]
                 nc.scalar.activation(out=planes[:, u % PACK, :], in_=sums, func=COPY, scale=c_inv[:, u : u + 1])
 
-        def weave(dst, planes):
-            nc.vector.tensor_copy(
-                out=dst.rearrange("p (x i j) -> p x j i", i=4, j=PACK),
-                in_=planes.rearrange("p j (x i) -> p x j i", i=4),
-            )
-
         def weave_a(chunk, half):
             woven = work.tile([P, CHUNK * PACK], BF16, name="a_woven", bufs=WOVEN_A_BUFS, align_bytes=64)
             tiles["a_woven", chunk, half] = woven
-            weave(woven[:], tiles["a_planes", chunk, half][:])
+            dst = woven[:].rearrange("p (x i j) -> p x j i", i=4, j=PACK)
+            src = tiles["a_planes", chunk, half][:].rearrange("p j (x i) -> p x j i", i=4)
+            if chunk >= FIRST_CHUNK_WOVEN_BY_SCALAR:
+                nc.scalar.copy(out=dst, in_=src)
+            else:
+                nc.vector.tensor_copy(out=dst, in_=src)
 
         def quant_a(chunk, half):
             nc.vector.quantize_mx(
@@ -303,31 +245,34 @@ def tile_curvature_scaled_pair_correction_d7_kernel(tc, G, S_bytes, S_scale, Y_b
                 in_=tiles["a_woven", chunk, half][:],
             )
 
-        def weave_y(strip, half):
-            woven = work.tile([P, STRIP * PACK], U8, name="y_woven", bufs=WOVEN_Y_BUFS)
-            tiles["y_woven", strip, half] = woven
-            first = (strip % 2) * STRIP
-            weave(woven[:], tiles["y_raw", half, strip // 2][:, :, first : first + STRIP])
-
         def widen_y(strip, half):
-            wide = work.tile([P, STRIP * PACK], BF16, name="y_wide", bufs=WIDE_Y_BUFS, align_bytes=64)
+            wide = work.tile([P, PACK, STRIP], BF16, name="y_wide", bufs=WIDE_Y_BUFS)
             tiles["y_wide", strip, half] = wide
+            raw = tiles["y_raw", strip, half][:].rearrange("p j n -> p (j n)")
+            nc.scalar.copy(out=wide[:].rearrange("p j n -> p (j n)"), in_=raw.bitcast(FP8))
+
+        def weave_y(strip, half):
+            woven = work.tile([P, STRIP * PACK], BF16, name="y_woven", bufs=WOVEN_Y_BUFS, align_bytes=64)
+            tiles["y_woven", strip, half] = woven
             for i in range(STRIP // P):
-                span = slice(P * PACK * i, P * PACK * (i + 1))
                 block = strip * (STRIP // P) + i
-                src = tiles["y_woven", strip, half][:, span].bitcast(FP8)
-                nc.scalar.activation(out=wide[:, span], in_=src, func=COPY, scale=scale[:, 1, half, block : block + 1])
+                nc.vector.tensor_scalar(
+                    out=woven[:, P * PACK * i : P * PACK * (i + 1)].rearrange("p (x i j) -> p x j i", i=4, j=PACK),
+                    in0=tiles["y_wide", strip, half][:, :, P * i : P * (i + 1)].rearrange("p j (x i) -> p x j i", i=4),
+                    scalar1=y_factor[half][:, block : block + 1],
+                    scalar2=None,
+                    op0=MULT,
+                )
 
         def quant_y(strip, half):
             nc.vector.quantize_mx(
                 out=y_codes[:, strip, half, :].bitcast(FP8X4),
                 scales=y_scales[:, strip, half, :],
-                in_=tiles["y_wide", strip, half][:],
+                in_=tiles["y_woven", strip, half][:],
             )
 
         def second_product(row_tile, strip):
-            on_turn_ring = strip >= FIRST_STRIP_ON_BOTH_RINGS and row_tile % 2 == 0
-            sums = bank("turn" if on_turn_ring else "acc", [P, STRIP])
+            sums = bank(out_ring(row_tile, strip), [P, STRIP])
             tiles["p_bank", row_tile, strip] = sums
             chunk, i = divmod(row_tile, CHUNK // P)
             for half in range(HALVES):
@@ -347,38 +292,92 @@ def tile_curvature_scaled_pair_correction_d7_kernel(tc, G, S_bytes, S_scale, Y_b
             nc.vector.tensor_tensor(out=res[:], in0=tiles["p_bank", row_tile, strip][:], in1=h_all[:, cols], op=MULT)
             nc.sync.dma_start(out=out[row_tile * P : (row_tile + 1) * P, cols], in_=res[:])
 
-        steps = {
-            "load_scales": load_scales,
-            "load_c": load_c,
-            "load_h": load_h,
-            "load_s": load_s,
-            "load_g": load_g,
-            "load_y": load_y,
-            "spread_scales": spread_scales,
-            "pick_scales": pick_scales,
-            "invert_c": invert_c,
-            "warm_tensor": warm_tensor,
-            "spread_h": spread_h,
-            "empty_h": empty_h,
-            "widen_s": widen_s,
-            "widen_s_scalar": widen_s_scalar,
-            "turn_s": turn_s,
-            "empty_s": empty_s,
-            "quant_s": quant_s,
-            "turn_g": turn_g,
-            "empty_g": empty_g,
-            "quant_g": quant_g,
-            "first_product": first_product,
-            "empty_u": empty_u,
-            "weave_a": weave_a,
-            "quant_a": quant_a,
-            "weave_y": weave_y,
-            "widen_y": widen_y,
-            "quant_y": quant_y,
-            "second_product": second_product,
-            "finish": finish,
+        def load_s_factor(half):
+            load_factor(s_factor, S_scale, half)
+
+        def load_y_factor(half):
+            load_factor(y_factor, Y_scale, half)
+
+        def out_ring(row_tile, strip):
+            return "turn" if strip < 2 or row_tile % 2 == 0 else "acc"
+
+        sync_steps = [(load_s_factor, 0), (load_s, 0), (load_y, 0, 0), (load_y, 0, 1), (load_y, 1, 0), (load_y, 1, 1), (load_y, 2, 0), (load_y, 2, 1), (load_s, 1), (load_h, ), (load_s, 2), (load_g, 0, 0), (load_g, 0, 1), (load_s, 3), (load_c, ), (load_s_factor, 1), (load_s, 4), (load_g, 1, 0), (load_g, 1, 1), (load_s, 5), (load_s, 6), (load_s, 7), (load_y_factor, 0), (load_y_factor, 1), (load_g, 2, 0), (load_g, 2, 1), (load_g, 3, 0), (load_g, 3, 1), (load_y, 3, 0), (load_y, 3, 1)]
+        vector_steps = [(widen_s, 0), (widen_s, 1), (widen_s, 2), (quant_s, 0), (widen_s, 3), (quant_s, 1), (quant_g, 0, 0), (invert_c, ), (widen_s, 4), (quant_g, 0, 1), (quant_s, 2), (widen_s, 5), (quant_s, 3), (quant_g, 1, 0), (widen_s, 6), (quant_g, 1, 1), (quant_s, 4), (widen_s, 7), (quant_s, 5), (weave_y, 0, 0), (weave_a, 0, 0), (quant_y, 0, 0), (quant_s, 6), (quant_a, 0, 0), (quant_s, 7), (weave_a, 1, 0), (weave_y, 0, 1), (quant_a, 1, 0), (quant_y, 0, 1), (weave_a, 0, 1), (quant_g, 2, 0), (quant_a, 0, 1), (weave_a, 1, 1), (quant_g, 2, 1), (quant_a, 1, 1), (finish, 0, 0), (weave_y, 1, 0), (finish, 1, 0), (quant_y, 1, 0), (finish, 2, 0), (weave_y, 1, 1), (finish, 3, 0), (quant_y, 1, 1), (quant_a, 2, 0), (finish, 0, 1), (quant_g, 3, 0), (finish, 1, 1), (quant_g, 3, 1), (finish, 2, 1), (weave_y, 2, 0), (finish, 3, 1), (quant_y, 2, 0), (quant_a, 2, 1), (weave_y, 2, 1), (finish, 4, 0), (quant_y, 2, 1), (finish, 5, 0), (finish, 4, 1), (quant_a, 3, 0), (finish, 5, 1), (weave_y, 3, 0), (finish, 0, 2), (quant_y, 3, 0), (finish, 1, 2), (quant_a, 3, 1), (finish, 2, 2), (finish, 3, 2), (weave_y, 3, 1), (finish, 4, 2), (quant_y, 3, 1), (finish, 5, 2), (finish, 6, 0), (finish, 7, 0), (finish, 6, 1), (finish, 7, 1), (finish, 6, 2), (finish, 7, 2), (finish, 0, 3), (finish, 1, 3), (finish, 2, 3), (finish, 3, 3), (finish, 4, 3), (finish, 5, 3), (finish, 6, 3), (finish, 7, 3)]
+        scalar_steps = [(widen_s_scalar, 0), (widen_y, 0, 0), (widen_y, 0, 1), (widen_y, 1, 0), (widen_y, 1, 1), (widen_y, 2, 0), (widen_y, 2, 1), (widen_s_scalar, 1), (widen_s_scalar, 2), (empty_s, 0), (empty_s, 1), (empty_g, 0, 0), (empty_g, 0, 1), (empty_s, 2), (empty_s, 3), (empty_h, 0), (empty_g, 1, 0), (empty_u, 0, 0), (empty_g, 1, 1), (empty_s, 4), (empty_u, 0, 1), (empty_s, 5), (empty_u, 1, 0), (empty_s, 6), (empty_u, 1, 1), (empty_s, 7), (empty_u, 0, 2), (empty_u, 1, 2), (empty_u, 0, 3), (empty_g, 2, 0), (empty_u, 1, 3), (empty_g, 2, 1), (empty_u, 2, 0), (empty_u, 2, 1), (weave_a, 2, 0), (empty_g, 3, 0), (empty_g, 3, 1), (empty_u, 2, 2), (empty_u, 2, 3), (weave_a, 2, 1), (empty_h, 1), (empty_u, 3, 0), (empty_u, 3, 1), (weave_a, 3, 0), (empty_u, 3, 2), (empty_u, 3, 3), (widen_y, 3, 0), (weave_a, 3, 1), (widen_y, 3, 1)]
+        tensor_steps = [(spread_h, 0), (turn_s, 0), (turn_s, 1), (turn_g, 0, 0), (turn_g, 0, 1), (turn_s, 2), (turn_s, 3), (turn_g, 1, 0), (first_product, 0, 0), (turn_g, 1, 1), (turn_s, 4), (first_product, 0, 1), (turn_s, 5), (first_product, 1, 0), (turn_s, 6), (first_product, 1, 1), (turn_s, 7), (first_product, 0, 2), (first_product, 1, 2), (turn_g, 2, 0), (first_product, 0, 3), (turn_g, 2, 1), (first_product, 1, 3), (spread_h, 1), (second_product, 0, 0), (second_product, 1, 0), (first_product, 2, 0), (first_product, 2, 1), (second_product, 2, 0), (second_product, 3, 0), (turn_g, 3, 0), (turn_g, 3, 1), (first_product, 2, 2), (first_product, 2, 3), (second_product, 0, 1), (second_product, 1, 1), (second_product, 2, 1), (second_product, 3, 1), (first_product, 3, 0), (first_product, 3, 1), (second_product, 4, 0), (second_product, 5, 0), (second_product, 4, 1), (second_product, 5, 1), (first_product, 3, 2), (first_product, 3, 3), (second_product, 0, 2), (second_product, 1, 2), (second_product, 2, 2), (second_product, 3, 2), (second_product, 4, 2), (second_product, 5, 2), (second_product, 6, 0), (second_product, 7, 0), (second_product, 6, 1), (second_product, 7, 1), (second_product, 6, 2), (second_product, 7, 2), (second_product, 0, 3), (second_product, 1, 3), (second_product, 2, 3), (second_product, 3, 3), (second_product, 4, 3), (second_product, 5, 3), (second_product, 6, 3), (second_product, 7, 3)]
+
+
+        def inputs(job, a=0, b=0):
+            table = {
+                widen_s: [(load_s, a), (load_s_factor, a // PACK)],
+                widen_s_scalar: [(load_s, a), (load_s_factor, a // PACK)],
+                turn_s: [(widen_s, a)] + ([(widen_s_scalar, a)] if job is turn_s and SCALAR_PASSES[a] else []),
+                empty_s: [(turn_s, a)],
+                quant_s: [(empty_s, a)],
+                turn_g: [(load_g, a, b)],
+                empty_g: [(turn_g, a, b)],
+                quant_g: [(empty_g, a, b)],
+                first_product: [(quant_s, 2 * b), (quant_s, 2 * b + 1), (quant_g, a, 0), (quant_g, a, 1)],
+                empty_u: [(first_product, a, b), (invert_c,)],
+                weave_a: [(empty_u, a, 2 * b), (empty_u, a, 2 * b + 1)],
+                quant_a: [(weave_a, a, b)],
+                widen_y: [(load_y, a, b)],
+                weave_y: [(widen_y, a, b), (load_y_factor, b)],
+                quant_y: [(weave_y, a, b)],
+                second_product: [(quant_a, a // 2, 0), (quant_a, a // 2, 1), (quant_y, b, 0), (quant_y, b, 1)],
+                finish: [(second_product, a, b), (empty_h, b // 2)],
+                invert_c: [(load_c,)],
+                spread_h: [(load_h,)],
+                empty_h: [(spread_h, a)],
+            }
+            return table.get(job, [])
+
+        def buffers(job, a=0, b=0):
+            table = {
+                widen_s: {"wide_s": 0 if job is widen_s and SCALAR_PASSES[a] else 1},
+                widen_s_scalar: {"wide_s": 1},
+                turn_s: {"wide_s": -1, "turn": 2},
+                turn_g: {"turn": 2},
+                empty_s: {"turn": -2, "turned": 1},
+                empty_g: {"turn": -2, "turned": 1},
+                quant_s: {"turned": -1},
+                quant_g: {"turned": -1},
+                spread_h: {"acc": 1},
+                empty_h: {"acc": -1},
+                first_product: {"acc": 1},
+                empty_u: {"acc": -1, "planes": 1 - b % 2},
+                weave_a: {"planes": -1, "a_woven": 1},
+                quant_a: {"a_woven": -1},
+                widen_y: {"y_wide": 1},
+                weave_y: {"y_wide": -1, "y_woven": 1},
+                quant_y: {"y_woven": -1},
+                second_product: {out_ring(a, b): 1},
+                finish: {out_ring(a, b): -1},
+            }
+            return table.get(job, {})
+
+        free = {
+            "wide_s": WIDE_S_BUFS,
+            "turn": RING_BANKS,
+            "acc": RING_BANKS,
+            "turned": TURNED_BUFS,
+            "planes": A_PLANE_BUFS,
+            "a_woven": WOVEN_A_BUFS,
+            "y_wide": WIDE_Y_BUFS,
+            "y_woven": WOVEN_Y_BUFS,
         }
-        for entry in ORDER.split(","):
-            parts = entry.split()
-            job, args = steps[parts[0]], [int(index) for index in parts[1:]]
-            job(*args)
+        queues = [sync_steps, scalar_steps, vector_steps, tensor_steps]
+        written = set()
+        for sweep in range(sum(len(queue) for queue in queues)):
+            for queue in queues:
+                todo = [step for step in queue if step not in written]
+                if not todo:
+                    continue
+                step = todo[0]
+                taken = buffers(*step)
+                if all(need in written for need in inputs(*step)) and all(free[kind] >= n for kind, n in taken.items()):
+                    step[0](*step[1:])
+                    written.add(step)
+                    for kind, n in taken.items():
+                        free[kind] = free[kind] - n
+        assert len(written) == sum(len(queue) for queue in queues)

@@ -28,16 +28,17 @@ CHUNKS = T // CHUNK
 STRIP = 512
 STRIPS = N // STRIP
 
-SCALAR_PASSES = (2, 1, 1, 0, 0, 0, 0, 0)
+SCALAR_PASSES = (2, 2, 0, 0, 0, 0, 0, 0)
 RING_BANKS = 4
-FIRST_CHUNK_WOVEN_BY_SCALAR = 2
+FIRST_TILE_ON_BOTH_RINGS = 4
+STORE_STRIPS = 1
 
 WIDE_S_BUFS = 4
 TURNED_BUFS = 4
 A_PLANE_BUFS = 4
 WOVEN_A_BUFS = 2
-WIDE_Y_BUFS = 6
-WOVEN_Y_BUFS = 2
+WIDE_Y_BUFS = 3
+WOVEN_Y_BUFS = 3
 RESULT_BUFS = 8
 
 
@@ -51,11 +52,6 @@ def tile_curvature_scaled_pair_correction_d7_kernel(tc, G, S_bytes, S_scale, Y_b
 
         ident = keep.tile([P, P], F32, name="ident")
         make_identity(nc, ident[:])
-
-        h_rows = keep.tile([P, STRIP], BF16, name="h_rows")
-        pick = keep.tile([P, STRIPS], BF16, name="pick")
-        nc.vector.memset(h_rows[:], 0.0)
-        nc.gpsimd.tensor_copy(out=pick[:], in_=ident[:, 0:STRIPS])
 
         s_factor = [keep.tile([P, COL_BLOCKS], F32, name="s_factor%d" % half) for half in range(HALVES)]
         y_factor = [keep.tile([P, COL_BLOCKS], F32, name="y_factor%d" % half) for half in range(HALVES)]
@@ -76,8 +72,12 @@ def tile_curvature_scaled_pair_correction_d7_kernel(tc, G, S_bytes, S_scale, Y_b
         y_rows = Y_bytes.rearrange("(half p j) n -> half p j n", half=HALVES, j=PACK)
         tiles = {}
 
-        def bank(ring, shape, dtype=F32):
-            return psum.tile(shape, dtype, name="bank", tag=ring, bufs=RING_BANKS)
+        def bank(key, ring, shape):
+            tiles[key] = psum.tile(shape, F32, name="bank", tag=ring, bufs=RING_BANKS)
+            return tiles[key]
+
+        def out_ring(row_tile, strip):
+            return "acc" if row_tile >= FIRST_TILE_ON_BOTH_RINGS and strip % 2 == 1 else "turn"
 
         def load_factor(factor, table, half):
             rows = table[PACK * half : PACK * (half + 1), :].partition_broadcast(QUAD)
@@ -90,19 +90,10 @@ def tile_curvature_scaled_pair_correction_d7_kernel(tc, G, S_bytes, S_scale, Y_b
             nc.vector.reciprocal(out=c_inv[:], in_=c_bf[:].rearrange("p half j -> p (half j)"))
 
         def load_h():
-            nc.sync.dma_start(out=h_rows[0:STRIPS, :], in_=h.rearrange("(i n) -> i n", i=STRIPS))
+            nc.sync.dma_start(out=h_all[:], in_=h.partition_broadcast(P))
 
-        def spread_h(b):
-            spread = bank("acc", [P, 2, STRIP], BF16)
-            tiles["h_bank", b] = spread
-            for i in range(2):
-                row = 2 * b + i
-                ones = pick[:, row : row + 1].to_broadcast([P, P])
-                nc.tensor.matmul(spread[:, i, :], lhsT=ones, rhs=h_rows[:], start=True, stop=True)
-
-        def empty_h(b):
-            cols = slice(2 * STRIP * b, 2 * STRIP * (b + 1))
-            nc.scalar.copy(out=h_all[:, cols], in_=tiles["h_bank", b][:].rearrange("p i n -> p (i n)"))
+        def copy_on(step):
+            return nc.vector.tensor_copy if step in vector_steps else nc.scalar.copy
 
         def load_s(u):
             raw = keep.tile([P, N], U8, name="s_raw%d" % u)
@@ -150,8 +141,7 @@ def tile_curvature_scaled_pair_correction_d7_kernel(tc, G, S_bytes, S_scale, Y_b
         def turn_s(u):
             words = tiles["s_wide", u][:].bitcast(F32)
             for b in range(2):
-                turned = bank("turn", [P, 2, 2, P])
-                tiles["s_bank", u, b] = turned
+                turned = bank(("s_bank", u, b), "turn", [P, 2, 2, P])
                 for i in range(2):
                     g = 2 * b + i
                     for w in range(2):
@@ -161,8 +151,8 @@ def tile_curvature_scaled_pair_correction_d7_kernel(tc, G, S_bytes, S_scale, Y_b
                             src = words[:, 2 * P * g + P * w : 2 * P * g + P * (w + 1)]
                         nc.tensor.transpose(turned[:, w, i, :], src, ident[:])
 
-        def join_words(dst, turned):
-            nc.scalar.copy(
+        def join_words(copy, dst, turned):
+            copy(
                 out=dst.rearrange("p (x i) w -> p x w i", i=2),
                 in_=turned[:].rearrange("p w a r -> p w (a r)").rearrange("p w (x i) -> p x w i", i=2),
             )
@@ -171,7 +161,7 @@ def tile_curvature_scaled_pair_correction_d7_kernel(tc, G, S_bytes, S_scale, Y_b
             joined = work.tile([P, 2, 2 * P, 2], F32, name="s_turned", tag="turned", bufs=TURNED_BUFS, align_bytes=64)
             tiles["s_turned", u] = joined
             for b in range(2):
-                join_words(joined[:, b], tiles["s_bank", u, b])
+                join_words(copy_on((empty_s, u)), joined[:, b], tiles["s_bank", u, b])
 
         def quant_s(u):
             nc.vector.quantize_mx(
@@ -182,8 +172,7 @@ def tile_curvature_scaled_pair_correction_d7_kernel(tc, G, S_bytes, S_scale, Y_b
 
         def turn_g(chunk, b):
             for g in range(2):
-                turned = bank("turn", [P, 2, 2, P])
-                tiles["g_bank", chunk, 2 * b + g] = turned
+                turned = bank(("g_bank", chunk, 2 * b + g), "turn", [P, 2, 2, P])
                 for i in range(2):
                     words = tiles["g_raw", chunk, b][:, i, :].bitcast(F32)
                     for w in range(2):
@@ -193,7 +182,7 @@ def tile_curvature_scaled_pair_correction_d7_kernel(tc, G, S_bytes, S_scale, Y_b
             joined = work.tile([P, 2, CHUNK, 2], F32, name="g_turned", tag="turned", bufs=TURNED_BUFS, align_bytes=64)
             tiles["g_turned", chunk, b] = joined
             for i in range(2):
-                join_words(joined[:, i], tiles["g_bank", chunk, 2 * b + i])
+                join_words(copy_on((empty_g, chunk, b)), joined[:, i], tiles["g_bank", chunk, 2 * b + i])
 
         def quant_g(chunk, b):
             nc.vector.quantize_mx(
@@ -202,21 +191,20 @@ def tile_curvature_scaled_pair_correction_d7_kernel(tc, G, S_bytes, S_scale, Y_b
                 in_=tiles["g_turned", chunk, b][:].rearrange("p g t w -> p (g t w)").bitcast(BF16),
             )
 
-        def first_product(chunk, b):
-            sums = bank("acc", [P, 2, CHUNK])
-            tiles["u_bank", chunk, b] = sums
-            for i in range(2):
-                u = 2 * b + i
-                for g in range(PASSES):
-                    nc.tensor.matmul_mx(
-                        out=sums[:, i, :],
-                        lhsT=s_codes[:, u, g, :].bitcast(FP8X4),
-                        lhsT_scale=s_scales[:, u, g, :],
-                        rhs=g_codes[:, chunk, g, :].bitcast(FP8X4),
-                        rhs_scale=g_scales[:, chunk, g, :],
-                        start=(g == 0),
-                        stop=(g == PASSES - 1),
-                    )
+        def first_product(chunk, u):
+            if u % 2 == 0:
+                bank(("u_bank", chunk, u // 2), "acc", [P, 2, CHUNK])
+            sums = tiles["u_bank", chunk, u // 2]
+            for g in range(PASSES):
+                nc.tensor.matmul_mx(
+                    out=sums[:, u % 2, :],
+                    lhsT=s_codes[:, u, g, :].bitcast(FP8X4),
+                    lhsT_scale=s_scales[:, u, g, :],
+                    rhs=g_codes[:, chunk, g, :].bitcast(FP8X4),
+                    rhs_scale=g_scales[:, chunk, g, :],
+                    start=(g == 0),
+                    stop=(g == PASSES - 1),
+                )
 
         def empty_u(chunk, b):
             half = b // 2
@@ -233,10 +221,7 @@ def tile_curvature_scaled_pair_correction_d7_kernel(tc, G, S_bytes, S_scale, Y_b
             tiles["a_woven", chunk, half] = woven
             dst = woven[:].rearrange("p (x i j) -> p x j i", i=4, j=PACK)
             src = tiles["a_planes", chunk, half][:].rearrange("p j (x i) -> p x j i", i=4)
-            if chunk >= FIRST_CHUNK_WOVEN_BY_SCALAR:
-                nc.scalar.copy(out=dst, in_=src)
-            else:
-                nc.vector.tensor_copy(out=dst, in_=src)
+            copy_on((weave_a, chunk, half))(out=dst, in_=src)
 
         def quant_a(chunk, half):
             nc.vector.quantize_mx(
@@ -256,13 +241,13 @@ def tile_curvature_scaled_pair_correction_d7_kernel(tc, G, S_bytes, S_scale, Y_b
             tiles["y_woven", strip, half] = woven
             for i in range(STRIP // P):
                 block = strip * (STRIP // P) + i
-                nc.vector.tensor_scalar(
-                    out=woven[:, P * PACK * i : P * PACK * (i + 1)].rearrange("p (x i j) -> p x j i", i=4, j=PACK),
-                    in0=tiles["y_wide", strip, half][:, :, P * i : P * (i + 1)].rearrange("p j (x i) -> p x j i", i=4),
-                    scalar1=y_factor[half][:, block : block + 1],
-                    scalar2=None,
-                    op0=MULT,
-                )
+                dst = woven[:, P * PACK * i : P * PACK * (i + 1)].rearrange("p (x i j) -> p x j i", i=4, j=PACK)
+                src = tiles["y_wide", strip, half][:, :, P * i : P * (i + 1)].rearrange("p j (x i) -> p x j i", i=4)
+                factor = y_factor[half][:, block : block + 1]
+                if (weave_y, strip, half) in vector_steps:
+                    nc.vector.tensor_scalar(out=dst, in0=src, scalar1=factor, scalar2=None, op0=MULT)
+                else:
+                    nc.scalar.activation(out=dst, in_=src, func=COPY, scale=factor)
 
         def quant_y(strip, half):
             nc.vector.quantize_mx(
@@ -272,8 +257,7 @@ def tile_curvature_scaled_pair_correction_d7_kernel(tc, G, S_bytes, S_scale, Y_b
             )
 
         def second_product(row_tile, strip):
-            sums = bank(out_ring(row_tile, strip), [P, STRIP])
-            tiles["p_bank", row_tile, strip] = sums
+            sums = bank(("p_bank", row_tile, strip), out_ring(row_tile, strip), [P, STRIP])
             chunk, i = divmod(row_tile, CHUNK // P)
             for half in range(HALVES):
                 nc.tensor.matmul_mx(
@@ -287,10 +271,15 @@ def tile_curvature_scaled_pair_correction_d7_kernel(tc, G, S_bytes, S_scale, Y_b
                 )
 
         def finish(row_tile, strip):
-            res = work.tile([P, STRIP], F32, name="res", bufs=RESULT_BUFS)
+            first = strip - strip % STORE_STRIPS
+            if strip == first:
+                tiles["res", row_tile, first] = work.tile([P, STORE_STRIPS * STRIP], F32, name="res", bufs=RESULT_BUFS)
+            res = tiles["res", row_tile, first]
             cols = slice(STRIP * strip, STRIP * (strip + 1))
-            nc.vector.tensor_tensor(out=res[:], in0=tiles["p_bank", row_tile, strip][:], in1=h_all[:, cols], op=MULT)
-            nc.sync.dma_start(out=out[row_tile * P : (row_tile + 1) * P, cols], in_=res[:])
+            part = res[:, STRIP * (strip - first) : STRIP * (strip - first + 1)]
+            nc.vector.tensor_tensor(out=part, in0=tiles["p_bank", row_tile, strip][:], in1=h_all[:, cols], op=MULT)
+            if strip == first + STORE_STRIPS - 1:
+                nc.sync.dma_start(out=out[row_tile * P : (row_tile + 1) * P, STRIP * first : STRIP * (strip + 1)], in_=res[:])
 
         def load_s_factor(half):
             load_factor(s_factor, S_scale, half)
@@ -298,13 +287,10 @@ def tile_curvature_scaled_pair_correction_d7_kernel(tc, G, S_bytes, S_scale, Y_b
         def load_y_factor(half):
             load_factor(y_factor, Y_scale, half)
 
-        def out_ring(row_tile, strip):
-            return "turn" if strip < 2 or row_tile % 2 == 0 else "acc"
-
-        sync_steps = [(load_s_factor, 0), (load_s, 0), (load_y, 0, 0), (load_y, 0, 1), (load_y, 1, 0), (load_y, 1, 1), (load_y, 2, 0), (load_y, 2, 1), (load_s, 1), (load_h, ), (load_s, 2), (load_g, 0, 0), (load_g, 0, 1), (load_s, 3), (load_c, ), (load_s_factor, 1), (load_s, 4), (load_g, 1, 0), (load_g, 1, 1), (load_s, 5), (load_s, 6), (load_s, 7), (load_y_factor, 0), (load_y_factor, 1), (load_g, 2, 0), (load_g, 2, 1), (load_g, 3, 0), (load_g, 3, 1), (load_y, 3, 0), (load_y, 3, 1)]
-        vector_steps = [(widen_s, 0), (widen_s, 1), (widen_s, 2), (quant_s, 0), (widen_s, 3), (quant_s, 1), (quant_g, 0, 0), (invert_c, ), (widen_s, 4), (quant_g, 0, 1), (quant_s, 2), (widen_s, 5), (quant_s, 3), (quant_g, 1, 0), (widen_s, 6), (quant_g, 1, 1), (quant_s, 4), (widen_s, 7), (quant_s, 5), (weave_y, 0, 0), (weave_a, 0, 0), (quant_y, 0, 0), (quant_s, 6), (quant_a, 0, 0), (quant_s, 7), (weave_a, 1, 0), (weave_y, 0, 1), (quant_a, 1, 0), (quant_y, 0, 1), (weave_a, 0, 1), (quant_g, 2, 0), (quant_a, 0, 1), (weave_a, 1, 1), (quant_g, 2, 1), (quant_a, 1, 1), (finish, 0, 0), (weave_y, 1, 0), (finish, 1, 0), (quant_y, 1, 0), (finish, 2, 0), (weave_y, 1, 1), (finish, 3, 0), (quant_y, 1, 1), (quant_a, 2, 0), (finish, 0, 1), (quant_g, 3, 0), (finish, 1, 1), (quant_g, 3, 1), (finish, 2, 1), (weave_y, 2, 0), (finish, 3, 1), (quant_y, 2, 0), (quant_a, 2, 1), (weave_y, 2, 1), (finish, 4, 0), (quant_y, 2, 1), (finish, 5, 0), (finish, 4, 1), (quant_a, 3, 0), (finish, 5, 1), (weave_y, 3, 0), (finish, 0, 2), (quant_y, 3, 0), (finish, 1, 2), (quant_a, 3, 1), (finish, 2, 2), (finish, 3, 2), (weave_y, 3, 1), (finish, 4, 2), (quant_y, 3, 1), (finish, 5, 2), (finish, 6, 0), (finish, 7, 0), (finish, 6, 1), (finish, 7, 1), (finish, 6, 2), (finish, 7, 2), (finish, 0, 3), (finish, 1, 3), (finish, 2, 3), (finish, 3, 3), (finish, 4, 3), (finish, 5, 3), (finish, 6, 3), (finish, 7, 3)]
-        scalar_steps = [(widen_s_scalar, 0), (widen_y, 0, 0), (widen_y, 0, 1), (widen_y, 1, 0), (widen_y, 1, 1), (widen_y, 2, 0), (widen_y, 2, 1), (widen_s_scalar, 1), (widen_s_scalar, 2), (empty_s, 0), (empty_s, 1), (empty_g, 0, 0), (empty_g, 0, 1), (empty_s, 2), (empty_s, 3), (empty_h, 0), (empty_g, 1, 0), (empty_u, 0, 0), (empty_g, 1, 1), (empty_s, 4), (empty_u, 0, 1), (empty_s, 5), (empty_u, 1, 0), (empty_s, 6), (empty_u, 1, 1), (empty_s, 7), (empty_u, 0, 2), (empty_u, 1, 2), (empty_u, 0, 3), (empty_g, 2, 0), (empty_u, 1, 3), (empty_g, 2, 1), (empty_u, 2, 0), (empty_u, 2, 1), (weave_a, 2, 0), (empty_g, 3, 0), (empty_g, 3, 1), (empty_u, 2, 2), (empty_u, 2, 3), (weave_a, 2, 1), (empty_h, 1), (empty_u, 3, 0), (empty_u, 3, 1), (weave_a, 3, 0), (empty_u, 3, 2), (empty_u, 3, 3), (widen_y, 3, 0), (weave_a, 3, 1), (widen_y, 3, 1)]
-        tensor_steps = [(spread_h, 0), (turn_s, 0), (turn_s, 1), (turn_g, 0, 0), (turn_g, 0, 1), (turn_s, 2), (turn_s, 3), (turn_g, 1, 0), (first_product, 0, 0), (turn_g, 1, 1), (turn_s, 4), (first_product, 0, 1), (turn_s, 5), (first_product, 1, 0), (turn_s, 6), (first_product, 1, 1), (turn_s, 7), (first_product, 0, 2), (first_product, 1, 2), (turn_g, 2, 0), (first_product, 0, 3), (turn_g, 2, 1), (first_product, 1, 3), (spread_h, 1), (second_product, 0, 0), (second_product, 1, 0), (first_product, 2, 0), (first_product, 2, 1), (second_product, 2, 0), (second_product, 3, 0), (turn_g, 3, 0), (turn_g, 3, 1), (first_product, 2, 2), (first_product, 2, 3), (second_product, 0, 1), (second_product, 1, 1), (second_product, 2, 1), (second_product, 3, 1), (first_product, 3, 0), (first_product, 3, 1), (second_product, 4, 0), (second_product, 5, 0), (second_product, 4, 1), (second_product, 5, 1), (first_product, 3, 2), (first_product, 3, 3), (second_product, 0, 2), (second_product, 1, 2), (second_product, 2, 2), (second_product, 3, 2), (second_product, 4, 2), (second_product, 5, 2), (second_product, 6, 0), (second_product, 7, 0), (second_product, 6, 1), (second_product, 7, 1), (second_product, 6, 2), (second_product, 7, 2), (second_product, 0, 3), (second_product, 1, 3), (second_product, 2, 3), (second_product, 3, 3), (second_product, 4, 3), (second_product, 5, 3), (second_product, 6, 3), (second_product, 7, 3)]
+        sync_steps = [(load_s_factor, 0), (load_g, 0, 0), (load_s, 0), (load_s, 1), (load_s, 2), (load_g, 0, 1), (load_s, 3), (load_y_factor, 0), (load_y, 0, 0), (load_s_factor, 1), (load_s, 4), (load_c, ), (load_g, 1, 0), (load_s, 5), (load_g, 1, 1), (load_y_factor, 1), (load_y, 0, 1), (load_s, 6), (load_g, 2, 0), (load_s, 7), (load_y, 1, 0), (load_g, 2, 1), (load_g, 3, 0), (load_y, 1, 1), (load_g, 3, 1), (load_y, 2, 0), (load_y, 2, 1), (load_h, ), (load_y, 3, 0), (load_y, 3, 1)]
+        vector_steps = [(widen_s, 0), (widen_s, 1), (widen_s, 2), (widen_s, 3), (quant_g, 0, 0), (quant_s, 0), (quant_g, 0, 1), (quant_s, 1), (widen_s, 4), (weave_y, 0, 0), (quant_s, 2), (widen_s, 5), (quant_y, 0, 0), (invert_c, ), (quant_s, 3), (quant_g, 1, 0), (widen_s, 6), (quant_g, 1, 1), (quant_s, 4), (widen_s, 7), (quant_g, 2, 0), (quant_s, 5), (weave_y, 0, 1), (quant_g, 2, 1), (quant_y, 0, 1), (quant_s, 6), (weave_y, 1, 0), (quant_s, 7), (quant_y, 1, 0), (quant_g, 3, 0), (quant_g, 3, 1), (weave_a, 0, 0), (weave_y, 1, 1), (quant_a, 0, 0), (quant_y, 1, 1), (weave_a, 0, 1), (weave_y, 2, 0), (quant_a, 0, 1), (quant_y, 2, 0), (weave_a, 1, 0), (weave_y, 2, 1), (quant_a, 1, 0), (weave_a, 1, 1), (quant_y, 2, 1), (quant_a, 1, 1), (finish, 0, 0), (finish, 0, 1), (finish, 1, 0), (finish, 1, 1), (finish, 0, 2), (finish, 1, 2), (finish, 2, 0), (quant_y, 3, 0), (finish, 2, 1), (finish, 2, 2), (quant_a, 2, 0), (finish, 3, 0), (quant_a, 2, 1), (finish, 3, 1), (finish, 3, 2), (quant_y, 3, 1), (finish, 4, 0), (finish, 4, 1), (finish, 4, 2), (finish, 0, 3), (quant_a, 3, 0), (finish, 1, 3), (finish, 2, 3), (finish, 3, 3), (finish, 4, 3), (quant_a, 3, 1), (finish, 5, 0), (finish, 5, 1), (finish, 5, 2), (finish, 5, 3), (finish, 6, 0), (finish, 6, 1), (finish, 6, 2), (finish, 6, 3), (finish, 7, 0), (finish, 7, 1), (finish, 7, 2), (finish, 7, 3)]
+        scalar_steps = [(widen_s_scalar, 0), (widen_s_scalar, 1), (empty_g, 0, 0), (empty_s, 0), (empty_g, 0, 1), (empty_s, 1), (widen_y, 0, 0), (empty_s, 2), (empty_s, 3), (widen_y, 0, 1), (empty_g, 1, 0), (empty_s, 4), (empty_u, 0, 0), (empty_g, 1, 1), (empty_s, 5), (widen_y, 1, 0), (empty_g, 2, 0), (empty_u, 0, 1), (empty_s, 6), (empty_g, 2, 1), (empty_s, 7), (empty_u, 1, 0), (widen_y, 1, 1), (empty_u, 0, 2), (empty_g, 3, 0), (empty_u, 1, 1), (empty_g, 3, 1), (widen_y, 2, 0), (empty_u, 0, 3), (widen_y, 2, 1), (empty_u, 1, 2), (empty_u, 1, 3), (widen_y, 3, 0), (empty_u, 2, 0), (empty_u, 2, 1), (weave_y, 3, 0), (empty_u, 2, 2), (empty_u, 2, 3), (widen_y, 3, 1), (weave_a, 2, 0), (weave_a, 2, 1), (empty_u, 3, 0), (empty_u, 3, 1), (weave_y, 3, 1), (weave_a, 3, 0), (empty_u, 3, 2), (empty_u, 3, 3), (weave_a, 3, 1)]
+        tensor_steps = [(turn_g, 0, 0), (turn_s, 0), (turn_g, 0, 1), (turn_s, 1), (turn_s, 2), (turn_s, 3), (first_product, 0, 0), (first_product, 0, 1), (turn_g, 1, 0), (turn_s, 4), (first_product, 0, 2), (turn_g, 1, 1), (first_product, 0, 3), (turn_s, 5), (turn_g, 2, 0), (first_product, 1, 0), (turn_s, 6), (first_product, 1, 1), (turn_g, 2, 1), (first_product, 0, 4), (turn_s, 7), (first_product, 0, 5), (first_product, 1, 2), (first_product, 1, 3), (turn_g, 3, 0), (first_product, 0, 6), (turn_g, 3, 1), (first_product, 0, 7), (first_product, 1, 4), (first_product, 1, 5), (first_product, 1, 6), (first_product, 1, 7), (first_product, 2, 0), (first_product, 2, 1), (first_product, 2, 2), (first_product, 2, 3), (first_product, 2, 4), (first_product, 2, 5), (first_product, 2, 6), (first_product, 2, 7), (second_product, 0, 0), (second_product, 0, 1), (first_product, 3, 0), (second_product, 1, 0), (second_product, 1, 1), (first_product, 3, 1), (second_product, 0, 2), (second_product, 1, 2), (first_product, 3, 2), (second_product, 2, 0), (second_product, 2, 1), (first_product, 3, 3), (second_product, 2, 2), (second_product, 3, 0), (first_product, 3, 4), (second_product, 3, 1), (second_product, 3, 2), (first_product, 3, 5), (first_product, 3, 6), (first_product, 3, 7), (second_product, 4, 0), (second_product, 4, 1), (second_product, 4, 2), (second_product, 0, 3), (second_product, 1, 3), (second_product, 2, 3), (second_product, 3, 3), (second_product, 4, 3), (second_product, 5, 0), (second_product, 5, 1), (second_product, 5, 2), (second_product, 5, 3), (second_product, 6, 0), (second_product, 6, 1), (second_product, 6, 2), (second_product, 6, 3), (second_product, 7, 0), (second_product, 7, 1), (second_product, 7, 2), (second_product, 7, 3)]
 
 
         def inputs(job, a=0, b=0):
@@ -317,18 +303,16 @@ def tile_curvature_scaled_pair_correction_d7_kernel(tc, G, S_bytes, S_scale, Y_b
                 turn_g: [(load_g, a, b)],
                 empty_g: [(turn_g, a, b)],
                 quant_g: [(empty_g, a, b)],
-                first_product: [(quant_s, 2 * b), (quant_s, 2 * b + 1), (quant_g, a, 0), (quant_g, a, 1)],
-                empty_u: [(first_product, a, b), (invert_c,)],
+                first_product: [(quant_s, b), (quant_g, a, 0), (quant_g, a, 1)],
+                empty_u: [(first_product, a, 2 * b + 1), (invert_c,)],
                 weave_a: [(empty_u, a, 2 * b), (empty_u, a, 2 * b + 1)],
                 quant_a: [(weave_a, a, b)],
                 widen_y: [(load_y, a, b)],
                 weave_y: [(widen_y, a, b), (load_y_factor, b)],
                 quant_y: [(weave_y, a, b)],
                 second_product: [(quant_a, a // 2, 0), (quant_a, a // 2, 1), (quant_y, b, 0), (quant_y, b, 1)],
-                finish: [(second_product, a, b), (empty_h, b // 2)],
+                finish: [(second_product, a, b), (load_h,)],
                 invert_c: [(load_c,)],
-                spread_h: [(load_h,)],
-                empty_h: [(spread_h, a)],
             }
             return table.get(job, [])
 
@@ -342,9 +326,7 @@ def tile_curvature_scaled_pair_correction_d7_kernel(tc, G, S_bytes, S_scale, Y_b
                 empty_g: {"turn": -2, "turned": 1},
                 quant_s: {"turned": -1},
                 quant_g: {"turned": -1},
-                spread_h: {"acc": 1},
-                empty_h: {"acc": -1},
-                first_product: {"acc": 1},
+                first_product: {"acc": 1 - b % 2},
                 empty_u: {"acc": -1, "planes": 1 - b % 2},
                 weave_a: {"planes": -1, "a_woven": 1},
                 quant_a: {"a_woven": -1},

@@ -216,12 +216,20 @@ def tile_curvature_scaled_pair_correction_d7_kernel(tc, G, S_bytes, S_scale, Y_b
                 sums = tiles["u_bank", chunk, b][:, i, :]
                 nc.scalar.activation(out=planes[:, u % PACK, :], in_=sums, func=COPY, scale=c_inv[:, u : u + 1])
 
+        def in_runs_out(woven):
+            return woven.rearrange("p (x i j) -> p x j i", i=4, j=PACK)
+
+        def in_runs_in(planes):
+            return planes.rearrange("p j (x i) -> p x j i", i=4)
+
         def weave_a(chunk, half):
             woven = work.tile([P, CHUNK * PACK], BF16, name="a_woven", bufs=WOVEN_A_BUFS, align_bytes=64)
             tiles["a_woven", chunk, half] = woven
-            dst = woven[:].rearrange("p (x i j) -> p x j i", i=4, j=PACK)
-            src = tiles["a_planes", chunk, half][:].rearrange("p j (x i) -> p x j i", i=4)
-            copy_on((weave_a, chunk, half))(out=dst, in_=src)
+            planes = tiles["a_planes", chunk, half][:]
+            if (weave_a, chunk, half) in vector_steps:
+                nc.vector.tensor_copy(out=in_runs_out(woven[:]), in_=in_runs_in(planes))
+            else:
+                nc.scalar.copy(out=woven[:].rearrange("p (n j) -> p n j", j=PACK), in_=planes.rearrange("p j n -> p n j"))
 
         def quant_a(chunk, half):
             nc.vector.quantize_mx(
@@ -241,13 +249,14 @@ def tile_curvature_scaled_pair_correction_d7_kernel(tc, G, S_bytes, S_scale, Y_b
             tiles["y_woven", strip, half] = woven
             for i in range(STRIP // P):
                 block = strip * (STRIP // P) + i
-                dst = woven[:, P * PACK * i : P * PACK * (i + 1)].rearrange("p (x i j) -> p x j i", i=4, j=PACK)
-                src = tiles["y_wide", strip, half][:, :, P * i : P * (i + 1)].rearrange("p j (x i) -> p x j i", i=4)
+                dst = woven[:, P * PACK * i : P * PACK * (i + 1)]
+                src = tiles["y_wide", strip, half][:, :, P * i : P * (i + 1)]
                 factor = y_factor[half][:, block : block + 1]
                 if (weave_y, strip, half) in vector_steps:
-                    nc.vector.tensor_scalar(out=dst, in0=src, scalar1=factor, scalar2=None, op0=MULT)
+                    nc.vector.tensor_scalar(out=in_runs_out(dst), in0=in_runs_in(src), scalar1=factor, scalar2=None, op0=MULT)
                 else:
-                    nc.scalar.activation(out=dst, in_=src, func=COPY, scale=factor)
+                    by_column = src.rearrange("p j n -> p n j")
+                    nc.scalar.activation(out=dst.rearrange("p (n j) -> p n j", j=PACK), in_=by_column, func=COPY, scale=factor)
 
         def quant_y(strip, half):
             nc.vector.quantize_mx(

@@ -152,10 +152,7 @@ def tile_curvature_scaled_pair_correction_d7_kernel(tc, G, S_bytes, S_scale, Y_b
                         nc.tensor.transpose(turned[:, w, i, :], src, ident[:])
 
         def join_words(copy, dst, turned):
-            copy(
-                out=dst.rearrange("p (x i) w -> p x w i", i=2),
-                in_=turned[:].rearrange("p w a r -> p w (a r)").rearrange("p w (x i) -> p x w i", i=2),
-            )
+            copy(out=dst, in_=turned[:].rearrange("p w a r -> p (a r) w"))
 
         def empty_s(u):
             joined = work.tile([P, 2, 2 * P, 2], F32, name="s_turned", tag="turned", bufs=TURNED_BUFS, align_bytes=64)

@@ -29,14 +29,30 @@ STRIP = 512
 STRIPS = N // STRIP
 
 SCALAR_PASSES = (2, 2, 0, 0, 0, 0, 0, 0)
+TURN = 4
+PORDER = 0
+QUANT_LEAD = 2
+QUANT_GAP = 2
+TILES_PER_PRODUCT = 2
+LATE_WEAVES_ON_VECTOR = ((2, 0),)
+CAST_FIRST = 4
+CAST_EVERY = 3
+EARLY_Y = 4
+WIDEN_LEAD = 4
+LOAD_LEAD = 3
+Y_LEAD = 1
+PRODUCT_LAG = 4
+PRODUCTS_PER_TURN = 1
+VECTOR_EMPTIES = (5, 11)
+WEAVE_LAG = 3
 RING_BANKS = 4
-FIRST_TILE_ON_BOTH_RINGS = 4
+FIRST_TILE_ON_BOTH_RINGS = 6
 STORE_STRIPS = 1
 
 WIDE_S_BUFS = 4
 TURNED_BUFS = 4
 A_PLANE_BUFS = 4
-WOVEN_A_BUFS = 2
+WOVEN_A_BUFS = 4
 WIDE_Y_BUFS = 3
 WOVEN_Y_BUFS = 3
 RESULT_BUFS = 8
@@ -293,10 +309,115 @@ def tile_curvature_scaled_pair_correction_d7_kernel(tc, G, S_bytes, S_scale, Y_b
         def load_y_factor(half):
             load_factor(y_factor, Y_scale, half)
 
-        sync_steps = [(load_s_factor, 0), (load_g, 0, 0), (load_s, 0), (load_s, 1), (load_s, 2), (load_g, 0, 1), (load_s, 3), (load_y_factor, 0), (load_y, 0, 0), (load_s_factor, 1), (load_s, 4), (load_c, ), (load_g, 1, 0), (load_s, 5), (load_g, 1, 1), (load_y_factor, 1), (load_y, 0, 1), (load_s, 6), (load_g, 2, 0), (load_s, 7), (load_y, 1, 0), (load_g, 2, 1), (load_g, 3, 0), (load_y, 1, 1), (load_g, 3, 1), (load_y, 2, 0), (load_y, 2, 1), (load_h, ), (load_y, 3, 0), (load_y, 3, 1)]
-        vector_steps = [(widen_s, 0), (widen_s, 1), (widen_s, 2), (widen_s, 3), (quant_g, 0, 0), (quant_s, 0), (quant_g, 0, 1), (quant_s, 1), (widen_s, 4), (weave_y, 0, 0), (quant_s, 2), (widen_s, 5), (quant_y, 0, 0), (invert_c, ), (quant_s, 3), (quant_g, 1, 0), (widen_s, 6), (quant_g, 1, 1), (quant_s, 4), (widen_s, 7), (quant_g, 2, 0), (quant_s, 5), (weave_y, 0, 1), (quant_g, 2, 1), (quant_y, 0, 1), (quant_s, 6), (weave_y, 1, 0), (quant_s, 7), (quant_y, 1, 0), (quant_g, 3, 0), (quant_g, 3, 1), (weave_a, 0, 0), (weave_y, 1, 1), (quant_a, 0, 0), (quant_y, 1, 1), (weave_a, 0, 1), (weave_y, 2, 0), (quant_a, 0, 1), (quant_y, 2, 0), (weave_a, 1, 0), (weave_y, 2, 1), (quant_a, 1, 0), (weave_a, 1, 1), (quant_y, 2, 1), (quant_a, 1, 1), (finish, 0, 0), (finish, 0, 1), (finish, 1, 0), (finish, 1, 1), (finish, 0, 2), (finish, 1, 2), (finish, 2, 0), (quant_y, 3, 0), (finish, 2, 1), (finish, 2, 2), (quant_a, 2, 0), (finish, 3, 0), (quant_a, 2, 1), (finish, 3, 1), (finish, 3, 2), (quant_y, 3, 1), (finish, 4, 0), (finish, 4, 1), (finish, 4, 2), (finish, 0, 3), (quant_a, 3, 0), (finish, 1, 3), (finish, 2, 3), (finish, 3, 3), (finish, 4, 3), (quant_a, 3, 1), (finish, 5, 0), (finish, 5, 1), (finish, 5, 2), (finish, 5, 3), (finish, 6, 0), (finish, 6, 1), (finish, 6, 2), (finish, 6, 3), (finish, 7, 0), (finish, 7, 1), (finish, 7, 2), (finish, 7, 3)]
-        scalar_steps = [(widen_s_scalar, 0), (widen_s_scalar, 1), (empty_g, 0, 0), (empty_s, 0), (empty_g, 0, 1), (empty_s, 1), (widen_y, 0, 0), (empty_s, 2), (empty_s, 3), (widen_y, 0, 1), (empty_g, 1, 0), (empty_s, 4), (empty_u, 0, 0), (empty_g, 1, 1), (empty_s, 5), (widen_y, 1, 0), (empty_g, 2, 0), (empty_u, 0, 1), (empty_s, 6), (empty_g, 2, 1), (empty_s, 7), (empty_u, 1, 0), (widen_y, 1, 1), (empty_u, 0, 2), (empty_g, 3, 0), (empty_u, 1, 1), (empty_g, 3, 1), (widen_y, 2, 0), (empty_u, 0, 3), (widen_y, 2, 1), (empty_u, 1, 2), (empty_u, 1, 3), (widen_y, 3, 0), (empty_u, 2, 0), (empty_u, 2, 1), (weave_y, 3, 0), (empty_u, 2, 2), (empty_u, 2, 3), (widen_y, 3, 1), (weave_a, 2, 0), (weave_a, 2, 1), (empty_u, 3, 0), (empty_u, 3, 1), (weave_y, 3, 1), (weave_a, 3, 0), (empty_u, 3, 2), (empty_u, 3, 3), (weave_a, 3, 1)]
-        tensor_steps = [(turn_g, 0, 0), (turn_s, 0), (turn_g, 0, 1), (turn_s, 1), (turn_s, 2), (turn_s, 3), (first_product, 0, 0), (first_product, 0, 1), (turn_g, 1, 0), (turn_s, 4), (first_product, 0, 2), (turn_g, 1, 1), (first_product, 0, 3), (turn_s, 5), (turn_g, 2, 0), (first_product, 1, 0), (turn_s, 6), (first_product, 1, 1), (turn_g, 2, 1), (first_product, 0, 4), (turn_s, 7), (first_product, 0, 5), (first_product, 1, 2), (first_product, 1, 3), (turn_g, 3, 0), (first_product, 0, 6), (turn_g, 3, 1), (first_product, 0, 7), (first_product, 1, 4), (first_product, 1, 5), (first_product, 1, 6), (first_product, 1, 7), (first_product, 2, 0), (first_product, 2, 1), (first_product, 2, 2), (first_product, 2, 3), (first_product, 2, 4), (first_product, 2, 5), (first_product, 2, 6), (first_product, 2, 7), (second_product, 0, 0), (second_product, 0, 1), (first_product, 3, 0), (second_product, 1, 0), (second_product, 1, 1), (first_product, 3, 1), (second_product, 0, 2), (second_product, 1, 2), (first_product, 3, 2), (second_product, 2, 0), (second_product, 2, 1), (first_product, 3, 3), (second_product, 2, 2), (second_product, 3, 0), (first_product, 3, 4), (second_product, 3, 1), (second_product, 3, 2), (first_product, 3, 5), (first_product, 3, 6), (first_product, 3, 7), (second_product, 4, 0), (second_product, 4, 1), (second_product, 4, 2), (second_product, 0, 3), (second_product, 1, 3), (second_product, 2, 3), (second_product, 3, 3), (second_product, 4, 3), (second_product, 5, 0), (second_product, 5, 1), (second_product, 5, 2), (second_product, 5, 3), (second_product, 6, 0), (second_product, 6, 1), (second_product, 6, 2), (second_product, 6, 3), (second_product, 7, 0), (second_product, 7, 1), (second_product, 7, 2), (second_product, 7, 3)]
+        g_parts = [(chunk, b) for chunk in range(CHUNKS) for b in range(2)]
+        y_parts = [(strip, half) for strip in range(STRIPS) for half in range(HALVES)]
+        s = [("s", u) for u in range(SLICES)]
+        g = [("g", *part) for part in g_parts]
+        units = {
+            0: [x for u in range(8) for x in (s[u], g[u])],
+            1: [s[0], g[0], g[1], s[1], s[2], s[3], g[2], g[3], s[4], g[4], s[5], g[5], s[6], s[7], g[6], g[7]],
+            2: [s[0], g[0], g[1], s[1], s[2], s[3], g[2], s[4], g[3], s[5], g[4], s[6], g[5], s[7], g[6], g[7]],
+            3: [s[0], g[0], s[1], g[1], s[2], s[3], g[2], g[3], s[4], s[5], g[4], g[5], s[6], s[7], g[6], g[7]],
+            4: [s[0], g[0], s[1], g[1], s[2], g[2], s[3], g[3], s[4], s[5], s[6], s[7], g[4], g[5], g[6], g[7]],
+            5: [s[0], g[0], s[1], g[1], s[2], s[3], g[2], s[4], g[3], s[5], g[4], s[6], g[5], s[7], g[6], g[7]],
+        }[TURN]
+        load = {"s": load_s, "g": load_g}
+        turn = {"s": turn_s, "g": turn_g}
+        empty = {"s": empty_s, "g": empty_g}
+        quant = {"s": quant_s, "g": quant_g}
+        products = [(chunk, u) for half in range(HALVES) for chunk in range(2) for u in range(PACK * half, PACK * (half + 1))]
+        if PORDER == 1:
+            products = [(chunk, u) for chunk in range(2) for u in range(SLICES)]
+        casts = {CAST_FIRST + CAST_EVERY * k: y_parts[k] for k in range(EARLY_Y)}
+
+        sync_steps = [(load_s_factor, 0)]
+        vector_steps = [(widen_s, u) for u in range(WIDEN_LEAD)] + [(invert_c,)]
+        scalar_steps = [(widen_s_scalar, u) for u in range(SLICES) if SCALAR_PASSES[u]]
+        tensor_steps = []
+        later = []
+        for i, unit in enumerate(units):
+            ahead = [x for x in units[i:] if x[0] == "s"][:LOAD_LEAD]
+            for x in ([unit] if unit[0] == "g" else []) + ahead:
+                if (load[x[0]], *x[1:]) not in sync_steps:
+                    if x == s[PACK]:
+                        sync_steps.extend([(load_s_factor, 1), (load_c,)])
+                    sync_steps.append((load[x[0]], *x[1:]))
+            if i + Y_LEAD in casts:
+                part = casts[i + Y_LEAD]
+                if part[0] == 0:
+                    sync_steps.append((load_y_factor, part[1]))
+                sync_steps.append((load_y, *part))
+            done = [x[1:] for x in tensor_steps if x[0] is first_product]
+            tensor_steps.append((turn[unit[0]], *unit[1:]))
+            seen = units[: max(0, i + 1 - PRODUCT_LAG)]
+            ready = [p for p in products[len(done) : len(done) + PRODUCTS_PER_TURN]]
+            for p in ready:
+                if s[p[1]] in seen and g[2 * p[0] + 1] in seen and (p == products[0] or (first_product, *products[products.index(p) - 1]) in tensor_steps):
+                    tensor_steps.append((first_product, *p))
+            on_vector = i in VECTOR_EMPTIES
+            if not on_vector:
+                scalar_steps.append((empty[unit[0]], *unit[1:]))
+            for chunk, u in done:
+                if u % 2 == 1 and (empty_u, chunk, u // 2) not in scalar_steps:
+                    scalar_steps.append((empty_u, chunk, u // 2))
+            if i in casts:
+                scalar_steps.append((widen_y, *casts[i]))
+            first = [(empty[unit[0]], *unit[1:])] if on_vector else [(quant[unit[0]], *unit[1:])]
+            middle = []
+            if i - WEAVE_LAG in casts:
+                middle.append((weave_y, *casts[i - WEAVE_LAG]))
+            widened = len([x for x in vector_steps if x[0] is widen_s])
+            if unit[0] == "s" and widened < SLICES:
+                middle.append((widen_s, widened))
+            vector_steps.extend(first + later + middle)
+            later = [(quant[unit[0]], *unit[1:])] if on_vector else []
+            if i - WEAVE_LAG in casts:
+                later.append((quant_y, *casts[i - WEAVE_LAG]))
+        vector_steps.extend(later)
+        for part in y_parts[:6]:
+            if (load_y, *part) not in sync_steps:
+                sync_steps.append((load_y, *part))
+        sync_steps.extend([(load_h,), (load_y, 3, 0), (load_y, 3, 1)])
+        tensor_steps.extend([(first_product, *p) for p in products if (first_product, *p) not in tensor_steps])
+        rest_u = [(empty_u, c, u // 2) for c, u in products if u % 2 == 1 and (empty_u, c, u // 2) not in scalar_steps]
+        rest_y = [(widen_y, *part) for part in y_parts[:6] if (widen_y, *part) not in scalar_steps]
+        for k in range(max(len(rest_u), len(rest_y))):
+            scalar_steps.extend(rest_u[k : k + 1] + rest_y[k : k + 1])
+        rest_y = [part for part in y_parts[:6] if (weave_y, *part) not in vector_steps]
+        rest_a = [(chunk, half) for chunk in range(2) for half in range(HALVES)]
+        for k in range(max(len(rest_a), len(rest_y))):
+            a = rest_a[k : k + 1]
+            y = rest_y[k : k + 1]
+            vector_steps.extend([(weave_a, *x) for x in a] + [(weave_y, *x) for x in y] + [(quant_a, *x) for x in a] + [(quant_y, *x) for x in y])
+        early_rows = range(T // P - CHUNK // P)
+        last_rows = range(T // P - CHUNK // P, T // P)
+        out_tiles = [(r, strip) for r in early_rows for strip in range(STRIPS - 1)] + [(r, STRIPS - 1) for r in early_rows]
+        out_tiles = out_tiles + [(r, strip) for r in last_rows for strip in range(STRIPS)]
+        tensor_steps.extend([(first_product, 2, u) for u in range(SLICES)])
+        late_products = [(first_product, 3, u) for u in range(SLICES)]
+        late_quants = {}
+        for chunk in (2, 3):
+            for half in range(HALVES):
+                own = [(weave_a, chunk, half)] if (chunk, half) in LATE_WEAVES_ON_VECTOR else []
+                at = out_tiles.index((2 * chunk, 0)) - QUANT_LEAD - QUANT_GAP * (1 - half)
+                late_quants.setdefault(at - 1, []).extend(own)
+                late_quants.setdefault(at, []).append((quant_a, chunk, half))
+        for half in range(HALVES):
+            at = out_tiles.index((0, STRIPS - 1)) - QUANT_LEAD - 2 * QUANT_GAP * (1 - half)
+            late_quants.setdefault(at, []).append((quant_y, STRIPS - 1, half))
+        for k, tile in enumerate(out_tiles):
+            tensor_steps.append((second_product, *tile))
+            if k % TILES_PER_PRODUCT == TILES_PER_PRODUCT - 1:
+                tensor_steps.extend(late_products[k // TILES_PER_PRODUCT : k // TILES_PER_PRODUCT + 1])
+            vector_steps.extend(late_quants.get(k, []) + [(finish, *tile)])
+        for chunk in (2, 3):
+            for half in range(HALVES):
+                scalar_steps.extend([(empty_u, chunk, 2 * half), (empty_u, chunk, 2 * half + 1)])
+                if (chunk, half) not in LATE_WEAVES_ON_VECTOR:
+                    scalar_steps.append((weave_a, chunk, half))
+            if chunk == 2:
+                for half in range(HALVES):
+                    scalar_steps.extend([(widen_y, STRIPS - 1, half), (weave_y, STRIPS - 1, half)])
 
 
         def inputs(job, a=0, b=0):

@@ -30,31 +30,33 @@ STRIPS = N // STRIP
 
 SCALAR_PASSES = (2, 2, 0, 0, 0, 0, 0, 0)
 TURN = 4
-PORDER = 0
+BANK_ORDER = (0, 1)
+PORDER = 1
 QUANT_LEAD = 2
 QUANT_GAP = 2
-TILES_PER_PRODUCT = 2
+LATE_PRODUCTS = 1
 LATE_WEAVES_ON_VECTOR = ((2, 0),)
-CAST_FIRST = 4
+CAST_FIRST = 5
 CAST_EVERY = 3
-EARLY_Y = 4
+EARLY_Y = 2
 WIDEN_LEAD = 4
 LOAD_LEAD = 3
-Y_LEAD = 1
+Y_LEAD = 0
 PRODUCT_LAG = 4
 PRODUCTS_PER_TURN = 1
-VECTOR_EMPTIES = (5, 11)
+VECTOR_EMPTIES = (11,)
 WEAVE_LAG = 3
-RING_BANKS = 4
-FIRST_TILE_ON_BOTH_RINGS = 6
+BANKS = 8
+SIDE_BANKS = 2
+OUT_SIDE = 3
 STORE_STRIPS = 1
 
 WIDE_S_BUFS = 4
 TURNED_BUFS = 4
 A_PLANE_BUFS = 4
-WOVEN_A_BUFS = 4
+WOVEN_A_BUFS = 2
 WIDE_Y_BUFS = 3
-WOVEN_Y_BUFS = 3
+WOVEN_Y_BUFS = 2
 RESULT_BUFS = 8
 
 
@@ -88,12 +90,9 @@ def tile_curvature_scaled_pair_correction_d7_kernel(tc, G, S_bytes, S_scale, Y_b
         y_rows = Y_bytes.rearrange("(half p j) n -> half p j n", half=HALVES, j=PACK)
         tiles = {}
 
-        def bank(key, ring, shape):
-            tiles[key] = psum.tile(shape, F32, name="bank", tag=ring, bufs=RING_BANKS)
+        def bank(key, shape):
+            tiles[key] = psum.tile(shape, F32, name="bank%d" % bank_of[key], bufs=1)
             return tiles[key]
-
-        def out_ring(row_tile, strip):
-            return "acc" if row_tile >= FIRST_TILE_ON_BOTH_RINGS and strip % 2 == 1 else "turn"
 
         def load_factor(factor, table, half):
             rows = table[PACK * half : PACK * (half + 1), :].partition_broadcast(QUAD)
@@ -117,7 +116,7 @@ def tile_curvature_scaled_pair_correction_d7_kernel(tc, G, S_bytes, S_scale, Y_b
             tiles["s_raw", u] = raw
 
         def load_g(chunk, b):
-            raw = keep.tile([P, CHUNK // P, 2 * K_PASS], BF16, name="g_raw%d%d" % (chunk, b))
+            raw = work.tile([P, CHUNK // P, 2 * K_PASS], BF16, name="g_raw", tag="rows", bufs=2 * CHUNKS)
             rows = G[chunk * CHUNK : (chunk + 1) * CHUNK, 2 * K_PASS * b : 2 * K_PASS * (b + 1)]
             nc.sync.dma_start(out=raw[:], in_=rows.rearrange("(i r) n -> r i n", r=P))
             tiles["g_raw", chunk, b] = raw
@@ -157,7 +156,7 @@ def tile_curvature_scaled_pair_correction_d7_kernel(tc, G, S_bytes, S_scale, Y_b
         def turn_s(u):
             words = tiles["s_wide", u][:].bitcast(F32)
             for b in range(2):
-                turned = bank(("s_bank", u, b), "turn", [P, 2, 2, P])
+                turned = bank(("s_bank", u, b), [P, 2, 2, P])
                 for i in range(2):
                     g = 2 * b + i
                     for w in range(2):
@@ -173,7 +172,7 @@ def tile_curvature_scaled_pair_correction_d7_kernel(tc, G, S_bytes, S_scale, Y_b
         def empty_s(u):
             joined = work.tile([P, 2, 2 * P, 2], F32, name="s_turned", tag="turned", bufs=TURNED_BUFS, align_bytes=64)
             tiles["s_turned", u] = joined
-            for b in range(2):
+            for b in BANK_ORDER:
                 join_words(copy_on((empty_s, u)), joined[:, b], tiles["s_bank", u, b])
 
         def quant_s(u):
@@ -185,7 +184,7 @@ def tile_curvature_scaled_pair_correction_d7_kernel(tc, G, S_bytes, S_scale, Y_b
 
         def turn_g(chunk, b):
             for g in range(2):
-                turned = bank(("g_bank", chunk, 2 * b + g), "turn", [P, 2, 2, P])
+                turned = bank(("g_bank", chunk, 2 * b + g), [P, 2, 2, P])
                 for i in range(2):
                     words = tiles["g_raw", chunk, b][:, i, :].bitcast(F32)
                     for w in range(2):
@@ -194,7 +193,7 @@ def tile_curvature_scaled_pair_correction_d7_kernel(tc, G, S_bytes, S_scale, Y_b
         def empty_g(chunk, b):
             joined = work.tile([P, 2, CHUNK, 2], F32, name="g_turned", tag="turned", bufs=TURNED_BUFS, align_bytes=64)
             tiles["g_turned", chunk, b] = joined
-            for i in range(2):
+            for i in BANK_ORDER:
                 join_words(copy_on((empty_g, chunk, b)), joined[:, i], tiles["g_bank", chunk, 2 * b + i])
 
         def quant_g(chunk, b):
@@ -206,7 +205,7 @@ def tile_curvature_scaled_pair_correction_d7_kernel(tc, G, S_bytes, S_scale, Y_b
 
         def first_product(chunk, u):
             if u % 2 == 0:
-                bank(("u_bank", chunk, u // 2), "acc", [P, 2, CHUNK])
+                bank(("u_bank", chunk, u // 2), [P, 2, CHUNK])
             sums = tiles["u_bank", chunk, u // 2]
             for g in range(PASSES):
                 nc.tensor.matmul_mx(
@@ -236,19 +235,20 @@ def tile_curvature_scaled_pair_correction_d7_kernel(tc, G, S_bytes, S_scale, Y_b
             return planes.rearrange("p j (x i) -> p x j i", i=4)
 
         def weave_a(chunk, half):
-            woven = work.tile([P, CHUNK * PACK], BF16, name="a_woven", bufs=WOVEN_A_BUFS, align_bytes=64)
-            tiles["a_woven", chunk, half] = woven
+            if half == 0:
+                tiles["a_woven", chunk] = work.tile([P, HALVES, CHUNK * PACK], BF16, name="a_woven", bufs=WOVEN_A_BUFS, align_bytes=64)
+            woven = tiles["a_woven", chunk][:, half, :]
             planes = tiles["a_planes", chunk, half][:]
             if (weave_a, chunk, half) in vector_steps:
-                nc.vector.tensor_copy(out=in_runs_out(woven[:]), in_=in_runs_in(planes))
+                nc.vector.tensor_copy(out=in_runs_out(woven), in_=in_runs_in(planes))
             else:
-                nc.scalar.copy(out=woven[:].rearrange("p (n j) -> p n j", j=PACK), in_=planes.rearrange("p j n -> p n j"))
+                nc.scalar.copy(out=woven.rearrange("p (n j) -> p n j", j=PACK), in_=planes.rearrange("p j n -> p n j"))
 
-        def quant_a(chunk, half):
+        def quant_a(chunk):
             nc.vector.quantize_mx(
-                out=a_codes[:, chunk, half, :].bitcast(FP8X4),
-                scales=a_scales[:, chunk, half, :],
-                in_=tiles["a_woven", chunk, half][:],
+                out=a_codes[:, chunk].rearrange("p g t -> p (g t)").bitcast(FP8X4),
+                scales=a_scales[:, chunk].rearrange("p g t -> p (g t)"),
+                in_=tiles["a_woven", chunk][:].rearrange("p g x -> p (g x)"),
             )
 
         def widen_y(strip, half):
@@ -258,8 +258,9 @@ def tile_curvature_scaled_pair_correction_d7_kernel(tc, G, S_bytes, S_scale, Y_b
             nc.scalar.copy(out=wide[:].rearrange("p j n -> p (j n)"), in_=raw.bitcast(FP8))
 
         def weave_y(strip, half):
-            woven = work.tile([P, STRIP * PACK], BF16, name="y_woven", bufs=WOVEN_Y_BUFS, align_bytes=64)
-            tiles["y_woven", strip, half] = woven
+            if half == 0:
+                tiles["y_woven", strip] = work.tile([P, HALVES, STRIP * PACK], BF16, name="y_woven", bufs=WOVEN_Y_BUFS, align_bytes=64)
+            woven = tiles["y_woven", strip][:, half, :]
             for i in range(STRIP // P):
                 block = strip * (STRIP // P) + i
                 dst = woven[:, P * PACK * i : P * PACK * (i + 1)]
@@ -271,15 +272,15 @@ def tile_curvature_scaled_pair_correction_d7_kernel(tc, G, S_bytes, S_scale, Y_b
                     by_column = src.rearrange("p j n -> p n j")
                     nc.scalar.activation(out=dst.rearrange("p (n j) -> p n j", j=PACK), in_=by_column, func=COPY, scale=factor)
 
-        def quant_y(strip, half):
+        def quant_y(strip):
             nc.vector.quantize_mx(
-                out=y_codes[:, strip, half, :].bitcast(FP8X4),
-                scales=y_scales[:, strip, half, :],
-                in_=tiles["y_woven", strip, half][:],
+                out=y_codes[:, strip].rearrange("p g n -> p (g n)").bitcast(FP8X4),
+                scales=y_scales[:, strip].rearrange("p g n -> p (g n)"),
+                in_=tiles["y_woven", strip][:].rearrange("p g x -> p (g x)"),
             )
 
         def second_product(row_tile, strip):
-            sums = bank(("p_bank", row_tile, strip), out_ring(row_tile, strip), [P, STRIP])
+            sums = bank(("p_bank", row_tile, strip), [P, STRIP])
             chunk, i = divmod(row_tile, CHUNK // P)
             for half in range(HALVES):
                 nc.tensor.matmul_mx(
@@ -292,16 +293,18 @@ def tile_curvature_scaled_pair_correction_d7_kernel(tc, G, S_bytes, S_scale, Y_b
                     stop=(half == HALVES - 1),
                 )
 
-        def finish(row_tile, strip):
-            first = strip - strip % STORE_STRIPS
-            if strip == first:
-                tiles["res", row_tile, first] = work.tile([P, STORE_STRIPS * STRIP], F32, name="res", bufs=RESULT_BUFS)
-            res = tiles["res", row_tile, first]
+        def finish(chunk, strip):
+            res = work.tile([P, CHUNK // P, STRIP], F32, name="res", tag="rows", bufs=2 * CHUNKS)
             cols = slice(STRIP * strip, STRIP * (strip + 1))
-            part = res[:, STRIP * (strip - first) : STRIP * (strip - first + 1)]
-            nc.vector.tensor_tensor(out=part, in0=tiles["p_bank", row_tile, strip][:], in1=h_all[:, cols], op=MULT)
-            if strip == first + STORE_STRIPS - 1:
-                nc.sync.dma_start(out=out[row_tile * P : (row_tile + 1) * P, STRIP * first : STRIP * (strip + 1)], in_=res[:])
+            rows = out[chunk * CHUNK : (chunk + 1) * CHUNK, cols].rearrange("(i r) n -> r i n", r=P)
+            last = (chunk, strip) == (CHUNKS - 1, STRIPS - 1)
+            for i in range(CHUNK // P) if last else reversed(range(CHUNK // P)):
+                sums = tiles["p_bank", 2 * chunk + i, strip]
+                nc.vector.tensor_tensor(out=res[:, i, :], in0=sums[:], in1=h_all[:, cols], op=MULT)
+                if last:
+                    nc.sync.dma_start(out=rows[:, i, :], in_=res[:, i, :])
+            if not last:
+                nc.sync.dma_start(out=rows, in_=res[:])
 
         def load_s_factor(half):
             load_factor(s_factor, S_scale, half)
@@ -371,8 +374,8 @@ def tile_curvature_scaled_pair_correction_d7_kernel(tc, G, S_bytes, S_scale, Y_b
                 middle.append((widen_s, widened))
             vector_steps.extend(first + later + middle)
             later = [(quant[unit[0]], *unit[1:])] if on_vector else []
-            if i - WEAVE_LAG in casts:
-                later.append((quant_y, *casts[i - WEAVE_LAG]))
+            if i - WEAVE_LAG in casts and casts[i - WEAVE_LAG][1] == 1:
+                later.append((quant_y, casts[i - WEAVE_LAG][0]))
         vector_steps.extend(later)
         for part in y_parts[:6]:
             if (load_y, *part) not in sync_steps:
@@ -388,28 +391,20 @@ def tile_curvature_scaled_pair_correction_d7_kernel(tc, G, S_bytes, S_scale, Y_b
         for k in range(max(len(rest_a), len(rest_y))):
             a = rest_a[k : k + 1]
             y = rest_y[k : k + 1]
-            vector_steps.extend([(weave_a, *x) for x in a] + [(weave_y, *x) for x in y] + [(quant_a, *x) for x in a] + [(quant_y, *x) for x in y])
-        early_rows = range(T // P - CHUNK // P)
-        last_rows = range(T // P - CHUNK // P, T // P)
-        out_tiles = [(r, strip) for r in early_rows for strip in range(STRIPS - 1)] + [(r, STRIPS - 1) for r in early_rows]
-        out_tiles = out_tiles + [(r, strip) for r in last_rows for strip in range(STRIPS)]
+            vector_steps.extend([(weave_a, *x) for x in a] + [(weave_y, *x) for x in y] + [(quant_a, x[0]) for x in a if x[1] == 1] + [(quant_y, x[0]) for x in y if x[1] == 1])
+        out_jobs = [(chunk, strip) for chunk in range(CHUNKS - 1) for strip in range(STRIPS - 1)]
+        out_jobs = out_jobs + [(chunk, STRIPS - 1) for chunk in range(CHUNKS - 1)] + [(CHUNKS - 1, strip) for strip in range(STRIPS)]
         tensor_steps.extend([(first_product, 2, u) for u in range(SLICES)])
-        late_products = [(first_product, 3, u) for u in range(SLICES)]
         late_quants = {}
         for chunk in (2, 3):
-            for half in range(HALVES):
-                own = [(weave_a, chunk, half)] if (chunk, half) in LATE_WEAVES_ON_VECTOR else []
-                at = out_tiles.index((2 * chunk, 0)) - QUANT_LEAD - QUANT_GAP * (1 - half)
-                late_quants.setdefault(at - 1, []).extend(own)
-                late_quants.setdefault(at, []).append((quant_a, chunk, half))
-        for half in range(HALVES):
-            at = out_tiles.index((0, STRIPS - 1)) - QUANT_LEAD - 2 * QUANT_GAP * (1 - half)
-            late_quants.setdefault(at, []).append((quant_y, STRIPS - 1, half))
-        for k, tile in enumerate(out_tiles):
-            tensor_steps.append((second_product, *tile))
-            if k % TILES_PER_PRODUCT == TILES_PER_PRODUCT - 1:
-                tensor_steps.extend(late_products[k // TILES_PER_PRODUCT : k // TILES_PER_PRODUCT + 1])
-            vector_steps.extend(late_quants.get(k, []) + [(finish, *tile)])
+            at = out_jobs.index((chunk, 0)) - QUANT_LEAD
+            late_quants.setdefault(at - 1, []).extend([(weave_a, *x) for x in LATE_WEAVES_ON_VECTOR if x[0] == chunk])
+            late_quants.setdefault(at, []).append((quant_a, chunk))
+        late_quants.setdefault(out_jobs.index((0, STRIPS - 1)) - QUANT_LEAD, []).append((quant_y, STRIPS - 1))
+        for k, (chunk, strip) in enumerate(out_jobs):
+            tensor_steps.extend([(second_product, 2 * chunk, strip), (second_product, 2 * chunk + 1, strip)])
+            tensor_steps.extend([(first_product, 3, u) for u in range(SLICES) if u // LATE_PRODUCTS == k])
+            vector_steps.extend(late_quants.get(k, []) + [(finish, chunk, strip)])
         for chunk in (2, 3):
             for half in range(HALVES):
                 scalar_steps.extend([(empty_u, chunk, 2 * half), (empty_u, chunk, 2 * half + 1)])
@@ -419,6 +414,40 @@ def tile_curvature_scaled_pair_correction_d7_kernel(tc, G, S_bytes, S_scale, Y_b
                 for half in range(HALVES):
                     scalar_steps.extend([(widen_y, STRIPS - 1, half), (weave_y, STRIPS - 1, half)])
 
+
+        def bank_keys(job, a=0, b=0):
+            table = {
+                turn_s: [("s_bank", a, 0), ("s_bank", a, 1)],
+                turn_g: [("g_bank", a, 2 * b), ("g_bank", a, 2 * b + 1)],
+                first_product: [("u_bank", a, b // 2)] if b % 2 == 0 else [],
+                second_product: [("p_bank", a, b)],
+                empty_s: [("s_bank", a, 0), ("s_bank", a, 1)],
+                empty_g: [("g_bank", a, 2 * b), ("g_bank", a, 2 * b + 1)],
+                empty_u: [("u_bank", a, b)],
+                finish: [("p_bank", 2 * a, b), ("p_bank", 2 * a + 1, b)],
+            }
+            return table.get(job, [])
+
+        bank_of = {}
+        last_turn = tensor_steps.index((turn_g, CHUNKS - 1, 1))
+        taken_so_far = {}
+        for k, step in enumerate(tensor_steps):
+            if step[0] in (turn_s, turn_g):
+                ring = range(BANKS - SIDE_BANKS)
+            elif step[0] is first_product and k < last_turn:
+                ring = range(BANKS - SIDE_BANKS, BANKS)
+            elif step[0] is first_product and step[1] < CHUNKS - 1:
+                ring = range(BANKS)
+            elif step[0] is first_product:
+                ring = range(BANKS - OUT_SIDE, BANKS)
+            elif step[1] < 2 * (CHUNKS - 1):
+                ring = range(0, BANKS - OUT_SIDE)
+            else:
+                ring = range(BANKS - 1, -1, -1)
+            for key in bank_keys(*step):
+                role = (step[0] is second_product, ring.start, ring.stop)
+                bank_of[key] = ring[taken_so_far.get(role, 0) % len(ring)]
+                taken_so_far[role] = taken_so_far.get(role, 0) + 1
 
         def inputs(job, a=0, b=0):
             table = {
@@ -432,13 +461,13 @@ def tile_curvature_scaled_pair_correction_d7_kernel(tc, G, S_bytes, S_scale, Y_b
                 quant_g: [(empty_g, a, b)],
                 first_product: [(quant_s, b), (quant_g, a, 0), (quant_g, a, 1)],
                 empty_u: [(first_product, a, 2 * b + 1), (invert_c,)],
-                weave_a: [(empty_u, a, 2 * b), (empty_u, a, 2 * b + 1)],
-                quant_a: [(weave_a, a, b)],
+                weave_a: [(empty_u, a, 2 * b), (empty_u, a, 2 * b + 1)] + [(weave_a, a, 0)] * b,
+                quant_a: [(weave_a, a, 0), (weave_a, a, 1)],
                 widen_y: [(load_y, a, b)],
-                weave_y: [(widen_y, a, b), (load_y_factor, b)],
-                quant_y: [(weave_y, a, b)],
-                second_product: [(quant_a, a // 2, 0), (quant_a, a // 2, 1), (quant_y, b, 0), (quant_y, b, 1)],
-                finish: [(second_product, a, b), (load_h,)],
+                weave_y: [(widen_y, a, b), (load_y_factor, b)] + [(weave_y, a, 0)] * b,
+                quant_y: [(weave_y, a, 0), (weave_y, a, 1)],
+                second_product: [(quant_a, a // 2), (quant_y, b)],
+                finish: [(second_product, 2 * a, b), (second_product, 2 * a + 1, b), (load_h,), (turn_g, CHUNKS - 1, 1)],
                 invert_c: [(load_c,)],
             }
             return table.get(job, [])
@@ -447,28 +476,24 @@ def tile_curvature_scaled_pair_correction_d7_kernel(tc, G, S_bytes, S_scale, Y_b
             table = {
                 widen_s: {"wide_s": 0 if job is widen_s and SCALAR_PASSES[a] else 1},
                 widen_s_scalar: {"wide_s": 1},
-                turn_s: {"wide_s": -1, "turn": 2},
-                turn_g: {"turn": 2},
-                empty_s: {"turn": -2, "turned": 1},
-                empty_g: {"turn": -2, "turned": 1},
+                turn_s: {"wide_s": -1},
+                empty_s: {"turned": 1},
+                empty_g: {"turned": 1},
                 quant_s: {"turned": -1},
                 quant_g: {"turned": -1},
-                first_product: {"acc": 1 - b % 2},
-                empty_u: {"acc": -1, "planes": 1 - b % 2},
-                weave_a: {"planes": -1, "a_woven": 1},
+                empty_u: {"planes": 1 - b % 2},
+                weave_a: {"planes": -1, "a_woven": 1 - b},
                 quant_a: {"a_woven": -1},
                 widen_y: {"y_wide": 1},
-                weave_y: {"y_wide": -1, "y_woven": 1},
+                weave_y: {"y_wide": -1, "y_woven": 1 - b},
                 quant_y: {"y_woven": -1},
-                second_product: {out_ring(a, b): 1},
-                finish: {out_ring(a, b): -1},
             }
-            return table.get(job, {})
+            sign = 1 if (job, a, b) in tensor_steps or (job, a) in tensor_steps else -1
+            return {**table.get(job, {}), **{bank_of[key]: sign for key in bank_keys(job, a, b)}}
 
         free = {
             "wide_s": WIDE_S_BUFS,
-            "turn": RING_BANKS,
-            "acc": RING_BANKS,
+            **{number: 1 for number in range(BANKS)},
             "turned": TURNED_BUFS,
             "planes": A_PLANE_BUFS,
             "a_woven": WOVEN_A_BUFS,

@@ -27,37 +27,27 @@ CHUNK = 256
 CHUNKS = T // CHUNK
 STRIP = 512
 STRIPS = N // STRIP
-
-SCALAR_PASSES = (2, 2, 0, 0, 0, 0, 0, 0)
-TURN = 4
-BANK_ORDER = (0, 1)
-PORDER = 1
-QUANT_LEAD = 2
-QUANT_GAP = 2
-LATE_PRODUCTS = 1
-LATE_WEAVES_ON_VECTOR = ((2, 0),)
-CAST_FIRST = 5
-CAST_EVERY = 3
-EARLY_Y = 2
-WIDEN_LEAD = 4
-LOAD_LEAD = 3
-Y_LEAD = 0
-PRODUCT_LAG = 4
-PRODUCTS_PER_TURN = 1
-VECTOR_EMPTIES = (11,)
-WEAVE_LAG = 3
+RUN = 4
 BANKS = 8
 SIDE_BANKS = 2
-OUT_SIDE = 3
-STORE_STRIPS = 1
 
-WIDE_S_BUFS = 4
+SCALAR_SLICES = 2
+SCALAR_Y_PARTS = 3
+
+WIDEN_LEAD = 4
+LOAD_LEAD = 3
+PRODUCT_LAG = 4
+CAST_FIRST = 5
+CAST_EVERY = 3
+QUANT_LEAD = 2
+
+WIDE_S_BUFS = WIDEN_LEAD
 TURNED_BUFS = 4
-A_PLANE_BUFS = 4
+A_PLANE_BUFS = 5
 WOVEN_A_BUFS = 2
 WIDE_Y_BUFS = 3
 WOVEN_Y_BUFS = 2
-RESULT_BUFS = 8
+ROW_BUFS = 2 * CHUNKS
 
 
 def tile_curvature_scaled_pair_correction_d7_kernel(tc, G, S_bytes, S_scale, Y_bytes, Y_scale, c, h, out):
@@ -98,17 +88,17 @@ def tile_curvature_scaled_pair_correction_d7_kernel(tc, G, S_bytes, S_scale, Y_b
             rows = table[PACK * half : PACK * (half + 1), :].partition_broadcast(QUAD)
             nc.sync.dma_start(out=factor[half][:], in_=rows.rearrange("r q k -> q r k"))
 
+        def load_s_factor(half):
+            load_factor(s_factor, S_scale, half)
+
+        def load_y_factor(half):
+            load_factor(y_factor, Y_scale, half)
+
         def load_c():
             nc.sync.dma_start(out=c_bf[:], in_=c.rearrange("(half p j) -> p half j", half=HALVES, j=PACK))
 
-        def invert_c():
-            nc.vector.reciprocal(out=c_inv[:], in_=c_bf[:].rearrange("p half j -> p (half j)"))
-
         def load_h():
             nc.sync.dma_start(out=h_all[:], in_=h.partition_broadcast(P))
-
-        def copy_on(step):
-            return nc.vector.tensor_copy if step in vector_steps else nc.scalar.copy
 
         def load_s(u):
             raw = keep.tile([P, N], U8, name="s_raw%d" % u)
@@ -116,7 +106,7 @@ def tile_curvature_scaled_pair_correction_d7_kernel(tc, G, S_bytes, S_scale, Y_b
             tiles["s_raw", u] = raw
 
         def load_g(chunk, b):
-            raw = work.tile([P, CHUNK // P, 2 * K_PASS], BF16, name="g_raw", tag="rows", bufs=2 * CHUNKS)
+            raw = work.tile([P, CHUNK // P, 2 * K_PASS], BF16, name="g_raw", tag="rows", bufs=ROW_BUFS)
             rows = G[chunk * CHUNK : (chunk + 1) * CHUNK, 2 * K_PASS * b : 2 * K_PASS * (b + 1)]
             nc.sync.dma_start(out=raw[:], in_=rows.rearrange("(i r) n -> r i n", r=P))
             tiles["g_raw", chunk, b] = raw
@@ -125,6 +115,12 @@ def tile_curvature_scaled_pair_correction_d7_kernel(tc, G, S_bytes, S_scale, Y_b
             raw = keep.tile([P, PACK, STRIP], U8, name="y_raw%d%d" % (strip, half))
             nc.sync.dma_start(out=raw[:], in_=y_rows[half][:, :, strip * STRIP : (strip + 1) * STRIP])
             tiles["y_raw", strip, half] = raw
+
+        def invert_c():
+            nc.vector.reciprocal(out=c_inv[:], in_=c_bf[:].rearrange("p half j -> p (half j)"))
+
+        def vector_passes(u):
+            return PASSES // 2 if u < SCALAR_SLICES else PASSES
 
         def wide_s_tile(u):
             if ("s_wide", u) not in tiles:
@@ -135,7 +131,7 @@ def tile_curvature_scaled_pair_correction_d7_kernel(tc, G, S_bytes, S_scale, Y_b
             raw = tiles["s_raw", u]
             sorted_by_w = wide_s_tile(u)[:].rearrange("r (g w p e) -> r g p w e", g=PASSES, w=2, e=2)
             for q in range(P // QUAD):
-                for g in range(PASSES - SCALAR_PASSES[u]):
+                for g in range(vector_passes(u)):
                     block = PACK * g + q
                     nc.vector.tensor_scalar(
                         out=sorted_by_w[:, g, QUAD * q : QUAD * (q + 1)],
@@ -148,7 +144,7 @@ def tile_curvature_scaled_pair_correction_d7_kernel(tc, G, S_bytes, S_scale, Y_b
         def widen_s_scalar(u):
             raw = tiles["s_raw", u]
             wide = wide_s_tile(u)
-            for block in range(COL_BLOCKS - PACK * SCALAR_PASSES[u], COL_BLOCKS):
+            for block in range(PACK * vector_passes(u), COL_BLOCKS):
                 cols = slice(block * P, (block + 1) * P)
                 factor = s_factor[u // PACK][:, block : block + 1]
                 nc.scalar.activation(out=wide[:, cols], in_=raw[:, cols].bitcast(FP8), func=COPY, scale=factor)
@@ -160,20 +156,21 @@ def tile_curvature_scaled_pair_correction_d7_kernel(tc, G, S_bytes, S_scale, Y_b
                 for i in range(2):
                     g = 2 * b + i
                     for w in range(2):
-                        if g >= PASSES - SCALAR_PASSES[u]:
-                            src = words[:, 2 * P * g + w : 2 * P * (g + 1) : 2]
-                        else:
+                        if g < vector_passes(u):
                             src = words[:, 2 * P * g + P * w : 2 * P * g + P * (w + 1)]
+                        else:
+                            src = words[:, 2 * P * g + w : 2 * P * (g + 1) : 2]
                         nc.tensor.transpose(turned[:, w, i, :], src, ident[:])
 
         def join_words(copy, dst, turned):
             copy(out=dst, in_=turned[:].rearrange("p w a r -> p (a r) w"))
 
         def empty_s(u):
+            copy = nc.vector.tensor_copy if (empty_s, u) in vector_steps else nc.scalar.copy
             joined = work.tile([P, 2, 2 * P, 2], F32, name="s_turned", tag="turned", bufs=TURNED_BUFS, align_bytes=64)
             tiles["s_turned", u] = joined
-            for b in BANK_ORDER:
-                join_words(copy_on((empty_s, u)), joined[:, b], tiles["s_bank", u, b])
+            for b in range(2):
+                join_words(copy, joined[:, b], tiles["s_bank", u, b])
 
         def quant_s(u):
             nc.vector.quantize_mx(
@@ -193,8 +190,8 @@ def tile_curvature_scaled_pair_correction_d7_kernel(tc, G, S_bytes, S_scale, Y_b
         def empty_g(chunk, b):
             joined = work.tile([P, 2, CHUNK, 2], F32, name="g_turned", tag="turned", bufs=TURNED_BUFS, align_bytes=64)
             tiles["g_turned", chunk, b] = joined
-            for i in BANK_ORDER:
-                join_words(copy_on((empty_g, chunk, b)), joined[:, i], tiles["g_bank", chunk, 2 * b + i])
+            for i in range(2):
+                join_words(nc.scalar.copy, joined[:, i], tiles["g_bank", chunk, 2 * b + i])
 
         def quant_g(chunk, b):
             nc.vector.quantize_mx(
@@ -220,7 +217,7 @@ def tile_curvature_scaled_pair_correction_d7_kernel(tc, G, S_bytes, S_scale, Y_b
 
         def empty_u(chunk, b):
             half = b // 2
-            if ("a_planes", chunk, half) not in tiles:
+            if b % 2 == 0:
                 tiles["a_planes", chunk, half] = work.tile([P, PACK, CHUNK], BF16, name="a_planes", bufs=A_PLANE_BUFS)
             planes = tiles["a_planes", chunk, half]
             for i in range(2):
@@ -228,21 +225,24 @@ def tile_curvature_scaled_pair_correction_d7_kernel(tc, G, S_bytes, S_scale, Y_b
                 sums = tiles["u_bank", chunk, b][:, i, :]
                 nc.scalar.activation(out=planes[:, u % PACK, :], in_=sums, func=COPY, scale=c_inv[:, u : u + 1])
 
-        def in_runs_out(woven):
-            return woven.rearrange("p (x i j) -> p x j i", i=4, j=PACK)
+        def vector_views(woven, planes):
+            return woven.rearrange("p (x i j) -> p x j i", i=RUN, j=PACK), planes.rearrange("p j (x i) -> p x j i", i=RUN)
 
-        def in_runs_in(planes):
-            return planes.rearrange("p j (x i) -> p x j i", i=4)
+        def scalar_views(woven, planes):
+            return woven.rearrange("p (n j) -> p n j", j=PACK), planes.rearrange("p j n -> p n j")
 
         def weave_a(chunk, half):
             if half == 0:
-                tiles["a_woven", chunk] = work.tile([P, HALVES, CHUNK * PACK], BF16, name="a_woven", bufs=WOVEN_A_BUFS, align_bytes=64)
+                shape = [P, HALVES, CHUNK * PACK]
+                tiles["a_woven", chunk] = work.tile(shape, BF16, name="a_woven", bufs=WOVEN_A_BUFS, align_bytes=64)
             woven = tiles["a_woven", chunk][:, half, :]
             planes = tiles["a_planes", chunk, half][:]
             if (weave_a, chunk, half) in vector_steps:
-                nc.vector.tensor_copy(out=in_runs_out(woven), in_=in_runs_in(planes))
+                dst, src = vector_views(woven, planes)
+                nc.vector.tensor_copy(out=dst, in_=src)
             else:
-                nc.scalar.copy(out=woven.rearrange("p (n j) -> p n j", j=PACK), in_=planes.rearrange("p j n -> p n j"))
+                dst, src = scalar_views(woven, planes)
+                nc.scalar.copy(out=dst, in_=src)
 
         def quant_a(chunk):
             nc.vector.quantize_mx(
@@ -251,7 +251,7 @@ def tile_curvature_scaled_pair_correction_d7_kernel(tc, G, S_bytes, S_scale, Y_b
                 in_=tiles["a_woven", chunk][:].rearrange("p g x -> p (g x)"),
             )
 
-        def widen_y(strip, half):
+        def cast_y(strip, half):
             wide = work.tile([P, PACK, STRIP], BF16, name="y_wide", bufs=WIDE_Y_BUFS)
             tiles["y_wide", strip, half] = wide
             raw = tiles["y_raw", strip, half][:].rearrange("p j n -> p (j n)")
@@ -259,18 +259,19 @@ def tile_curvature_scaled_pair_correction_d7_kernel(tc, G, S_bytes, S_scale, Y_b
 
         def weave_y(strip, half):
             if half == 0:
-                tiles["y_woven", strip] = work.tile([P, HALVES, STRIP * PACK], BF16, name="y_woven", bufs=WOVEN_Y_BUFS, align_bytes=64)
-            woven = tiles["y_woven", strip][:, half, :]
+                shape = [P, HALVES, STRIP * PACK]
+                tiles["y_woven", strip] = work.tile(shape, BF16, name="y_woven", bufs=WOVEN_Y_BUFS, align_bytes=64)
             for i in range(STRIP // P):
+                woven = tiles["y_woven", strip][:, half, P * PACK * i : P * PACK * (i + 1)]
+                planes = tiles["y_wide", strip, half][:, :, P * i : P * (i + 1)]
                 block = strip * (STRIP // P) + i
-                dst = woven[:, P * PACK * i : P * PACK * (i + 1)]
-                src = tiles["y_wide", strip, half][:, :, P * i : P * (i + 1)]
                 factor = y_factor[half][:, block : block + 1]
                 if (weave_y, strip, half) in vector_steps:
-                    nc.vector.tensor_scalar(out=in_runs_out(dst), in0=in_runs_in(src), scalar1=factor, scalar2=None, op0=MULT)
+                    dst, src = vector_views(woven, planes)
+                    nc.vector.tensor_scalar(out=dst, in0=src, scalar1=factor, scalar2=None, op0=MULT)
                 else:
-                    by_column = src.rearrange("p j n -> p n j")
-                    nc.scalar.activation(out=dst.rearrange("p (n j) -> p n j", j=PACK), in_=by_column, func=COPY, scale=factor)
+                    dst, src = scalar_views(woven, planes)
+                    nc.scalar.activation(out=dst, in_=src, func=COPY, scale=factor)
 
         def quant_y(strip):
             nc.vector.quantize_mx(
@@ -279,202 +280,166 @@ def tile_curvature_scaled_pair_correction_d7_kernel(tc, G, S_bytes, S_scale, Y_b
                 in_=tiles["y_woven", strip][:].rearrange("p g x -> p (g x)"),
             )
 
-        def second_product(row_tile, strip):
-            sums = bank(("p_bank", row_tile, strip), [P, STRIP])
-            chunk, i = divmod(row_tile, CHUNK // P)
-            for half in range(HALVES):
-                nc.tensor.matmul_mx(
-                    out=sums[:],
-                    lhsT=a_codes[:, chunk, half, i * P : (i + 1) * P].bitcast(FP8X4),
-                    lhsT_scale=a_scales[:, chunk, half, i * P : (i + 1) * P],
-                    rhs=y_codes[:, strip, half, :].bitcast(FP8X4),
-                    rhs_scale=y_scales[:, strip, half, :],
-                    start=(half == 0),
-                    stop=(half == HALVES - 1),
-                )
+        def second_product(chunk, strip):
+            for i in range(CHUNK // P):
+                sums = bank(("p_bank", chunk, strip, i), [P, STRIP])
+                for half in range(HALVES):
+                    nc.tensor.matmul_mx(
+                        out=sums[:],
+                        lhsT=a_codes[:, chunk, half, i * P : (i + 1) * P].bitcast(FP8X4),
+                        lhsT_scale=a_scales[:, chunk, half, i * P : (i + 1) * P],
+                        rhs=y_codes[:, strip, half, :].bitcast(FP8X4),
+                        rhs_scale=y_scales[:, strip, half, :],
+                        start=(half == 0),
+                        stop=(half == HALVES - 1),
+                    )
 
         def finish(chunk, strip):
-            res = work.tile([P, CHUNK // P, STRIP], F32, name="res", tag="rows", bufs=2 * CHUNKS)
+            res = work.tile([P, CHUNK // P, STRIP], F32, name="res", tag="rows", bufs=ROW_BUFS)
             cols = slice(STRIP * strip, STRIP * (strip + 1))
             rows = out[chunk * CHUNK : (chunk + 1) * CHUNK, cols].rearrange("(i r) n -> r i n", r=P)
-            last = (chunk, strip) == (CHUNKS - 1, STRIPS - 1)
-            for i in range(CHUNK // P) if last else reversed(range(CHUNK // P)):
-                sums = tiles["p_bank", 2 * chunk + i, strip]
+            last = (chunk, strip) == out_steps[-1]
+            for i in (0, 1) if last else (1, 0):
+                sums = tiles["p_bank", chunk, strip, i]
                 nc.vector.tensor_tensor(out=res[:, i, :], in0=sums[:], in1=h_all[:, cols], op=MULT)
                 if last:
                     nc.sync.dma_start(out=rows[:, i, :], in_=res[:, i, :])
             if not last:
                 nc.sync.dma_start(out=rows, in_=res[:])
 
-        def load_s_factor(half):
-            load_factor(s_factor, S_scale, half)
-
-        def load_y_factor(half):
-            load_factor(y_factor, Y_scale, half)
-
         g_parts = [(chunk, b) for chunk in range(CHUNKS) for b in range(2)]
         y_parts = [(strip, half) for strip in range(STRIPS) for half in range(HALVES)]
-        s = [("s", u) for u in range(SLICES)]
-        g = [("g", *part) for part in g_parts]
-        units = {
-            0: [x for u in range(8) for x in (s[u], g[u])],
-            1: [s[0], g[0], g[1], s[1], s[2], s[3], g[2], g[3], s[4], g[4], s[5], g[5], s[6], s[7], g[6], g[7]],
-            2: [s[0], g[0], g[1], s[1], s[2], s[3], g[2], s[4], g[3], s[5], g[4], s[6], g[5], s[7], g[6], g[7]],
-            3: [s[0], g[0], s[1], g[1], s[2], s[3], g[2], g[3], s[4], s[5], g[4], g[5], s[6], s[7], g[6], g[7]],
-            4: [s[0], g[0], s[1], g[1], s[2], g[2], s[3], g[3], s[4], s[5], s[6], s[7], g[4], g[5], g[6], g[7]],
-            5: [s[0], g[0], s[1], g[1], s[2], s[3], g[2], s[4], g[3], s[5], g[4], s[6], g[5], s[7], g[6], g[7]],
-        }[TURN]
-        load = {"s": load_s, "g": load_g}
+        last_chunk, last_strip = CHUNKS - 1, STRIPS - 1
+
+        units = [unit for u in range(PACK) for unit in (("s", u), ("g", *g_parts[u]))]
+        units = units + [("s", u) for u in range(PACK, SLICES)] + [("g", *part) for part in g_parts[PACK:]]
         turn = {"s": turn_s, "g": turn_g}
         empty = {"s": empty_s, "g": empty_g}
         quant = {"s": quant_s, "g": quant_g}
-        products = [(chunk, u) for half in range(HALVES) for chunk in range(2) for u in range(PACK * half, PACK * (half + 1))]
-        if PORDER == 1:
-            products = [(chunk, u) for chunk in range(2) for u in range(SLICES)]
-        casts = {CAST_FIRST + CAST_EVERY * k: y_parts[k] for k in range(EARLY_Y)}
+        cast_at = {i: y_parts[k] for k, i in enumerate(range(CAST_FIRST, len(units) - CAST_EVERY, CAST_EVERY))}
 
         sync_steps = [(load_s_factor, 0)]
         vector_steps = [(widen_s, u) for u in range(WIDEN_LEAD)] + [(invert_c,)]
-        scalar_steps = [(widen_s_scalar, u) for u in range(SLICES) if SCALAR_PASSES[u]]
+        scalar_steps = [(widen_s_scalar, u) for u in range(SCALAR_SLICES)]
         tensor_steps = []
-        later = []
-        for i, unit in enumerate(units):
-            ahead = [x for x in units[i:] if x[0] == "s"][:LOAD_LEAD]
-            for x in ([unit] if unit[0] == "g" else []) + ahead:
-                if (load[x[0]], *x[1:]) not in sync_steps:
-                    if x == s[PACK]:
-                        sync_steps.extend([(load_s_factor, 1), (load_c,)])
-                    sync_steps.append((load[x[0]], *x[1:]))
-            if i + Y_LEAD in casts:
-                part = casts[i + Y_LEAD]
-                if part[0] == 0:
-                    sync_steps.append((load_y_factor, part[1]))
-                sync_steps.append((load_y, *part))
-            done = [x[1:] for x in tensor_steps if x[0] is first_product]
-            tensor_steps.append((turn[unit[0]], *unit[1:]))
-            seen = units[: max(0, i + 1 - PRODUCT_LAG)]
-            ready = [p for p in products[len(done) : len(done) + PRODUCTS_PER_TURN]]
-            for p in ready:
-                if s[p[1]] in seen and g[2 * p[0] + 1] in seen and (p == products[0] or (first_product, *products[products.index(p) - 1]) in tensor_steps):
-                    tensor_steps.append((first_product, *p))
-            on_vector = i in VECTOR_EMPTIES
-            if not on_vector:
-                scalar_steps.append((empty[unit[0]], *unit[1:]))
-            for chunk, u in done:
-                if u % 2 == 1 and (empty_u, chunk, u // 2) not in scalar_steps:
-                    scalar_steps.append((empty_u, chunk, u // 2))
-            if i in casts:
-                scalar_steps.append((widen_y, *casts[i]))
-            first = [(empty[unit[0]], *unit[1:])] if on_vector else [(quant[unit[0]], *unit[1:])]
-            middle = []
-            if i - WEAVE_LAG in casts:
-                middle.append((weave_y, *casts[i - WEAVE_LAG]))
-            widened = len([x for x in vector_steps if x[0] is widen_s])
-            if unit[0] == "s" and widened < SLICES:
-                middle.append((widen_s, widened))
-            vector_steps.extend(first + later + middle)
-            later = [(quant[unit[0]], *unit[1:])] if on_vector else []
-            if i - WEAVE_LAG in casts and casts[i - WEAVE_LAG][1] == 1:
-                later.append((quant_y, casts[i - WEAVE_LAG][0]))
-        vector_steps.extend(later)
-        for part in y_parts[:6]:
-            if (load_y, *part) not in sync_steps:
-                sync_steps.append((load_y, *part))
-        sync_steps.extend([(load_h,), (load_y, 3, 0), (load_y, 3, 1)])
-        tensor_steps.extend([(first_product, *p) for p in products if (first_product, *p) not in tensor_steps])
-        rest_u = [(empty_u, c, u // 2) for c, u in products if u % 2 == 1 and (empty_u, c, u // 2) not in scalar_steps]
-        rest_y = [(widen_y, *part) for part in y_parts[:6] if (widen_y, *part) not in scalar_steps]
-        for k in range(max(len(rest_u), len(rest_y))):
-            scalar_steps.extend(rest_u[k : k + 1] + rest_y[k : k + 1])
-        rest_y = [part for part in y_parts[:6] if (weave_y, *part) not in vector_steps]
-        rest_a = [(chunk, half) for chunk in range(2) for half in range(HALVES)]
-        for k in range(max(len(rest_a), len(rest_y))):
-            a = rest_a[k : k + 1]
-            y = rest_y[k : k + 1]
-            vector_steps.extend([(weave_a, *x) for x in a] + [(weave_y, *x) for x in y] + [(quant_a, x[0]) for x in a if x[1] == 1] + [(quant_y, x[0]) for x in y if x[1] == 1])
-        out_jobs = [(chunk, strip) for chunk in range(CHUNKS - 1) for strip in range(STRIPS - 1)]
-        out_jobs = out_jobs + [(chunk, STRIPS - 1) for chunk in range(CHUNKS - 1)] + [(CHUNKS - 1, strip) for strip in range(STRIPS)]
-        tensor_steps.extend([(first_product, 2, u) for u in range(SLICES)])
-        late_quants = {}
-        for chunk in (2, 3):
-            at = out_jobs.index((chunk, 0)) - QUANT_LEAD
-            late_quants.setdefault(at - 1, []).extend([(weave_a, *x) for x in LATE_WEAVES_ON_VECTOR if x[0] == chunk])
-            late_quants.setdefault(at, []).append((quant_a, chunk))
-        late_quants.setdefault(out_jobs.index((0, STRIPS - 1)) - QUANT_LEAD, []).append((quant_y, STRIPS - 1))
-        for k, (chunk, strip) in enumerate(out_jobs):
-            tensor_steps.extend([(second_product, 2 * chunk, strip), (second_product, 2 * chunk + 1, strip)])
-            tensor_steps.extend([(first_product, 3, u) for u in range(SLICES) if u // LATE_PRODUCTS == k])
-            vector_steps.extend(late_quants.get(k, []) + [(finish, chunk, strip)])
-        for chunk in (2, 3):
-            for half in range(HALVES):
-                scalar_steps.extend([(empty_u, chunk, 2 * half), (empty_u, chunk, 2 * half + 1)])
-                if (chunk, half) not in LATE_WEAVES_ON_VECTOR:
-                    scalar_steps.append((weave_a, chunk, half))
-            if chunk == 2:
-                for half in range(HALVES):
-                    scalar_steps.extend([(widen_y, STRIPS - 1, half), (weave_y, STRIPS - 1, half)])
+        multiplied = 0
+        held = []
+        for i, (kind, *index) in enumerate(units):
+            if kind == "g":
+                sync_steps.append((load_g, *index))
+            for u in [unit[1] for unit in units[i:] if unit[0] == "s"][:LOAD_LEAD]:
+                if u == PACK and (load_s, u) not in sync_steps:
+                    sync_steps.extend([(load_s_factor, 1), (load_c,)])
+                if (load_s, u) not in sync_steps:
+                    sync_steps.append((load_s, u))
+            if i in cast_at:
+                strip, half = cast_at[i]
+                sync_steps.extend([(load_y_factor, half)] * (strip == 0) + [(load_y, strip, half)])
 
+            tensor_steps.append((turn[kind], *index))
+            emptied = multiplied // 2
+            ready = units[: max(0, i + 1 - PRODUCT_LAG)]
+            if ("s", multiplied) in ready and ("g", 0, 1) in ready:
+                tensor_steps.append((first_product, 0, multiplied))
+                multiplied = multiplied + 1
+
+            own = (kind, *index) == ("s", SLICES - 1)
+            scalar_steps.extend([] if own else [(empty[kind], *index)])
+            scalar_steps.extend([(empty_u, 0, b) for b in range(emptied) if (empty_u, 0, b) not in scalar_steps])
+            scalar_steps.extend([(cast_y, *cast_at[i])] if i in cast_at else [])
+
+            vector_steps.extend([(empty_s, *index) if own else (quant[kind], *index)] + held)
+            held = [(quant_s, *index)] if own else []
+            if i - CAST_EVERY in cast_at:
+                strip, half = cast_at[i - CAST_EVERY]
+                vector_steps.append((weave_y, strip, half))
+                held = held + [(quant_y, strip)] * half
+            if kind == "s" and index[0] + WIDEN_LEAD < SLICES:
+                vector_steps.append((widen_s, index[0] + WIDEN_LEAD))
+
+        later_y = y_parts[len(cast_at) :]
+        sync_steps.extend([(load_y, *part) for part in later_y[:-HALVES]] + [(load_h,)])
+        sync_steps.extend([(load_y, last_strip, half) for half in range(HALVES)])
+        tensor_steps.extend([(first_product, 0, u) for u in range(multiplied, SLICES)])
+        tensor_steps.extend([(first_product, chunk, u) for chunk in (1, 2) for u in range(SLICES)])
+        pairs = [(empty_u, chunk, b) for chunk in (0, 1) for b in range(PACK) if (empty_u, chunk, b) not in scalar_steps]
+        for k, step in enumerate(pairs):
+            scalar_steps.extend([step] + [(cast_y, *part) for part in later_y[:-HALVES][k : k + 1]])
+        vector_steps.extend([(weave_a, 0, 0), (weave_y, 1, 1), (weave_a, 0, 1), (quant_y, 1), (quant_a, 0)])
+        vector_steps.extend([(weave_a, 1, 0), (weave_a, 1, 1), (weave_y, 2, 0), (quant_a, 1)])
+
+        out_steps = [(chunk, strip) for chunk in range(last_chunk) for strip in (0, 1)]
+        out_steps = out_steps + [(chunk, strip) for strip in (2, 3) for chunk in range(last_chunk)]
+        out_steps = out_steps + [(last_chunk, strip) for strip in range(STRIPS)]
+        before = {k: [] for k in range(len(out_steps))}
+        before[1].append((weave_a, 2, 0))
+        for step, first_use in (((quant_a, 2), (2, 0)), ((quant_y, 2), (0, 2)), ((quant_a, last_chunk), (last_chunk, 0))):
+            before[out_steps.index(first_use) - QUANT_LEAD].append(step)
+        before[out_steps.index((0, last_strip)) - 1].append((quant_y, last_strip))
+        for k, step in enumerate(out_steps):
+            tensor_steps.extend([(second_product, *step)] + [(first_product, last_chunk, u) for u in range(SLICES)][k : k + 1])
+            vector_steps.extend(before[k] + [(finish, *step)])
+        scalar_steps.extend([(empty_u, 2, b) for b in range(PACK)] + [(weave_a, 2, 1)])
+        scalar_steps.extend([(weave_y, *part) for part in y_parts[-SCALAR_Y_PARTS:-HALVES]])
+        for half in range(HALVES):
+            scalar_steps.extend([(empty_u, last_chunk, half), (cast_y, last_strip, half), (weave_y, last_strip, half)])
+        for half in range(HALVES):
+            scalar_steps.extend([(empty_u, last_chunk, HALVES + half), (weave_a, last_chunk, half)])
 
         def bank_keys(job, a=0, b=0):
-            table = {
-                turn_s: [("s_bank", a, 0), ("s_bank", a, 1)],
-                turn_g: [("g_bank", a, 2 * b), ("g_bank", a, 2 * b + 1)],
-                first_product: [("u_bank", a, b // 2)] if b % 2 == 0 else [],
-                second_product: [("p_bank", a, b)],
-                empty_s: [("s_bank", a, 0), ("s_bank", a, 1)],
-                empty_g: [("g_bank", a, 2 * b), ("g_bank", a, 2 * b + 1)],
-                empty_u: [("u_bank", a, b)],
-                finish: [("p_bank", 2 * a, b), ("p_bank", 2 * a + 1, b)],
-            }
-            return table.get(job, [])
+            if job in (turn_s, empty_s):
+                return [("s_bank", a, 0), ("s_bank", a, 1)]
+            if job in (turn_g, empty_g):
+                return [("g_bank", a, 2 * b), ("g_bank", a, 2 * b + 1)]
+            if job in (second_product, finish):
+                return [("p_bank", a, b, 0), ("p_bank", a, b, 1)]
+            if job is first_product and b % 2 == 0:
+                return [("u_bank", a, b // 2)]
+            return [("u_bank", a, b)] if job is empty_u else []
 
+        main_ring, side_ring = range(BANKS - SIDE_BANKS), range(BANKS - SIDE_BANKS, BANKS)
+        end_of_phase_1 = tensor_steps.index((turn_g, *g_parts[-1]))
         bank_of = {}
-        last_turn = tensor_steps.index((turn_g, CHUNKS - 1, 1))
-        taken_so_far = {}
-        for k, step in enumerate(tensor_steps):
-            if step[0] in (turn_s, turn_g):
-                ring = range(BANKS - SIDE_BANKS)
-            elif step[0] is first_product and k < last_turn:
-                ring = range(BANKS - SIDE_BANKS, BANKS)
-            elif step[0] is first_product and step[1] < CHUNKS - 1:
-                ring = range(BANKS)
-            elif step[0] is first_product:
-                ring = range(BANKS - OUT_SIDE, BANKS)
-            elif step[1] < 2 * (CHUNKS - 1):
-                ring = range(0, BANKS - OUT_SIDE)
+        taken = {}
+        for k, (job, *index) in enumerate(tensor_steps):
+            if job in (turn_s, turn_g):
+                role, ring = "turn", main_ring
+            elif job is first_product and k < end_of_phase_1:
+                role, ring = "early product", side_ring
+            elif job is first_product:
+                role, ring = ("late product", side_ring) if index[0] == last_chunk else ("product", range(BANKS))
             else:
-                ring = range(BANKS - 1, -1, -1)
-            for key in bank_keys(*step):
-                role = (step[0] is second_product, ring.start, ring.stop)
-                bank_of[key] = ring[taken_so_far.get(role, 0) % len(ring)]
-                taken_so_far[role] = taken_so_far.get(role, 0) + 1
+                role, ring = ("last output", range(BANKS - 1, -1, -1)) if index[0] == last_chunk else ("output", main_ring)
+            for key in bank_keys(job, *index):
+                bank_of[key] = ring[taken.get(role, 0) % len(ring)]
+                taken[role] = taken.get(role, 0) + 1
 
         def inputs(job, a=0, b=0):
             table = {
                 widen_s: [(load_s, a), (load_s_factor, a // PACK)],
                 widen_s_scalar: [(load_s, a), (load_s_factor, a // PACK)],
-                turn_s: [(widen_s, a)] + ([(widen_s_scalar, a)] if job is turn_s and SCALAR_PASSES[a] else []),
+                turn_s: [(widen_s, a)] + [(widen_s_scalar, a)] * (a < SCALAR_SLICES),
                 empty_s: [(turn_s, a)],
                 quant_s: [(empty_s, a)],
                 turn_g: [(load_g, a, b)],
                 empty_g: [(turn_g, a, b)],
                 quant_g: [(empty_g, a, b)],
                 first_product: [(quant_s, b), (quant_g, a, 0), (quant_g, a, 1)],
+                invert_c: [(load_c,)],
                 empty_u: [(first_product, a, 2 * b + 1), (invert_c,)],
                 weave_a: [(empty_u, a, 2 * b), (empty_u, a, 2 * b + 1)] + [(weave_a, a, 0)] * b,
                 quant_a: [(weave_a, a, 0), (weave_a, a, 1)],
-                widen_y: [(load_y, a, b)],
-                weave_y: [(widen_y, a, b), (load_y_factor, b)] + [(weave_y, a, 0)] * b,
+                cast_y: [(load_y, a, b)],
+                weave_y: [(cast_y, a, b), (load_y_factor, b)] + [(weave_y, a, 0)] * b,
                 quant_y: [(weave_y, a, 0), (weave_y, a, 1)],
-                second_product: [(quant_a, a // 2), (quant_y, b)],
-                finish: [(second_product, 2 * a, b), (second_product, 2 * a + 1, b), (load_h,), (turn_g, CHUNKS - 1, 1)],
-                invert_c: [(load_c,)],
+                second_product: [(quant_a, a), (quant_y, b)],
+                finish: [(second_product, a, b), (load_h,)],
             }
             return table.get(job, [])
 
         def buffers(job, a=0, b=0):
             table = {
-                widen_s: {"wide_s": 0 if job is widen_s and SCALAR_PASSES[a] else 1},
+                widen_s: {"wide_s": int(a >= SCALAR_SLICES)},
                 widen_s_scalar: {"wide_s": 1},
                 turn_s: {"wide_s": -1},
                 empty_s: {"turned": 1},
@@ -484,34 +449,24 @@ def tile_curvature_scaled_pair_correction_d7_kernel(tc, G, S_bytes, S_scale, Y_b
                 empty_u: {"planes": 1 - b % 2},
                 weave_a: {"planes": -1, "a_woven": 1 - b},
                 quant_a: {"a_woven": -1},
-                widen_y: {"y_wide": 1},
+                cast_y: {"y_wide": 1},
                 weave_y: {"y_wide": -1, "y_woven": 1 - b},
                 quant_y: {"y_woven": -1},
             }
-            sign = 1 if (job, a, b) in tensor_steps or (job, a) in tensor_steps else -1
+            sign = 1 if job in (turn_s, turn_g, first_product, second_product) else -1
             return {**table.get(job, {}), **{bank_of[key]: sign for key in bank_keys(job, a, b)}}
 
-        free = {
-            "wide_s": WIDE_S_BUFS,
-            **{number: 1 for number in range(BANKS)},
-            "turned": TURNED_BUFS,
-            "planes": A_PLANE_BUFS,
-            "a_woven": WOVEN_A_BUFS,
-            "y_wide": WIDE_Y_BUFS,
-            "y_woven": WOVEN_Y_BUFS,
-        }
+        free = {"wide_s": WIDE_S_BUFS, "turned": TURNED_BUFS, "planes": A_PLANE_BUFS, "a_woven": WOVEN_A_BUFS}
+        free = {**free, "y_wide": WIDE_Y_BUFS, "y_woven": WOVEN_Y_BUFS, **{number: 1 for number in range(BANKS)}}
         queues = [sync_steps, scalar_steps, vector_steps, tensor_steps]
         written = set()
         for sweep in range(sum(len(queue) for queue in queues)):
             for queue in queues:
-                todo = [step for step in queue if step not in written]
-                if not todo:
-                    continue
-                step = todo[0]
-                taken = buffers(*step)
-                if all(need in written for need in inputs(*step)) and all(free[kind] >= n for kind, n in taken.items()):
-                    step[0](*step[1:])
-                    written.add(step)
-                    for kind, n in taken.items():
-                        free[kind] = free[kind] - n
+                for step in [step for step in queue if step not in written][:1]:
+                    use = buffers(*step)
+                    if all(need in written for need in inputs(*step)) and all(free[kind] >= n for kind, n in use.items()):
+                        step[0](*step[1:])
+                        written.add(step)
+                        for kind, n in use.items():
+                            free[kind] = free[kind] - n
         assert len(written) == sum(len(queue) for queue in queues)

@@ -32,13 +32,14 @@ BANKS = 8
 SIDE_BANKS = 2
 
 SCALAR_SLICES = 2
-SCALAR_Y_PARTS = 3
 
 WIDEN_LEAD = 4
 LOAD_LEAD = 3
 PRODUCT_LAG = 4
 CAST_FIRST = 5
 CAST_EVERY = 3
+LATE_PRODUCTS = 2
+LATE_BANKS = 3
 QUANT_LEAD = 2
 
 WIDE_S_BUFS = WIDEN_LEAD
@@ -280,9 +281,14 @@ def tile_curvature_scaled_pair_correction_d7_kernel(tc, G, S_bytes, S_scale, Y_b
                 in_=tiles["y_woven", strip][:].rearrange("p g x -> p (g x)"),
             )
 
-        def second_product(chunk, strip):
-            for i in range(CHUNK // P):
-                sums = bank(("p_bank", chunk, strip, i), [P, STRIP])
+        def out_tiles(k):
+            row_tile, strip, along_row = out_steps[k]
+            return [(row_tile, strip), (row_tile, strip + 1) if along_row else (row_tile + 1, strip)]
+
+        def second_product(k):
+            for row_tile, strip in out_tiles(k):
+                sums = bank(("p_bank", row_tile, strip), [P, STRIP])
+                chunk, i = divmod(row_tile, CHUNK // P)
                 for half in range(HALVES):
                     nc.tensor.matmul_mx(
                         out=sums[:],
@@ -294,14 +300,20 @@ def tile_curvature_scaled_pair_correction_d7_kernel(tc, G, S_bytes, S_scale, Y_b
                         stop=(half == HALVES - 1),
                     )
 
-        def finish(chunk, strip):
-            res = work.tile([P, CHUNK // P, STRIP], F32, name="res", tag="rows", bufs=ROW_BUFS)
-            cols = slice(STRIP * strip, STRIP * (strip + 1))
-            rows = out[chunk * CHUNK : (chunk + 1) * CHUNK, cols].rearrange("(i r) n -> r i n", r=P)
-            last = (chunk, strip) == out_steps[-1]
+        def finish(k):
+            row_tile, strip, along_row = out_steps[k]
+            res = work.tile([P, 2, STRIP], F32, name="res", tag="rows", bufs=ROW_BUFS)
+            if along_row:
+                rows = out[row_tile * P : (row_tile + 1) * P, STRIP * strip : STRIP * (strip + 2)]
+                rows = rows.rearrange("r (i n) -> r i n", i=2)
+            else:
+                rows = out[row_tile * P : (row_tile + 2) * P, STRIP * strip : STRIP * (strip + 1)]
+                rows = rows.rearrange("(i r) n -> r i n", i=2)
+            last = k == len(out_steps) - 1
             for i in (0, 1) if last else (1, 0):
-                sums = tiles["p_bank", chunk, strip, i]
-                nc.vector.tensor_tensor(out=res[:, i, :], in0=sums[:], in1=h_all[:, cols], op=MULT)
+                tile = out_tiles(k)[i]
+                factor = h_all[:, STRIP * tile[1] : STRIP * (tile[1] + 1)]
+                nc.vector.tensor_tensor(out=res[:, i, :], in0=tiles[("p_bank", *tile)][:], in1=factor, op=MULT)
                 if last:
                     nc.sync.dma_start(out=rows[:, i, :], in_=res[:, i, :])
             if not last:
@@ -316,7 +328,7 @@ def tile_curvature_scaled_pair_correction_d7_kernel(tc, G, S_bytes, S_scale, Y_b
         turn = {"s": turn_s, "g": turn_g}
         empty = {"s": empty_s, "g": empty_g}
         quant = {"s": quant_s, "g": quant_g}
-        cast_at = {i: y_parts[k] for k, i in enumerate(range(CAST_FIRST, len(units) - CAST_EVERY, CAST_EVERY))}
+        cast_at = {i: y_parts[k] for k, i in enumerate((CAST_FIRST, CAST_FIRST + CAST_EVERY))}
 
         sync_steps = [(load_s_factor, 0)]
         vector_steps = [(widen_s, u) for u in range(WIDEN_LEAD)] + [(invert_c,)]
@@ -365,26 +377,27 @@ def tile_curvature_scaled_pair_correction_d7_kernel(tc, G, S_bytes, S_scale, Y_b
         pairs = [(empty_u, chunk, b) for chunk in (0, 1) for b in range(PACK) if (empty_u, chunk, b) not in scalar_steps]
         for k, step in enumerate(pairs):
             scalar_steps.extend([step] + [(cast_y, *part) for part in later_y[:-HALVES][k : k + 1]])
-        vector_steps.extend([(weave_a, 0, 0), (weave_y, 1, 1), (weave_a, 0, 1), (quant_y, 1), (quant_a, 0)])
+        vector_steps.extend([(weave_a, 0, 0), (weave_y, 1, 0), (weave_a, 0, 1), (weave_y, 1, 1), (quant_a, 0), (quant_y, 1)])
         vector_steps.extend([(weave_a, 1, 0), (weave_a, 1, 1), (weave_y, 2, 0), (quant_a, 1)])
 
-        out_steps = [(chunk, strip) for chunk in range(last_chunk) for strip in (0, 1)]
-        out_steps = out_steps + [(chunk, strip) for strip in (2, 3) for chunk in range(last_chunk)]
-        out_steps = out_steps + [(last_chunk, strip) for strip in range(STRIPS)]
+        first_rows, last_rows = range(2 * last_chunk), range(2 * last_chunk, 2 * CHUNKS)
+        out_steps = [(row_tile, 0, True) for row_tile in first_rows]
+        out_steps = out_steps + [(row_tile, strip, False) for strip in (2, 3) for row_tile in first_rows[::2]]
+        out_steps = out_steps + [(row_tile, strip, True) for row_tile in last_rows for strip in (0, 2)]
         before = {k: [] for k in range(len(out_steps))}
-        before[1].append((weave_a, 2, 0))
-        for step, first_use in (((quant_a, 2), (2, 0)), ((quant_y, 2), (0, 2)), ((quant_a, last_chunk), (last_chunk, 0))):
-            before[out_steps.index(first_use) - QUANT_LEAD].append(step)
-        before[out_steps.index((0, last_strip)) - 1].append((quant_y, last_strip))
-        for k, step in enumerate(out_steps):
-            tensor_steps.extend([(second_product, *step)] + [(first_product, last_chunk, u) for u in range(SLICES)][k : k + 1])
-            vector_steps.extend(before[k] + [(finish, *step)])
-        scalar_steps.extend([(empty_u, 2, b) for b in range(PACK)] + [(weave_a, 2, 1)])
-        scalar_steps.extend([(weave_y, *part) for part in y_parts[-SCALAR_Y_PARTS:-HALVES]])
-        for half in range(HALVES):
-            scalar_steps.extend([(empty_u, last_chunk, half), (cast_y, last_strip, half), (weave_y, last_strip, half)])
-        for half in range(HALVES):
-            scalar_steps.extend([(empty_u, last_chunk, HALVES + half), (weave_a, last_chunk, half)])
+        before[1].extend([(weave_y, 2, 1), (weave_a, 2, 0)])
+        before[out_steps.index((4, 0, True)) - QUANT_LEAD].append((quant_a, 2))
+        before[out_steps.index((0, 2, False)) - QUANT_LEAD].append((quant_y, 2))
+        before[out_steps.index((0, 3, False)) - QUANT_LEAD].append((quant_y, 3))
+        before[out_steps.index((6, 0, True)) - QUANT_LEAD].append((quant_a, 3))
+        for k in range(len(out_steps)):
+            tensor_steps.append((second_product, k))
+            tensor_steps.extend([(first_product, last_chunk, u) for u in range(SLICES) if u // LATE_PRODUCTS == k])
+            vector_steps.extend(before[k] + [(finish, k)])
+        scalar_steps.extend([(empty_u, 2, b) for b in range(PACK)] + [(cast_y, last_strip, 0), (weave_a, 2, 1)])
+        scalar_steps.extend([(empty_u, last_chunk, 0), (weave_y, last_strip, 0), (cast_y, last_strip, 1)])
+        scalar_steps.extend([(empty_u, last_chunk, 1), (weave_y, last_strip, 1), (empty_u, last_chunk, 2)])
+        scalar_steps.extend([(empty_u, last_chunk, 3), (weave_a, last_chunk, 0), (weave_a, last_chunk, 1)])
 
         def bank_keys(job, a=0, b=0):
             if job in (turn_s, empty_s):
@@ -392,7 +405,7 @@ def tile_curvature_scaled_pair_correction_d7_kernel(tc, G, S_bytes, S_scale, Y_b
             if job in (turn_g, empty_g):
                 return [("g_bank", a, 2 * b), ("g_bank", a, 2 * b + 1)]
             if job in (second_product, finish):
-                return [("p_bank", a, b, 0), ("p_bank", a, b, 1)]
+                return [("p_bank", *tile) for tile in out_tiles(a)]
             if job is first_product and b % 2 == 0:
                 return [("u_bank", a, b // 2)]
             return [("u_bank", a, b)] if job is empty_u else []
@@ -407,9 +420,9 @@ def tile_curvature_scaled_pair_correction_d7_kernel(tc, G, S_bytes, S_scale, Y_b
             elif job is first_product and k < end_of_phase_1:
                 role, ring = "early product", side_ring
             elif job is first_product:
-                role, ring = ("late product", side_ring) if index[0] == last_chunk else ("product", range(BANKS))
+                role, ring = ("late product", range(BANKS - LATE_BANKS, BANKS)) if index[0] == last_chunk else ("product", range(BANKS))
             else:
-                role, ring = ("last output", range(BANKS - 1, -1, -1)) if index[0] == last_chunk else ("output", main_ring)
+                role, ring = ("last output", range(BANKS - 1, -1, -1)) if out_steps[index[0]][0] in last_rows else ("output", range(BANKS - LATE_BANKS))
             for key in bank_keys(job, *index):
                 bank_of[key] = ring[taken.get(role, 0) % len(ring)]
                 taken[role] = taken.get(role, 0) + 1
@@ -432,9 +445,10 @@ def tile_curvature_scaled_pair_correction_d7_kernel(tc, G, S_bytes, S_scale, Y_b
                 cast_y: [(load_y, a, b)],
                 weave_y: [(cast_y, a, b), (load_y_factor, b)] + [(weave_y, a, 0)] * b,
                 quant_y: [(weave_y, a, 0), (weave_y, a, 1)],
-                second_product: [(quant_a, a), (quant_y, b)],
-                finish: [(second_product, a, b), (load_h,)],
+                finish: [(second_product, a), (load_h,)],
             }
+            if job is second_product:
+                return [need for row_tile, strip in out_tiles(a) for need in ((quant_a, row_tile // 2), (quant_y, strip))]
             return table.get(job, [])
 
         def buffers(job, a=0, b=0):

@@ -27,22 +27,29 @@ CHUNK = 256
 CHUNKS = T // CHUNK
 STRIP = 512
 STRIPS = N // STRIP
+FIRST_SORTED = 4
+SORT_LEAD = 4
+OWN = 11
+QY_LEAD = 2
+COUNT = 1
+FIRST_OUT = 0
+GLEAD = 0
 RUN = 4
 BANKS = 8
 SIDE_BANKS = 2
 
-SCALAR_SLICES = 2
+SCALAR_SLICES = 1
 
 WIDEN_LEAD = 4
 LOAD_LEAD = 3
 PRODUCT_LAG = 4
-CAST_FIRST = 5
+CAST_FIRST = 7
 CAST_EVERY = 3
-LATE_PRODUCTS = 2
-LATE_BANKS = 3
+LATE_PRODUCTS = 1
+LATE_BANKS = 2
 QUANT_LEAD = 2
 
-WIDE_S_BUFS = WIDEN_LEAD
+WIDE_S_BUFS = 6
 TURNED_BUFS = 4
 A_PLANE_BUFS = 5
 WOVEN_A_BUFS = 2
@@ -180,13 +187,27 @@ def tile_curvature_scaled_pair_correction_d7_kernel(tc, G, S_bytes, S_scale, Y_b
                 in_=tiles["s_turned", u][:].rearrange("p b x w -> p (b x w)").bitcast(BF16),
             )
 
+        def sort_g(chunk, b):
+            ordered = work.tile([P, CHUNK // P, 2 * K_PASS], BF16, name="g_sorted", tag="s_wide", bufs=WIDE_S_BUFS)
+            tiles["g_sorted", chunk, b] = ordered
+            words = tiles["g_raw", chunk, b][:].rearrange("r i n -> r (i n)").bitcast(F32)
+            nc.vector.tensor_copy(
+                out=ordered[:].rearrange("r i n -> r (i n)").bitcast(F32).rearrange("r (x w p) -> r x w p", w=2, p=P),
+                in_=words.rearrange("r (x p w) -> r x w p", w=2, p=P),
+            )
+
         def turn_g(chunk, b):
             for g in range(2):
                 turned = bank(("g_bank", chunk, 2 * b + g), [P, 2, 2, P])
                 for i in range(2):
-                    words = tiles["g_raw", chunk, b][:, i, :].bitcast(F32)
                     for w in range(2):
-                        nc.tensor.transpose(turned[:, w, i, :], words[:, 2 * P * g + w : 2 * P * (g + 1) : 2], ident[:])
+                        if (sort_g, chunk, b) in vector_steps:
+                            words = tiles["g_sorted", chunk, b][:, i, :].bitcast(F32)
+                            src = words[:, 2 * P * g + P * w : 2 * P * g + P * (w + 1)]
+                        else:
+                            words = tiles["g_raw", chunk, b][:, i, :].bitcast(F32)
+                            src = words[:, 2 * P * g + w : 2 * P * (g + 1) : 2]
+                        nc.tensor.transpose(turned[:, w, i, :], src, ident[:])
 
         def empty_g(chunk, b):
             joined = work.tile([P, 2, CHUNK, 2], F32, name="g_turned", tag="turned", bufs=TURNED_BUFS, align_bytes=64)
@@ -335,10 +356,12 @@ def tile_curvature_scaled_pair_correction_d7_kernel(tc, G, S_bytes, S_scale, Y_b
         scalar_steps = [(widen_s_scalar, u) for u in range(SCALAR_SLICES)]
         tensor_steps = []
         multiplied = 0
+        second = 0
         held = []
         for i, (kind, *index) in enumerate(units):
-            if kind == "g":
-                sync_steps.append((load_g, *index))
+            for unit in units[i : i + 1 + (GLEAD if i > 3 else 0)]:
+                if unit[0] == "g" and (load_g, *unit[1:]) not in sync_steps:
+                    sync_steps.append((load_g, *unit[1:]))
             for u in [unit[1] for unit in units[i:] if unit[0] == "s"][:LOAD_LEAD]:
                 if u == PACK and (load_s, u) not in sync_steps:
                     sync_steps.extend([(load_s_factor, 1), (load_c,)])
@@ -350,14 +373,20 @@ def tile_curvature_scaled_pair_correction_d7_kernel(tc, G, S_bytes, S_scale, Y_b
 
             tensor_steps.append((turn[kind], *index))
             emptied = multiplied // 2
+            emptied1 = second // 2
             ready = units[: max(0, i + 1 - PRODUCT_LAG)]
             if ("s", multiplied) in ready and ("g", 0, 1) in ready:
                 tensor_steps.append((first_product, 0, multiplied))
                 multiplied = multiplied + 1
+            for n in range(COUNT - 1):
+                if ("s", second) in ready and ("g", 1, 1) in ready:
+                    tensor_steps.append((first_product, 1, second))
+                    second = second + 1
 
-            own = (kind, *index) == ("s", SLICES - 1)
+            own = i == OWN
             scalar_steps.extend([] if own else [(empty[kind], *index)])
             scalar_steps.extend([(empty_u, 0, b) for b in range(emptied) if (empty_u, 0, b) not in scalar_steps])
+            scalar_steps.extend([(empty_u, 1, b) for b in range(emptied1) if (empty_u, 1, b) not in scalar_steps])
             scalar_steps.extend([(cast_y, *cast_at[i])] if i in cast_at else [])
 
             vector_steps.extend([(empty_s, *index) if own else (quant[kind], *index)] + held)
@@ -368,12 +397,15 @@ def tile_curvature_scaled_pair_correction_d7_kernel(tc, G, S_bytes, S_scale, Y_b
                 held = held + [(quant_y, strip)] * half
             if kind == "s" and index[0] + WIDEN_LEAD < SLICES:
                 vector_steps.append((widen_s, index[0] + WIDEN_LEAD))
+            for unit in units[i + SORT_LEAD : i + SORT_LEAD + 1]:
+                if unit[0] == "g" and g_parts.index(unit[1:]) >= FIRST_SORTED:
+                    vector_steps.append((sort_g, *unit[1:]))
 
         later_y = y_parts[len(cast_at) :]
         sync_steps.extend([(load_y, *part) for part in later_y[:-HALVES]] + [(load_h,)])
         sync_steps.extend([(load_y, last_strip, half) for half in range(HALVES)])
         tensor_steps.extend([(first_product, 0, u) for u in range(multiplied, SLICES)])
-        tensor_steps.extend([(first_product, chunk, u) for chunk in (1, 2) for u in range(SLICES)])
+        tensor_steps.extend([(first_product, chunk, u) for chunk in (1, 2) for u in range(SLICES) if (first_product, chunk, u) not in tensor_steps])
         pairs = [(empty_u, chunk, b) for chunk in (0, 1) for b in range(PACK) if (empty_u, chunk, b) not in scalar_steps]
         for k, step in enumerate(pairs):
             scalar_steps.extend([step] + [(cast_y, *part) for part in later_y[:-HALVES][k : k + 1]])
@@ -387,12 +419,13 @@ def tile_curvature_scaled_pair_correction_d7_kernel(tc, G, S_bytes, S_scale, Y_b
         before = {k: [] for k in range(len(out_steps))}
         before[1].extend([(weave_y, 2, 1), (weave_a, 2, 0)])
         before[out_steps.index((4, 0, True)) - QUANT_LEAD].append((quant_a, 2))
-        before[out_steps.index((0, 2, False)) - QUANT_LEAD].append((quant_y, 2))
-        before[out_steps.index((0, 3, False)) - QUANT_LEAD].append((quant_y, 3))
+        before[out_steps.index((0, 2, False)) - QY_LEAD].append((quant_y, 2))
+        before[out_steps.index((0, 3, False)) - QY_LEAD].append((quant_y, 3))
         before[out_steps.index((6, 0, True)) - QUANT_LEAD].append((quant_a, 3))
+        tensor_steps.extend([(first_product, last_chunk, u) for u in range(FIRST_OUT)])
         for k in range(len(out_steps)):
             tensor_steps.append((second_product, k))
-            tensor_steps.extend([(first_product, last_chunk, u) for u in range(SLICES) if u // LATE_PRODUCTS == k])
+            tensor_steps.extend([(first_product, last_chunk, u) for u in range(FIRST_OUT, SLICES) if (u - FIRST_OUT) // LATE_PRODUCTS == k])
             vector_steps.extend(before[k] + [(finish, k)])
         scalar_steps.extend([(empty_u, 2, b) for b in range(PACK)] + [(cast_y, last_strip, 0), (weave_a, 2, 1)])
         scalar_steps.extend([(empty_u, last_chunk, 0), (weave_y, last_strip, 0), (cast_y, last_strip, 1)])
@@ -434,7 +467,8 @@ def tile_curvature_scaled_pair_correction_d7_kernel(tc, G, S_bytes, S_scale, Y_b
                 turn_s: [(widen_s, a)] + [(widen_s_scalar, a)] * (a < SCALAR_SLICES),
                 empty_s: [(turn_s, a)],
                 quant_s: [(empty_s, a)],
-                turn_g: [(load_g, a, b)],
+                sort_g: [(load_g, a, b)],
+                turn_g: [(load_g, a, b)] + [(sort_g, a, b)] * ((sort_g, a, b) in vector_steps),
                 empty_g: [(turn_g, a, b)],
                 quant_g: [(empty_g, a, b)],
                 first_product: [(quant_s, b), (quant_g, a, 0), (quant_g, a, 1)],
@@ -456,6 +490,8 @@ def tile_curvature_scaled_pair_correction_d7_kernel(tc, G, S_bytes, S_scale, Y_b
                 widen_s: {"wide_s": int(a >= SCALAR_SLICES)},
                 widen_s_scalar: {"wide_s": 1},
                 turn_s: {"wide_s": -1},
+                sort_g: {"wide_s": 1},
+                turn_g: {"wide_s": -int((sort_g, a, b) in vector_steps)},
                 empty_s: {"turned": 1},
                 empty_g: {"turned": 1},
                 quant_s: {"turned": -1},

@@ -27,29 +27,21 @@ CHUNK = 256
 CHUNKS = T // CHUNK
 STRIP = 512
 STRIPS = N // STRIP
-FIRST_SORTED = 4
-SORT_LEAD = 4
-OWN = 11
-QY_LEAD = 2
-COUNT = 1
-FIRST_OUT = 0
-GLEAD = 0
+MOVING = 256
 RUN = 4
 BANKS = 8
 SIDE_BANKS = 2
 
-SCALAR_SLICES = 1
+SCALAR_SLICES = 2
 
 WIDEN_LEAD = 4
 LOAD_LEAD = 3
 PRODUCT_LAG = 4
-CAST_FIRST = 7
+CAST_FIRST = 6
 CAST_EVERY = 3
-LATE_PRODUCTS = 1
-LATE_BANKS = 2
 QUANT_LEAD = 2
 
-WIDE_S_BUFS = 6
+WIDE_BUFS = 6
 TURNED_BUFS = 4
 A_PLANE_BUFS = 5
 WOVEN_A_BUFS = 2
@@ -132,7 +124,7 @@ def tile_curvature_scaled_pair_correction_d7_kernel(tc, G, S_bytes, S_scale, Y_b
 
         def wide_s_tile(u):
             if ("s_wide", u) not in tiles:
-                tiles["s_wide", u] = work.tile([P, N], BF16, name="s_wide", bufs=WIDE_S_BUFS)
+                tiles["s_wide", u] = work.tile([P, N], BF16, name="s_wide", tag="wide", bufs=WIDE_BUFS)
             return tiles["s_wide", u]
 
         def widen_s(u):
@@ -188,7 +180,7 @@ def tile_curvature_scaled_pair_correction_d7_kernel(tc, G, S_bytes, S_scale, Y_b
             )
 
         def sort_g(chunk, b):
-            ordered = work.tile([P, CHUNK // P, 2 * K_PASS], BF16, name="g_sorted", tag="s_wide", bufs=WIDE_S_BUFS)
+            ordered = work.tile([P, CHUNK // P, 2 * K_PASS], BF16, name="g_sorted", tag="wide", bufs=WIDE_BUFS)
             tiles["g_sorted", chunk, b] = ordered
             words = tiles["g_raw", chunk, b][:].rearrange("r i n -> r (i n)").bitcast(F32)
             nc.vector.tensor_copy(
@@ -310,16 +302,18 @@ def tile_curvature_scaled_pair_correction_d7_kernel(tc, G, S_bytes, S_scale, Y_b
             for row_tile, strip in out_tiles(k):
                 sums = bank(("p_bank", row_tile, strip), [P, STRIP])
                 chunk, i = divmod(row_tile, CHUNK // P)
-                for half in range(HALVES):
-                    nc.tensor.matmul_mx(
-                        out=sums[:],
-                        lhsT=a_codes[:, chunk, half, i * P : (i + 1) * P].bitcast(FP8X4),
-                        lhsT_scale=a_scales[:, chunk, half, i * P : (i + 1) * P],
-                        rhs=y_codes[:, strip, half, :].bitcast(FP8X4),
-                        rhs_scale=y_scales[:, strip, half, :],
-                        start=(half == 0),
-                        stop=(half == HALVES - 1),
-                    )
+                for part in range(STRIP // MOVING):
+                    cols = slice(MOVING * part, MOVING * (part + 1))
+                    for half in range(HALVES):
+                        nc.tensor.matmul_mx(
+                            out=sums[:, cols],
+                            lhsT=a_codes[:, chunk, half, i * P : (i + 1) * P].bitcast(FP8X4),
+                            lhsT_scale=a_scales[:, chunk, half, i * P : (i + 1) * P],
+                            rhs=y_codes[:, strip, half, cols].bitcast(FP8X4),
+                            rhs_scale=y_scales[:, strip, half, cols],
+                            start=(half == 0),
+                            stop=(half == HALVES - 1),
+                        )
 
         def finish(k):
             row_tile, strip, along_row = out_steps[k]
@@ -356,12 +350,10 @@ def tile_curvature_scaled_pair_correction_d7_kernel(tc, G, S_bytes, S_scale, Y_b
         scalar_steps = [(widen_s_scalar, u) for u in range(SCALAR_SLICES)]
         tensor_steps = []
         multiplied = 0
-        second = 0
         held = []
         for i, (kind, *index) in enumerate(units):
-            for unit in units[i : i + 1 + (GLEAD if i > 3 else 0)]:
-                if unit[0] == "g" and (load_g, *unit[1:]) not in sync_steps:
-                    sync_steps.append((load_g, *unit[1:]))
+            if kind == "g":
+                sync_steps.append((load_g, *index))
             for u in [unit[1] for unit in units[i:] if unit[0] == "s"][:LOAD_LEAD]:
                 if u == PACK and (load_s, u) not in sync_steps:
                     sync_steps.extend([(load_s_factor, 1), (load_c,)])
@@ -373,20 +365,14 @@ def tile_curvature_scaled_pair_correction_d7_kernel(tc, G, S_bytes, S_scale, Y_b
 
             tensor_steps.append((turn[kind], *index))
             emptied = multiplied // 2
-            emptied1 = second // 2
             ready = units[: max(0, i + 1 - PRODUCT_LAG)]
             if ("s", multiplied) in ready and ("g", 0, 1) in ready:
                 tensor_steps.append((first_product, 0, multiplied))
                 multiplied = multiplied + 1
-            for n in range(COUNT - 1):
-                if ("s", second) in ready and ("g", 1, 1) in ready:
-                    tensor_steps.append((first_product, 1, second))
-                    second = second + 1
 
-            own = i == OWN
+            own = (kind, *index) == ("s", SLICES - 1)
             scalar_steps.extend([] if own else [(empty[kind], *index)])
             scalar_steps.extend([(empty_u, 0, b) for b in range(emptied) if (empty_u, 0, b) not in scalar_steps])
-            scalar_steps.extend([(empty_u, 1, b) for b in range(emptied1) if (empty_u, 1, b) not in scalar_steps])
             scalar_steps.extend([(cast_y, *cast_at[i])] if i in cast_at else [])
 
             vector_steps.extend([(empty_s, *index) if own else (quant[kind], *index)] + held)
@@ -397,15 +383,14 @@ def tile_curvature_scaled_pair_correction_d7_kernel(tc, G, S_bytes, S_scale, Y_b
                 held = held + [(quant_y, strip)] * half
             if kind == "s" and index[0] + WIDEN_LEAD < SLICES:
                 vector_steps.append((widen_s, index[0] + WIDEN_LEAD))
-            for unit in units[i + SORT_LEAD : i + SORT_LEAD + 1]:
-                if unit[0] == "g" and g_parts.index(unit[1:]) >= FIRST_SORTED:
-                    vector_steps.append((sort_g, *unit[1:]))
+            ahead = units[i + WIDEN_LEAD : i + WIDEN_LEAD + 1]
+            vector_steps.extend([(sort_g, *unit[1:]) for unit in ahead if unit in units[-PACK:]])
 
         later_y = y_parts[len(cast_at) :]
         sync_steps.extend([(load_y, *part) for part in later_y[:-HALVES]] + [(load_h,)])
         sync_steps.extend([(load_y, last_strip, half) for half in range(HALVES)])
         tensor_steps.extend([(first_product, 0, u) for u in range(multiplied, SLICES)])
-        tensor_steps.extend([(first_product, chunk, u) for chunk in (1, 2) for u in range(SLICES) if (first_product, chunk, u) not in tensor_steps])
+        tensor_steps.extend([(first_product, chunk, u) for chunk in (1, 2) for u in range(SLICES)])
         pairs = [(empty_u, chunk, b) for chunk in (0, 1) for b in range(PACK) if (empty_u, chunk, b) not in scalar_steps]
         for k, step in enumerate(pairs):
             scalar_steps.extend([step] + [(cast_y, *part) for part in later_y[:-HALVES][k : k + 1]])
@@ -418,14 +403,11 @@ def tile_curvature_scaled_pair_correction_d7_kernel(tc, G, S_bytes, S_scale, Y_b
         out_steps = out_steps + [(row_tile, strip, True) for row_tile in last_rows for strip in (0, 2)]
         before = {k: [] for k in range(len(out_steps))}
         before[1].extend([(weave_y, 2, 1), (weave_a, 2, 0)])
-        before[out_steps.index((4, 0, True)) - QUANT_LEAD].append((quant_a, 2))
-        before[out_steps.index((0, 2, False)) - QY_LEAD].append((quant_y, 2))
-        before[out_steps.index((0, 3, False)) - QY_LEAD].append((quant_y, 3))
-        before[out_steps.index((6, 0, True)) - QUANT_LEAD].append((quant_a, 3))
-        tensor_steps.extend([(first_product, last_chunk, u) for u in range(FIRST_OUT)])
+        first_uses = {(quant_a, 2): (4, 0, True), (quant_y, 2): (0, 2, False), (quant_y, 3): (0, 3, False)}
+        for step, first_use in {**first_uses, (quant_a, last_chunk): (last_rows[0], 0, True)}.items():
+            before[out_steps.index(first_use) - QUANT_LEAD].append(step)
         for k in range(len(out_steps)):
-            tensor_steps.append((second_product, k))
-            tensor_steps.extend([(first_product, last_chunk, u) for u in range(FIRST_OUT, SLICES) if (u - FIRST_OUT) // LATE_PRODUCTS == k])
+            tensor_steps.extend([(second_product, k)] + [(first_product, last_chunk, k)] * (k < SLICES))
             vector_steps.extend(before[k] + [(finish, k)])
         scalar_steps.extend([(empty_u, 2, b) for b in range(PACK)] + [(cast_y, last_strip, 0), (weave_a, 2, 1)])
         scalar_steps.extend([(empty_u, last_chunk, 0), (weave_y, last_strip, 0), (cast_y, last_strip, 1)])
@@ -452,10 +434,14 @@ def tile_curvature_scaled_pair_correction_d7_kernel(tc, G, S_bytes, S_scale, Y_b
                 role, ring = "turn", main_ring
             elif job is first_product and k < end_of_phase_1:
                 role, ring = "early product", side_ring
+            elif job is first_product and index[0] < last_chunk:
+                role, ring = "product", range(BANKS)
             elif job is first_product:
-                role, ring = ("late product", range(BANKS - LATE_BANKS, BANKS)) if index[0] == last_chunk else ("product", range(BANKS))
+                role, ring = "late product", side_ring
+            elif out_steps[index[0]][0] in first_rows:
+                role, ring = "output", main_ring
             else:
-                role, ring = ("last output", range(BANKS - 1, -1, -1)) if out_steps[index[0]][0] in last_rows else ("output", range(BANKS - LATE_BANKS))
+                role, ring = "last output", range(BANKS - 1, -1, -1)
             for key in bank_keys(job, *index):
                 bank_of[key] = ring[taken.get(role, 0) % len(ring)]
                 taken[role] = taken.get(role, 0) + 1
@@ -487,11 +473,11 @@ def tile_curvature_scaled_pair_correction_d7_kernel(tc, G, S_bytes, S_scale, Y_b
 
         def buffers(job, a=0, b=0):
             table = {
-                widen_s: {"wide_s": int(a >= SCALAR_SLICES)},
-                widen_s_scalar: {"wide_s": 1},
-                turn_s: {"wide_s": -1},
-                sort_g: {"wide_s": 1},
-                turn_g: {"wide_s": -int((sort_g, a, b) in vector_steps)},
+                widen_s: {"wide": int(a >= SCALAR_SLICES)},
+                widen_s_scalar: {"wide": 1},
+                turn_s: {"wide": -1},
+                sort_g: {"wide": 1},
+                turn_g: {"wide": -int((sort_g, a, b) in vector_steps)},
                 empty_s: {"turned": 1},
                 empty_g: {"turned": 1},
                 quant_s: {"turned": -1},
@@ -506,7 +492,7 @@ def tile_curvature_scaled_pair_correction_d7_kernel(tc, G, S_bytes, S_scale, Y_b
             sign = 1 if job in (turn_s, turn_g, first_product, second_product) else -1
             return {**table.get(job, {}), **{bank_of[key]: sign for key in bank_keys(job, a, b)}}
 
-        free = {"wide_s": WIDE_S_BUFS, "turned": TURNED_BUFS, "planes": A_PLANE_BUFS, "a_woven": WOVEN_A_BUFS}
+        free = {"wide": WIDE_BUFS, "turned": TURNED_BUFS, "planes": A_PLANE_BUFS, "a_woven": WOVEN_A_BUFS}
         free = {**free, "y_wide": WIDE_Y_BUFS, "y_woven": WOVEN_Y_BUFS, **{number: 1 for number in range(BANKS)}}
         queues = [sync_steps, scalar_steps, vector_steps, tensor_steps]
         written = set()

@@ -30,6 +30,7 @@ STRIPS = N // STRIP
 MOVING = 256
 RUN = 4
 BANKS = 8
+SPAN = 256
 SIDE_BANKS = 2
 
 SCALAR_SLICES = 2
@@ -67,14 +68,18 @@ def tile_curvature_scaled_pair_correction_d7_kernel(tc, G, S_bytes, S_scale, Y_b
         c_inv = keep.tile([P, SLICES], F32, name="c_inv")
         h_all = keep.tile([P, N], BF16, name="h_all")
 
-        s_codes = keep.tile([P, SLICES, PASSES, P], U32, name="s_codes", align_bytes=64)
-        s_scales = keep.tile([P, SLICES, PASSES, P], U8, name="s_scales", align_bytes=64)
-        g_codes = keep.tile([P, CHUNKS, PASSES, CHUNK], U32, name="g_codes", align_bytes=64)
-        g_scales = keep.tile([P, CHUNKS, PASSES, CHUNK], U8, name="g_scales", align_bytes=64)
-        a_codes = keep.tile([P, CHUNKS, HALVES, CHUNK], U32, name="a_codes", align_bytes=64)
-        a_scales = keep.tile([P, CHUNKS, HALVES, CHUNK], U8, name="a_scales", align_bytes=64)
-        y_codes = keep.tile([P, STRIPS, HALVES, STRIP], U32, name="y_codes", align_bytes=64)
-        y_scales = keep.tile([P, STRIPS, HALVES, STRIP], U8, name="y_scales", align_bytes=64)
+        def operand(name, groups, passes, columns, codes_at, scales_at):
+            count = groups * passes * columns
+            codes = keep.tile([P, SPAN // 4 + count], U32, name=name + "_codes", align_bytes=SPAN)
+            scales = keep.tile([P, SPAN + count], U8, name=name + "_scales", align_bytes=SPAN)
+            codes = codes[:, codes_at // 4 : codes_at // 4 + count]
+            scales = scales[:, scales_at : scales_at + count]
+            return [part.rearrange("p (a g x) -> p a g x", a=groups, g=passes) for part in (codes, scales)]
+
+        s_codes, s_scales = operand("s", SLICES, PASSES, P, SPAN // 4, 3 * SPAN // 4)
+        g_codes, g_scales = operand("g", CHUNKS, PASSES, CHUNK, 0, SPAN // 2)
+        a_codes, a_scales = operand("a", CHUNKS, HALVES, CHUNK, SPAN // 4, 3 * SPAN // 4)
+        y_codes, y_scales = operand("y", STRIPS, HALVES, STRIP, 0, SPAN // 2)
 
         s_rows = S_bytes.rearrange("(half r j) n -> half j r n", half=HALVES, j=PACK)
         y_rows = Y_bytes.rearrange("(half p j) n -> half p j n", half=HALVES, j=PACK)

@@ -13,6 +13,7 @@ U8 = mybir.dt.uint8
 FP8 = mybir.dt.float8_e4m3fn
 FP8X4 = mybir.dt.float8_e4m3fn_x4
 MULT = mybir.AluOpType.mult
+ADD = mybir.AluOpType.add
 COPY = mybir.ActivationFunctionType.Copy
 
 P = 128
@@ -27,26 +28,17 @@ CHUNK = 256
 CHUNKS = T // CHUNK
 STRIP = 512
 STRIPS = N // STRIP
-MOVING = 256
+MOVING = 512
 RUN = 4
 BANKS = 8
 SPAN = 256
-SIDE_BANKS = 2
 
 SCALAR_SLICES = 2
-
-WIDEN_LEAD = 4
-LOAD_LEAD = 3
-PRODUCT_LAG = 4
-CAST_FIRST = 6
-CAST_EVERY = 3
-QUANT_LEAD = 2
-
 WIDE_BUFS = 6
 TURNED_BUFS = 4
 A_PLANE_BUFS = 5
 WOVEN_A_BUFS = 2
-WIDE_Y_BUFS = 3
+WIDE_Y_BUFS = 4
 WOVEN_Y_BUFS = 2
 ROW_BUFS = 2 * CHUNKS
 
@@ -174,7 +166,7 @@ def tile_curvature_scaled_pair_correction_d7_kernel(tc, G, S_bytes, S_scale, Y_b
             copy = nc.vector.tensor_copy if (empty_s, u) in vector_steps else nc.scalar.copy
             joined = work.tile([P, 2, 2 * P, 2], F32, name="s_turned", tag="turned", bufs=TURNED_BUFS, align_bytes=64)
             tiles["s_turned", u] = joined
-            for b in range(2):
+            for b in (1, 0):
                 join_words(copy, joined[:, b], tiles["s_bank", u, b])
 
         def quant_s(u):
@@ -207,10 +199,11 @@ def tile_curvature_scaled_pair_correction_d7_kernel(tc, G, S_bytes, S_scale, Y_b
                         nc.tensor.transpose(turned[:, w, i, :], src, ident[:])
 
         def empty_g(chunk, b):
+            copy = nc.vector.tensor_copy if (empty_g, chunk, b) in vector_steps else nc.scalar.copy
             joined = work.tile([P, 2, CHUNK, 2], F32, name="g_turned", tag="turned", bufs=TURNED_BUFS, align_bytes=64)
             tiles["g_turned", chunk, b] = joined
-            for i in range(2):
-                join_words(nc.scalar.copy, joined[:, i], tiles["g_bank", chunk, 2 * b + i])
+            for i in (1, 0):
+                join_words(copy, joined[:, i], tiles["g_bank", chunk, 2 * b + i])
 
         def quant_g(chunk, b):
             nc.vector.quantize_mx(
@@ -242,7 +235,10 @@ def tile_curvature_scaled_pair_correction_d7_kernel(tc, G, S_bytes, S_scale, Y_b
             for i in range(2):
                 u = 2 * b + i
                 sums = tiles["u_bank", chunk, b][:, i, :]
-                nc.scalar.activation(out=planes[:, u % PACK, :], in_=sums, func=COPY, scale=c_inv[:, u : u + 1])
+                if (empty_u, chunk, b) in vector_steps:
+                    nc.vector.tensor_scalar(out=planes[:, u % PACK, :], in0=sums, scalar1=c_inv[:, u : u + 1], scalar2=None, op0=MULT)
+                else:
+                    nc.scalar.activation(out=planes[:, u % PACK, :], in_=sums, func=COPY, scale=c_inv[:, u : u + 1])
 
         def vector_views(woven, planes):
             return woven.rearrange("p (x i j) -> p x j i", i=RUN, j=PACK), planes.rearrange("p j (x i) -> p x j i", i=RUN)
@@ -259,6 +255,9 @@ def tile_curvature_scaled_pair_correction_d7_kernel(tc, G, S_bytes, S_scale, Y_b
             if (weave_a, chunk, half) in vector_steps:
                 dst, src = vector_views(woven, planes)
                 nc.vector.tensor_copy(out=dst, in_=src)
+            elif (weave_a, chunk, half) in gpsimd_steps:
+                dst, src = scalar_views(woven, planes)
+                nc.gpsimd.tensor_scalar(out=dst, in0=src, scalar1=1.0, scalar2=0.0, op0=MULT, op1=ADD)
             else:
                 dst, src = scalar_views(woven, planes)
                 nc.scalar.copy(out=dst, in_=src)
@@ -288,6 +287,9 @@ def tile_curvature_scaled_pair_correction_d7_kernel(tc, G, S_bytes, S_scale, Y_b
                 if (weave_y, strip, half) in vector_steps:
                     dst, src = vector_views(woven, planes)
                     nc.vector.tensor_scalar(out=dst, in0=src, scalar1=factor, scalar2=None, op0=MULT)
+                elif (weave_y, strip, half) in gpsimd_steps:
+                    dst, src = scalar_views(woven, planes)
+                    nc.gpsimd.tensor_scalar(out=dst, in0=src, scalar1=factor, scalar2=0.0, op0=MULT, op1=ADD)
                 else:
                     dst, src = scalar_views(woven, planes)
                     nc.scalar.activation(out=dst, in_=src, func=COPY, scale=factor)
@@ -339,85 +341,12 @@ def tile_curvature_scaled_pair_correction_d7_kernel(tc, G, S_bytes, S_scale, Y_b
             if not last:
                 nc.sync.dma_start(out=rows, in_=res[:])
 
-        g_parts = [(chunk, b) for chunk in range(CHUNKS) for b in range(2)]
-        y_parts = [(strip, half) for strip in range(STRIPS) for half in range(HALVES)]
-        last_chunk, last_strip = CHUNKS - 1, STRIPS - 1
-
-        units = [unit for u in range(PACK) for unit in (("s", u), ("g", *g_parts[u]))]
-        units = units + [("s", u) for u in range(PACK, SLICES)] + [("g", *part) for part in g_parts[PACK:]]
-        turn = {"s": turn_s, "g": turn_g}
-        empty = {"s": empty_s, "g": empty_g}
-        quant = {"s": quant_s, "g": quant_g}
-        cast_at = {i: y_parts[k] for k, i in enumerate((CAST_FIRST, CAST_FIRST + CAST_EVERY))}
-
-        sync_steps = [(load_s_factor, 0)]
-        vector_steps = [(widen_s, u) for u in range(WIDEN_LEAD)] + [(invert_c,)]
-        scalar_steps = [(widen_s_scalar, u) for u in range(SCALAR_SLICES)]
-        tensor_steps = []
-        multiplied = 0
-        held = []
-        for i, (kind, *index) in enumerate(units):
-            if kind == "g":
-                sync_steps.append((load_g, *index))
-            for u in [unit[1] for unit in units[i:] if unit[0] == "s"][:LOAD_LEAD]:
-                if u == PACK and (load_s, u) not in sync_steps:
-                    sync_steps.extend([(load_s_factor, 1), (load_c,)])
-                if (load_s, u) not in sync_steps:
-                    sync_steps.append((load_s, u))
-            if i in cast_at:
-                strip, half = cast_at[i]
-                sync_steps.extend([(load_y_factor, half)] * (strip == 0) + [(load_y, strip, half)])
-
-            tensor_steps.append((turn[kind], *index))
-            emptied = multiplied // 2
-            ready = units[: max(0, i + 1 - PRODUCT_LAG)]
-            if ("s", multiplied) in ready and ("g", 0, 1) in ready:
-                tensor_steps.append((first_product, 0, multiplied))
-                multiplied = multiplied + 1
-
-            own = (kind, *index) == ("s", SLICES - 1)
-            scalar_steps.extend([] if own else [(empty[kind], *index)])
-            scalar_steps.extend([(empty_u, 0, b) for b in range(emptied) if (empty_u, 0, b) not in scalar_steps])
-            scalar_steps.extend([(cast_y, *cast_at[i])] if i in cast_at else [])
-
-            vector_steps.extend([(empty_s, *index) if own else (quant[kind], *index)] + held)
-            held = [(quant_s, *index)] if own else []
-            if i - CAST_EVERY in cast_at:
-                strip, half = cast_at[i - CAST_EVERY]
-                vector_steps.append((weave_y, strip, half))
-                held = held + [(quant_y, strip)] * half
-            if kind == "s" and index[0] + WIDEN_LEAD < SLICES:
-                vector_steps.append((widen_s, index[0] + WIDEN_LEAD))
-            ahead = units[i + WIDEN_LEAD : i + WIDEN_LEAD + 1]
-            vector_steps.extend([(sort_g, *unit[1:]) for unit in ahead if unit in units[-PACK:]])
-
-        later_y = y_parts[len(cast_at) :]
-        sync_steps.extend([(load_y, *part) for part in later_y[:-HALVES]] + [(load_h,)])
-        sync_steps.extend([(load_y, last_strip, half) for half in range(HALVES)])
-        tensor_steps.extend([(first_product, 0, u) for u in range(multiplied, SLICES)])
-        tensor_steps.extend([(first_product, chunk, u) for chunk in (1, 2) for u in range(SLICES)])
-        pairs = [(empty_u, chunk, b) for chunk in (0, 1) for b in range(PACK) if (empty_u, chunk, b) not in scalar_steps]
-        for k, step in enumerate(pairs):
-            scalar_steps.extend([step] + [(cast_y, *part) for part in later_y[:-HALVES][k : k + 1]])
-        vector_steps.extend([(weave_a, 0, 0), (weave_y, 1, 0), (weave_a, 0, 1), (weave_y, 1, 1), (quant_a, 0), (quant_y, 1)])
-        vector_steps.extend([(weave_a, 1, 0), (weave_a, 1, 1), (weave_y, 2, 0), (quant_a, 1)])
-
-        first_rows, last_rows = range(2 * last_chunk), range(2 * last_chunk, 2 * CHUNKS)
-        out_steps = [(row_tile, 0, True) for row_tile in first_rows]
-        out_steps = out_steps + [(row_tile, strip, False) for strip in (2, 3) for row_tile in first_rows[::2]]
-        out_steps = out_steps + [(row_tile, strip, True) for row_tile in last_rows for strip in (0, 2)]
-        before = {k: [] for k in range(len(out_steps))}
-        before[1].extend([(weave_y, 2, 1), (weave_a, 2, 0)])
-        first_uses = {(quant_a, 2): (4, 0, True), (quant_y, 2): (0, 2, False), (quant_y, 3): (0, 3, False)}
-        for step, first_use in {**first_uses, (quant_a, last_chunk): (last_rows[0], 0, True)}.items():
-            before[out_steps.index(first_use) - QUANT_LEAD].append(step)
-        for k in range(len(out_steps)):
-            tensor_steps.extend([(second_product, k)] + [(first_product, last_chunk, k)] * (k < SLICES))
-            vector_steps.extend(before[k] + [(finish, k)])
-        scalar_steps.extend([(empty_u, 2, b) for b in range(PACK)] + [(cast_y, last_strip, 0), (weave_a, 2, 1)])
-        scalar_steps.extend([(empty_u, last_chunk, 0), (weave_y, last_strip, 0), (cast_y, last_strip, 1)])
-        scalar_steps.extend([(empty_u, last_chunk, 1), (weave_y, last_strip, 1), (empty_u, last_chunk, 2)])
-        scalar_steps.extend([(empty_u, last_chunk, 3), (weave_a, last_chunk, 0), (weave_a, last_chunk, 1)])
+        out_steps = [(r, 0, True) for r in range(4)] + [(0, 2, False), (2, 2, False), (4, 0, True), (5, 0, True), (4, 2, False), (6, 0, True), (7, 0, True), (6, 2, False)] + [(r, 3, False) for r in (0, 2, 4, 6)]
+        sync_steps = [(load_s_factor, 0), (load_s, 0), (load_s, 1), (load_s, 2), (load_s, 3), (load_g, 0, 0), (load_s_factor, 1), (load_s, 4), (load_g, 0, 1), (load_s, 5), (load_g, 1, 0), (load_g, 1, 1), (load_s, 6), (load_c,), (load_g, 2, 0), (load_s, 7), (load_g, 2, 1), (load_y_factor, 0), (load_y, 0, 0), (load_g, 3, 0), (load_y_factor, 1), (load_y, 0, 1), (load_g, 3, 1), (load_y, 1, 0), (load_y, 1, 1), (load_y, 2, 0), (load_y, 2, 1), (load_h,), (load_y, 3, 0), (load_y, 3, 1)]
+        tensor_steps = [(turn_s, 0), (turn_s, 1), (turn_s, 2), (turn_g, 0, 0), (turn_s, 3), (turn_g, 0, 1), (turn_s, 4), (turn_g, 1, 0), (turn_g, 1, 1), (turn_s, 5), (turn_g, 2, 0), (first_product, 0, 0), (first_product, 0, 1), (turn_s, 6), (turn_g, 2, 1), (turn_s, 7), (turn_g, 3, 0), (turn_g, 3, 1), (first_product, 0, 2), (first_product, 0, 3), (first_product, 0, 4), (first_product, 0, 5), (first_product, 0, 6), (first_product, 0, 7), (first_product, 1, 0), (first_product, 1, 1), (first_product, 1, 2), (first_product, 1, 3), (first_product, 1, 4), (first_product, 1, 5), (first_product, 1, 6), (first_product, 1, 7), (first_product, 2, 0), (first_product, 2, 1), (first_product, 2, 2), (first_product, 2, 3), (first_product, 2, 4), (first_product, 2, 5), (first_product, 2, 6), (first_product, 2, 7), (first_product, 3, 0), (first_product, 3, 1), (second_product, 0), (first_product, 3, 2), (first_product, 3, 3), (second_product, 1), (first_product, 3, 4), (first_product, 3, 5), (second_product, 2), (first_product, 3, 6), (first_product, 3, 7), (second_product, 3), (second_product, 4), (second_product, 5), (second_product, 6), (second_product, 7), (second_product, 8), (second_product, 9), (second_product, 10), (second_product, 11), (second_product, 12), (second_product, 13), (second_product, 14), (second_product, 15)]
+        scalar_steps = [(widen_s_scalar, 0), (widen_s_scalar, 1), (empty_s, 0), (empty_s, 1), (empty_s, 2), (empty_g, 0, 0), (empty_s, 3), (empty_g, 0, 1), (empty_s, 4), (empty_g, 1, 0), (empty_g, 1, 1), (empty_s, 5), (empty_g, 2, 0), (cast_y, 0, 0), (empty_u, 0, 0), (empty_g, 2, 1), (empty_s, 7), (empty_g, 3, 0), (empty_g, 3, 1), (cast_y, 0, 1), (empty_u, 0, 1), (empty_u, 0, 2), (cast_y, 1, 0), (empty_u, 0, 3), (empty_u, 1, 0), (cast_y, 1, 1), (empty_u, 1, 1), (cast_y, 2, 0), (empty_u, 1, 2), (empty_u, 1, 3), (cast_y, 2, 1), (empty_u, 2, 0), (empty_u, 2, 1), (empty_u, 2, 2), (empty_u, 2, 3), (weave_a, 2, 0), (empty_u, 3, 0), (cast_y, 3, 0), (empty_u, 3, 1), (cast_y, 3, 1), (empty_u, 3, 2), (empty_u, 3, 3), (weave_a, 3, 0), (weave_a, 3, 1), (weave_y, 3, 0), (weave_y, 3, 1)]
+        vector_steps = [(widen_s, 0), (widen_s, 1), (widen_s, 2), (widen_s, 3), (quant_s, 0), (widen_s, 4), (quant_s, 1), (quant_s, 2), (widen_s, 5), (quant_g, 0, 0), (quant_s, 3), (widen_s, 6), (quant_g, 0, 1), (quant_s, 4), (widen_s, 7), (invert_c,), (quant_g, 1, 0), (quant_g, 1, 1), (quant_s, 5), (empty_s, 6), (quant_g, 2, 0), (weave_y, 0, 0), (quant_s, 6), (quant_g, 2, 1), (quant_s, 7), (quant_g, 3, 0), (quant_g, 3, 1), (weave_y, 0, 1), (weave_a, 0, 0), (quant_y, 0), (weave_y, 1, 0), (weave_a, 0, 1), (weave_y, 1, 1), (quant_a, 0), (quant_y, 1), (weave_a, 1, 0), (weave_y, 2, 0), (weave_a, 1, 1), (weave_y, 2, 1), (quant_a, 1), (finish, 0), (weave_a, 2, 1), (finish, 1), (quant_y, 2), (finish, 2), (quant_a, 2), (finish, 3), (finish, 4), (finish, 5), (quant_a, 3), (finish, 6), (finish, 7), (finish, 8), (finish, 9), (quant_y, 3), (finish, 10), (finish, 11), (finish, 12), (finish, 13), (finish, 14), (finish, 15)]
+        gpsimd_steps = []
 
         def bank_keys(job, a=0, b=0):
             if job in (turn_s, empty_s):
@@ -430,26 +359,8 @@ def tile_curvature_scaled_pair_correction_d7_kernel(tc, G, S_bytes, S_scale, Y_b
                 return [("u_bank", a, b // 2)]
             return [("u_bank", a, b)] if job is empty_u else []
 
-        main_ring, side_ring = range(BANKS - SIDE_BANKS), range(BANKS - SIDE_BANKS, BANKS)
-        end_of_phase_1 = tensor_steps.index((turn_g, *g_parts[-1]))
-        bank_of = {}
-        taken = {}
-        for k, (job, *index) in enumerate(tensor_steps):
-            if job in (turn_s, turn_g):
-                role, ring = "turn", main_ring
-            elif job is first_product and k < end_of_phase_1:
-                role, ring = "early product", side_ring
-            elif job is first_product and index[0] < last_chunk:
-                role, ring = "product", range(BANKS)
-            elif job is first_product:
-                role, ring = "late product", side_ring
-            elif out_steps[index[0]][0] in first_rows:
-                role, ring = "output", main_ring
-            else:
-                role, ring = "last output", range(BANKS - 1, -1, -1)
-            for key in bank_keys(job, *index):
-                bank_of[key] = ring[taken.get(role, 0) % len(ring)]
-                taken[role] = taken.get(role, 0) + 1
+        keys = [key for step in tensor_steps for key in bank_keys(*step)]
+        bank_of = {key: k % BANKS for k, key in enumerate(keys)}
 
         def inputs(job, a=0, b=0):
             table = {
@@ -462,9 +373,9 @@ def tile_curvature_scaled_pair_correction_d7_kernel(tc, G, S_bytes, S_scale, Y_b
                 turn_g: [(load_g, a, b)] + [(sort_g, a, b)] * ((sort_g, a, b) in vector_steps),
                 empty_g: [(turn_g, a, b)],
                 quant_g: [(empty_g, a, b)],
-                first_product: [(quant_s, b), (quant_g, a, 0), (quant_g, a, 1)],
+                first_product: [(quant_s, b), (quant_g, a, 0), (quant_g, a, 1)] + [(first_product, a, b - 1)] * (b % 2),
                 invert_c: [(load_c,)],
-                empty_u: [(first_product, a, 2 * b + 1), (invert_c,)],
+                empty_u: [(first_product, a, 2 * b + 1), (invert_c,)] + [(empty_u, a, b - 1)] * (b % 2),
                 weave_a: [(empty_u, a, 2 * b), (empty_u, a, 2 * b + 1)] + [(weave_a, a, 0)] * b,
                 quant_a: [(weave_a, a, 0), (weave_a, a, 1)],
                 cast_y: [(load_y, a, b)],
@@ -477,37 +388,50 @@ def tile_curvature_scaled_pair_correction_d7_kernel(tc, G, S_bytes, S_scale, Y_b
             return table.get(job, [])
 
         def buffers(job, a=0, b=0):
+            banks = [(bank_of[key], key) for key in bank_keys(job, a, b)]
+            wide, rows, ordered = [("wide", a)], [("rows", (a, b))], [("wide", (a, b))]
+            turned = [("turned", (job in (empty_s, quant_s), a, b))]
+            a_planes, y_planes = [("a_planes", (a, b))], [("y_wide", (a, b))]
+            a_woven, y_woven = [("a_woven", a)], [("y_woven", a)]
             table = {
-                widen_s: {"wide": int(a >= SCALAR_SLICES)},
-                widen_s_scalar: {"wide": 1},
-                turn_s: {"wide": -1},
-                sort_g: {"wide": 1},
-                turn_g: {"wide": -int((sort_g, a, b) in vector_steps)},
-                empty_s: {"turned": 1},
-                empty_g: {"turned": 1},
-                quant_s: {"turned": -1},
-                quant_g: {"turned": -1},
-                empty_u: {"planes": 1 - b % 2},
-                weave_a: {"planes": -1, "a_woven": 1 - b},
-                quant_a: {"a_woven": -1},
-                cast_y: {"y_wide": 1},
-                weave_y: {"y_wide": -1, "y_woven": 1 - b},
-                quant_y: {"y_woven": -1},
+                widen_s: (wide * (a >= SCALAR_SLICES), []),
+                widen_s_scalar: (wide, []),
+                turn_s: (banks, wide),
+                load_g: (rows, []),
+                sort_g: (ordered, []),
+                turn_g: (banks, rows + ordered),
+                empty_s: (turned, banks),
+                empty_g: (turned, banks),
+                quant_s: ([], turned),
+                quant_g: ([], turned),
+                first_product: (banks, []),
+                empty_u: ([("a_planes", (a, b // 2))] * (b % 2 == 0), banks),
+                cast_y: (y_planes, []),
+                weave_a: (a_woven * (1 - b), a_planes),
+                weave_y: (y_woven * (1 - b), y_planes),
+                quant_a: ([], a_woven),
+                quant_y: ([], y_woven),
+                second_product: (banks, []),
+                finish: ([], banks),
             }
-            sign = 1 if job in (turn_s, turn_g, first_product, second_product) else -1
-            return {**table.get(job, {}), **{bank_of[key]: sign for key in bank_keys(job, a, b)}}
+            return table.get(job, ([], []))
 
-        free = {"wide": WIDE_BUFS, "turned": TURNED_BUFS, "planes": A_PLANE_BUFS, "a_woven": WOVEN_A_BUFS}
-        free = {**free, "y_wide": WIDE_Y_BUFS, "y_woven": WOVEN_Y_BUFS, **{number: 1 for number in range(BANKS)}}
-        queues = [sync_steps, scalar_steps, vector_steps, tensor_steps]
+        depth = {"wide": WIDE_BUFS, "turned": TURNED_BUFS, "a_planes": A_PLANE_BUFS, "a_woven": WOVEN_A_BUFS}
+        depth = {**depth, "y_wide": WIDE_Y_BUFS, "y_woven": WOVEN_Y_BUFS, "rows": ROW_BUFS}
+        owners = {kind: [] for kind in [*depth, *range(BANKS)]}
+        queues = [sync_steps, scalar_steps, vector_steps, gpsimd_steps, tensor_steps]
         written = set()
+        given = set()
         for sweep in range(sum(len(queue) for queue in queues)):
             for queue in queues:
                 for step in [step for step in queue if step not in written][:1]:
-                    use = buffers(*step)
-                    if all(need in written for need in inputs(*step)) and all(free[kind] >= n for kind, n in use.items()):
+                    takes, gives = buffers(*step)
+                    before = [owners[kind][-depth.get(kind, 1) :] for kind, owner in takes]
+                    room = all(len(last) < depth.get(kind, 1) or last[0] in given for last, (kind, owner) in zip(before, takes))
+                    if room and all(need in written for need in inputs(*step)):
                         step[0](*step[1:])
                         written.add(step)
-                        for kind, n in use.items():
-                            free[kind] = free[kind] - n
-        assert len(written) == sum(len(queue) for queue in queues)
+                        given.update(gives)
+                        for buffer in takes:
+                            owners[buffer[0]].append(buffer)
+        assert len(written) == sum(len(queue) for queue in queues), [[(s[0], s[1:]) for s in q if s not in written][:1] for q in queues]

@@ -33,7 +33,7 @@ RUN = 4
 BANKS = 8
 SPAN = 256
 
-SCALAR_SLICES = 2
+SHARED = (0, 1)
 WIDE_BUFS = 6
 TURNED_BUFS = 4
 A_PLANE_BUFS = 5
@@ -81,6 +81,10 @@ def tile_curvature_scaled_pair_correction_d7_kernel(tc, G, S_bytes, S_scale, Y_b
             tiles[key] = psum.tile(shape, F32, name="bank%d" % bank_of[key], bufs=1)
             return tiles[key]
 
+        def warm_up(k):
+            idle = bank(("idle", k), [P, P])
+            nc.tensor.matmul(out=idle[:], lhsT=ident[:], rhs=ident[:], start=True, stop=True)
+
         def load_factor(factor, table, half):
             rows = table[PACK * half : PACK * (half + 1), :].partition_broadcast(QUAD)
             nc.sync.dma_start(out=factor[half][:], in_=rows.rearrange("r q k -> q r k"))
@@ -117,7 +121,7 @@ def tile_curvature_scaled_pair_correction_d7_kernel(tc, G, S_bytes, S_scale, Y_b
             nc.vector.reciprocal(out=c_inv[:], in_=c_bf[:].rearrange("p half j -> p (half j)"))
 
         def vector_passes(u):
-            return PASSES // 2 if u < SCALAR_SLICES else PASSES
+            return PASSES // 2 if u in SHARED else PASSES
 
         def wide_s_tile(u):
             if ("s_wide", u) not in tiles:
@@ -322,30 +326,47 @@ def tile_curvature_scaled_pair_correction_d7_kernel(tc, G, S_bytes, S_scale, Y_b
                             stop=(half == HALVES - 1),
                         )
 
+        def result(k):
+            if ("res", k) not in tiles:
+                tiles["res", k] = work.tile([P, 2, STRIP], F32, name="res", tag="rows", bufs=ROW_BUFS)
+            return tiles["res", k]
+
+        def factor_h(k, i):
+            strip = out_tiles(k)[i][1]
+            return h_all[:, STRIP * strip : STRIP * (strip + 1)]
+
         def finish(k):
-            row_tile, strip, along_row = out_steps[k]
-            res = work.tile([P, 2, STRIP], F32, name="res", tag="rows", bufs=ROW_BUFS)
-            if along_row:
-                rows = out[row_tile * P : (row_tile + 1) * P, STRIP * strip : STRIP * (strip + 2)]
-                rows = rows.rearrange("r (i n) -> r i n", i=2)
-            else:
-                rows = out[row_tile * P : (row_tile + 2) * P, STRIP * strip : STRIP * (strip + 1)]
-                rows = rows.rearrange("(i r) n -> r i n", i=2)
             last = k == len(out_steps) - 1
             for i in (0, 1) if last else (1, 0):
-                tile = out_tiles(k)[i]
-                factor = h_all[:, STRIP * tile[1] : STRIP * (tile[1] + 1)]
-                nc.vector.tensor_tensor(out=res[:, i, :], in0=tiles[("p_bank", *tile)][:], in1=factor, op=MULT)
+                sums = tiles[("p_bank", *out_tiles(k)[i])][:]
+                nc.vector.tensor_tensor(out=result(k)[:, i, :], in0=sums, in1=factor_h(k, i), op=MULT)
                 if last:
-                    nc.sync.dma_start(out=rows[:, i, :], in_=res[:, i, :])
-            if not last:
-                nc.sync.dma_start(out=rows, in_=res[:])
+                    nc.sync.dma_start(out=out_rows(k)[:, i, :], in_=result(k)[:, i, :])
+
+        def drain(k):
+            for i in (1, 0):
+                nc.scalar.copy(out=result(k)[:, i, :], in_=tiles[("p_bank", *out_tiles(k)[i])][:])
+
+        def scale(k):
+            for i in (1, 0):
+                nc.gpsimd.tensor_tensor(out=result(k)[:, i, :], in0=result(k)[:, i, :], in1=factor_h(k, i), op=MULT)
+
+        def out_rows(k):
+            row_tile, strip, along_row = out_steps[k]
+            if along_row:
+                rows = out[row_tile * P : (row_tile + 1) * P, STRIP * strip : STRIP * (strip + 2)]
+                return rows.rearrange("r (i n) -> r i n", i=2)
+            rows = out[row_tile * P : (row_tile + 2) * P, STRIP * strip : STRIP * (strip + 1)]
+            return rows.rearrange("(i r) n -> r i n", i=2)
+
+        def store(k):
+            nc.sync.dma_start(out=out_rows(k), in_=result(k)[:])
 
         out_steps = [(r, 0, True) for r in range(4)] + [(0, 2, False), (2, 2, False), (4, 0, True), (5, 0, True), (4, 2, False), (6, 0, True), (7, 0, True), (6, 2, False)] + [(r, 3, False) for r in (0, 2, 4, 6)]
-        sync_steps = [(load_s_factor, 0), (load_s, 0), (load_s, 1), (load_s, 2), (load_s, 3), (load_g, 0, 0), (load_s_factor, 1), (load_s, 4), (load_g, 0, 1), (load_s, 5), (load_g, 1, 0), (load_g, 1, 1), (load_s, 6), (load_c,), (load_g, 2, 0), (load_s, 7), (load_g, 2, 1), (load_y_factor, 0), (load_y, 0, 0), (load_g, 3, 0), (load_y_factor, 1), (load_y, 0, 1), (load_g, 3, 1), (load_y, 1, 0), (load_y, 1, 1), (load_y, 2, 0), (load_y, 2, 1), (load_h,), (load_y, 3, 0), (load_y, 3, 1)]
-        tensor_steps = [(turn_s, 0), (turn_s, 1), (turn_s, 2), (turn_g, 0, 0), (turn_s, 3), (turn_g, 0, 1), (turn_s, 4), (turn_g, 1, 0), (turn_g, 1, 1), (turn_s, 5), (turn_g, 2, 0), (first_product, 0, 0), (first_product, 0, 1), (turn_s, 6), (turn_g, 2, 1), (turn_s, 7), (turn_g, 3, 0), (turn_g, 3, 1), (first_product, 0, 2), (first_product, 0, 3), (first_product, 0, 4), (first_product, 0, 5), (first_product, 0, 6), (first_product, 0, 7), (first_product, 1, 0), (first_product, 1, 1), (first_product, 1, 2), (first_product, 1, 3), (first_product, 1, 4), (first_product, 1, 5), (first_product, 1, 6), (first_product, 1, 7), (first_product, 2, 0), (first_product, 2, 1), (first_product, 2, 2), (first_product, 2, 3), (first_product, 2, 4), (first_product, 2, 5), (first_product, 2, 6), (first_product, 2, 7), (first_product, 3, 0), (first_product, 3, 1), (second_product, 0), (first_product, 3, 2), (first_product, 3, 3), (second_product, 1), (first_product, 3, 4), (first_product, 3, 5), (second_product, 2), (first_product, 3, 6), (first_product, 3, 7), (second_product, 3), (second_product, 4), (second_product, 5), (second_product, 6), (second_product, 7), (second_product, 8), (second_product, 9), (second_product, 10), (second_product, 11), (second_product, 12), (second_product, 13), (second_product, 14), (second_product, 15)]
-        scalar_steps = [(widen_s_scalar, 0), (widen_s_scalar, 1), (empty_s, 0), (empty_s, 1), (empty_s, 2), (empty_g, 0, 0), (empty_s, 3), (empty_g, 0, 1), (empty_s, 4), (empty_g, 1, 0), (empty_g, 1, 1), (empty_s, 5), (empty_g, 2, 0), (cast_y, 0, 0), (empty_u, 0, 0), (empty_g, 2, 1), (empty_s, 7), (empty_g, 3, 0), (empty_g, 3, 1), (cast_y, 0, 1), (empty_u, 0, 1), (empty_u, 0, 2), (cast_y, 1, 0), (empty_u, 0, 3), (empty_u, 1, 0), (cast_y, 1, 1), (empty_u, 1, 1), (cast_y, 2, 0), (empty_u, 1, 2), (empty_u, 1, 3), (cast_y, 2, 1), (empty_u, 2, 0), (empty_u, 2, 1), (empty_u, 2, 2), (empty_u, 2, 3), (weave_a, 2, 0), (empty_u, 3, 0), (cast_y, 3, 0), (empty_u, 3, 1), (cast_y, 3, 1), (empty_u, 3, 2), (empty_u, 3, 3), (weave_a, 3, 0), (weave_a, 3, 1), (weave_y, 3, 0), (weave_y, 3, 1)]
-        vector_steps = [(widen_s, 0), (widen_s, 1), (widen_s, 2), (widen_s, 3), (quant_s, 0), (widen_s, 4), (quant_s, 1), (quant_s, 2), (widen_s, 5), (quant_g, 0, 0), (quant_s, 3), (widen_s, 6), (quant_g, 0, 1), (quant_s, 4), (widen_s, 7), (invert_c,), (quant_g, 1, 0), (quant_g, 1, 1), (quant_s, 5), (empty_s, 6), (quant_g, 2, 0), (weave_y, 0, 0), (quant_s, 6), (quant_g, 2, 1), (quant_s, 7), (quant_g, 3, 0), (quant_g, 3, 1), (weave_y, 0, 1), (weave_a, 0, 0), (quant_y, 0), (weave_y, 1, 0), (weave_a, 0, 1), (weave_y, 1, 1), (quant_a, 0), (quant_y, 1), (weave_a, 1, 0), (weave_y, 2, 0), (weave_a, 1, 1), (weave_y, 2, 1), (quant_a, 1), (finish, 0), (weave_a, 2, 1), (finish, 1), (quant_y, 2), (finish, 2), (quant_a, 2), (finish, 3), (finish, 4), (finish, 5), (quant_a, 3), (finish, 6), (finish, 7), (finish, 8), (finish, 9), (quant_y, 3), (finish, 10), (finish, 11), (finish, 12), (finish, 13), (finish, 14), (finish, 15)]
+        sync_steps = [(load_s_factor, 0), (load_s, 0), (load_s, 1), (load_s, 2), (load_s, 3), (load_g, 0, 0), (load_s_factor, 1), (load_s, 4), (load_g, 0, 1), (load_c,), (load_s, 5), (load_g, 1, 0), (load_s, 6), (load_g, 1, 1), (load_s, 7), (load_g, 2, 0), (load_y_factor, 0), (load_y, 0, 0), (load_g, 3, 0), (load_g, 2, 1), (load_g, 3, 1), (load_y_factor, 1), (load_y, 0, 1), (load_y, 1, 0), (load_y, 1, 1), (load_y, 2, 0), (load_y, 2, 1), (load_h,), (load_y, 3, 0), (load_y, 3, 1), (store, 0), (store, 1), (store, 2), (store, 3), (store, 4), (store, 5), (store, 6), (store, 7), (store, 8), (store, 9), (store, 10), (store, 11), (store, 12), (store, 13), (store, 14)]
+        tensor_steps = [(warm_up, 0), (warm_up, 1), (warm_up, 2), (warm_up, 3), (turn_s, 0), (turn_s, 1), (turn_g, 0, 0), (warm_up, 4), (turn_s, 2), (turn_g, 0, 1), (turn_s, 3), (turn_g, 1, 0), (turn_s, 4), (first_product, 0, 0), (first_product, 0, 1), (turn_g, 1, 1), (turn_s, 5), (first_product, 0, 2), (first_product, 0, 3), (turn_g, 2, 0), (turn_s, 6), (first_product, 1, 0), (first_product, 1, 1), (turn_g, 2, 1), (turn_s, 7), (first_product, 1, 2), (first_product, 1, 3), (turn_g, 3, 0), (turn_g, 3, 1), (first_product, 0, 4), (first_product, 0, 5), (first_product, 0, 6), (first_product, 0, 7), (first_product, 1, 4), (first_product, 1, 5), (first_product, 1, 6), (first_product, 1, 7), (first_product, 2, 0), (first_product, 2, 1), (first_product, 2, 2), (first_product, 2, 3), (first_product, 2, 4), (first_product, 2, 5), (first_product, 2, 6), (first_product, 2, 7), (first_product, 3, 0), (first_product, 3, 1), (first_product, 3, 2), (first_product, 3, 3), (second_product, 0), (first_product, 3, 4), (first_product, 3, 5), (second_product, 1), (first_product, 3, 6), (first_product, 3, 7), (second_product, 2), (second_product, 3), (second_product, 4), (second_product, 5), (second_product, 6), (second_product, 7), (second_product, 8), (second_product, 9), (second_product, 10), (second_product, 11), (second_product, 12), (second_product, 13), (second_product, 14), (second_product, 15)]
+        scalar_steps = [(widen_s_scalar, 0), (widen_s_scalar, 1), (empty_s, 0), (empty_s, 1), (empty_g, 0, 0), (empty_s, 2), (empty_g, 0, 1), (empty_s, 3), (empty_g, 1, 0), (empty_s, 4), (empty_u, 0, 0), (empty_g, 1, 1), (empty_s, 5), (empty_u, 0, 1), (cast_y, 0, 0), (empty_g, 2, 0), (empty_s, 6), (empty_u, 1, 0), (empty_g, 2, 1), (cast_y, 0, 1), (cast_y, 1, 0), (empty_g, 3, 0), (empty_g, 3, 1), (cast_y, 1, 1), (empty_u, 0, 2), (empty_u, 0, 3), (cast_y, 2, 0), (empty_u, 1, 2), (cast_y, 2, 1), (weave_a, 0, 1), (empty_u, 1, 3), (weave_a, 1, 0), (empty_u, 2, 0), (empty_u, 2, 1), (empty_u, 2, 2), (empty_u, 2, 3), (empty_u, 3, 0), (empty_u, 3, 1), (empty_u, 3, 2), (weave_a, 2, 1), (cast_y, 3, 0), (weave_a, 3, 0), (empty_u, 3, 3), (weave_a, 3, 1), (cast_y, 3, 1), (weave_y, 3, 0), (weave_y, 3, 1)]
+        vector_steps = [(widen_s, 0), (widen_s, 1), (widen_s, 2), (widen_s, 3), (quant_s, 0), (widen_s, 4), (quant_s, 1), (quant_g, 0, 0), (widen_s, 5), (quant_s, 2), (quant_g, 0, 1), (widen_s, 6), (invert_c,), (quant_s, 3), (quant_g, 1, 0), (widen_s, 7), (quant_s, 4), (quant_g, 1, 1), (sort_g, 3, 0), (sort_g, 3, 1), (quant_s, 5), (weave_a, 0, 0), (weave_y, 0, 0), (quant_g, 2, 0), (quant_s, 6), (empty_s, 7), (empty_u, 1, 1), (quant_g, 2, 1), (quant_s, 7), (weave_y, 0, 1), (weave_y, 1, 0), (quant_g, 3, 0), (quant_y, 0), (quant_g, 3, 1), (weave_y, 1, 1), (weave_y, 2, 0), (quant_y, 1), (quant_a, 0), (weave_a, 1, 1), (weave_y, 2, 1), (quant_a, 1), (weave_a, 2, 0), (finish, 0), (quant_y, 2), (finish, 1), (quant_a, 2), (finish, 2), (finish, 3), (finish, 4), (quant_a, 3), (finish, 5), (finish, 6), (finish, 7), (finish, 8), (finish, 9), (quant_y, 3), (finish, 10), (finish, 11), (finish, 12), (finish, 13), (finish, 14), (finish, 15)]
         gpsimd_steps = []
 
         def bank_keys(job, a=0, b=0):
@@ -353,20 +374,22 @@ def tile_curvature_scaled_pair_correction_d7_kernel(tc, G, S_bytes, S_scale, Y_b
                 return [("s_bank", a, 0), ("s_bank", a, 1)]
             if job in (turn_g, empty_g):
                 return [("g_bank", a, 2 * b), ("g_bank", a, 2 * b + 1)]
-            if job in (second_product, finish):
+            if job in (second_product, finish, drain):
                 return [("p_bank", *tile) for tile in out_tiles(a)]
+            if job is warm_up:
+                return [("idle", a)]
             if job is first_product and b % 2 == 0:
                 return [("u_bank", a, b // 2)]
             return [("u_bank", a, b)] if job is empty_u else []
 
         keys = [key for step in tensor_steps for key in bank_keys(*step)]
-        bank_of = {key: k % BANKS for k, key in enumerate(keys)}
+        bank_of = {key: len([other for other in keys[:k] if other[0] != "idle"]) % BANKS for k, key in enumerate(keys)}
 
         def inputs(job, a=0, b=0):
             table = {
-                widen_s: [(load_s, a), (load_s_factor, a // PACK)],
+                widen_s: [(load_s, a), (load_s_factor, a // PACK)] + [(widen_s_scalar, a)] * (a in SHARED),
                 widen_s_scalar: [(load_s, a), (load_s_factor, a // PACK)],
-                turn_s: [(widen_s, a)] + [(widen_s_scalar, a)] * (a < SCALAR_SLICES),
+                turn_s: [(widen_s, a)] + [(widen_s_scalar, a)] * (a in SHARED),
                 empty_s: [(turn_s, a)],
                 quant_s: [(empty_s, a)],
                 sort_g: [(load_g, a, b)],
@@ -382,6 +405,9 @@ def tile_curvature_scaled_pair_correction_d7_kernel(tc, G, S_bytes, S_scale, Y_b
                 weave_y: [(cast_y, a, b), (load_y_factor, b)] + [(weave_y, a, 0)] * b,
                 quant_y: [(weave_y, a, 0), (weave_y, a, 1)],
                 finish: [(second_product, a), (load_h,)],
+                drain: [(second_product, a)],
+                scale: [(drain, a), (load_h,)],
+                store: [(finish, a) if (finish, a) in vector_steps else (scale, a)],
             }
             if job is second_product:
                 return [need for row_tile, strip in out_tiles(a) for need in ((quant_a, row_tile // 2), (quant_y, strip))]
@@ -394,7 +420,7 @@ def tile_curvature_scaled_pair_correction_d7_kernel(tc, G, S_bytes, S_scale, Y_b
             a_planes, y_planes = [("a_planes", (a, b))], [("y_wide", (a, b))]
             a_woven, y_woven = [("a_woven", a)], [("y_woven", a)]
             table = {
-                widen_s: (wide * (a >= SCALAR_SLICES), []),
+                widen_s: (wide * (a not in SHARED), []),
                 widen_s_scalar: (wide, []),
                 turn_s: (banks, wide),
                 load_g: (rows, []),
@@ -404,6 +430,7 @@ def tile_curvature_scaled_pair_correction_d7_kernel(tc, G, S_bytes, S_scale, Y_b
                 empty_g: (turned, banks),
                 quant_s: ([], turned),
                 quant_g: ([], turned),
+                warm_up: (banks, banks),
                 first_product: (banks, []),
                 empty_u: ([("a_planes", (a, b // 2))] * (b % 2 == 0), banks),
                 cast_y: (y_planes, []),
@@ -412,7 +439,9 @@ def tile_curvature_scaled_pair_correction_d7_kernel(tc, G, S_bytes, S_scale, Y_b
                 quant_a: ([], a_woven),
                 quant_y: ([], y_woven),
                 second_product: (banks, []),
-                finish: ([], banks),
+                finish: ([("rows", a)], banks),
+                drain: ([("rows", a)], banks),
+                store: ([], [("rows", a)]),
             }
             return table.get(job, ([], []))
 

@@ -37,7 +37,7 @@ SHARED = (0, 1)
 WIDE_BUFS = 6
 TURNED_BUFS = 4
 A_PLANE_BUFS = 5
-WOVEN_A_BUFS = 2
+WOVEN_A_BUFS = 3
 WIDE_Y_BUFS = 4
 WOVEN_Y_BUFS = 2
 ROW_BUFS = 2 * CHUNKS
@@ -363,10 +363,10 @@ def tile_curvature_scaled_pair_correction_d7_kernel(tc, G, S_bytes, S_scale, Y_b
             nc.sync.dma_start(out=out_rows(k), in_=result(k)[:])
 
         out_steps = [(r, 0, True) for r in range(4)] + [(0, 2, False), (2, 2, False), (4, 0, True), (5, 0, True), (4, 2, False), (6, 0, True), (7, 0, True), (6, 2, False)] + [(r, 3, False) for r in (0, 2, 4, 6)]
-        sync_steps = [(load_s_factor, 0), (load_s, 0), (load_s, 1), (load_s, 2), (load_s, 3), (load_g, 0, 0), (load_s_factor, 1), (load_s, 4), (load_g, 0, 1), (load_c,), (load_s, 5), (load_g, 1, 0), (load_s, 6), (load_g, 1, 1), (load_s, 7), (load_g, 2, 0), (load_y_factor, 0), (load_y, 0, 0), (load_g, 3, 0), (load_g, 2, 1), (load_g, 3, 1), (load_y_factor, 1), (load_y, 0, 1), (load_y, 1, 0), (load_y, 1, 1), (load_y, 2, 0), (load_y, 2, 1), (load_h,), (load_y, 3, 0), (load_y, 3, 1), (store, 0), (store, 1), (store, 2), (store, 3), (store, 4), (store, 5), (store, 6), (store, 7), (store, 8), (store, 9), (store, 10), (store, 11), (store, 12), (store, 13), (store, 14)]
-        tensor_steps = [(warm_up, 0), (warm_up, 1), (warm_up, 2), (warm_up, 3), (turn_s, 0), (turn_s, 1), (turn_g, 0, 0), (warm_up, 4), (turn_s, 2), (turn_g, 0, 1), (turn_s, 3), (turn_g, 1, 0), (turn_s, 4), (first_product, 0, 0), (first_product, 0, 1), (turn_g, 1, 1), (turn_s, 5), (first_product, 0, 2), (first_product, 0, 3), (turn_g, 2, 0), (turn_s, 6), (first_product, 1, 0), (first_product, 1, 1), (turn_g, 2, 1), (turn_s, 7), (first_product, 1, 2), (first_product, 1, 3), (turn_g, 3, 0), (turn_g, 3, 1), (first_product, 0, 4), (first_product, 0, 5), (first_product, 0, 6), (first_product, 0, 7), (first_product, 1, 4), (first_product, 1, 5), (first_product, 1, 6), (first_product, 1, 7), (first_product, 2, 0), (first_product, 2, 1), (first_product, 2, 2), (first_product, 2, 3), (first_product, 2, 4), (first_product, 2, 5), (first_product, 2, 6), (first_product, 2, 7), (first_product, 3, 0), (first_product, 3, 1), (first_product, 3, 2), (first_product, 3, 3), (second_product, 0), (first_product, 3, 4), (first_product, 3, 5), (second_product, 1), (first_product, 3, 6), (first_product, 3, 7), (second_product, 2), (second_product, 3), (second_product, 4), (second_product, 5), (second_product, 6), (second_product, 7), (second_product, 8), (second_product, 9), (second_product, 10), (second_product, 11), (second_product, 12), (second_product, 13), (second_product, 14), (second_product, 15)]
-        scalar_steps = [(widen_s_scalar, 0), (widen_s_scalar, 1), (empty_s, 0), (empty_s, 1), (empty_g, 0, 0), (empty_s, 2), (empty_g, 0, 1), (empty_s, 3), (empty_g, 1, 0), (empty_s, 4), (empty_u, 0, 0), (empty_g, 1, 1), (empty_s, 5), (empty_u, 0, 1), (cast_y, 0, 0), (empty_g, 2, 0), (empty_s, 6), (empty_u, 1, 0), (empty_g, 2, 1), (cast_y, 0, 1), (cast_y, 1, 0), (empty_g, 3, 0), (empty_g, 3, 1), (cast_y, 1, 1), (empty_u, 0, 2), (empty_u, 0, 3), (cast_y, 2, 0), (empty_u, 1, 2), (cast_y, 2, 1), (weave_a, 0, 1), (empty_u, 1, 3), (weave_a, 1, 0), (empty_u, 2, 0), (empty_u, 2, 1), (empty_u, 2, 2), (empty_u, 2, 3), (empty_u, 3, 0), (empty_u, 3, 1), (empty_u, 3, 2), (weave_a, 2, 1), (cast_y, 3, 0), (weave_a, 3, 0), (empty_u, 3, 3), (weave_a, 3, 1), (cast_y, 3, 1), (weave_y, 3, 0), (weave_y, 3, 1)]
-        vector_steps = [(widen_s, 0), (widen_s, 1), (widen_s, 2), (widen_s, 3), (quant_s, 0), (widen_s, 4), (quant_s, 1), (quant_g, 0, 0), (widen_s, 5), (quant_s, 2), (quant_g, 0, 1), (widen_s, 6), (invert_c,), (quant_s, 3), (quant_g, 1, 0), (widen_s, 7), (quant_s, 4), (quant_g, 1, 1), (sort_g, 3, 0), (sort_g, 3, 1), (quant_s, 5), (weave_a, 0, 0), (weave_y, 0, 0), (quant_g, 2, 0), (quant_s, 6), (empty_s, 7), (empty_u, 1, 1), (quant_g, 2, 1), (quant_s, 7), (weave_y, 0, 1), (weave_y, 1, 0), (quant_g, 3, 0), (quant_y, 0), (quant_g, 3, 1), (weave_y, 1, 1), (weave_y, 2, 0), (quant_y, 1), (quant_a, 0), (weave_a, 1, 1), (weave_y, 2, 1), (quant_a, 1), (weave_a, 2, 0), (finish, 0), (quant_y, 2), (finish, 1), (quant_a, 2), (finish, 2), (finish, 3), (finish, 4), (quant_a, 3), (finish, 5), (finish, 6), (finish, 7), (finish, 8), (finish, 9), (quant_y, 3), (finish, 10), (finish, 11), (finish, 12), (finish, 13), (finish, 14), (finish, 15)]
+        sync_steps = [(load_s_factor, 0), (load_s, 0), (load_s, 1), (load_s, 2), (load_s, 3), (load_g, 0, 0), (load_s_factor, 1), (load_s, 4), (load_g, 0, 1), (load_s, 5), (load_g, 1, 0), (load_c,), (load_y_factor, 0), (load_y, 0, 0), (load_g, 1, 1), (load_s, 6), (load_g, 2, 0), (load_g, 2, 1), (load_g, 3, 0), (load_g, 3, 1), (load_s, 7), (load_y_factor, 1), (load_y, 0, 1), (load_y, 1, 0), (load_y, 1, 1), (load_y, 2, 0), (load_y, 2, 1), (load_h,), (load_y, 3, 0), (load_y, 3, 1), (store, 0), (store, 1), (store, 2), (store, 3), (store, 4), (store, 5), (store, 6), (store, 7), (store, 8), (store, 9), (store, 10), (store, 11), (store, 12), (store, 13), (store, 14)]
+        tensor_steps = [(turn_s, 0), (turn_s, 1), (turn_g, 0, 0), (turn_s, 2), (turn_g, 0, 1), (turn_s, 3), (turn_g, 1, 0), (turn_s, 4), (turn_g, 1, 1), (turn_s, 5), (first_product, 0, 0), (turn_g, 2, 0), (first_product, 0, 1), (turn_g, 2, 1), (turn_g, 3, 0), (turn_g, 3, 1), (turn_s, 6), (turn_s, 7), (first_product, 0, 2), (first_product, 0, 3), (first_product, 1, 0), (first_product, 1, 1), (first_product, 1, 2), (first_product, 1, 3), (first_product, 0, 4), (first_product, 0, 5), (first_product, 1, 4), (first_product, 1, 5), (first_product, 0, 6), (first_product, 0, 7), (first_product, 1, 6), (first_product, 1, 7), (first_product, 2, 0), (first_product, 2, 1), (first_product, 2, 2), (first_product, 2, 3), (first_product, 2, 4), (first_product, 2, 5), (first_product, 2, 6), (first_product, 2, 7), (first_product, 3, 0), (first_product, 3, 1), (first_product, 3, 2), (first_product, 3, 3), (second_product, 0), (first_product, 3, 4), (first_product, 3, 5), (second_product, 1), (first_product, 3, 6), (first_product, 3, 7), (second_product, 2), (second_product, 3), (second_product, 4), (second_product, 5), (second_product, 6), (second_product, 7), (second_product, 8), (second_product, 9), (second_product, 10), (second_product, 11), (second_product, 12), (second_product, 13), (second_product, 14), (second_product, 15)]
+        scalar_steps = [(widen_s_scalar, 0), (widen_s_scalar, 1), (empty_s, 0), (empty_s, 1), (empty_g, 0, 0), (empty_s, 2), (empty_g, 0, 1), (empty_s, 3), (empty_g, 1, 0), (cast_y, 0, 0), (empty_s, 4), (empty_g, 1, 1), (empty_s, 5), (empty_g, 2, 0), (empty_g, 2, 1), (empty_g, 3, 0), (empty_g, 3, 1), (empty_s, 6), (cast_y, 0, 1), (cast_y, 1, 0), (cast_y, 1, 1), (cast_y, 2, 0), (empty_u, 1, 0), (empty_u, 1, 1), (empty_u, 0, 2), (cast_y, 2, 1), (empty_u, 1, 2), (empty_u, 0, 3), (empty_u, 1, 3), (weave_a, 0, 1), (empty_u, 2, 0), (empty_u, 2, 1), (weave_a, 1, 1), (empty_u, 2, 2), (empty_u, 2, 3), (weave_a, 2, 0), (empty_u, 3, 0), (weave_a, 2, 1), (empty_u, 3, 1), (empty_u, 3, 2), (weave_a, 3, 0), (empty_u, 3, 3), (cast_y, 3, 0), (weave_a, 3, 1), (cast_y, 3, 1), (weave_y, 3, 0), (weave_y, 3, 1)]
+        vector_steps = [(widen_s, 0), (widen_s, 1), (widen_s, 2), (widen_s, 3), (quant_s, 0), (widen_s, 4), (quant_s, 1), (quant_g, 0, 0), (widen_s, 5), (quant_s, 2), (quant_g, 0, 1), (widen_s, 6), (invert_c,), (quant_s, 3), (quant_g, 1, 0), (sort_g, 2, 1), (quant_s, 4), (sort_g, 3, 0), (quant_g, 1, 1), (sort_g, 3, 1), (empty_u, 0, 0), (widen_s, 7), (quant_s, 5), (quant_g, 2, 0), (weave_y, 0, 0), (quant_g, 2, 1), (empty_s, 7), (quant_g, 3, 0), (quant_s, 6), (quant_s, 7), (empty_u, 0, 1), (weave_y, 0, 1), (weave_y, 1, 0), (quant_g, 3, 1), (weave_y, 1, 1), (quant_y, 0), (weave_a, 0, 0), (quant_y, 1), (weave_a, 1, 0), (quant_a, 0), (weave_y, 2, 0), (quant_a, 1), (weave_y, 2, 1), (finish, 0), (quant_y, 2), (finish, 1), (quant_a, 2), (finish, 2), (finish, 3), (finish, 4), (quant_a, 3), (finish, 5), (finish, 6), (finish, 7), (finish, 8), (finish, 9), (quant_y, 3), (finish, 10), (finish, 11), (finish, 12), (finish, 13), (finish, 14), (finish, 15)]
         gpsimd_steps = []
 
         def bank_keys(job, a=0, b=0):
@@ -385,16 +385,19 @@ def tile_curvature_scaled_pair_correction_d7_kernel(tc, G, S_bytes, S_scale, Y_b
         keys = [key for step in tensor_steps for key in bank_keys(*step)]
         bank_of = {key: len([other for other in keys[:k] if other[0] != "idle"]) % BANKS for k, key in enumerate(keys)}
 
+        empties = [({turn_s: empty_s, turn_g: empty_g}[job], *index) for job, *index in tensor_steps if job in (turn_s, turn_g)]
+        after = dict(zip(empties[1:], empties))
+
         def inputs(job, a=0, b=0):
             table = {
                 widen_s: [(load_s, a), (load_s_factor, a // PACK)] + [(widen_s_scalar, a)] * (a in SHARED),
                 widen_s_scalar: [(load_s, a), (load_s_factor, a // PACK)],
                 turn_s: [(widen_s, a)] + [(widen_s_scalar, a)] * (a in SHARED),
-                empty_s: [(turn_s, a)],
+                empty_s: [(turn_s, a), after.get((empty_s, a), (turn_s, a))],
                 quant_s: [(empty_s, a)],
                 sort_g: [(load_g, a, b)],
                 turn_g: [(load_g, a, b)] + [(sort_g, a, b)] * ((sort_g, a, b) in vector_steps),
-                empty_g: [(turn_g, a, b)],
+                empty_g: [(turn_g, a, b), after.get((empty_g, a, b), (turn_g, a, b))],
                 quant_g: [(empty_g, a, b)],
                 first_product: [(quant_s, b), (quant_g, a, 0), (quant_g, a, 1)] + [(first_product, a, b - 1)] * (b % 2),
                 invert_c: [(load_c,)],

@@ -13,7 +13,6 @@ U8 = mybir.dt.uint8
 FP8 = mybir.dt.float8_e4m3fn
 FP8X4 = mybir.dt.float8_e4m3fn_x4
 MULT = mybir.AluOpType.mult
-ADD = mybir.AluOpType.add
 COPY = mybir.ActivationFunctionType.Copy
 
 P = 128
@@ -28,12 +27,18 @@ CHUNK = 256
 CHUNKS = T // CHUNK
 STRIP = 512
 STRIPS = N // STRIP
-MOVING = 512
 RUN = 4
 BANKS = 8
 SPAN = 256
 
 SHARED = (0, 1)
+LEAD = 4
+FIRST_PAIR = 7
+LATE_PAIRS = 2
+CASTS_FROM = 11
+AHEAD = 2
+WARM_UPS = 0
+
 WIDE_BUFS = 6
 TURNED_BUFS = 4
 A_PLANE_BUFS = 5
@@ -203,11 +208,10 @@ def tile_curvature_scaled_pair_correction_d7_kernel(tc, G, S_bytes, S_scale, Y_b
                         nc.tensor.transpose(turned[:, w, i, :], src, ident[:])
 
         def empty_g(chunk, b):
-            copy = nc.vector.tensor_copy if (empty_g, chunk, b) in vector_steps else nc.scalar.copy
             joined = work.tile([P, 2, CHUNK, 2], F32, name="g_turned", tag="turned", bufs=TURNED_BUFS, align_bytes=64)
             tiles["g_turned", chunk, b] = joined
             for i in (1, 0):
-                join_words(copy, joined[:, i], tiles["g_bank", chunk, 2 * b + i])
+                join_words(nc.scalar.copy, joined[:, i], tiles["g_bank", chunk, 2 * b + i])
 
         def quant_g(chunk, b):
             nc.vector.quantize_mx(
@@ -259,9 +263,6 @@ def tile_curvature_scaled_pair_correction_d7_kernel(tc, G, S_bytes, S_scale, Y_b
             if (weave_a, chunk, half) in vector_steps:
                 dst, src = vector_views(woven, planes)
                 nc.vector.tensor_copy(out=dst, in_=src)
-            elif (weave_a, chunk, half) in gpsimd_steps:
-                dst, src = scalar_views(woven, planes)
-                nc.gpsimd.tensor_scalar(out=dst, in0=src, scalar1=1.0, scalar2=0.0, op0=MULT, op1=ADD)
             else:
                 dst, src = scalar_views(woven, planes)
                 nc.scalar.copy(out=dst, in_=src)
@@ -291,9 +292,6 @@ def tile_curvature_scaled_pair_correction_d7_kernel(tc, G, S_bytes, S_scale, Y_b
                 if (weave_y, strip, half) in vector_steps:
                     dst, src = vector_views(woven, planes)
                     nc.vector.tensor_scalar(out=dst, in0=src, scalar1=factor, scalar2=None, op0=MULT)
-                elif (weave_y, strip, half) in gpsimd_steps:
-                    dst, src = scalar_views(woven, planes)
-                    nc.gpsimd.tensor_scalar(out=dst, in0=src, scalar1=factor, scalar2=0.0, op0=MULT, op1=ADD)
                 else:
                     dst, src = scalar_views(woven, planes)
                     nc.scalar.activation(out=dst, in_=src, func=COPY, scale=factor)
@@ -313,43 +311,27 @@ def tile_curvature_scaled_pair_correction_d7_kernel(tc, G, S_bytes, S_scale, Y_b
             for row_tile, strip in out_tiles(k):
                 sums = bank(("p_bank", row_tile, strip), [P, STRIP])
                 chunk, i = divmod(row_tile, CHUNK // P)
-                for part in range(STRIP // MOVING):
-                    cols = slice(MOVING * part, MOVING * (part + 1))
-                    for half in range(HALVES):
-                        nc.tensor.matmul_mx(
-                            out=sums[:, cols],
-                            lhsT=a_codes[:, chunk, half, i * P : (i + 1) * P].bitcast(FP8X4),
-                            lhsT_scale=a_scales[:, chunk, half, i * P : (i + 1) * P],
-                            rhs=y_codes[:, strip, half, cols].bitcast(FP8X4),
-                            rhs_scale=y_scales[:, strip, half, cols],
-                            start=(half == 0),
-                            stop=(half == HALVES - 1),
-                        )
-
-        def result(k):
-            if ("res", k) not in tiles:
-                tiles["res", k] = work.tile([P, 2, STRIP], F32, name="res", tag="rows", bufs=ROW_BUFS)
-            return tiles["res", k]
-
-        def factor_h(k, i):
-            strip = out_tiles(k)[i][1]
-            return h_all[:, STRIP * strip : STRIP * (strip + 1)]
+                for half in range(HALVES):
+                    nc.tensor.matmul_mx(
+                        out=sums[:],
+                        lhsT=a_codes[:, chunk, half, i * P : (i + 1) * P].bitcast(FP8X4),
+                        lhsT_scale=a_scales[:, chunk, half, i * P : (i + 1) * P],
+                        rhs=y_codes[:, strip, half].bitcast(FP8X4),
+                        rhs_scale=y_scales[:, strip, half],
+                        start=(half == 0),
+                        stop=(half == HALVES - 1),
+                    )
 
         def finish(k):
             last = k == len(out_steps) - 1
+            res = work.tile([P, 2, STRIP], F32, name="res", tag="rows", bufs=ROW_BUFS)
+            tiles["res", k] = res
             for i in (0, 1) if last else (1, 0):
-                sums = tiles[("p_bank", *out_tiles(k)[i])][:]
-                nc.vector.tensor_tensor(out=result(k)[:, i, :], in0=sums, in1=factor_h(k, i), op=MULT)
+                row_tile, strip = out_tiles(k)[i]
+                factor = h_all[:, STRIP * strip : STRIP * (strip + 1)]
+                nc.vector.tensor_tensor(out=res[:, i, :], in0=tiles["p_bank", row_tile, strip][:], in1=factor, op=MULT)
                 if last:
-                    nc.sync.dma_start(out=out_rows(k)[:, i, :], in_=result(k)[:, i, :])
-
-        def drain(k):
-            for i in (1, 0):
-                nc.scalar.copy(out=result(k)[:, i, :], in_=tiles[("p_bank", *out_tiles(k)[i])][:])
-
-        def scale(k):
-            for i in (1, 0):
-                nc.gpsimd.tensor_tensor(out=result(k)[:, i, :], in0=result(k)[:, i, :], in1=factor_h(k, i), op=MULT)
+                    nc.sync.dma_start(out=out_rows(k)[:, i, :], in_=res[:, i, :])
 
         def out_rows(k):
             row_tile, strip, along_row = out_steps[k]
@@ -360,21 +342,107 @@ def tile_curvature_scaled_pair_correction_d7_kernel(tc, G, S_bytes, S_scale, Y_b
             return rows.rearrange("(i r) n -> r i n", i=2)
 
         def store(k):
-            nc.sync.dma_start(out=out_rows(k), in_=result(k)[:])
+            nc.sync.dma_start(out=out_rows(k), in_=tiles["res", k][:])
 
-        out_steps = [(r, 0, True) for r in range(4)] + [(0, 2, False), (2, 2, False), (4, 0, True), (5, 0, True), (4, 2, False), (6, 0, True), (7, 0, True), (6, 2, False)] + [(r, 3, False) for r in (0, 2, 4, 6)]
-        sync_steps = [(load_s_factor, 0), (load_s, 0), (load_s, 1), (load_s, 2), (load_s, 3), (load_g, 0, 0), (load_s_factor, 1), (load_s, 4), (load_g, 0, 1), (load_s, 5), (load_g, 1, 0), (load_c,), (load_y_factor, 0), (load_y, 0, 0), (load_g, 1, 1), (load_s, 6), (load_g, 2, 0), (load_g, 2, 1), (load_g, 3, 0), (load_g, 3, 1), (load_s, 7), (load_y_factor, 1), (load_y, 0, 1), (load_y, 1, 0), (load_y, 1, 1), (load_y, 2, 0), (load_y, 2, 1), (load_h,), (load_y, 3, 0), (load_y, 3, 1), (store, 0), (store, 1), (store, 2), (store, 3), (store, 4), (store, 5), (store, 6), (store, 7), (store, 8), (store, 9), (store, 10), (store, 11), (store, 12), (store, 13), (store, 14)]
-        tensor_steps = [(turn_s, 0), (turn_s, 1), (turn_g, 0, 0), (turn_s, 2), (turn_g, 0, 1), (turn_s, 3), (turn_g, 1, 0), (turn_s, 4), (turn_g, 1, 1), (turn_s, 5), (first_product, 0, 0), (turn_g, 2, 0), (first_product, 0, 1), (turn_g, 2, 1), (turn_g, 3, 0), (turn_g, 3, 1), (turn_s, 6), (turn_s, 7), (first_product, 0, 2), (first_product, 0, 3), (first_product, 1, 0), (first_product, 1, 1), (first_product, 1, 2), (first_product, 1, 3), (first_product, 0, 4), (first_product, 0, 5), (first_product, 1, 4), (first_product, 1, 5), (first_product, 0, 6), (first_product, 0, 7), (first_product, 1, 6), (first_product, 1, 7), (first_product, 2, 0), (first_product, 2, 1), (first_product, 2, 2), (first_product, 2, 3), (first_product, 2, 4), (first_product, 2, 5), (first_product, 2, 6), (first_product, 2, 7), (first_product, 3, 0), (first_product, 3, 1), (first_product, 3, 2), (first_product, 3, 3), (second_product, 0), (first_product, 3, 4), (first_product, 3, 5), (second_product, 1), (first_product, 3, 6), (first_product, 3, 7), (second_product, 2), (second_product, 3), (second_product, 4), (second_product, 5), (second_product, 6), (second_product, 7), (second_product, 8), (second_product, 9), (second_product, 10), (second_product, 11), (second_product, 12), (second_product, 13), (second_product, 14), (second_product, 15)]
-        scalar_steps = [(widen_s_scalar, 0), (widen_s_scalar, 1), (empty_s, 0), (empty_s, 1), (empty_g, 0, 0), (empty_s, 2), (empty_g, 0, 1), (empty_s, 3), (empty_g, 1, 0), (cast_y, 0, 0), (empty_s, 4), (empty_g, 1, 1), (empty_s, 5), (empty_g, 2, 0), (empty_g, 2, 1), (empty_g, 3, 0), (empty_g, 3, 1), (empty_s, 6), (cast_y, 0, 1), (cast_y, 1, 0), (cast_y, 1, 1), (cast_y, 2, 0), (empty_u, 1, 0), (empty_u, 1, 1), (empty_u, 0, 2), (cast_y, 2, 1), (empty_u, 1, 2), (empty_u, 0, 3), (empty_u, 1, 3), (weave_a, 0, 1), (empty_u, 2, 0), (empty_u, 2, 1), (weave_a, 1, 1), (empty_u, 2, 2), (empty_u, 2, 3), (weave_a, 2, 0), (empty_u, 3, 0), (weave_a, 2, 1), (empty_u, 3, 1), (empty_u, 3, 2), (weave_a, 3, 0), (empty_u, 3, 3), (cast_y, 3, 0), (weave_a, 3, 1), (cast_y, 3, 1), (weave_y, 3, 0), (weave_y, 3, 1)]
-        vector_steps = [(widen_s, 0), (widen_s, 1), (widen_s, 2), (widen_s, 3), (quant_s, 0), (widen_s, 4), (quant_s, 1), (quant_g, 0, 0), (widen_s, 5), (quant_s, 2), (quant_g, 0, 1), (widen_s, 6), (invert_c,), (quant_s, 3), (quant_g, 1, 0), (sort_g, 2, 1), (quant_s, 4), (sort_g, 3, 0), (quant_g, 1, 1), (sort_g, 3, 1), (empty_u, 0, 0), (widen_s, 7), (quant_s, 5), (quant_g, 2, 0), (weave_y, 0, 0), (quant_g, 2, 1), (empty_s, 7), (quant_g, 3, 0), (quant_s, 6), (quant_s, 7), (empty_u, 0, 1), (weave_y, 0, 1), (weave_y, 1, 0), (quant_g, 3, 1), (weave_y, 1, 1), (quant_y, 0), (weave_a, 0, 0), (quant_y, 1), (weave_a, 1, 0), (quant_a, 0), (weave_y, 2, 0), (quant_a, 1), (weave_y, 2, 1), (finish, 0), (quant_y, 2), (finish, 1), (quant_a, 2), (finish, 2), (finish, 3), (finish, 4), (quant_a, 3), (finish, 5), (finish, 6), (finish, 7), (finish, 8), (finish, 9), (quant_y, 3), (finish, 10), (finish, 11), (finish, 12), (finish, 13), (finish, 14), (finish, 15)]
-        gpsimd_steps = []
+        g_parts = [(chunk, b) for chunk in range(CHUNKS) for b in range(2)]
+        units = [(turn_s, 0), (turn_s, 1)]
+        for k, part in enumerate(g_parts):
+            units.extend([(turn_g, *part)] + [(turn_s, u) for u in range(SLICES) if u == k + 2])
+        emptying = {turn_s: empty_s, turn_g: empty_g}
+        quantising = {turn_s: quant_s, turn_g: quant_g}
+        last_slice, last_chunk, last_strip = SLICES - 1, CHUNKS - 1, STRIPS - 1
+
+        pairs = [(chunk, b) for chunk in range(2) for b in (0, 1)] + [(chunk, b) for b in (2, 3) for chunk in range(2)]
+        pairs.extend([(chunk, b) for chunk in range(2, CHUNKS) for b in range(SLICES // 2)])
+
+        out_steps = []
+        for group in ((0, 1), (2,), (3,)):
+            out_steps.extend([(2 * chunk + i, 0, True) for chunk in group for i in range(2)])
+            out_steps.extend([(2 * chunk, 2, False) for chunk in group])
+        out_steps.extend([(2 * chunk, last_strip, False) for chunk in range(CHUNKS)])
+
+        def products(pair):
+            return [(first_product, pair[0], 2 * pair[1] + i) for i in range(2)]
+
+        warm_ups = [(warm_up, k) for k in range(WARM_UPS)]
+        tensor_steps = warm_ups[:-1] + units[:1] + warm_ups[-1:]
+        waiting = list(pairs)
+        for i in range(1, len(units)):
+            tensor_steps.append(units[i])
+            if FIRST_PAIR <= i < len(units) - 1 and (i - FIRST_PAIR) % 2 == 0:
+                tensor_steps.extend(products(waiting.pop(0)))
+        while len(waiting) > LATE_PAIRS:
+            tensor_steps.extend(products(waiting.pop(0)))
+        for k in range(len(out_steps)):
+            tensor_steps.append((second_product, k))
+            if waiting and k % 2 == 1:
+                tensor_steps.extend(products(waiting.pop(0)))
+
+        parts = [(strip, half) for strip in range(STRIPS) for half in range(HALVES)]
+        taken = [(empty_u, 1, 0), (empty_u, 1, 1)]
+        filled = []
+        for job, *index in tensor_steps:
+            if job in emptying:
+                filled.append((emptying[job], *index))
+            elif job is first_product and index[1] % 2 == 1:
+                filled.append((empty_u, index[0], index[1] // 2))
+        filled = [step for step in filled if step not in taken + [(empty_s, last_slice)]]
+        scalar_steps = [(widen_s_scalar, u) for u in SHARED]
+        uncast = list(parts)
+        whole = []
+        for i, (job, *index) in enumerate(filled):
+            scalar_steps.append((job, *index))
+            late = i >= len(filled) - LATE_PAIRS
+            if late or (i >= CASTS_FROM and (i - CASTS_FROM) % 2 == 0 and len(uncast) > HALVES):
+                scalar_steps.append((cast_y, *uncast.pop(0)))
+            scalar_steps.extend(whole)
+            mine = job is empty_u and (index[1] == 3 or index == [last_chunk, 1])
+            whole = [(weave_a, index[0], index[1] // 2)] if mine else []
+        scalar_steps.extend(whole + [(weave_y, last_strip, half) for half in range(HALVES)])
+
+        long_jobs = [[(widen_s, u)] for u in range(LEAD, SLICES)]
+        long_jobs[-2].append((invert_c,))
+        long_jobs.append([(sort_g, last_chunk, b) for b in range(2)])
+        long_jobs.extend([[(weave_y, *part)] for part in parts[:3]])
+        short_jobs = [(weave_a, 0, 0), *taken, (weave_a, 1, 0)]
+        vector_steps = [(widen_s, u) for u in range(LEAD)]
+        for i, (job, *index) in enumerate(units):
+            quant = [(quantising[job], *index)]
+            if units[i + 1 : i + 2] == [(turn_s, last_slice)]:
+                vector_steps.append((empty_s, last_slice))
+            if i % 2 == 0:
+                beside = long_jobs.pop(0)
+                vector_steps.extend(beside + quant if beside[0][0] is weave_y else quant + beside)
+            else:
+                vector_steps.extend(quant + [short_jobs.pop(0) for k in range(i >= len(units) - 2 * len(short_jobs))])
+        vector_steps.extend([(quant_y, 0), (weave_y, 1, 1), (weave_y, 2, 0), (quant_y, 1), (quant_a, 0)])
+        vector_steps.extend([(weave_y, 2, 1), (quant_a, 1), (weave_a, 2, 0)])
+        ahead = [[] for k in out_steps]
+        for index in (2, 3):
+            ahead[min(k for k, step in enumerate(out_steps) if step[1] == index) - AHEAD].append((quant_y, index))
+            ahead[min(k for k, step in enumerate(out_steps) if step[0] == 2 * index) - AHEAD].append((quant_a, index))
+        for k in range(len(out_steps)):
+            vector_steps.extend(ahead[k] + [(finish, k)])
+
+        sync_steps = [(load_s_factor, 0)] + [(load_s, u) for u in range(LEAD)]
+        for k, part in enumerate(g_parts):
+            if k == len(g_parts) - 3:
+                sync_steps.extend([(load_y_factor, 0), (load_y, 0, 0)])
+            sync_steps.append((load_g, *part))
+            if k == 0:
+                sync_steps.extend([(load_s_factor, 1), (load_c,)])
+            sync_steps.extend([(load_s, u) for u in range(SLICES) if u == LEAD + k])
+        sync_steps.append((load_y_factor, 1))
+        sync_steps.extend([(load_y, *part) for part in parts[1:-HALVES]] + [(load_h,)])
+        sync_steps.extend([(load_y, *part) for part in parts[-HALVES:]])
+        sync_steps.extend([(store, k) for k in range(len(out_steps) - 1)])
 
         def bank_keys(job, a=0, b=0):
             if job in (turn_s, empty_s):
                 return [("s_bank", a, 0), ("s_bank", a, 1)]
             if job in (turn_g, empty_g):
                 return [("g_bank", a, 2 * b), ("g_bank", a, 2 * b + 1)]
-            if job in (second_product, finish, drain):
+            if job in (second_product, finish):
                 return [("p_bank", *tile) for tile in out_tiles(a)]
             if job is warm_up:
                 return [("idle", a)]
@@ -385,7 +453,7 @@ def tile_curvature_scaled_pair_correction_d7_kernel(tc, G, S_bytes, S_scale, Y_b
         keys = [key for step in tensor_steps for key in bank_keys(*step)]
         bank_of = {key: len([other for other in keys[:k] if other[0] != "idle"]) % BANKS for k, key in enumerate(keys)}
 
-        empties = [({turn_s: empty_s, turn_g: empty_g}[job], *index) for job, *index in tensor_steps if job in (turn_s, turn_g)]
+        empties = [(emptying[job], *index) for job, *index in units]
         after = dict(zip(empties[1:], empties))
 
         def inputs(job, a=0, b=0):
@@ -408,9 +476,7 @@ def tile_curvature_scaled_pair_correction_d7_kernel(tc, G, S_bytes, S_scale, Y_b
                 weave_y: [(cast_y, a, b), (load_y_factor, b)] + [(weave_y, a, 0)] * b,
                 quant_y: [(weave_y, a, 0), (weave_y, a, 1)],
                 finish: [(second_product, a), (load_h,)],
-                drain: [(second_product, a)],
-                scale: [(drain, a), (load_h,)],
-                store: [(finish, a) if (finish, a) in vector_steps else (scale, a)],
+                store: [(finish, a)],
             }
             if job is second_product:
                 return [need for row_tile, strip in out_tiles(a) for need in ((quant_a, row_tile // 2), (quant_y, strip))]
@@ -443,7 +509,6 @@ def tile_curvature_scaled_pair_correction_d7_kernel(tc, G, S_bytes, S_scale, Y_b
                 quant_y: ([], y_woven),
                 second_product: (banks, []),
                 finish: ([("rows", a)], banks),
-                drain: ([("rows", a)], banks),
                 store: ([], [("rows", a)]),
             }
             return table.get(job, ([], []))
@@ -451,7 +516,7 @@ def tile_curvature_scaled_pair_correction_d7_kernel(tc, G, S_bytes, S_scale, Y_b
         depth = {"wide": WIDE_BUFS, "turned": TURNED_BUFS, "a_planes": A_PLANE_BUFS, "a_woven": WOVEN_A_BUFS}
         depth = {**depth, "y_wide": WIDE_Y_BUFS, "y_woven": WOVEN_Y_BUFS, "rows": ROW_BUFS}
         owners = {kind: [] for kind in [*depth, *range(BANKS)]}
-        queues = [sync_steps, scalar_steps, vector_steps, gpsimd_steps, tensor_steps]
+        queues = [sync_steps, scalar_steps, vector_steps, tensor_steps]
         written = set()
         given = set()
         for sweep in range(sum(len(queue) for queue in queues)):
@@ -466,4 +531,4 @@ def tile_curvature_scaled_pair_correction_d7_kernel(tc, G, S_bytes, S_scale, Y_b
                         given.update(gives)
                         for buffer in takes:
                             owners[buffer[0]].append(buffer)
-        assert len(written) == sum(len(queue) for queue in queues), [[(s[0], s[1:]) for s in q if s not in written][:1] for q in queues]
+        assert len(written) == sum(len(queue) for queue in queues)

@@ -13,6 +13,7 @@ U8 = mybir.dt.uint8
 FP8 = mybir.dt.float8_e4m3fn
 FP8X4 = mybir.dt.float8_e4m3fn_x4
 MULT = mybir.AluOpType.mult
+ADD = mybir.AluOpType.add
 COPY = mybir.ActivationFunctionType.Copy
 
 P = 128
@@ -32,19 +33,11 @@ BANKS = 8
 SPAN = 256
 
 SHARED = (0, 1)
-LEAD = 4
-FIRST_PAIR = 7
-LATE_PAIRS = 2
-CASTS_FROM = 11
-AHEAD = 2
-WARM_UPS = 0
-
-WIDE_BUFS = 6
+WIDE_BUFS = 5
 TURNED_BUFS = 4
-A_PLANE_BUFS = 5
 WOVEN_A_BUFS = 3
 WIDE_Y_BUFS = 4
-WOVEN_Y_BUFS = 2
+WOVEN_Y_BUFS = 3
 ROW_BUFS = 2 * CHUNKS
 
 
@@ -64,6 +57,10 @@ def tile_curvature_scaled_pair_correction_d7_kernel(tc, G, S_bytes, S_scale, Y_b
         c_bf = keep.tile([P, HALVES, PACK], BF16, name="c_bf")
         c_inv = keep.tile([P, SLICES], F32, name="c_inv")
         h_all = keep.tile([P, N], BF16, name="h_all")
+        a_planes = {}
+        for half in range(HALVES):
+            for two in range(CHUNKS // 2):
+                a_planes[half, two] = keep.tile([P, PACK, 2 * CHUNK], BF16, name="a_planes%d%d" % (half, two))
 
         def operand(name, groups, passes, columns, codes_at, scales_at):
             count = groups * passes * columns
@@ -75,7 +72,7 @@ def tile_curvature_scaled_pair_correction_d7_kernel(tc, G, S_bytes, S_scale, Y_b
 
         s_codes, s_scales = operand("s", SLICES, PASSES, P, SPAN // 4, 3 * SPAN // 4)
         g_codes, g_scales = operand("g", CHUNKS, PASSES, CHUNK, 0, SPAN // 2)
-        a_codes, a_scales = operand("a", CHUNKS, HALVES, CHUNK, SPAN // 4, 3 * SPAN // 4)
+        a_codes, a_scales = operand("a", 1, HALVES, T, SPAN // 4, 3 * SPAN // 4)
         y_codes, y_scales = operand("y", STRIPS, HALVES, STRIP, 0, SPAN // 2)
 
         s_rows = S_bytes.rearrange("(half r j) n -> half j r n", half=HALVES, j=PACK)
@@ -85,10 +82,6 @@ def tile_curvature_scaled_pair_correction_d7_kernel(tc, G, S_bytes, S_scale, Y_b
         def bank(key, shape):
             tiles[key] = psum.tile(shape, F32, name="bank%d" % bank_of[key], bufs=1)
             return tiles[key]
-
-        def warm_up(k):
-            idle = bank(("idle", k), [P, P])
-            nc.tensor.matmul(out=idle[:], lhsT=ident[:], rhs=ident[:], start=True, stop=True)
 
         def load_factor(factor, table, half):
             rows = table[PACK * half : PACK * (half + 1), :].partition_broadcast(QUAD)
@@ -208,10 +201,11 @@ def tile_curvature_scaled_pair_correction_d7_kernel(tc, G, S_bytes, S_scale, Y_b
                         nc.tensor.transpose(turned[:, w, i, :], src, ident[:])
 
         def empty_g(chunk, b):
+            copy = nc.vector.tensor_copy if (empty_g, chunk, b) in vector_steps else nc.scalar.copy
             joined = work.tile([P, 2, CHUNK, 2], F32, name="g_turned", tag="turned", bufs=TURNED_BUFS, align_bytes=64)
             tiles["g_turned", chunk, b] = joined
             for i in (1, 0):
-                join_words(nc.scalar.copy, joined[:, i], tiles["g_bank", chunk, 2 * b + i])
+                join_words(copy, joined[:, i], tiles["g_bank", chunk, 2 * b + i])
 
         def quant_g(chunk, b):
             nc.vector.quantize_mx(
@@ -220,58 +214,64 @@ def tile_curvature_scaled_pair_correction_d7_kernel(tc, G, S_bytes, S_scale, Y_b
                 in_=tiles["g_turned", chunk, b][:].rearrange("p g t w -> p (g t w)").bitcast(BF16),
             )
 
-        def first_product(chunk, u):
-            if u % 2 == 0:
-                bank(("u_bank", chunk, u // 2), [P, 2, CHUNK])
-            sums = tiles["u_bank", chunk, u // 2]
-            for g in range(PASSES):
-                nc.tensor.matmul_mx(
-                    out=sums[:, u % 2, :],
-                    lhsT=s_codes[:, u, g, :].bitcast(FP8X4),
-                    lhsT_scale=s_scales[:, u, g, :],
-                    rhs=g_codes[:, chunk, g, :].bitcast(FP8X4),
-                    rhs_scale=g_scales[:, chunk, g, :],
-                    start=(g == 0),
-                    stop=(g == PASSES - 1),
-                )
+        def members(u, chunk, along_chunks):
+            return [(u, chunk), (u, chunk + 1) if along_chunks else (u + 1, chunk)]
 
-        def empty_u(chunk, b):
-            half = b // 2
-            if b % 2 == 0:
-                tiles["a_planes", chunk, half] = work.tile([P, PACK, CHUNK], BF16, name="a_planes", bufs=A_PLANE_BUFS)
-            planes = tiles["a_planes", chunk, half]
-            for i in range(2):
-                u = 2 * b + i
-                sums = tiles["u_bank", chunk, b][:, i, :]
-                if (empty_u, chunk, b) in vector_steps:
-                    nc.vector.tensor_scalar(out=planes[:, u % PACK, :], in0=sums, scalar1=c_inv[:, u : u + 1], scalar2=None, op0=MULT)
+        def first_pair(u, chunk, along_chunks):
+            sums = bank(("u_bank", u, chunk), [P, 2, CHUNK])
+            for i, (v, k) in enumerate(members(u, chunk, along_chunks)):
+                for g in range(PASSES):
+                    nc.tensor.matmul_mx(
+                        out=sums[:, i, :],
+                        lhsT=s_codes[:, v, g, :].bitcast(FP8X4),
+                        lhsT_scale=s_scales[:, v, g, :],
+                        rhs=g_codes[:, k, g, :].bitcast(FP8X4),
+                        rhs_scale=g_scales[:, k, g, :],
+                        start=(g == 0),
+                        stop=(g == PASSES - 1),
+                    )
+
+        def empty_u(u, chunk, along_chunks):
+            sums = tiles["u_bank", u, chunk][:].rearrange("p i t -> p (i t)")
+            width = 2 * CHUNK if along_chunks else CHUNK
+            for i in range(2 * CHUNK // width):
+                v = u + i
+                at = chunk % 2 * CHUNK
+                dst = a_planes[v // PACK, chunk // 2][:, v % PACK, at : at + width]
+                src = sums[:, i * width : (i + 1) * width]
+                if (empty_u, u, chunk, along_chunks) in vector_steps:
+                    nc.vector.tensor_scalar(out=dst, in0=src, scalar1=c_inv[:, v : v + 1], scalar2=None, op0=MULT)
                 else:
-                    nc.scalar.activation(out=planes[:, u % PACK, :], in_=sums, func=COPY, scale=c_inv[:, u : u + 1])
+                    nc.scalar.activation(out=dst, in_=src, func=COPY, scale=c_inv[:, v : v + 1])
 
         def vector_views(woven, planes):
             return woven.rearrange("p (x i j) -> p x j i", i=RUN, j=PACK), planes.rearrange("p j (x i) -> p x j i", i=RUN)
 
-        def scalar_views(woven, planes):
+        def plain_views(woven, planes):
             return woven.rearrange("p (n j) -> p n j", j=PACK), planes.rearrange("p j n -> p n j")
 
-        def weave_a(chunk, half):
-            if half == 0:
-                shape = [P, HALVES, CHUNK * PACK]
-                tiles["a_woven", chunk] = work.tile(shape, BF16, name="a_woven", bufs=WOVEN_A_BUFS, align_bytes=64)
-            woven = tiles["a_woven", chunk][:, half, :]
-            planes = tiles["a_planes", chunk, half][:]
-            if (weave_a, chunk, half) in vector_steps:
+        def weave_a(half, chunk, count):
+            step = (weave_a, half, chunk, count)
+            name = "gated" if step in gated else "a_woven"
+            tile = work.tile([P, 2 * CHUNK * PACK], BF16, name=name, bufs=depth[name], align_bytes=64)
+            woven = tile[:, : count * CHUNK * PACK]
+            tiles["a_woven", half, chunk] = woven
+            at = chunk % 2 * CHUNK
+            planes = a_planes[half, chunk // 2][:, :, at : at + count * CHUNK]
+            if step in vector_steps:
                 dst, src = vector_views(woven, planes)
                 nc.vector.tensor_copy(out=dst, in_=src)
+            elif step in gpsimd_steps:
+                dst, src = plain_views(woven, planes)
+                nc.gpsimd.tensor_scalar(out=dst, in0=src, scalar1=1.0, scalar2=0.0, op0=MULT, op1=ADD)
             else:
-                dst, src = scalar_views(woven, planes)
+                dst, src = plain_views(woven, planes)
                 nc.scalar.copy(out=dst, in_=src)
 
-        def quant_a(chunk):
+        def quant_a(half, chunk, count):
+            cols = slice(chunk * CHUNK, (chunk + count) * CHUNK)
             nc.vector.quantize_mx(
-                out=a_codes[:, chunk].rearrange("p g t -> p (g t)").bitcast(FP8X4),
-                scales=a_scales[:, chunk].rearrange("p g t -> p (g t)"),
-                in_=tiles["a_woven", chunk][:].rearrange("p g x -> p (g x)"),
+                out=a_codes[:, 0, half, cols].bitcast(FP8X4), scales=a_scales[:, 0, half, cols], in_=tiles["a_woven", half, chunk]
             )
 
         def cast_y(strip, half):
@@ -280,27 +280,32 @@ def tile_curvature_scaled_pair_correction_d7_kernel(tc, G, S_bytes, S_scale, Y_b
             raw = tiles["y_raw", strip, half][:].rearrange("p j n -> p (j n)")
             nc.scalar.copy(out=wide[:].rearrange("p j n -> p (j n)"), in_=raw.bitcast(FP8))
 
-        def weave_y(strip, half):
-            if half == 0:
-                shape = [P, HALVES, STRIP * PACK]
-                tiles["y_woven", strip] = work.tile(shape, BF16, name="y_woven", bufs=WOVEN_Y_BUFS, align_bytes=64)
-            for i in range(STRIP // P):
-                woven = tiles["y_woven", strip][:, half, P * PACK * i : P * PACK * (i + 1)]
-                planes = tiles["y_wide", strip, half][:, :, P * i : P * (i + 1)]
-                block = strip * (STRIP // P) + i
+        def weave_y(strip, half, first, count):
+            step = (weave_y, strip, half, first, count)
+            name = "gated" if step in gated else "y_woven"
+            tile = work.tile([P, STRIP * PACK], BF16, name=name, bufs=depth[name], align_bytes=64)
+            tiles["y_woven", strip, half, first] = tile[:, : count * P * PACK]
+            for i in range(count):
+                woven = tile[:, P * PACK * i : P * PACK * (i + 1)]
+                planes = tiles["y_wide", strip, half][:, :, P * (first + i) : P * (first + i + 1)]
+                block = strip * (STRIP // P) + first + i
                 factor = y_factor[half][:, block : block + 1]
-                if (weave_y, strip, half) in vector_steps:
+                if step in vector_steps:
                     dst, src = vector_views(woven, planes)
                     nc.vector.tensor_scalar(out=dst, in0=src, scalar1=factor, scalar2=None, op0=MULT)
+                elif step in gpsimd_steps:
+                    dst, src = plain_views(woven, planes)
+                    nc.gpsimd.tensor_scalar(out=dst, in0=src, scalar1=factor, scalar2=0.0, op0=MULT, op1=ADD)
                 else:
-                    dst, src = scalar_views(woven, planes)
+                    dst, src = plain_views(woven, planes)
                     nc.scalar.activation(out=dst, in_=src, func=COPY, scale=factor)
 
-        def quant_y(strip):
+        def quant_y(strip, half, first, count):
+            cols = slice(first * P, (first + count) * P)
             nc.vector.quantize_mx(
-                out=y_codes[:, strip].rearrange("p g n -> p (g n)").bitcast(FP8X4),
-                scales=y_scales[:, strip].rearrange("p g n -> p (g n)"),
-                in_=tiles["y_woven", strip][:].rearrange("p g x -> p (g x)"),
+                out=y_codes[:, strip, half, cols].bitcast(FP8X4),
+                scales=y_scales[:, strip, half, cols],
+                in_=tiles["y_woven", strip, half, first],
             )
 
         def out_tiles(k):
@@ -310,12 +315,12 @@ def tile_curvature_scaled_pair_correction_d7_kernel(tc, G, S_bytes, S_scale, Y_b
         def second_product(k):
             for row_tile, strip in out_tiles(k):
                 sums = bank(("p_bank", row_tile, strip), [P, STRIP])
-                chunk, i = divmod(row_tile, CHUNK // P)
+                rows = slice(row_tile * P, (row_tile + 1) * P)
                 for half in range(HALVES):
                     nc.tensor.matmul_mx(
                         out=sums[:],
-                        lhsT=a_codes[:, chunk, half, i * P : (i + 1) * P].bitcast(FP8X4),
-                        lhsT_scale=a_scales[:, chunk, half, i * P : (i + 1) * P],
+                        lhsT=a_codes[:, 0, half, rows].bitcast(FP8X4),
+                        lhsT_scale=a_scales[:, 0, half, rows],
                         rhs=y_codes[:, strip, half].bitcast(FP8X4),
                         rhs_scale=y_scales[:, strip, half],
                         start=(half == 0),
@@ -344,119 +349,82 @@ def tile_curvature_scaled_pair_correction_d7_kernel(tc, G, S_bytes, S_scale, Y_b
         def store(k):
             nc.sync.dma_start(out=out_rows(k), in_=tiles["res", k][:])
 
-        g_parts = [(chunk, b) for chunk in range(CHUNKS) for b in range(2)]
-        units = [(turn_s, 0), (turn_s, 1)]
-        for k, part in enumerate(g_parts):
-            units.extend([(turn_g, *part)] + [(turn_s, u) for u in range(SLICES) if u == k + 2])
-        emptying = {turn_s: empty_s, turn_g: empty_g}
+        emptying = {turn_s: empty_s, turn_g: empty_g, first_pair: empty_u}
         quantising = {turn_s: quant_s, turn_g: quant_g}
-        last_slice, last_chunk, last_strip = SLICES - 1, CHUNKS - 1, STRIPS - 1
 
-        pairs = [(chunk, b) for chunk in range(2) for b in (0, 1)] + [(chunk, b) for b in (2, 3) for chunk in range(2)]
-        pairs.extend([(chunk, b) for chunk in range(2, CHUNKS) for b in range(SLICES // 2)])
 
-        out_steps = []
-        for group in ((0, 1), (2,), (3,)):
-            out_steps.extend([(2 * chunk + i, 0, True) for chunk in group for i in range(2)])
-            out_steps.extend([(2 * chunk, 2, False) for chunk in group])
-        out_steps.extend([(2 * chunk, last_strip, False) for chunk in range(CHUNKS)])
-
-        def products(pair):
-            return [(first_product, pair[0], 2 * pair[1] + i) for i in range(2)]
-
-        warm_ups = [(warm_up, k) for k in range(WARM_UPS)]
-        tensor_steps = warm_ups[:-1] + units[:1] + warm_ups[-1:]
-        waiting = list(pairs)
-        for i in range(1, len(units)):
-            tensor_steps.append(units[i])
-            if FIRST_PAIR <= i < len(units) - 1 and (i - FIRST_PAIR) % 2 == 0:
-                tensor_steps.extend(products(waiting.pop(0)))
-        while len(waiting) > LATE_PAIRS:
-            tensor_steps.extend(products(waiting.pop(0)))
+        S = [(turn_s, u) for u in range(SLICES)]
+        Gp = [(turn_g, chunk, b) for chunk in range(CHUNKS) for b in range(2)]
+        units = [S[0], Gp[0], S[1], Gp[1], Gp[2], Gp[3]] + S[2:6] + Gp[4:6] + S[6:] + Gp[6:]
+        pairs = [(0, 0, False), (0, 1, False)] + [(u, 0, True) for u in range(2, 6)] + [(0, 2, False), (2, 2, False), (6, 0, True), (7, 0, True), (4, 2, False), (6, 2, False)] + [(u, 3, False) for u in (0, 2, 4, 6)]
+        pieces = [(0, 0, 2), (1, 0, 2), (0, 2, 1), (1, 2, 1), (0, 3, 1), (1, 3, 1)]
+        y_pieces = [(0, 0, 0, 2), (0, 0, 2, 2), (0, 1, 0, 4), (1, 0, 0, 4), (1, 1, 0, 4), (2, 0, 0, 4), (2, 1, 0, 2), (2, 1, 2, 2), (3, 1, 0, 2), (3, 1, 2, 2), (3, 0, 0, 4)]
+        out_steps = [(0, 0, False), (2, 0, False), (0, 1, False), (2, 1, False), (4, 0, True), (5, 0, True)] + [(2 * chunk, strip, False) for strip in (2, 3) for chunk in range(3)] + [(row, strip, True) for strip in (0, 2) for row in (6, 7)]
+        F = [(first_pair, *pair) for pair in pairs]
+        per_round = [0, 0, 1, 1, 2, 2, 4]
+        tensor_steps = []
+        for r in range(len(per_round)):
+            tensor_steps.extend(units[2 * r : 2 * r + 2] + F[sum(per_round[:r]) : sum(per_round[: r + 1])])
+        late = {-1: units[14:16] + F[10:12], 1: F[12:14], 5: F[14:15], 7: F[15:16]}
+        tensor_steps.extend(late.get(-1, []))
         for k in range(len(out_steps)):
-            tensor_steps.append((second_product, k))
-            if waiting and k % 2 == 1:
-                tensor_steps.extend(products(waiting.pop(0)))
-
-        parts = [(strip, half) for strip in range(STRIPS) for half in range(HALVES)]
-        taken = [(empty_u, 1, 0), (empty_u, 1, 1)]
-        filled = []
-        for job, *index in tensor_steps:
-            if job in emptying:
-                filled.append((emptying[job], *index))
-            elif job is first_product and index[1] % 2 == 1:
-                filled.append((empty_u, index[0], index[1] // 2))
-        filled = [step for step in filled if step not in taken + [(empty_s, last_slice)]]
+            tensor_steps.extend([(second_product, k)] + late.get(k, []))
+        filled = [(emptying[job], *index) for job, *index in tensor_steps if job in emptying]
+        E = [(emptying[job], *index) for job, *index in F]
+        U = [(emptying[job], *index) for job, *index in units]
+        Q = [(quantising[job], *index) for job, *index in units]
+        W = [(widen_s, u) for u in range(SLICES)]
+        C = lambda s, h: (cast_y, s, h)
+        WY = lambda s, h, a=0, n=4: (weave_y, s, h, a, n)
+        QY = lambda s, h, a=0, n=4: (quant_y, s, h, a, n)
+        WA = lambda h, k, n=1: (weave_a, h, k, n)
+        QA = lambda h, k, n=1: (quant_a, h, k, n)
+        gated = [WY(1, 1), WY(2, 1, 0, 2), WY(2, 1, 2, 2), WY(3, 1, 0, 2), WY(3, 1, 2, 2), WA(0, 3)]
+        gpsimd_steps = gated[1:]
+        vector_steps = W[:4] + [Q[0], Q[1], Q[2], (invert_c,), Q[3], W[4], Q[4], Q[5], W[5], WY(0, 0, 0, 2), Q[6], WY(0, 0, 2, 2), Q[7], W[6], Q[8], QY(0, 0, 0, 2), QY(0, 0, 2, 2), Q[9], W[7], WA(0, 0, 2), Q[10], Q[11], QA(0, 0, 2), WY(0, 1), Q[12], (sort_g, 3, 0), Q[13], (sort_g, 3, 1), QY(0, 1), WY(1, 0), WA(1, 0, 2), QY(1, 0), QA(1, 0, 2), WA(0, 2), Q[14], Q[15], WY(1, 1), QA(0, 2), QY(1, 1)]
+        ahead = {2: [QA(1, 2), QY(2, 1, 0, 2)], 4: [QY(2, 0), QY(2, 1, 2, 2)], 6: [QY(3, 1, 0, 2)], 8: [QY(3, 0), QY(3, 1, 2, 2)], 10: [QA(0, 3), QA(1, 3)]}
+        for k in range(len(out_steps)):
+            vector_steps.extend(ahead.get(k, []) + [(finish, k)] * ((finish, k) not in vector_steps))
+        extra = {U[5]: [C(0, 0)], E[3]: [C(0, 1)], U[13]: [C(1, 0)], E[9]: [C(1, 1)], U[15]: [C(2, 1)], E[11]: [WA(1, 2), C(2, 0)], E[13]: [WY(2, 0), C(3, 1), C(3, 0)], E[14]: [WY(3, 0)], E[15]: [WA(1, 3)]}
         scalar_steps = [(widen_s_scalar, u) for u in SHARED]
-        uncast = list(parts)
-        whole = []
-        for i, (job, *index) in enumerate(filled):
-            scalar_steps.append((job, *index))
-            late = i >= len(filled) - LATE_PAIRS
-            if late or (i >= CASTS_FROM and (i - CASTS_FROM) % 2 == 0 and len(uncast) > HALVES):
-                scalar_steps.append((cast_y, *uncast.pop(0)))
-            scalar_steps.extend(whole)
-            mine = job is empty_u and (index[1] == 3 or index == [last_chunk, 1])
-            whole = [(weave_a, index[0], index[1] // 2)] if mine else []
-        scalar_steps.extend(whole + [(weave_y, last_strip, half) for half in range(HALVES)])
-
-        long_jobs = [[(widen_s, u)] for u in range(LEAD, SLICES)]
-        long_jobs[-2].append((invert_c,))
-        long_jobs.append([(sort_g, last_chunk, b) for b in range(2)])
-        long_jobs.extend([[(weave_y, *part)] for part in parts[:3]])
-        short_jobs = [(weave_a, 0, 0), *taken, (weave_a, 1, 0)]
-        vector_steps = [(widen_s, u) for u in range(LEAD)]
-        for i, (job, *index) in enumerate(units):
-            quant = [(quantising[job], *index)]
-            if units[i + 1 : i + 2] == [(turn_s, last_slice)]:
-                vector_steps.append((empty_s, last_slice))
-            if i % 2 == 0:
-                beside = long_jobs.pop(0)
-                vector_steps.extend(beside + quant if beside[0][0] is weave_y else quant + beside)
-            else:
-                vector_steps.extend(quant + [short_jobs.pop(0) for k in range(i >= len(units) - 2 * len(short_jobs))])
-        vector_steps.extend([(quant_y, 0), (weave_y, 1, 1), (weave_y, 2, 0), (quant_y, 1), (quant_a, 0)])
-        vector_steps.extend([(weave_y, 2, 1), (quant_a, 1), (weave_a, 2, 0)])
-        ahead = [[] for k in out_steps]
-        for index in (2, 3):
-            ahead[min(k for k, step in enumerate(out_steps) if step[1] == index) - AHEAD].append((quant_y, index))
-            ahead[min(k for k, step in enumerate(out_steps) if step[0] == 2 * index) - AHEAD].append((quant_a, index))
-        for k in range(len(out_steps)):
-            vector_steps.extend(ahead[k] + [(finish, k)])
-
-        sync_steps = [(load_s_factor, 0)] + [(load_s, u) for u in range(LEAD)]
-        for k, part in enumerate(g_parts):
-            if k == len(g_parts) - 3:
-                sync_steps.extend([(load_y_factor, 0), (load_y, 0, 0)])
-            sync_steps.append((load_g, *part))
-            if k == 0:
-                sync_steps.extend([(load_s_factor, 1), (load_c,)])
-            sync_steps.extend([(load_s, u) for u in range(SLICES) if u == LEAD + k])
-        sync_steps.append((load_y_factor, 1))
-        sync_steps.extend([(load_y, *part) for part in parts[1:-HALVES]] + [(load_h,)])
-        sync_steps.extend([(load_y, *part) for part in parts[-HALVES:]])
+        for step in filled:
+            scalar_steps.extend([step] * (step not in vector_steps) + extra.get(step, []))
+        ls = [(load_s, u) for u in range(SLICES)]
+        lg = [(load_g, chunk, b) for chunk in range(CHUNKS) for b in range(2)]
+        ly = lambda s, h: (load_y, s, h)
+        sync_steps = [(load_s_factor, 0), ls[0], ls[1], ls[2], lg[0], ls[3], lg[1], lg[2], lg[3], (load_c,), (load_s_factor, 1), ls[4], ls[5], (load_y_factor, 0), ly(0, 0), ls[6], lg[4], lg[5], ls[7], (load_y_factor, 1), ly(0, 1), lg[6], lg[7], ly(1, 0), ly(1, 1), (load_h,), ly(2, 1), ly(2, 0), ly(3, 1), ly(3, 0)]
         sync_steps.extend([(store, k) for k in range(len(out_steps) - 1)])
 
-        def bank_keys(job, a=0, b=0):
+        def bank_keys(job, a=0, b=0, *rest):
             if job in (turn_s, empty_s):
                 return [("s_bank", a, 0), ("s_bank", a, 1)]
             if job in (turn_g, empty_g):
                 return [("g_bank", a, 2 * b), ("g_bank", a, 2 * b + 1)]
             if job in (second_product, finish):
                 return [("p_bank", *tile) for tile in out_tiles(a)]
-            if job is warm_up:
-                return [("idle", a)]
-            if job is first_product and b % 2 == 0:
-                return [("u_bank", a, b // 2)]
-            return [("u_bank", a, b)] if job is empty_u else []
+            return [("u_bank", a, b)] if job in (first_pair, empty_u) else []
 
         keys = [key for step in tensor_steps for key in bank_keys(*step)]
-        bank_of = {key: len([other for other in keys[:k] if other[0] != "idle"]) % BANKS for k, key in enumerate(keys)}
+        bank_of = {key: k % BANKS for k, key in enumerate(keys)}
 
         empties = [(emptying[job], *index) for job, *index in units]
         after = dict(zip(empties[1:], empties))
 
-        def inputs(job, a=0, b=0):
+        def a_pieces(half, chunk):
+            return [piece for piece in pieces if piece[0] == half and piece[1] <= chunk < piece[1] + piece[2]]
+
+        def inputs(job, a=0, b=0, *rest):
+            step = (job, a, b, *rest)
+            earlier = gated[: gated.index(step)] if step in gated else []
+            if job is first_pair:
+                return [need for v, k in members(a, b, *rest) for need in ((quant_s, v), (quant_g, k, 0), (quant_g, k, 1))]
+            if job is weave_a:
+                return earlier + [(empty_u, *pair) for pair in pairs if any(v // PACK == a and b <= k < b + rest[0] for v, k in members(*pair))]
+            if job is second_product:
+                needs = [(quant_y, *piece) for row_tile, strip in out_tiles(a) for piece in y_pieces if piece[0] == strip]
+                for row_tile, strip in out_tiles(a):
+                    needs.extend([(quant_a, *piece) for half in range(HALVES) for piece in a_pieces(half, row_tile // 2)])
+                return needs
             table = {
                 widen_s: [(load_s, a), (load_s_factor, a // PACK)] + [(widen_s_scalar, a)] * (a in SHARED),
                 widen_s_scalar: [(load_s, a), (load_s_factor, a // PACK)],
@@ -467,27 +435,24 @@ def tile_curvature_scaled_pair_correction_d7_kernel(tc, G, S_bytes, S_scale, Y_b
                 turn_g: [(load_g, a, b)] + [(sort_g, a, b)] * ((sort_g, a, b) in vector_steps),
                 empty_g: [(turn_g, a, b), after.get((empty_g, a, b), (turn_g, a, b))],
                 quant_g: [(empty_g, a, b)],
-                first_product: [(quant_s, b), (quant_g, a, 0), (quant_g, a, 1)] + [(first_product, a, b - 1)] * (b % 2),
                 invert_c: [(load_c,)],
-                empty_u: [(first_product, a, 2 * b + 1), (invert_c,)] + [(empty_u, a, b - 1)] * (b % 2),
-                weave_a: [(empty_u, a, 2 * b), (empty_u, a, 2 * b + 1)] + [(weave_a, a, 0)] * b,
-                quant_a: [(weave_a, a, 0), (weave_a, a, 1)],
+                empty_u: [(first_pair, a, b, *rest), (invert_c,)],
+                quant_a: [(weave_a, a, b, *rest)],
                 cast_y: [(load_y, a, b)],
-                weave_y: [(cast_y, a, b), (load_y_factor, b)] + [(weave_y, a, 0)] * b,
-                quant_y: [(weave_y, a, 0), (weave_y, a, 1)],
+                weave_y: [(cast_y, a, b), (load_y_factor, b)] + earlier,
+                quant_y: [(weave_y, a, b, *rest)],
                 finish: [(second_product, a), (load_h,)],
                 store: [(finish, a)],
             }
-            if job is second_product:
-                return [need for row_tile, strip in out_tiles(a) for need in ((quant_a, row_tile // 2), (quant_y, strip))]
             return table.get(job, [])
 
-        def buffers(job, a=0, b=0):
+        def buffers(job, a=0, b=0, *rest):
             banks = [(bank_of[key], key) for key in bank_keys(job, a, b)]
             wide, rows, ordered = [("wide", a)], [("rows", (a, b))], [("wide", (a, b))]
             turned = [("turned", (job in (empty_s, quant_s), a, b))]
-            a_planes, y_planes = [("a_planes", (a, b))], [("y_wide", (a, b))]
-            a_woven, y_woven = [("a_woven", a)], [("y_woven", a)]
+            y_planes, a_woven = [("y_wide", (a, b))], [("gated" if (weave_a, a, b, *rest) in gated else "a_woven", ("a", a, b))]
+            y_woven = [("gated" if (weave_y, a, b, *rest) in gated else "y_woven", (a, b, *rest))]
+            others = [piece for piece in y_pieces if piece[:2] == (a, b) and piece[2:] != rest]
             table = {
                 widen_s: (wide * (a not in SHARED), []),
                 widen_s_scalar: (wide, []),
@@ -499,12 +464,11 @@ def tile_curvature_scaled_pair_correction_d7_kernel(tc, G, S_bytes, S_scale, Y_b
                 empty_g: (turned, banks),
                 quant_s: ([], turned),
                 quant_g: ([], turned),
-                warm_up: (banks, banks),
-                first_product: (banks, []),
-                empty_u: ([("a_planes", (a, b // 2))] * (b % 2 == 0), banks),
+                first_pair: (banks, []),
+                empty_u: ([], banks),
                 cast_y: (y_planes, []),
-                weave_a: (a_woven * (1 - b), a_planes),
-                weave_y: (y_woven * (1 - b), y_planes),
+                weave_a: (a_woven, []),
+                weave_y: (y_woven, y_planes * all((weave_y, *piece) in written for piece in others)),
                 quant_a: ([], a_woven),
                 quant_y: ([], y_woven),
                 second_product: (banks, []),
@@ -513,10 +477,10 @@ def tile_curvature_scaled_pair_correction_d7_kernel(tc, G, S_bytes, S_scale, Y_b
             }
             return table.get(job, ([], []))
 
-        depth = {"wide": WIDE_BUFS, "turned": TURNED_BUFS, "a_planes": A_PLANE_BUFS, "a_woven": WOVEN_A_BUFS}
-        depth = {**depth, "y_wide": WIDE_Y_BUFS, "y_woven": WOVEN_Y_BUFS, "rows": ROW_BUFS}
+        depth = {"wide": WIDE_BUFS, "turned": TURNED_BUFS, "a_woven": WOVEN_A_BUFS, "y_wide": WIDE_Y_BUFS, "rows": ROW_BUFS}
+        depth = {**depth, "y_woven": WOVEN_Y_BUFS, "gated": 1}
         owners = {kind: [] for kind in [*depth, *range(BANKS)]}
-        queues = [sync_steps, scalar_steps, vector_steps, tensor_steps]
+        queues = [sync_steps, scalar_steps, vector_steps, gpsimd_steps, tensor_steps]
         written = set()
         given = set()
         for sweep in range(sum(len(queue) for queue in queues)):
@@ -531,4 +495,4 @@ def tile_curvature_scaled_pair_correction_d7_kernel(tc, G, S_bytes, S_scale, Y_b
                         given.update(gives)
                         for buffer in takes:
                             owners[buffer[0]].append(buffer)
-        assert len(written) == sum(len(queue) for queue in queues)
+        assert len(written) == sum(len(queue) for queue in queues), "stuck"

@@ -39,6 +39,7 @@ WOVEN_A_BUFS = 3
 WIDE_Y_BUFS = 4
 WOVEN_Y_BUFS = 3
 ROW_BUFS = 2 * CHUNKS
+SINGLE = 1
 
 
 def tile_curvature_scaled_pair_correction_d7_kernel(tc, G, S_bytes, S_scale, Y_bytes, Y_scale, c, h, out):
@@ -328,7 +329,7 @@ def tile_curvature_scaled_pair_correction_d7_kernel(tc, G, S_bytes, S_scale, Y_b
                     )
 
         def finish(k):
-            last = k == len(out_steps) - 1
+            last = k >= len(out_steps) - SINGLE
             res = work.tile([P, 2, STRIP], F32, name="res", tag="rows", bufs=ROW_BUFS)
             tiles["res", k] = res
             for i in (0, 1) if last else (1, 0):
@@ -358,14 +359,14 @@ def tile_curvature_scaled_pair_correction_d7_kernel(tc, G, S_bytes, S_scale, Y_b
         units = [S[0], Gp[0], S[1], Gp[1], Gp[2], Gp[3]] + S[2:6] + Gp[4:6] + S[6:] + Gp[6:]
         pairs = [(0, 0, False), (0, 1, False)] + [(u, 0, True) for u in range(2, 6)] + [(0, 2, False), (2, 2, False), (6, 0, True), (7, 0, True), (4, 2, False), (6, 2, False)] + [(u, 3, False) for u in (0, 2, 4, 6)]
         pieces = [(0, 0, 2), (1, 0, 2), (0, 2, 1), (1, 2, 1), (0, 3, 1), (1, 3, 1)]
-        y_pieces = [(0, 0, 0, 2), (0, 0, 2, 2), (0, 1, 0, 4), (1, 0, 0, 4), (1, 1, 0, 4), (2, 0, 0, 4), (2, 1, 0, 2), (2, 1, 2, 2), (3, 1, 0, 2), (3, 1, 2, 2), (3, 0, 0, 4)]
+        y_pieces = [(0, 0, 0, 2), (0, 0, 2, 2), (0, 1, 0, 4), (1, 0, 0, 4), (1, 1, 0, 4), (2, 0, 0, 4), (2, 1, 0, 2), (2, 1, 2, 2), (3, 1, 0, 4), (3, 0, 0, 4)]
         out_steps = [(0, 0, False), (2, 0, False), (0, 1, False), (2, 1, False), (4, 0, True), (5, 0, True)] + [(2 * chunk, strip, False) for strip in (2, 3) for chunk in range(3)] + [(row, strip, True) for strip in (0, 2) for row in (6, 7)]
         F = [(first_pair, *pair) for pair in pairs]
         per_round = [0, 0, 1, 1, 2, 2, 4]
         tensor_steps = []
         for r in range(len(per_round)):
             tensor_steps.extend(units[2 * r : 2 * r + 2] + F[sum(per_round[:r]) : sum(per_round[: r + 1])])
-        late = {-1: units[14:16] + F[10:12], 1: F[12:14], 5: F[14:15], 7: F[15:16]}
+        late = {-1: units[14:16] + F[10:12], 1: F[12:13], 5: F[13:14], 7: F[14:15], 8: F[15:16]}
         tensor_steps.extend(late.get(-1, []))
         for k in range(len(out_steps)):
             tensor_steps.extend([(second_product, k)] + late.get(k, []))
@@ -379,21 +380,21 @@ def tile_curvature_scaled_pair_correction_d7_kernel(tc, G, S_bytes, S_scale, Y_b
         QY = lambda s, h, a=0, n=4: (quant_y, s, h, a, n)
         WA = lambda h, k, n=1: (weave_a, h, k, n)
         QA = lambda h, k, n=1: (quant_a, h, k, n)
-        gated = [WY(1, 1), WY(2, 1, 0, 2), WY(2, 1, 2, 2), WY(3, 1, 0, 2), WY(3, 1, 2, 2), WA(0, 3)]
+        gated = [WY(1, 1), WY(2, 1, 0, 2), WY(2, 1, 2, 2), WY(3, 1), WA(0, 3)]
         gpsimd_steps = gated[1:]
-        vector_steps = W[:4] + [Q[0], Q[1], Q[2], (invert_c,), Q[3], W[4], Q[4], Q[5], W[5], WY(0, 0, 0, 2), Q[6], WY(0, 0, 2, 2), Q[7], W[6], Q[8], QY(0, 0, 0, 2), QY(0, 0, 2, 2), Q[9], W[7], WA(0, 0, 2), Q[10], Q[11], QA(0, 0, 2), WY(0, 1), Q[12], (sort_g, 3, 0), Q[13], (sort_g, 3, 1), QY(0, 1), WY(1, 0), WA(1, 0, 2), QY(1, 0), QA(1, 0, 2), WA(0, 2), Q[14], Q[15], WY(1, 1), QA(0, 2), QY(1, 1)]
-        ahead = {2: [QA(1, 2), QY(2, 1, 0, 2)], 4: [QY(2, 0), QY(2, 1, 2, 2)], 6: [QY(3, 1, 0, 2)], 8: [QY(3, 0), QY(3, 1, 2, 2)], 10: [QA(0, 3), QA(1, 3)]}
+        vector_steps = W[:4] + [Q[0], Q[1], U[3], Q[2], Q[3], W[4], Q[4], (invert_c,), Q[5], W[5], WY(0, 0, 0, 2), Q[6], WY(0, 0, 2, 2), Q[7], W[6], Q[8], QY(0, 0, 0, 2), QY(0, 0, 2, 2), Q[9], W[7], WA(0, 0, 2), Q[10], QA(0, 0, 2), Q[11], WY(0, 1), Q[12], (sort_g, 3, 0), Q[13], (sort_g, 3, 1), QY(0, 1), WY(1, 0), WA(1, 0, 2), QY(1, 0), QA(1, 0, 2), WA(0, 2), Q[14], Q[15], WY(1, 1), QA(0, 2), QY(1, 1)]
+        ahead = {2: [QA(1, 2), QY(2, 1, 0, 2)], 4: [QY(2, 0), QY(2, 1, 2, 2)], 8: [QY(3, 0), QY(3, 1)], 10: [QA(0, 3), QA(1, 3)]}
         for k in range(len(out_steps)):
             vector_steps.extend(ahead.get(k, []) + [(finish, k)] * ((finish, k) not in vector_steps))
-        extra = {U[5]: [C(0, 0)], E[3]: [C(0, 1)], U[13]: [C(1, 0)], E[9]: [C(1, 1)], U[15]: [C(2, 1)], E[11]: [WA(1, 2), C(2, 0)], E[13]: [WY(2, 0), C(3, 1), C(3, 0)], E[14]: [WY(3, 0)], E[15]: [WA(1, 3)]}
+        extra = {U[2]: [C(0, 0)], U[5]: [C(0, 1)], E[3]: [C(1, 0)], U[13]: [C(1, 1)], E[9]: [C(2, 1)], E[11]: [WA(1, 2), C(2, 0), WY(2, 0)], E[12]: [C(3, 1), C(3, 0)], E[13]: [WY(3, 0)], E[15]: [WA(1, 3)]}
         scalar_steps = [(widen_s_scalar, u) for u in SHARED]
         for step in filled:
             scalar_steps.extend([step] * (step not in vector_steps) + extra.get(step, []))
         ls = [(load_s, u) for u in range(SLICES)]
         lg = [(load_g, chunk, b) for chunk in range(CHUNKS) for b in range(2)]
         ly = lambda s, h: (load_y, s, h)
-        sync_steps = [(load_s_factor, 0), ls[0], ls[1], ls[2], lg[0], ls[3], lg[1], lg[2], lg[3], (load_c,), (load_s_factor, 1), ls[4], ls[5], (load_y_factor, 0), ly(0, 0), ls[6], lg[4], lg[5], ls[7], (load_y_factor, 1), ly(0, 1), lg[6], lg[7], ly(1, 0), ly(1, 1), (load_h,), ly(2, 1), ly(2, 0), ly(3, 1), ly(3, 0)]
-        sync_steps.extend([(store, k) for k in range(len(out_steps) - 1)])
+        sync_steps = [(load_s_factor, 0), ls[0], ls[1], ls[2], lg[0], ls[3], lg[1], (load_y_factor, 0), ly(0, 0), lg[2], lg[3], (load_c,), (load_s_factor, 1), ls[4], ls[5], (load_y_factor, 1), ly(0, 1), ls[6], lg[4], lg[5], ls[7], ly(1, 0), lg[6], lg[7], ly(1, 1), (load_h,), ly(2, 1), ly(2, 0), ly(3, 1), ly(3, 0)]
+        sync_steps.extend([(store, k) for k in range(len(out_steps) - SINGLE)])
 
         def bank_keys(job, a=0, b=0, *rest):
             if job in (turn_s, empty_s):

@@ -40,6 +40,7 @@ WIDE_Y_BUFS = 4
 WOVEN_Y_BUFS = 3
 ROW_BUFS = 2 * CHUNKS
 SINGLE = 1
+TABLE_WARM = 1
 
 
 def tile_curvature_scaled_pair_correction_d7_kernel(tc, G, S_bytes, S_scale, Y_bytes, Y_scale, c, h, out):
@@ -52,6 +53,9 @@ def tile_curvature_scaled_pair_correction_d7_kernel(tc, G, S_bytes, S_scale, Y_b
 
         ident = keep.tile([P, P], F32, name="ident")
         make_identity(nc, ident[:])
+
+        idle = keep.tile([P, 1], F32, name="idle")
+        nc.scalar.activation(out=idle[:], in_=ident[:, 0:1], func=COPY)
 
         s_factor = [keep.tile([P, COL_BLOCKS], F32, name="s_factor%d" % half) for half in range(HALVES)]
         y_factor = [keep.tile([P, COL_BLOCKS], F32, name="y_factor%d" % half) for half in range(HALVES)]

@@ -41,6 +41,7 @@ WOVEN_Y_BUFS = 3
 ROW_BUFS = 2 * CHUNKS
 SINGLE = 1
 TABLE_WARM = 1
+SINGLES = (9, 10, 11, 15)
 
 
 def tile_curvature_scaled_pair_correction_d7_kernel(tc, G, S_bytes, S_scale, Y_bytes, Y_scale, c, h, out):
@@ -333,7 +334,7 @@ def tile_curvature_scaled_pair_correction_d7_kernel(tc, G, S_bytes, S_scale, Y_b
                     )
 
         def finish(k):
-            last = k >= len(out_steps) - SINGLE
+            last = k in SINGLES
             res = work.tile([P, 2, STRIP], F32, name="res", tag="rows", bufs=ROW_BUFS)
             tiles["res", k] = res
             for i in (0, 1) if last else (1, 0):
@@ -370,7 +371,7 @@ def tile_curvature_scaled_pair_correction_d7_kernel(tc, G, S_bytes, S_scale, Y_b
         tensor_steps = []
         for r in range(len(per_round)):
             tensor_steps.extend(units[2 * r : 2 * r + 2] + F[sum(per_round[:r]) : sum(per_round[: r + 1])])
-        late = {-1: units[14:16] + F[10:12], 1: F[12:13], 5: F[13:14], 7: F[14:15], 8: F[15:16]}
+        late = {-1: units[14:16] + F[10:12], 1: F[12:14], 5: F[14:15], 7: F[15:16]}
         tensor_steps.extend(late.get(-1, []))
         for k in range(len(out_steps)):
             tensor_steps.extend([(second_product, k)] + late.get(k, []))
@@ -390,15 +391,15 @@ def tile_curvature_scaled_pair_correction_d7_kernel(tc, G, S_bytes, S_scale, Y_b
         ahead = {2: [QA(1, 2), QY(2, 1, 0, 2)], 4: [QY(2, 0), QY(2, 1, 2, 2)], 8: [QY(3, 0), QY(3, 1)], 10: [QA(0, 3), QA(1, 3)]}
         for k in range(len(out_steps)):
             vector_steps.extend(ahead.get(k, []) + [(finish, k)] * ((finish, k) not in vector_steps))
-        extra = {U[2]: [C(0, 0)], U[5]: [C(0, 1)], E[3]: [C(1, 0)], U[13]: [C(1, 1)], E[9]: [C(2, 1)], E[11]: [WA(1, 2), C(2, 0), WY(2, 0)], E[12]: [C(3, 1), C(3, 0)], E[13]: [WY(3, 0)], E[15]: [WA(1, 3)]}
+        extra = {U[2]: [C(0, 0)], U[5]: [C(0, 1)], E[3]: [C(1, 0)], U[13]: [C(1, 1)], E[9]: [C(2, 1)], E[11]: [WA(1, 2), C(2, 0), WY(2, 0)], E[13]: [C(3, 1), C(3, 0)], E[14]: [WY(3, 0)], E[15]: [WA(1, 3)]}
         scalar_steps = [(widen_s_scalar, u) for u in SHARED]
         for step in filled:
             scalar_steps.extend([step] * (step not in vector_steps) + extra.get(step, []))
         ls = [(load_s, u) for u in range(SLICES)]
         lg = [(load_g, chunk, b) for chunk in range(CHUNKS) for b in range(2)]
         ly = lambda s, h: (load_y, s, h)
-        sync_steps = [(load_s_factor, 0), ls[0], ls[1], ls[2], lg[0], ls[3], lg[1], (load_y_factor, 0), ly(0, 0), lg[2], lg[3], (load_c,), (load_s_factor, 1), ls[4], ls[5], (load_y_factor, 1), ly(0, 1), ls[6], lg[4], lg[5], ls[7], ly(1, 0), lg[6], lg[7], ly(1, 1), (load_h,), ly(2, 1), ly(2, 0), ly(3, 1), ly(3, 0)]
-        sync_steps.extend([(store, k) for k in range(len(out_steps) - SINGLE)])
+        sync_steps = [(load_s_factor, 0), ls[0], ls[1], ls[2], lg[0], ls[3], lg[1], ly(0, 0), lg[2], lg[3], (load_s_factor, 1), ls[4], (load_c,), ls[5], ly(0, 1), (load_y_factor, 0), ls[6], lg[4], lg[5], ls[7], (load_y_factor, 1), ly(1, 0), lg[6], lg[7], ly(1, 1), (load_h,), ly(2, 1), ly(2, 0), ly(3, 1), ly(3, 0)]
+        sync_steps.extend([(store, k) for k in range(len(out_steps)) if k not in SINGLES])
 
         def bank_keys(job, a=0, b=0, *rest):
             if job in (turn_s, empty_s):

@@ -41,7 +41,13 @@ WOVEN_Y_BUFS = 3
 ROW_BUFS = 2 * CHUNKS
 SINGLE = 1
 TABLE_WARM = 1
-SINGLES = (9, 10, 11, 15)
+V2 = 1
+SINGLES = tuple(range(8, 16))
+HELPED = ()
+PLAIN_BUFS = 1
+STORE_LAG = 2
+SECOND_QUEUE = 99
+FIRSTQ = 1
 
 
 def tile_curvature_scaled_pair_correction_d7_kernel(tc, G, S_bytes, S_scale, Y_bytes, Y_scale, c, h, out):
@@ -54,9 +60,6 @@ def tile_curvature_scaled_pair_correction_d7_kernel(tc, G, S_bytes, S_scale, Y_b
 
         ident = keep.tile([P, P], F32, name="ident")
         make_identity(nc, ident[:])
-
-        idle = keep.tile([P, 1], F32, name="idle")
-        nc.scalar.activation(out=idle[:], in_=ident[:, 0:1], func=COPY)
 
         s_factor = [keep.tile([P, COL_BLOCKS], F32, name="s_factor%d" % half) for half in range(HALVES)]
         y_factor = [keep.tile([P, COL_BLOCKS], F32, name="y_factor%d" % half) for half in range(HALVES)]
@@ -89,15 +92,19 @@ def tile_curvature_scaled_pair_correction_d7_kernel(tc, G, S_bytes, S_scale, Y_b
             tiles[key] = psum.tile(shape, F32, name="bank%d" % bank_of[key], bufs=1)
             return tiles[key]
 
-        def load_factor(factor, table, half):
+        def load_factor(queue, factor, table, half):
             rows = table[PACK * half : PACK * (half + 1), :].partition_broadcast(QUAD)
-            nc.sync.dma_start(out=factor[half][:], in_=rows.rearrange("r q k -> q r k"))
+            queue.dma_start(out=factor[half][:], in_=rows.rearrange("r q k -> q r k"))
+
+        load_factor(nc.scalar, s_factor, S_scale, 0)
+        idle = keep.tile([P, 1], F32, name="idle")
+        nc.scalar.activation(out=idle[:], in_=ident[:, 0:1], func=COPY)
 
         def load_s_factor(half):
-            load_factor(s_factor, S_scale, half)
+            load_factor(nc.sync, s_factor, S_scale, half)
 
         def load_y_factor(half):
-            load_factor(y_factor, Y_scale, half)
+            load_factor(nc.sync, y_factor, Y_scale, half)
 
         def load_c():
             nc.sync.dma_start(out=c_bf[:], in_=c.rearrange("(half p j) -> p half j", half=HALVES, j=PACK))
@@ -334,15 +341,25 @@ def tile_curvature_scaled_pair_correction_d7_kernel(tc, G, S_bytes, S_scale, Y_b
                     )
 
         def finish(k):
-            last = k in SINGLES
             res = work.tile([P, 2, STRIP], F32, name="res", tag="rows", bufs=ROW_BUFS)
             tiles["res", k] = res
-            for i in (0, 1) if last else (1, 0):
+            for i in (1,) if k in HELPED else (0, 1) if k in SINGLES else (1, 0):
                 row_tile, strip = out_tiles(k)[i]
                 factor = h_all[:, STRIP * strip : STRIP * (strip + 1)]
                 nc.vector.tensor_tensor(out=res[:, i, :], in0=tiles["p_bank", row_tile, strip][:], in1=factor, op=MULT)
-                if last:
-                    nc.sync.dma_start(out=out_rows(k)[:, i, :], in_=res[:, i, :])
+
+        def empty_p(k):
+            res = work.tile([P, STRIP], F32, name="plain", bufs=PLAIN_BUFS)
+            tiles["plain", k] = res
+            nc.scalar.copy(out=res[:], in_=tiles[("p_bank", *out_tiles(k)[0])][:])
+
+        def scale_p(k):
+            strip = out_tiles(k)[0][1]
+            res = tiles["plain", k]
+            nc.gpsimd.tensor_tensor(out=res[:], in0=res[:], in1=h_all[:, STRIP * strip : STRIP * (strip + 1)], op=MULT)
+
+        def store_p(k):
+            nc.sync.dma_start(out=out_rows(k)[:, 0, :], in_=tiles["plain", k][:])
 
         def out_rows(k):
             row_tile, strip, along_row = out_steps[k]
@@ -353,7 +370,10 @@ def tile_curvature_scaled_pair_correction_d7_kernel(tc, G, S_bytes, S_scale, Y_b
             return rows.rearrange("(i r) n -> r i n", i=2)
 
         def store(k):
-            nc.sync.dma_start(out=out_rows(k), in_=tiles["res", k][:])
+            parts = [slice(1, 2)] if k in HELPED else [slice(0, 1), slice(1, 2)] if k in SINGLES else [slice(0, 2)]
+            for n, part in enumerate(parts):
+                queue = nc.scalar if k >= SECOND_QUEUE and n == 0 else nc.sync
+                queue.dma_start(out=out_rows(k)[:, part, :], in_=tiles["res", k][:, part, :])
 
         emptying = {turn_s: empty_s, turn_g: empty_g, first_pair: empty_u}
         quantising = {turn_s: quant_s, turn_g: quant_g}
@@ -387,7 +407,7 @@ def tile_curvature_scaled_pair_correction_d7_kernel(tc, G, S_bytes, S_scale, Y_b
         QA = lambda h, k, n=1: (quant_a, h, k, n)
         gated = [WY(1, 1), WY(2, 1, 0, 2), WY(2, 1, 2, 2), WY(3, 1), WA(0, 3)]
         gpsimd_steps = gated[1:]
-        vector_steps = W[:4] + [Q[0], Q[1], U[3], Q[2], Q[3], W[4], Q[4], (invert_c,), Q[5], W[5], WY(0, 0, 0, 2), Q[6], WY(0, 0, 2, 2), Q[7], W[6], Q[8], QY(0, 0, 0, 2), QY(0, 0, 2, 2), Q[9], W[7], WA(0, 0, 2), Q[10], QA(0, 0, 2), Q[11], WY(0, 1), Q[12], (sort_g, 3, 0), Q[13], (sort_g, 3, 1), QY(0, 1), WY(1, 0), WA(1, 0, 2), QY(1, 0), QA(1, 0, 2), WA(0, 2), Q[14], Q[15], WY(1, 1), QA(0, 2), QY(1, 1)]
+        vector_steps = W[:4] + [Q[0], Q[1], U[3], Q[2], Q[3], W[4], Q[4], (invert_c,), Q[5], W[5], WY(0, 0, 0, 2), Q[6], WY(0, 0, 2, 2), Q[7], W[6], Q[8], QY(0, 0, 0, 2), QY(0, 0, 2, 2), Q[9], W[7], WA(0, 0, 2), Q[10], QA(0, 0, 2), Q[11], WY(0, 1), Q[12], (sort_g, 3, 0), Q[13], (sort_g, 3, 1), QY(0, 1), WY(1, 0), WA(0, 2), WA(1, 0, 2), QY(1, 0), QA(1, 0, 2), Q[14], Q[15], WY(1, 1), QA(0, 2), QY(1, 1)]
         ahead = {2: [QA(1, 2), QY(2, 1, 0, 2)], 4: [QY(2, 0), QY(2, 1, 2, 2)], 8: [QY(3, 0), QY(3, 1)], 10: [QA(0, 3), QA(1, 3)]}
         for k in range(len(out_steps)):
             vector_steps.extend(ahead.get(k, []) + [(finish, k)] * ((finish, k) not in vector_steps))
@@ -398,16 +418,21 @@ def tile_curvature_scaled_pair_correction_d7_kernel(tc, G, S_bytes, S_scale, Y_b
         ls = [(load_s, u) for u in range(SLICES)]
         lg = [(load_g, chunk, b) for chunk in range(CHUNKS) for b in range(2)]
         ly = lambda s, h: (load_y, s, h)
-        sync_steps = [(load_s_factor, 0), ls[0], ls[1], ls[2], lg[0], ls[3], lg[1], ly(0, 0), lg[2], lg[3], (load_s_factor, 1), ls[4], (load_c,), ls[5], ly(0, 1), (load_y_factor, 0), ls[6], lg[4], lg[5], ls[7], (load_y_factor, 1), ly(1, 0), lg[6], lg[7], ly(1, 1), (load_h,), ly(2, 1), ly(2, 0), ly(3, 1), ly(3, 0)]
-        sync_steps.extend([(store, k) for k in range(len(out_steps)) if k not in SINGLES])
+        sync_steps = [ls[0], ls[1], ls[2], lg[0], ls[3], lg[1], ly(0, 0), lg[2], lg[3], (load_s_factor, 1), ls[4], (load_c,), ls[5], ly(0, 1), (load_y_factor, 0), ls[6], lg[4], lg[5], ls[7], (load_y_factor, 1), ly(1, 0), lg[6], lg[7], ly(1, 1), (load_h,), ly(2, 1), ly(2, 0), ly(3, 1), ly(3, 0)]
+        scalar_steps.extend([(empty_p, k) for k in HELPED])
+        gpsimd_steps.extend([(scale_p, k) for k in HELPED])
+        for k in range(len(out_steps)):
+            sync_steps.extend([(store, k)] + [(store_p, k - STORE_LAG)] * (k - STORE_LAG in HELPED))
 
         def bank_keys(job, a=0, b=0, *rest):
             if job in (turn_s, empty_s):
                 return [("s_bank", a, 0), ("s_bank", a, 1)]
             if job in (turn_g, empty_g):
                 return [("g_bank", a, 2 * b), ("g_bank", a, 2 * b + 1)]
+            if job is empty_p:
+                return [("p_bank", *out_tiles(a)[0])]
             if job in (second_product, finish):
-                return [("p_bank", *tile) for tile in out_tiles(a)]
+                return [("p_bank", *tile) for tile in out_tiles(a)[job is finish and a in HELPED :]]
             return [("u_bank", a, b)] if job in (first_pair, empty_u) else []
 
         keys = [key for step in tensor_steps for key in bank_keys(*step)]
@@ -432,8 +457,8 @@ def tile_curvature_scaled_pair_correction_d7_kernel(tc, G, S_bytes, S_scale, Y_b
                     needs.extend([(quant_a, *piece) for half in range(HALVES) for piece in a_pieces(half, row_tile // 2)])
                 return needs
             table = {
-                widen_s: [(load_s, a), (load_s_factor, a // PACK)] + [(widen_s_scalar, a)] * (a in SHARED),
-                widen_s_scalar: [(load_s, a), (load_s_factor, a // PACK)],
+                widen_s: [(load_s, a)] + [(load_s_factor, 1)] * (a // PACK) + [(widen_s_scalar, a)] * (a in SHARED),
+                widen_s_scalar: [(load_s, a)] + [(load_s_factor, 1)] * (a // PACK),
                 turn_s: [(widen_s, a)] + [(widen_s_scalar, a)] * (a in SHARED),
                 empty_s: [(turn_s, a), after.get((empty_s, a), (turn_s, a))],
                 quant_s: [(empty_s, a)],
@@ -449,6 +474,9 @@ def tile_curvature_scaled_pair_correction_d7_kernel(tc, G, S_bytes, S_scale, Y_b
                 quant_y: [(weave_y, a, b, *rest)],
                 finish: [(second_product, a), (load_h,)],
                 store: [(finish, a)],
+                empty_p: [(second_product, a)],
+                scale_p: [(empty_p, a), (load_h,)],
+                store_p: [(scale_p, a)],
             }
             return table.get(job, [])
 
@@ -480,11 +508,13 @@ def tile_curvature_scaled_pair_correction_d7_kernel(tc, G, S_bytes, S_scale, Y_b
                 second_product: (banks, []),
                 finish: ([("rows", a)], banks),
                 store: ([], [("rows", a)]),
+                empty_p: ([("plain", a)], banks),
+                store_p: ([], [("plain", a)]),
             }
             return table.get(job, ([], []))
 
         depth = {"wide": WIDE_BUFS, "turned": TURNED_BUFS, "a_woven": WOVEN_A_BUFS, "y_wide": WIDE_Y_BUFS, "rows": ROW_BUFS}
-        depth = {**depth, "y_woven": WOVEN_Y_BUFS, "gated": 1}
+        depth = {**depth, "y_woven": WOVEN_Y_BUFS, "gated": 1, "plain": PLAIN_BUFS}
         owners = {kind: [] for kind in [*depth, *range(BANKS)]}
         queues = [sync_steps, scalar_steps, vector_steps, gpsimd_steps, tensor_steps]
         written = set()

@@ -46,8 +46,9 @@ SINGLES = tuple(range(8, 16))
 HELPED = ()
 PLAIN_BUFS = 1
 STORE_LAG = 2
-SECOND_QUEUE = 99
+SECOND_QUEUE = 11
 FIRSTQ = 1
+QSPLIT = 1
 
 
 def tile_curvature_scaled_pair_correction_d7_kernel(tc, G, S_bytes, S_scale, Y_bytes, Y_scale, c, h, out):
@@ -281,10 +282,12 @@ def tile_curvature_scaled_pair_correction_d7_kernel(tc, G, S_bytes, S_scale, Y_b
                 dst, src = plain_views(woven, planes)
                 nc.scalar.copy(out=dst, in_=src)
 
-        def quant_a(half, chunk, count):
-            cols = slice(chunk * CHUNK, (chunk + count) * CHUNK)
+        def quant_a(half, chunk, count, first, rows):
+            at = chunk * CHUNK + first * P
             nc.vector.quantize_mx(
-                out=a_codes[:, 0, half, cols].bitcast(FP8X4), scales=a_scales[:, 0, half, cols], in_=tiles["a_woven", half, chunk]
+                out=a_codes[:, 0, half, at : at + rows * P].bitcast(FP8X4),
+                scales=a_scales[:, 0, half, at : at + rows * P],
+                in_=tiles["a_woven", half, chunk][:, first * P * PACK : (first + rows) * P * PACK],
             )
 
         def cast_y(strip, half):
@@ -385,7 +388,7 @@ def tile_curvature_scaled_pair_correction_d7_kernel(tc, G, S_bytes, S_scale, Y_b
         pairs = [(0, 0, False), (0, 1, False)] + [(u, 0, True) for u in range(2, 6)] + [(0, 2, False), (2, 2, False), (6, 0, True), (7, 0, True), (4, 2, False), (6, 2, False)] + [(u, 3, False) for u in (0, 2, 4, 6)]
         pieces = [(0, 0, 2), (1, 0, 2), (0, 2, 1), (1, 2, 1), (0, 3, 1), (1, 3, 1)]
         y_pieces = [(0, 0, 0, 2), (0, 0, 2, 2), (0, 1, 0, 4), (1, 0, 0, 4), (1, 1, 0, 4), (2, 0, 0, 4), (2, 1, 0, 2), (2, 1, 2, 2), (3, 1, 0, 4), (3, 0, 0, 4)]
-        out_steps = [(0, 0, False), (2, 0, False), (0, 1, False), (2, 1, False), (4, 0, True), (5, 0, True)] + [(2 * chunk, strip, False) for strip in (2, 3) for chunk in range(3)] + [(row, strip, True) for strip in (0, 2) for row in (6, 7)]
+        out_steps = [(0, 0, False), (2, 0, False), (0, 1, False), (2, 1, False), (4, 0, True), (5, 0, True)] + [(2 * chunk, strip, False) for strip in (2, 3) for chunk in range(3)] + [(row, strip, True) for row in (6, 7) for strip in (0, 2)]
         F = [(first_pair, *pair) for pair in pairs]
         per_round = [0, 0, 1, 1, 2, 2, 4]
         tensor_steps = []
@@ -404,11 +407,11 @@ def tile_curvature_scaled_pair_correction_d7_kernel(tc, G, S_bytes, S_scale, Y_b
         WY = lambda s, h, a=0, n=4: (weave_y, s, h, a, n)
         QY = lambda s, h, a=0, n=4: (quant_y, s, h, a, n)
         WA = lambda h, k, n=1: (weave_a, h, k, n)
-        QA = lambda h, k, n=1: (quant_a, h, k, n)
+        QA = lambda h, k, n=1, a=0, r=0: (quant_a, h, k, n, a, r or 2 * n)
         gated = [WY(1, 1), WY(2, 1, 0, 2), WY(2, 1, 2, 2), WY(3, 1), WA(0, 3)]
         gpsimd_steps = gated[1:]
         vector_steps = W[:4] + [Q[0], Q[1], U[3], Q[2], Q[3], W[4], Q[4], (invert_c,), Q[5], W[5], WY(0, 0, 0, 2), Q[6], WY(0, 0, 2, 2), Q[7], W[6], Q[8], QY(0, 0, 0, 2), QY(0, 0, 2, 2), Q[9], W[7], WA(0, 0, 2), Q[10], QA(0, 0, 2), Q[11], WY(0, 1), Q[12], (sort_g, 3, 0), Q[13], (sort_g, 3, 1), QY(0, 1), WY(1, 0), WA(0, 2), WA(1, 0, 2), QY(1, 0), QA(1, 0, 2), Q[14], Q[15], WY(1, 1), QA(0, 2), QY(1, 1)]
-        ahead = {2: [QA(1, 2), QY(2, 1, 0, 2)], 4: [QY(2, 0), QY(2, 1, 2, 2)], 8: [QY(3, 0), QY(3, 1)], 10: [QA(0, 3), QA(1, 3)]}
+        ahead = {2: [QA(1, 2), QY(2, 1, 0, 2)], 4: [QY(2, 0), QY(2, 1, 2, 2)], 8: [QY(3, 0), QY(3, 1)], 10: [QA(0, 3, 1, 0, 1)], 11: [QA(1, 3, 1, 0, 1)], 12: [QA(0, 3, 1, 1, 1)], 13: [QA(1, 3, 1, 1, 1)]}
         for k in range(len(out_steps)):
             vector_steps.extend(ahead.get(k, []) + [(finish, k)] * ((finish, k) not in vector_steps))
         extra = {U[2]: [C(0, 0)], U[5]: [C(0, 1)], E[3]: [C(1, 0)], U[13]: [C(1, 1)], E[9]: [C(2, 1)], E[11]: [WA(1, 2), C(2, 0), WY(2, 0)], E[13]: [C(3, 1), C(3, 0)], E[14]: [WY(3, 0)], E[15]: [WA(1, 3)]}
@@ -454,7 +457,7 @@ def tile_curvature_scaled_pair_correction_d7_kernel(tc, G, S_bytes, S_scale, Y_b
             if job is second_product:
                 needs = [(quant_y, *piece) for row_tile, strip in out_tiles(a) for piece in y_pieces if piece[0] == strip]
                 for row_tile, strip in out_tiles(a):
-                    needs.extend([(quant_a, *piece) for half in range(HALVES) for piece in a_pieces(half, row_tile // 2)])
+                    needs.extend([q for q in vector_steps if q[0] is quant_a and 0 <= row_tile - 2 * q[2] - q[4] < q[5]])
                 return needs
             table = {
                 widen_s: [(load_s, a)] + [(load_s_factor, 1)] * (a // PACK) + [(widen_s_scalar, a)] * (a in SHARED),
@@ -468,7 +471,7 @@ def tile_curvature_scaled_pair_correction_d7_kernel(tc, G, S_bytes, S_scale, Y_b
                 quant_g: [(empty_g, a, b)],
                 invert_c: [(load_c,)],
                 empty_u: [(first_pair, a, b, *rest), (invert_c,)],
-                quant_a: [(weave_a, a, b, *rest)],
+                quant_a: [(weave_a, a, b, *rest[:1])],
                 cast_y: [(load_y, a, b)],
                 weave_y: [(cast_y, a, b), (load_y_factor, b)] + earlier,
                 quant_y: [(weave_y, a, b, *rest)],
@@ -484,7 +487,7 @@ def tile_curvature_scaled_pair_correction_d7_kernel(tc, G, S_bytes, S_scale, Y_b
             banks = [(bank_of[key], key) for key in bank_keys(job, a, b)]
             wide, rows, ordered = [("wide", a)], [("rows", (a, b))], [("wide", (a, b))]
             turned = [("turned", (job in (empty_s, quant_s), a, b))]
-            y_planes, a_woven = [("y_wide", (a, b))], [("gated" if (weave_a, a, b, *rest) in gated else "a_woven", ("a", a, b))]
+            y_planes, a_woven = [("y_wide", (a, b))], [("gated" if (weave_a, a, b, *rest[:1]) in gated else "a_woven", ("a", a, b))]
             y_woven = [("gated" if (weave_y, a, b, *rest) in gated else "y_woven", (a, b, *rest))]
             others = [piece for piece in y_pieces if piece[:2] == (a, b) and piece[2:] != rest]
             table = {
@@ -503,7 +506,7 @@ def tile_curvature_scaled_pair_correction_d7_kernel(tc, G, S_bytes, S_scale, Y_b
                 cast_y: (y_planes, []),
                 weave_a: (a_woven, []),
                 weave_y: (y_woven, y_planes * all((weave_y, *piece) in written for piece in others)),
-                quant_a: ([], a_woven),
+                quant_a: ([], a_woven * all(q in written for q in vector_steps if q[:3] == (quant_a, a, b) and q[3:] != rest)),
                 quant_y: ([], y_woven),
                 second_product: (banks, []),
                 finish: ([("rows", a)], banks),

from contextlib import ExitStack

import concourse.mybir as mybir
from concourse.masks import make_identity

T, M, N = 1024, 1024, 2048
FLOPS = 2 * 2 * T * M * N

F32 = mybir.dt.float32
BF16 = mybir.dt.bfloat16
U32 = mybir.dt.uint32
U8 = mybir.dt.uint8
FP8 = mybir.dt.float8_e4m3fn
FP8X4 = mybir.dt.float8_e4m3fn_x4
MULT = mybir.AluOpType.mult
ADD = mybir.AluOpType.add
COPY = mybir.ActivationFunctionType.Copy

P = 128
QUAD = 32
PACK = 4
K_PASS = P * PACK
PASSES = N // K_PASS
HALVES = M // K_PASS
SLICES = HALVES * PACK
COL_BLOCKS = N // P
CHUNK = 256
CHUNKS = T // CHUNK
STRIP = 512
STRIPS = N // STRIP
RUN = 4
BANKS = 8
SPAN = 256

SHARED = (0, 1)
WIDE_BUFS = 5
TURNED_BUFS = 4
WOVEN_A_BUFS = 3
WIDE_Y_BUFS = 4
WOVEN_Y_BUFS = 3
ROW_BUFS = 2 * CHUNKS
SINGLE = 1
TABLE_WARM = 1
V2 = 1
SINGLES = tuple(range(8, 16))
HELPED = ()
PLAIN_BUFS = 1
STORE_LAG = 2
SECOND_QUEUE = 11
FIRSTQ = 1
QSPLIT = 1


def tile_curvature_scaled_pair_correction_d7_kernel(tc, G, S_bytes, S_scale, Y_bytes, Y_scale, c, h, out):
    nc = tc.nc
    with ExitStack() as ctx:
        keep = ctx.enter_context(tc.tile_pool(name="keep", bufs=1))
        work = ctx.enter_context(tc.tile_pool(name="work", bufs=3))
        psum = ctx.enter_context(tc.psum_pool(name="psum", bufs=1))
        ctx.enter_context(tc.manual_schedule())

        ident = keep.tile([P, P], F32, name="ident")
        make_identity(nc, ident[:])

        s_factor = [keep.tile([P, COL_BLOCKS], F32, name="s_factor%d" % half) for half in range(HALVES)]
        y_factor = [keep.tile([P, COL_BLOCKS], F32, name="y_factor%d" % half) for half in range(HALVES)]
        c_bf = keep.tile([P, HALVES, PACK], BF16, name="c_bf")
        c_inv = keep.tile([P, SLICES], F32, name="c_inv")
        h_all = keep.tile([P, N], BF16, name="h_all")
        a_planes = {}
        for half in range(HALVES):
            for two in range(CHUNKS // 2):
                a_planes[half, two] = keep.tile([P, PACK, 2 * CHUNK], BF16, name="a_planes%d%d" % (half, two))

        def operand(name, groups, passes, columns, codes_at, scales_at):
            count = groups * passes * columns
            codes = keep.tile([P, SPAN // 4 + count], U32, name=name + "_codes", align_bytes=SPAN)
            scales = keep.tile([P, SPAN + count], U8, name=name + "_scales", align_bytes=SPAN)
            codes = codes[:, codes_at // 4 : codes_at // 4 + count]
            scales = scales[:, scales_at : scales_at + count]
            return [part.rearrange("p (a g x) -> p a g x", a=groups, g=passes) for part in (codes, scales)]

        s_codes, s_scales = operand("s", SLICES, PASSES, P, SPAN // 4, 3 * SPAN // 4)
        g_codes, g_scales = operand("g", CHUNKS, PASSES, CHUNK, 0, SPAN // 2)
        a_codes, a_scales = operand("a", 1, HALVES, T, SPAN // 4, 3 * SPAN // 4)
        y_codes, y_scales = operand("y", STRIPS, HALVES, STRIP, 0, SPAN // 2)

        s_rows = S_bytes.rearrange("(half r j) n -> half j r n", half=HALVES, j=PACK)
        y_rows = Y_bytes.rearrange("(half p j) n -> half p j n", half=HALVES, j=PACK)
        tiles = {}

        def bank(key, shape):
            tiles[key] = psum.tile(shape, F32, name="bank%d" % bank_of[key], bufs=1)
            return tiles[key]

        def load_factor(queue, factor, table, half):
            rows = table[PACK * half : PACK * (half + 1), :].partition_broadcast(QUAD)
            queue.dma_start(out=factor[half][:], in_=rows.rearrange("r q k -> q r k"))

        load_factor(nc.scalar, s_factor, S_scale, 0)
        idle = keep.tile([P, 1], F32, name="idle")
        nc.scalar.activation(out=idle[:], in_=ident[:, 0:1], func=COPY)

        def load_s_factor(half):
            load_factor(nc.sync, s_factor, S_scale, half)

        def load_y_factor(half):
            load_factor(nc.sync, y_factor, Y_scale, half)

        def load_c():
            nc.sync.dma_start(out=c_bf[:], in_=c.rearrange("(half p j) -> p half j", half=HALVES, j=PACK))

        def load_h():
            nc.sync.dma_start(out=h_all[:], in_=h.partition_broadcast(P))

        def load_s(u):
            raw = keep.tile([P, N], U8, name="s_raw%d" % u)
            nc.sync.dma_start(out=raw[:], in_=s_rows[u // PACK, u % PACK])
            tiles["s_raw", u] = raw

        def load_g(chunk, b):
            raw = work.tile([P, CHUNK // P, 2 * K_PASS], BF16, name="g_raw", tag="rows", bufs=ROW_BUFS)
            rows = G[chunk * CHUNK : (chunk + 1) * CHUNK, 2 * K_PASS * b : 2 * K_PASS * (b + 1)]
            nc.sync.dma_start(out=raw[:], in_=rows.rearrange("(i r) n -> r i n", r=P))
            tiles["g_raw", chunk, b] = raw

        def load_y(strip, half):
            raw = keep.tile([P, PACK, STRIP], U8, name="y_raw%d%d" % (strip, half))
            nc.sync.dma_start(out=raw[:], in_=y_rows[half][:, :, strip * STRIP : (strip + 1) * STRIP])
            tiles["y_raw", strip, half] = raw

        def invert_c():
            nc.vector.reciprocal(out=c_inv[:], in_=c_bf[:].rearrange("p half j -> p (half j)"))

        def vector_passes(u):
            return PASSES // 2 if u in SHARED else PASSES

        def wide_s_tile(u):
            if ("s_wide", u) not in tiles:
                tiles["s_wide", u] = work.tile([P, N], BF16, name="s_wide", tag="wide", bufs=WIDE_BUFS)
            return tiles["s_wide", u]

        def widen_s(u):
            raw = tiles["s_raw", u]
            sorted_by_w = wide_s_tile(u)[:].rearrange("r (g w p e) -> r g p w e", g=PASSES, w=2, e=2)
            for q in range(P // QUAD):
                for g in range(vector_passes(u)):
                    block = PACK * g + q
                    nc.vector.tensor_scalar(
                        out=sorted_by_w[:, g, QUAD * q : QUAD * (q + 1)],
                        in0=raw[:, block * P : (block + 1) * P].bitcast(FP8).rearrange("r (p w e) -> r p w e", w=2, e=2),
                        scalar1=s_factor[u // PACK][:, block : block + 1],
                        scalar2=None,
                        op0=MULT,
                    )

        def widen_s_scalar(u):
            raw = tiles["s_raw", u]
            wide = wide_s_tile(u)
            for block in range(PACK * vector_passes(u), COL_BLOCKS):
                cols = slice(block * P, (block + 1) * P)
                factor = s_factor[u // PACK][:, block : block + 1]
                nc.scalar.activation(out=wide[:, cols], in_=raw[:, cols].bitcast(FP8), func=COPY, scale=factor)

        def turn_s(u):
            words = tiles["s_wide", u][:].bitcast(F32)
            for b in range(2):
                turned = bank(("s_bank", u, b), [P, 2, 2, P])
                for i in range(2):
                    g = 2 * b + i
                    for w in range(2):
                        if g < vector_passes(u):
                            src = words[:, 2 * P * g + P * w : 2 * P * g + P * (w + 1)]
                        else:
                            src = words[:, 2 * P * g + w : 2 * P * (g + 1) : 2]
                        nc.tensor.transpose(turned[:, w, i, :], src, ident[:])

        def join_words(copy, dst, turned):
            copy(out=dst, in_=turned[:].rearrange("p w a r -> p (a r) w"))

        def empty_s(u):
            copy = nc.vector.tensor_copy if (empty_s, u) in vector_steps else nc.scalar.copy
            joined = work.tile([P, 2, 2 * P, 2], F32, name="s_turned", tag="turned", bufs=TURNED_BUFS, align_bytes=64)
            tiles["s_turned", u] = joined
            for b in (1, 0):
                join_words(copy, joined[:, b], tiles["s_bank", u, b])

        def quant_s(u):
            nc.vector.quantize_mx(
                out=s_codes[:, u].rearrange("p g r -> p (g r)").bitcast(FP8X4),
                scales=s_scales[:, u].rearrange("p g r -> p (g r)"),
                in_=tiles["s_turned", u][:].rearrange("p b x w -> p (b x w)").bitcast(BF16),
            )

        def sort_g(chunk, b):
            ordered = work.tile([P, CHUNK // P, 2 * K_PASS], BF16, name="g_sorted", tag="wide", bufs=WIDE_BUFS)
            tiles["g_sorted", chunk, b] = ordered
            words = tiles["g_raw", chunk, b][:].rearrange("r i n -> r (i n)").bitcast(F32)
            nc.vector.tensor_copy(
                out=ordered[:].rearrange("r i n -> r (i n)").bitcast(F32).rearrange("r (x w p) -> r x w p", w=2, p=P),
                in_=words.rearrange("r (x p w) -> r x w p", w=2, p=P),
            )

        def turn_g(chunk, b):
            for g in range(2):
                turned = bank(("g_bank", chunk, 2 * b + g), [P, 2, 2, P])
                for i in range(2):
                    for w in range(2):
                        if (sort_g, chunk, b) in vector_steps:
                            words = tiles["g_sorted", chunk, b][:, i, :].bitcast(F32)
                            src = words[:, 2 * P * g + P * w : 2 * P * g + P * (w + 1)]
                        else:
                            words = tiles["g_raw", chunk, b][:, i, :].bitcast(F32)
                            src = words[:, 2 * P * g + w : 2 * P * (g + 1) : 2]
                        nc.tensor.transpose(turned[:, w, i, :], src, ident[:])

        def empty_g(chunk, b):
            copy = nc.vector.tensor_copy if (empty_g, chunk, b) in vector_steps else nc.scalar.copy
            joined = work.tile([P, 2, CHUNK, 2], F32, name="g_turned", tag="turned", bufs=TURNED_BUFS, align_bytes=64)
            tiles["g_turned", chunk, b] = joined
            for i in (1, 0):
                join_words(copy, joined[:, i], tiles["g_bank", chunk, 2 * b + i])

        def quant_g(chunk, b):
            nc.vector.quantize_mx(
                out=g_codes[:, chunk, 2 * b : 2 * b + 2].rearrange("p g t -> p (g t)").bitcast(FP8X4),
                scales=g_scales[:, chunk, 2 * b : 2 * b + 2].rearrange("p g t -> p (g t)"),
                in_=tiles["g_turned", chunk, b][:].rearrange("p g t w -> p (g t w)").bitcast(BF16),
            )

        def members(u, chunk, along_chunks):
            return [(u, chunk), (u, chunk + 1) if along_chunks else (u + 1, chunk)]

        def first_pair(u, chunk, along_chunks):
            sums = bank(("u_bank", u, chunk), [P, 2, CHUNK])
            for i, (v, k) in enumerate(members(u, chunk, along_chunks)):
                for g in range(PASSES):
                    nc.tensor.matmul_mx(
                        out=sums[:, i, :],
                        lhsT=s_codes[:, v, g, :].bitcast(FP8X4),
                        lhsT_scale=s_scales[:, v, g, :],
                        rhs=g_codes[:, k, g, :].bitcast(FP8X4),
                        rhs_scale=g_scales[:, k, g, :],
                        start=(g == 0),
                        stop=(g == PASSES - 1),
                    )

        def empty_u(u, chunk, along_chunks):
            sums = tiles["u_bank", u, chunk][:].rearrange("p i t -> p (i t)")
            width = 2 * CHUNK if along_chunks else CHUNK
            for i in range(2 * CHUNK // width):
                v = u + i
                at = chunk % 2 * CHUNK
                dst = a_planes[v // PACK, chunk // 2][:, v % PACK, at : at + width]
                src = sums[:, i * width : (i + 1) * width]
                if (empty_u, u, chunk, along_chunks) in vector_steps:
                    nc.vector.tensor_scalar(out=dst, in0=src, scalar1=c_inv[:, v : v + 1], scalar2=None, op0=MULT)
                else:
                    nc.scalar.activation(out=dst, in_=src, func=COPY, scale=c_inv[:, v : v + 1])

        def vector_views(woven, planes):
            return woven.rearrange("p (x i j) -> p x j i", i=RUN, j=PACK), planes.rearrange("p j (x i) -> p x j i", i=RUN)

        def plain_views(woven, planes):
            return woven.rearrange("p (n j) -> p n j", j=PACK), planes.rearrange("p j n -> p n j")

        def weave_a(half, chunk, count):
            step = (weave_a, half, chunk, count)
            name = "gated" if step in gated else "a_woven"
            tile = work.tile([P, 2 * CHUNK * PACK], BF16, name=name, bufs=depth[name], align_bytes=64)
            woven = tile[:, : count * CHUNK * PACK]
            tiles["a_woven", half, chunk] = woven
            at = chunk % 2 * CHUNK
            planes = a_planes[half, chunk // 2][:, :, at : at + count * CHUNK]
            if step in vector_steps:
                dst, src = vector_views(woven, planes)
                nc.vector.tensor_copy(out=dst, in_=src)
            elif step in gpsimd_steps:
                dst, src = plain_views(woven, planes)
                nc.gpsimd.tensor_scalar(out=dst, in0=src, scalar1=1.0, scalar2=0.0, op0=MULT, op1=ADD)
            else:
                dst, src = plain_views(woven, planes)
                nc.scalar.copy(out=dst, in_=src)

        def quant_a(half, chunk, count, first, rows):
            at = chunk * CHUNK + first * P
            nc.vector.quantize_mx(
                out=a_codes[:, 0, half, at : at + rows * P].bitcast(FP8X4),
                scales=a_scales[:, 0, half, at : at + rows * P],
                in_=tiles["a_woven", half, chunk][:, first * P * PACK : (first + rows) * P * PACK],
            )

        def cast_y(strip, half):
            wide = work.tile([P, PACK, STRIP], BF16, name="y_wide", bufs=WIDE_Y_BUFS)
            tiles["y_wide", strip, half] = wide
            raw = tiles["y_raw", strip, half][:].rearrange("p j n -> p (j n)")
            nc.scalar.copy(out=wide[:].rearrange("p j n -> p (j n)"), in_=raw.bitcast(FP8))

        def weave_y(strip, half, first, count):
            step = (weave_y, strip, half, first, count)
            name = "gated" if step in gated else "y_woven"
            tile = work.tile([P, STRIP * PACK], BF16, name=name, bufs=depth[name], align_bytes=64)
            tiles["y_woven", strip, half, first] = tile[:, : count * P * PACK]
            for i in range(count):
                woven = tile[:, P * PACK * i : P * PACK * (i + 1)]
                planes = tiles["y_wide", strip, half][:, :, P * (first + i) : P * (first + i + 1)]
                block = strip * (STRIP // P) + first + i
                factor = y_factor[half][:, block : block + 1]
                if step in vector_steps:
                    dst, src = vector_views(woven, planes)
                    nc.vector.tensor_scalar(out=dst, in0=src, scalar1=factor, scalar2=None, op0=MULT)
                elif step in gpsimd_steps:
                    dst, src = plain_views(woven, planes)
                    nc.gpsimd.tensor_scalar(out=dst, in0=src, scalar1=factor, scalar2=0.0, op0=MULT, op1=ADD)
                else:
                    dst, src = plain_views(woven, planes)
                    nc.scalar.activation(out=dst, in_=src, func=COPY, scale=factor)

        def quant_y(strip, half, first, count):
            cols = slice(first * P, (first + count) * P)
            nc.vector.quantize_mx(
                out=y_codes[:, strip, half, cols].bitcast(FP8X4),
                scales=y_scales[:, strip, half, cols],
                in_=tiles["y_woven", strip, half, first],
            )

        def out_tiles(k):
            row_tile, strip, along_row = out_steps[k]
            return [(row_tile, strip), (row_tile, strip + 1) if along_row else (row_tile + 1, strip)]

        def second_product(k):
            for row_tile, strip in out_tiles(k):
                sums = bank(("p_bank", row_tile, strip), [P, STRIP])
                rows = slice(row_tile * P, (row_tile + 1) * P)
                for half in range(HALVES):
                    nc.tensor.matmul_mx(
                        out=sums[:],
                        lhsT=a_codes[:, 0, half, rows].bitcast(FP8X4),
                        lhsT_scale=a_scales[:, 0, half, rows],
                        rhs=y_codes[:, strip, half].bitcast(FP8X4),
                        rhs_scale=y_scales[:, strip, half],
                        start=(half == 0),
                        stop=(half == HALVES - 1),
                    )

        def finish(k):
            res = work.tile([P, 2, STRIP], F32, name="res", tag="rows", bufs=ROW_BUFS)
            tiles["res", k] = res
            for i in (1,) if k in HELPED else (0, 1) if k in SINGLES else (1, 0):
                row_tile, strip = out_tiles(k)[i]
                factor = h_all[:, STRIP * strip : STRIP * (strip + 1)]
                nc.vector.tensor_tensor(out=res[:, i, :], in0=tiles["p_bank", row_tile, strip][:], in1=factor, op=MULT)

        def empty_p(k):
            res = work.tile([P, STRIP], F32, name="plain", bufs=PLAIN_BUFS)
            tiles["plain", k] = res
            nc.scalar.copy(out=res[:], in_=tiles[("p_bank", *out_tiles(k)[0])][:])

        def scale_p(k):
            strip = out_tiles(k)[0][1]
            res = tiles["plain", k]
            nc.gpsimd.tensor_tensor(out=res[:], in0=res[:], in1=h_all[:, STRIP * strip : STRIP * (strip + 1)], op=MULT)

        def store_p(k):
            nc.sync.dma_start(out=out_rows(k)[:, 0, :], in_=tiles["plain", k][:])

        def out_rows(k):
            row_tile, strip, along_row = out_steps[k]
            if along_row:
                rows = out[row_tile * P : (row_tile + 1) * P, STRIP * strip : STRIP * (strip + 2)]
                return rows.rearrange("r (i n) -> r i n", i=2)
            rows = out[row_tile * P : (row_tile + 2) * P, STRIP * strip : STRIP * (strip + 1)]
            return rows.rearrange("(i r) n -> r i n", i=2)

        def store(k):
            parts = [slice(1, 2)] if k in HELPED else [slice(0, 1), slice(1, 2)] if k in SINGLES else [slice(0, 2)]
            for n, part in enumerate(parts):
                queue = nc.scalar if k >= SECOND_QUEUE and n == 0 else nc.sync
                queue.dma_start(out=out_rows(k)[:, part, :], in_=tiles["res", k][:, part, :])

        emptying = {turn_s: empty_s, turn_g: empty_g, first_pair: empty_u}
        quantising = {turn_s: quant_s, turn_g: quant_g}


        S = [(turn_s, u) for u in range(SLICES)]
        Gp = [(turn_g, chunk, b) for chunk in range(CHUNKS) for b in range(2)]
        units = [S[0], Gp[0], S[1], Gp[1], Gp[2], Gp[3]] + S[2:6] + Gp[4:6] + S[6:] + Gp[6:]
        pairs = [(0, 0, False), (0, 1, False)] + [(u, 0, True) for u in range(2, 6)] + [(0, 2, False), (2, 2, False), (6, 0, True), (7, 0, True), (4, 2, False), (6, 2, False)] + [(u, 3, False) for u in (0, 2, 4, 6)]
        pieces = [(0, 0, 2), (1, 0, 2), (0, 2, 1), (1, 2, 1), (0, 3, 1), (1, 3, 1)]
        y_pieces = [(0, 0, 0, 2), (0, 0, 2, 2), (0, 1, 0, 4), (1, 0, 0, 4), (1, 1, 0, 4), (2, 0, 0, 4), (2, 1, 0, 2), (2, 1, 2, 2), (3, 1, 0, 4), (3, 0, 0, 4)]
        out_steps = [(0, 0, False), (2, 0, False), (0, 1, False), (2, 1, False), (4, 0, True), (5, 0, True)] + [(2 * chunk, strip, False) for strip in (2, 3) for chunk in range(3)] + [(row, strip, True) for row in (6, 7) for strip in (0, 2)]
        F = [(first_pair, *pair) for pair in pairs]
        per_round = [0, 0, 1, 1, 2, 2, 4]
        tensor_steps = []
        for r in range(len(per_round)):
            tensor_steps.extend(units[2 * r : 2 * r + 2] + F[sum(per_round[:r]) : sum(per_round[: r + 1])])
        late = {-1: units[14:16] + F[10:12], 1: F[12:14], 5: F[14:15], 7: F[15:16]}
        tensor_steps.extend(late.get(-1, []))
        for k in range(len(out_steps)):
            tensor_steps.extend([(second_product, k)] + late.get(k, []))
        filled = [(emptying[job], *index) for job, *index in tensor_steps if job in emptying]
        E = [(emptying[job], *index) for job, *index in F]
        U = [(emptying[job], *index) for job, *index in units]
        Q = [(quantising[job], *index) for job, *index in units]
        W = [(widen_s, u) for u in range(SLICES)]
        C = lambda s, h: (cast_y, s, h)
        WY = lambda s, h, a=0, n=4: (weave_y, s, h, a, n)
        QY = lambda s, h, a=0, n=4: (quant_y, s, h, a, n)
        WA = lambda h, k, n=1: (weave_a, h, k, n)
        QA = lambda h, k, n=1, a=0, r=0: (quant_a, h, k, n, a, r or 2 * n)
        gated = [WY(1, 1), WY(2, 1, 0, 2), WY(2, 1, 2, 2), WY(3, 1), WA(0, 3)]
        gpsimd_steps = gated[1:]
        vector_steps = W[:4] + [Q[0], Q[1], U[3], Q[2], Q[3], W[4], Q[4], (invert_c,), Q[5], W[5], WY(0, 0, 0, 2), Q[6], WY(0, 0, 2, 2), Q[7], W[6], Q[8], QY(0, 0, 0, 2), QY(0, 0, 2, 2), Q[9], W[7], WA(0, 0, 2), Q[10], QA(0, 0, 2), Q[11], WY(0, 1), Q[12], (sort_g, 3, 0), Q[13], (sort_g, 3, 1), QY(0, 1), WY(1, 0), WA(0, 2), WA(1, 0, 2), QY(1, 0), QA(1, 0, 2), Q[14], Q[15], WY(1, 1), QA(0, 2), QY(1, 1)]
        ahead = {2: [QA(1, 2), QY(2, 1, 0, 2)], 4: [QY(2, 0), QY(2, 1, 2, 2)], 8: [QY(3, 0), QY(3, 1)], 10: [QA(0, 3, 1, 0, 1)], 11: [QA(1, 3, 1, 0, 1)], 12: [QA(0, 3, 1, 1, 1)], 13: [QA(1, 3, 1, 1, 1)]}
        for k in range(len(out_steps)):
            vector_steps.extend(ahead.get(k, []) + [(finish, k)] * ((finish, k) not in vector_steps))
        extra = {U[2]: [C(0, 0)], U[5]: [C(0, 1)], E[3]: [C(1, 0)], U[13]: [C(1, 1)], E[9]: [C(2, 1)], E[11]: [WA(1, 2), C(2, 0), WY(2, 0)], E[13]: [C(3, 1), C(3, 0)], E[14]: [WY(3, 0)], E[15]: [WA(1, 3)]}
        scalar_steps = [(widen_s_scalar, u) for u in SHARED]
        for step in filled:
            scalar_steps.extend([step] * (step not in vector_steps) + extra.get(step, []))
        ls = [(load_s, u) for u in range(SLICES)]
        lg = [(load_g, chunk, b) for chunk in range(CHUNKS) for b in range(2)]
        ly = lambda s, h: (load_y, s, h)
        sync_steps = [ls[0], ls[1], ls[2], lg[0], ls[3], lg[1], ly(0, 0), lg[2], lg[3], (load_s_factor, 1), ls[4], (load_c,), ls[5], ly(0, 1), (load_y_factor, 0), ls[6], lg[4], lg[5], ls[7], (load_y_factor, 1), ly(1, 0), lg[6], lg[7], ly(1, 1), (load_h,), ly(2, 1), ly(2, 0), ly(3, 1), ly(3, 0)]
        scalar_steps.extend([(empty_p, k) for k in HELPED])
        gpsimd_steps.extend([(scale_p, k) for k in HELPED])
        for k in range(len(out_steps)):
            sync_steps.extend([(store, k)] + [(store_p, k - STORE_LAG)] * (k - STORE_LAG in HELPED))

        def bank_keys(job, a=0, b=0, *rest):
            if job in (turn_s, empty_s):
                return [("s_bank", a, 0), ("s_bank", a, 1)]
            if job in (turn_g, empty_g):
                return [("g_bank", a, 2 * b), ("g_bank", a, 2 * b + 1)]
            if job is empty_p:
                return [("p_bank", *out_tiles(a)[0])]
            if job in (second_product, finish):
                return [("p_bank", *tile) for tile in out_tiles(a)[job is finish and a in HELPED :]]
            return [("u_bank", a, b)] if job in (first_pair, empty_u) else []

        keys = [key for step in tensor_steps for key in bank_keys(*step)]
        bank_of = {key: k % BANKS for k, key in enumerate(keys)}

        empties = [(emptying[job], *index) for job, *index in units]
        after = dict(zip(empties[1:], empties))

        def a_pieces(half, chunk):
            return [piece for piece in pieces if piece[0] == half and piece[1] <= chunk < piece[1] + piece[2]]

        def inputs(job, a=0, b=0, *rest):
            step = (job, a, b, *rest)
            earlier = gated[: gated.index(step)] if step in gated else []
            if job is first_pair:
                return [need for v, k in members(a, b, *rest) for need in ((quant_s, v), (quant_g, k, 0), (quant_g, k, 1))]
            if job is weave_a:
                return earlier + [(empty_u, *pair) for pair in pairs if any(v // PACK == a and b <= k < b + rest[0] for v, k in members(*pair))]
            if job is second_product:
                needs = [(quant_y, *piece) for row_tile, strip in out_tiles(a) for piece in y_pieces if piece[0] == strip]
                for row_tile, strip in out_tiles(a):
                    needs.extend([q for q in vector_steps if q[0] is quant_a and 0 <= row_tile - 2 * q[2] - q[4] < q[5]])
                return needs
            table = {
                widen_s: [(load_s, a)] + [(load_s_factor, 1)] * (a // PACK) + [(widen_s_scalar, a)] * (a in SHARED),
                widen_s_scalar: [(load_s, a)] + [(load_s_factor, 1)] * (a // PACK),
                turn_s: [(widen_s, a)] + [(widen_s_scalar, a)] * (a in SHARED),
                empty_s: [(turn_s, a), after.get((empty_s, a), (turn_s, a))],
                quant_s: [(empty_s, a)],
                sort_g: [(load_g, a, b)],
                turn_g: [(load_g, a, b)] + [(sort_g, a, b)] * ((sort_g, a, b) in vector_steps),
                empty_g: [(turn_g, a, b), after.get((empty_g, a, b), (turn_g, a, b))],
                quant_g: [(empty_g, a, b)],
                invert_c: [(load_c,)],
                empty_u: [(first_pair, a, b, *rest), (invert_c,)],
                quant_a: [(weave_a, a, b, *rest[:1])],
                cast_y: [(load_y, a, b)],
                weave_y: [(cast_y, a, b), (load_y_factor, b)] + earlier,
                quant_y: [(weave_y, a, b, *rest)],
                finish: [(second_product, a), (load_h,)],
                store: [(finish, a)],
                empty_p: [(second_product, a)],
                scale_p: [(empty_p, a), (load_h,)],
                store_p: [(scale_p, a)],
            }
            return table.get(job, [])

        def buffers(job, a=0, b=0, *rest):
            banks = [(bank_of[key], key) for key in bank_keys(job, a, b)]
            wide, rows, ordered = [("wide", a)], [("rows", (a, b))], [("wide", (a, b))]
            turned = [("turned", (job in (empty_s, quant_s), a, b))]
            y_planes, a_woven = [("y_wide", (a, b))], [("gated" if (weave_a, a, b, *rest[:1]) in gated else "a_woven", ("a", a, b))]
            y_woven = [("gated" if (weave_y, a, b, *rest) in gated else "y_woven", (a, b, *rest))]
            others = [piece for piece in y_pieces if piece[:2] == (a, b) and piece[2:] != rest]
            table = {
                widen_s: (wide * (a not in SHARED), []),
                widen_s_scalar: (wide, []),
                turn_s: (banks, wide),
                load_g: (rows, []),
                sort_g: (ordered, []),
                turn_g: (banks, rows + ordered),
                empty_s: (turned, banks),
                empty_g: (turned, banks),
                quant_s: ([], turned),
                quant_g: ([], turned),
                first_pair: (banks, []),
                empty_u: ([], banks),
                cast_y: (y_planes, []),
                weave_a: (a_woven, []),
                weave_y: (y_woven, y_planes * all((weave_y, *piece) in written for piece in others)),
                quant_a: ([], a_woven * all(q in written for q in vector_steps if q[:3] == (quant_a, a, b) and q[3:] != rest)),
                quant_y: ([], y_woven),
                second_product: (banks, []),
                finish: ([("rows", a)], banks),
                store: ([], [("rows", a)]),
                empty_p: ([("plain", a)], banks),
                store_p: ([], [("plain", a)]),
            }
            return table.get(job, ([], []))

        depth = {"wide": WIDE_BUFS, "turned": TURNED_BUFS, "a_woven": WOVEN_A_BUFS, "y_wide": WIDE_Y_BUFS, "rows": ROW_BUFS}
        depth = {**depth, "y_woven": WOVEN_Y_BUFS, "gated": 1, "plain": PLAIN_BUFS}
        owners = {kind: [] for kind in [*depth, *range(BANKS)]}
        queues = [sync_steps, scalar_steps, vector_steps, gpsimd_steps, tensor_steps]
        written = set()
        given = set()
        for sweep in range(sum(len(queue) for queue in queues)):
            for queue in queues:
                for step in [step for step in queue if step not in written][:1]:
                    takes, gives = buffers(*step)
                    before = [owners[kind][-depth.get(kind, 1) :] for kind, owner in takes]
                    room = all(len(last) < depth.get(kind, 1) or last[0] in given for last, (kind, owner) in zip(before, takes))
                    if room and all(need in written for need in inputs(*step)):
                        step[0](*step[1:])
                        written.add(step)
                        given.update(gives)
                        for buffer in takes:
                            owners[buffer[0]].append(buffer)
        assert len(written) == sum(len(queue) for queue in queues), "stuck"
